import numpy as np, ml_dtypes
CORES = [13,21,141,149]
N = 4
BF = ml_dtypes.bfloat16
def gentries(a):
    return np.ascontiguousarray(a.reshape(8, 16, -1).transpose(0, 2, 1)).reshape(8, -1)
def gtable(e):
    e = np.asarray(e); return np.ascontiguousarray(e.reshape(8, -1, 16).transpose(0, 2, 1)).reshape(128, -1).astype(np.int32)
C, T, G, K1, K2, SC, ST, EPS, RO, BO = 288, 640, 128, 112, 160, 72, 120, 12, 4, 256
H = (N - 1) * G
WB = 16 * C + H
def ghosts(a):
    r, g = np.arange(N), np.arange(8)
    return np.concatenate([a[..., (d - 1) * G:d * G][r ^ d][:, g ^ d] for d in range(1, N)], axis=-1)
def ghostly(rng, c):
    u = np.ones(16 * H, bool); u[c[c >= 16 * T] - 16 * T] = False
    i = np.flatnonzero(c < 0); c[i] = 16 * T + rng.permutation(np.flatnonzero(u))[:len(i)]
    return c
def links(rng, room, share, far):
    ct = np.full((N, 8, 16 * C), -1, np.int64); tv = np.full((N, 8, 16 * T), WB, np.int64)
    for q in range(N):
        for g in range(8):
            for d in range(1, N):
                h = (d - 1) * G + np.flatnonzero(rng.random(G) < share); s = 16 * (d - 1) * G + rng.permutation(16 * G)[:len(h)]
                ct[q, g, h] = 16 * T + s; tv[q ^ d, g ^ d, s] = 16 * C + h
    for q in range(N):
        for g in range(8):
            o = rng.permutation(np.flatnonzero(ct[q, g] < 0)); nf = int(far * len(o))
            rk = np.argsort(rng.random((T, 16)), axis=1)
            own = rng.permutation(np.flatnonzero((rk < room[q, g][:, None]).reshape(-1) & (tv[q, g] == WB)))[:len(o) - nf]
            o = o[:len(own)]; ct[q, g, o] = own; tv[q, g, own] = o
            ct[q, g] = ghostly(rng, ct[q, g])
    return ct, tv
def stir(rng, tv, share):
    for q in range(N):
        for g in range(8):
            s = np.flatnonzero((tv[q, g] < WB) & (rng.random(16 * T) < share)); tv[q, g, s] = rng.permutation(tv[q, g, s])
    return tv
def see(x, ct):
    return np.take_along_axis(np.concatenate([x, ghosts(x)], axis=3), (ct >> 4)[:, :, None, :], 3)
def whole(rng, lo, hi, *shape):
    return rng.integers(lo, hi, shape, dtype=np.int16)
def geo(rng, ct):
    x = whole(rng, 60, 192, N, 8, 16, T); pose = np.repeat(whole(rng, -60, 61, N, 8, 16, C), 16, axis=3)
    e = (whole(rng, -64, 65, N, 8, 16, 16 * C) * whole(rng, 0, EPS + 4, N, 8, 1, 16 * C)) >> 6
    bad = rng.random((N, 8, 1, 16 * C)) < np.repeat(rng.choice(np.array([0.03, 0.1, 0.2, 0.75]), (N, 8, 1, C), p=[0.35, 0.35, 0.2, 0.1]), 16, axis=3)
    o = np.where(bad, whole(rng, 0, 256, N, 8, 16, 16 * C), see(x, ct) - pose + e)
    x0 = np.where(rng.random((N, 8, 1, T)) < 0.15, whole(rng, 0, 256, N, 8, 16, T), x + whole(rng, -2, 3, N, 8, 16, T))
    return o, x0
def pack(o, x, ct, tv):
    return {"obs": np.clip(o, 0, 255).reshape(N, 128, 16 * C).astype(np.float32).astype(BF), "x0": np.clip(x, 0, 255).reshape(N, 128, T).astype(np.float32).astype(BF),
            "ct": np.stack([gtable(a) for a in ct]), "tv": np.stack([gtable(a) for a in tv])}
def setup_inputs(rng):
    ct, tv = links(rng, np.minimum(rng.integers(2, 24, (N, 8, T)), 16), 0.6, 0.08); tv = stir(rng, tv, 0.06)
    o, x0 = geo(rng, ct)
    return pack(o, x0, ct, tv)
def setup_inputs_spread(rng):
    ct, tv = links(rng, rng.integers(1, 17, (N, 8, T)), 0.8, 0.15); tv = stir(rng, tv, 0.1)
    x = np.minimum(np.exp2(8 * rng.random((N, 8, 1, T))) * rng.random((N, 8, 16, T)), 255).astype(np.int16)
    pose = np.repeat((np.exp2(6 * rng.random((N, 8, 1, C))) * (rng.random((N, 8, 16, C)) - 0.6)).astype(np.int16), 16, axis=3)
    e = (np.exp2(6 * rng.random((N, 8, 1, 16 * C), dtype=np.float32)) * (rng.random((N, 8, 16, 16 * C), dtype=np.float32) - 0.5)).astype(np.int16)
    o = see(x, ct) - pose + e; o = np.where(rng.random((N, 8, 1, 16 * C)) < 0.1, whole(rng, 0, 256, N, 8, 16, 16 * C), o)
    x = np.where(rng.random((N, 8, 1, T)) < 0.1, whole(rng, 0, 256, N, 8, 16, T), x)
    return pack(o, x, ct, tv)
def setup_inputs_ends(rng):
    a = 16 * (C // 3); top = 16 * (T + H); sl = np.concatenate([np.arange(a), np.arange(16 * T - a, 16 * T), np.arange(top - (16 * C - 2 * a), top)])
    ct = np.zeros((N, 8, 16 * C), np.int64); tv = np.full((N, 8, 16 * T), WB, np.int64)
    for q in range(N):
        for g in range(8):
            p = rng.permutation(16 * C); j = int(np.argmin(p)); p[j] = p[0]; p[0] = 0
            ct[q, g, p] = sl; tv[q, g, sl[:2 * a]] = p[:2 * a]
            s = 1 + rng.permutation(2 * a - 1)[:H // 2]; tv[q, g, sl[s]] = WB - 1 - rng.permutation(H // 2)[:len(s)]
    rk = np.argsort(rng.random((N, 8, 16)), axis=2)[..., None]
    x = (255 * (rng.random((N, 8, 16, T)) < np.where(rk == 0, 0.875, np.where(rk == 1, 0.125, 0.5)))).astype(np.int16)
    s = see(x, ct); pf = rng.choice(np.array([0.0, 0.0, 0.05, 0.1, 0.15, 0.8]), (N, 8, 1, 16 * C))
    o = np.where(rng.random(s.shape, dtype=np.float32) < pf, 255 - s, s)
    cs = np.repeat(rng.random((N, 8, 16, C)) < np.where(rk == 0, 0.25, np.where(rk == 1, 0.75, 0.5)), 16, axis=3) ^ (rng.random(s.shape, dtype=np.float32) < 0.1)
    o = np.where(rk < 4, 255 * cs, o); last = 255 * (np.arange(16) == 15)
    for c in (0, C - 1):
        o[..., 16 * c:16 * c + 16] = np.where(rk == 0, last, np.where(rk == 1, 255 - last, s[..., 16 * c:16 * c + 16]))
    return pack(o, x, ct, tv)
def setup_inputs_corners(rng):
    ct = np.full((N, 8, 16 * C), -1, np.int64); tv = np.full((N, 8, 16 * T), WB, np.int64); far = np.zeros((N, 8, T), bool)
    pa = [16 * int(rng.integers(G // 16, G // 8)) + rng.permutation(16) for q in range(N)]; plant = []
    for q in range(N):
        for g in range(8):
            k = (g + q) % 8
            if 1 <= k <= 3:
                rf = k if q % 2 else 3 * K1 - C + (0, -1, 1)[k - 1]
                t = rng.permutation(T)[:(rf + 11) // 12]; far[q, g, t] = True; cs = rng.permutation(SC); s = 16 * t[:, None] + np.arange(16)
                ct[q, g, 16 * cs[:len(t)] + rng.integers(0, 16, len(t))] = 16 * t + rng.integers(0, 16, len(t))
                tv[q, g, s[:, :12].reshape(-1)[:rf]] = 16 * cs[:rf] + rng.integers(0, 16, rf)
                tv[q, g, s[:, 12:].reshape(-1)] = 16 * C + rng.permutation(H)[:4 * len(t)]
            elif 4 <= k <= 6:
                t = rng.permutation(T)[:K2 + k - 5]; s = (16 * t[:, None] + np.argsort(rng.random((len(t), 16)), axis=1))
                s = np.concatenate([s[:, 0], rng.permutation(s[:, 1:].reshape(-1))])[:8 * K1]
                p = rng.permutation(16 * K1)[:len(s)]; ct[q, g, p] = s; tv[q, g, s] = p
            elif k == 7:
                room = rng.choice(np.array([0, 1, 2, 3, 15, 16]), T); rk = np.argsort(rng.random((T, 16)), axis=1)
                s = np.flatnonzero((rk < room[:, None]).reshape(-1))[:16 * C]; p = rng.permutation(16 * C)[:len(s)]
                ct[q, g, p] = s; tv[q, g, s] = p
            elif q % 2:
                t = rng.permutation(T)[:6]; z = rng.permutation(16); a = pa[q]; f = 16 * int(rng.integers(G // 8, SC)) + rng.permutation(16)
                e = 16 * int(rng.integers(2 * K1, C)) + rng.permutation(16)[:3]; s = 16 * t[:, None] + np.argsort(rng.random((6, 16)), axis=1)
                ct[q, g, z[:10]] = s[0, :10]; ct[q, g, z[10:]] = s[1, :6]; ct[q, g, a[:10]] = s[1, 6:]; ct[q, g, f] = s[2]; ct[q, g, e] = s[3:, 0]
                s = 16 * t[:, None] + np.argsort(rng.random((6, 16)), axis=1)
                tv[q, g, s[0, :5]] = z[:5]; tv[q, g, s[1, :4]] = f[:4]; tv[q, g, s[2, 0]] = a[0]; tv[q, g, s[3, :4]] = f[4:8]; tv[q, g, s[4, :4]] = 16 * C + pa[q ^ 2][:4]
                plant.append((q, g, t, z, a, f))
            ct[q, g] = ghostly(rng, ct[q, g])
    o, x0 = geo(rng, ct); x0 = np.where(far[:, :, None, :], 255, x0)
    for q, g, t, z, a, f in plant:
        m = 80 * rng.integers(0, 2, 16); w = rng.integers(70, 100, (3, 16)); w[1] += m; w[2] += 80 - m; pose = rng.integers(-60, 61, (3, 16))
        x0[q, g][:, t[:3]] = w.T
        for p, j, c in ((z[:10], 0, 0), (z[10:], 1, 0), (a[:10], 1, 1), (f, 2, 2)):
            o[q, g][:, p] = (w[j] - pose[c])[:, None]
    return pack(o, x0, ct, tv)
def setup_inputs_crowd(rng):
    ct, tv = links(rng, np.full((N, 8, T), 16), 0.6, 0.05)
    for q in range(N):
        for g in range(0, 8, 2):
            c = (16 * rng.permutation(T)[:C, None] + np.argsort(rng.random((C, 16)), axis=1)).reshape(-1)
            tv[q, g] = WB; tv[q, g, c] = np.arange(16 * C)
            m = np.flatnonzero(rng.random(C) < 0.5); p = 16 * m + rng.integers(0, 16, len(m))
            tv[q, g, c[p]] = WB; c[p] = -1; ct[q, g] = ghostly(rng, c)
    o, x0 = geo(rng, ct)
    return pack(o, x0, ct, tv)
def setup_inputs_ties(rng):
    ct, tv = links(rng, rng.choice(np.array([1, 2, 3, 4, 8, 16]), (N, 8, T)), 0.7, 0.05)
    x = whole(rng, 80, 171, N, 8, 16, T); pose = np.repeat(whole(rng, -50, 51, N, 8, 16, C), 16, axis=3)
    nf = rng.choice(np.array([0, 5, 6, 7, 10, 16]), (N, 8, C, 1), p=[0.05, 0.15, 0.25, 0.15, 0.2, 0.2])
    m = np.where(np.argsort(rng.random((N, 8, C, 16)), axis=3) < nf, 4, 5).reshape(N, 8, 1, 16 * C)
    r = np.argsort(rng.random((N, 8, 16 * C, 16), dtype=np.float32), axis=3).transpose(0, 1, 3, 2)
    sg = 2 * whole(rng, 0, 2, N, 8, 16, 16 * C) - 1
    e = np.where(r < m, sg * (EPS + 1), np.where(rng.random(sg.shape, dtype=np.float32) < 0.8, 0, sg * EPS))
    return pack(see(x, ct) - pose + e, x, ct, tv)
def check_inputs(d):
    bad = []
    for k, hi in (("obs", 255), ("x0", 255), ("ct", 16 * (T + H) - 1), ("tv", WB)):
        v = np.asarray(d[k]).astype(np.float64)
        if not np.all((v >= 0) & (v <= hi) & (v == np.floor(v))): bad.append("range of " + k)
    s = np.sort(np.stack([gentries(a) for a in d["ct"]]), axis=-1)
    if np.any(s[..., 1:] == s[..., :-1]): bad.append("entries of ct differ")
    s = np.sort(np.stack([gentries(a) for a in d["tv"]]), axis=-1)
    if np.any((s[..., 1:] == s[..., :-1]) & (s[..., 1:] < WB)): bad.append("entries of tv that are not empty differ")
    return bad
def first(flag, start, k):
    f = np.roll(flag, -start, axis=-1); ix = np.argsort(~f, axis=-1, kind="stable")[..., :k]
    return (ix + start) % flag.shape[-1], np.take_along_axis(f, ix, -1)
def med(v, e):
    n = np.sum(e.reshape(N, 8, -1, 16), axis=3)
    s = np.sort(np.where(e[:, :, None, :], v, np.int16(9999)).reshape(N, 8, 16, -1, 16), axis=4)
    i = np.maximum((n + 1) // 2 - 1, 0)
    return np.take_along_axis(s, i[:, :, None, :, None], 4)[..., 0], n
def reference(obs, x0, ct, tv):
    o = obs.astype(np.int16).reshape(N, 8, 16, 16 * C); x = x0.astype(np.int16).reshape(N, 8, 16, T); xe = np.ones((N, 8, T), bool)
    lk = np.stack([gentries(a) for a in ct]).astype(np.int64); vw = np.stack([gentries(a) for a in tv]).astype(np.int64)
    live = np.ones((N, 8, 16 * C), bool); b = np.zeros((N, 8, 16, 16 * C), np.int16); be = np.zeros((N, 8, 16 * C), bool)
    fc = np.ones((N, 8, C), bool); ft = np.zeros((N, 8, T), bool)
    qi = np.arange(N)[:, None, None]; gi = np.arange(8)[None, :, None]; s16 = np.arange(16)
    for u in range(RO):
        ix, ok = first(fc, u * SC, K1); okp = np.repeat(ok, 16, axis=2)
        pt = (16 * ix[..., None] + s16).reshape(N, 8, 16 * K1); pt4 = pt[:, :, None, :]
        tr = np.take_along_axis(lk, pt, 2) >> 4
        wx = np.concatenate([x, ghosts(x)], axis=3); we = np.concatenate([xe, ghosts(xe)], axis=2)
        op = np.take_along_axis(o, pt4, 3); al = np.take_along_axis(live, pt, 2)
        ex = al & np.take_along_axis(we, tr, 2)
        dif = np.take_along_axis(wx, tr[:, :, None, :], 3) - op
        p, n = med(dif, ex); pp = np.repeat(p, 16, axis=3)
        fit = ex & (np.sum(np.abs(dif - pp) <= EPS, axis=2) >= 12)
        good = np.repeat(np.sum(fit.reshape(N, 8, K1, 16), axis=3) >= 6, 16, axis=2)
        al2 = al & ~(good & ex & ~fit)
        np.put_along_axis(live, pt, np.where(okp, al2, al), 2)
        np.put_along_axis(be, pt, np.where(okp, good & al2, np.take_along_axis(be, pt, 2)), 2)
        np.put_along_axis(b, pt4, np.where(okp[:, :, None, :], np.clip(pp + op, 0, 255), np.take_along_axis(b, pt4, 3)), 3)
        np.put_along_axis(fc, ix, False, 2)
        mk = np.zeros((N, 8, T + H), bool); mk[qi, gi, np.where(okp, tr, T)] = True
        ft = ft | mk[..., :T]
        ix, ok = first(ft, u * ST, K2); okp = np.repeat(ok, 16, axis=2); ix4 = ix[:, :, None, :]
        sl = (16 * ix[..., None] + s16).reshape(N, 8, 16 * K2); v = np.take_along_axis(vw, sl, 2)
        wb = np.concatenate([b, ghosts(b), np.zeros((N, 8, 16, 1), np.int16)], axis=3)
        we = np.concatenate([be, ghosts(be), np.zeros((N, 8, 1), bool)], axis=2)
        ex = np.take_along_axis(we, v, 2); bv = np.take_along_axis(wb, v[:, :, None, :], 3)
        m, n = med(bv, ex); has = n >= 3
        fit = np.sum(np.abs(bv - np.repeat(m, 16, axis=3)) <= EPS, axis=2) >= 12
        rej = okp & np.repeat(has, 16, axis=2) & ex & ~fit
        ox = np.take_along_axis(x, ix4, 3); oe = np.take_along_axis(xe, ix, 2)
        chg = ok & ((has != oe) | (has & oe & np.any(m != ox, axis=2)))
        np.put_along_axis(x, ix4, np.where((ok & has)[:, :, None, :], m, ox), 3)
        np.put_along_axis(xe, ix, np.where(ok, has, oe), 2)
        np.put_along_axis(vw, sl, np.where(rej, WB, v), 2)
        kill = np.zeros((N, 8, WB + 1), bool); kill[qi, gi, np.where(rej, v, WB)] = True
        live = live & ~kill[..., :16 * C]; be = be & ~kill[..., :16 * C]
        np.put_along_axis(ft, ix, False, 2)
        mk = np.zeros((N, 8, WB + 1), bool); mk[qi, gi, np.where(np.repeat(chg, 16, axis=2), v, WB)] = True
        fc = fc | np.any(mk[..., :16 * C].reshape(N, 8, C, 16), axis=3)
    yx = np.where(xe[:, :, None, :], x, 512).reshape(N, 128, T)
    yb = np.where(be[:, :, None, 16 * C - BO:], b[..., 16 * C - BO:], 512).reshape(N, 128, BO)
    yc = np.sum(live.reshape(N, 8, C, 16), axis=3) + 32 * fc
    yt = np.sum((vw < WB).reshape(N, 8, T, 16), axis=3) + 32 * ft
    return {"yx": yx.astype(np.float32).astype(BF), "yb": yb.astype(np.float32).astype(BF), "yc": yc.astype(np.float32), "yt": yt.astype(np.float32)}

@@ -1,0 +1,774 @@
+from concourse.mybir import AluOpType, AxisListType, ActivationFunctionType
+from concourse.bass import DstId, RemoteDMATransfer
+A = AluOpType
+F = ActivationFunctionType
+BF, F32, I32, U16 = "bfloat16", "float32", "int32", "uint16"
+C, NT, K1, K2, RO = 288, 640, 112, 160, 4
+XN = 1184
+EC = 312
+MW = 13824
+SW = 1040
+ONE = 1.278465
+CH1 = [(0, 64), (64, 48)]
+CH2 = [(0, 64), (64, 64), (128, 32)]
+T_CYC, T_GATH, T_SCAT, T_FIX, T_PE, T_HOP, T_DMA, T_KB, T_REMOTE = 0.001, 1.5, 3.5, 0.05, 0.0006, 0.08, 2.0, 288.0, 2.5
+LA, NA, SO, EA, SA = True, 0, True, (1, 1, 0, 1), False
+MA, PA, OA = 96, 96, 64
+PLAN, TURNS = {}, 6
+CUTS = sorted(set([k0 for k0, nk in CH2] + [MA, K2] + list(range(0, MA, 48))))
+CALLS = list(zip(CUTS[:-1], CUTS[1:]))
+SB = {
+    "WA": (MW + 768, F32), "WB": (MW + 1024, BF), "ONA": (896, F32), "ONM": (768, F32), "ONB": (1024, BF),
+    "O": (4608, BF), "LOG": (400 + RO * 1792, BF), "OG": (1792, BF), "PG": (2560, BF), "FS": (640, BF), "FN": (16, F32),
+    "M32": (864, F32), "M16": (864, BF), "MC": (864, BF), "Z32": (864, F32), "Z16": (864, BF),
+    "CTL": (432, F32), "CTO": (432, F32), "OO": (432, F32), "PTR": (432, BF), "PTD": (448, BF),
+    "TC": (800, F32), "LO": (800, BF), "LW": (1280, F32), "TID": (640, F32), "DI": (160, F32), "X": (1200, BF),
+    "EXP": (1024, BF), "SEL": (2048, BF), "CP": (1024, BF), "D": (1792, BF), "BG": (2560, BF), "S": (8 * SW, BF), "KP": (640, BF), "DG": (160, BF),
+    "ID": (128, BF), "NI": (128, BF), "BO": (128, BF), "M1": (128, BF), "M2": (128, BF), "I200": (128, BF),
+    "IXN": (128, BF), "PM": (384, BF), "TRI": (512, BF), "ZE": (144, BF), "RQ": (128, F32), "RG": (128, F32),
+    "SI": (16, I32), "SF": (32, F32), "D16": (16, F32), "CI": (640, I32),
+    "SNX": (384, BF), "SNB": (384, BF), "SG": (384, BF),
+    "DU1": (112, F32), "DU2": (160, F32), "RB": (40, F32), "RB1": (40, F32), "OFF": (16, F32), "DM": (16, F32),
+    "TH5": (16, F32), "PB": (16, F32), "FL": (288, BF), "QC": (304, BF), "NP": (288, BF), "CAP": (288, BF),
+    "JK": (288, BF), "FG": (288, BF), "ACC": (8, F32), "W1": (16, F32), "W2": (16, F32), "W3": (16, F32),
+    "WL": (8, U16), "XO": (112, U16), "OU": (112, U16), "FU": (112, U16), "XF": (112, F32), "FO": (112, F32),
+    "UH": (160, BF), "TH1": (160, F32), "LV": (112, BF), "LU": (112, BF), "FIT": (112, BF), "NONE": (112, BF),
+    "DIE": (112, F32), "KI": (16, I32), "PU": (16, U16), "PC": (160, BF), "PT": (384, BF),
+    "G1": (32, F32), "G2": (32, F32), "GU": (32, U16),
+    "FB": (40, BF), "FA": (40, BF), "PP": (40, BF), "B1": (40, F32), "B2": (40, F32), "BU": (40, U16),
+    "L1": (160, F32), "L2": (160, F32), "TL": (16, U16), "CF": (160, F32), "CU": (160, U16), "LO4": (160, F32),
+    "IU": (160, U16), "MO": (160, BF), "PEN": (160, BF), "IF": (128, F32), "I864": (128, BF), "IBG": (128, BF), "NH": (160, BF), "XNW": (160, BF), "NE": (160, BF),
+    "SN": (160, BF), "DL": (160, F32), "REJ": (160, F32), "MU": (160, U16), "YT": (40, F32),
+}
+SCRATCH = {k: ("sbuf", [128, v[0]], v[1]) for k, v in SB.items()}
+for _b in range(8):
+    SCRATCH["PS%d" % _b] = ("psum", [128, 512], F32)
+NDMA = 40
+SEMAPHORES = ["cv", "ca", "ct", "cg", "loc0", "loc1"] + ["arr%d" % i for i in range(8)] + ["dm%d" % i for i in range(NDMA)]
+
+
+def relay_of(T, topo, r, d):
+    src = T.cores[r]
+    far = [e for e in (1, 2, 3) if not topo.may_write(src, T.cores[r ^ e])]
+    if d not in far:
+        return None
+    can = [c for c in topo.cores_of(src) if T.rank_of(c) is None and topo.may_write(c, T.cores[r ^ d])]
+    can.sort(key=lambda c: (topo.die(c) != topo.die(src), c))
+    return can[far.index(d) % len(can)]
+
+
+def bits(engines):
+    return sum(1 << e for e in engines)
+
+
+def landing(T, n, d):
+    return T.X[:, 800 + 128 * (d - 1):800 + 128 * d] if n % 2 == 0 else T.LOG[:, 128 * (d - 1):128 * d]
+
+
+def relay_program(g, core, T, topo):
+    for r in range(len(T.cores)):
+        for d in (1, 2, 3):
+            if relay_of(T, topo, r, d) == core:
+                dst = T.cores[r ^ d]
+                rid, pid = topo.addr(dst, core)
+                eng = topo.engines(core, dst)
+                for n in range(2 * RO):
+                    g.wait_ge(T.sem["arr%d" % n], 4)
+                    g.remote_dma(landing(T, n, d), T.O[:, 128 * n:128 * n + 128], T.sem["arr%d" % n], T.sem.loc0,
+                                 pid, rid, bits(eng))
+                g.wait_ge(T.sem.loc0, 2 * RO * len(eng))
+
+
+def rank_program(g, core, T, topo):
+    rank = T.rank_of(core)
+    if rank is None:
+        relay_program(g, core, T, topo)
+        return
+    Q = {"v": g.vector, "a": g.scalar, "t": g.tensor, "g": g, "s": g.sync}
+    own = {"v": "cv", "a": "ca", "t": "ct", "g": "cg"}
+    total = {}
+    known = {q: {} for q in Q}
+    writer, readers = {}, {}
+    nodes = []
+
+    def node(q, rd, wr, busy, lat, issue):
+        deps = set()
+        rd, wr = rd.split(), wr.split()
+        for k in rd:
+            if k in writer:
+                deps.add(writer[k])
+            if k.startswith("PS"):
+                deps.update(e for e in readers.get(k, []) if nodes[e][0] != q)
+        for k in wr:
+            if k in writer:
+                deps.add(writer[k])
+            deps.update(readers.get(k, []))
+        nodes.append((q, busy, lat, sorted(deps), issue))
+        for k in rd:
+            readers.setdefault(k, []).append(len(nodes) - 1)
+        for k in wr:
+            writer[k] = len(nodes) - 1
+            readers[k] = []
+
+    def op(q, rd, wr, dur, call):
+        def issue():
+            total[own[q]] = total.get(own[q], 0) + 1
+            call().then_inc(T.sem[own[q]], 1)
+            return own[q], total[own[q]]
+        node(q, rd, wr, dur, dur, issue)
+
+    ndma = [0]
+
+    def dma(q, rd, wr, out, in_, kb):
+        sem = "dm%d" % ndma[0]
+        ndma[0] += 1
+
+        def issue():
+            total[sem] = 16
+            Q[q].dma_start(out, in_).then_inc(T.sem[sem], 16)
+            return sem, 16
+        node(q, rd, wr, 0.06, T_DMA + kb / T_KB, issue)
+
+    def emit():
+        n = len(nodes)
+        level = [0.0] * n
+        for i in range(n - 1, -1, -1):
+            level[i] += nodes[i][2]
+            for d in nodes[i][3]:
+                level[d] = max(level[d], level[i] + (T_HOP if nodes[d][0] != nodes[i][0] else 0.0))
+        after = [[] for _ in range(n)]
+        for i in range(n):
+            for d in nodes[i][3]:
+                after[d].append(i)
+
+        def place(seq, back):
+            at0, slots = [0.0] * n, {q: [] for q in list(Q) + ["x"]}
+            for i in seq:
+                q, busy, lat = nodes[i][0], nodes[i][1], nodes[i][2]
+                at = 0.0
+                for d in (after[i] if back else nodes[i][3]):
+                    at = max(at, at0[d] + (nodes[d][1] + lat - busy if back else nodes[d][2]) + (T_HOP if nodes[d][0] != q else 0.0))
+                if back and not after[i]:
+                    at = lat - busy
+                row = slots[q]
+                lo, hi = 0, len(row)
+                while lo < hi:
+                    mid = (lo + hi) // 2
+                    if row[mid][1] <= at:
+                        lo = mid + 1
+                    else:
+                        hi = mid
+                while lo < len(row) and at + busy > row[lo][0] + 1e-9:
+                    at = max(at, row[lo][1])
+                    lo += 1
+                row.insert(lo, (at, at + busy))
+                at0[i] = at
+            return at0
+        if "start" not in PLAN:
+            start = place(sorted(range(n), key=lambda k: (-level[k], k)), False)
+            best = (max(start), start)
+            for _ in range(TURNS):
+                late = place(sorted(range(n), key=lambda k: (-start[k] - nodes[k][1], -k)), True)
+                start = place(sorted(range(n), key=lambda k: (-late[k] - nodes[k][1], k)), False)
+                if max(start) < best[0]:
+                    best = (max(start), start)
+            PLAN["start"] = best[1]
+        start = PLAN["start"]
+        event = [None] * n
+        for i in sorted(range(n), key=lambda k: (start[k], k)):
+            q = nodes[i][0]
+            if q != "x":
+                for d in sorted(nodes[i][3], key=lambda k: -event[k][1]):
+                    sem, cnt, clock = event[d]
+                    if not (q == "t" and sem == "ct"):
+                        if known[q].get(sem, 0) < cnt:
+                            Q[q].wait_ge(T.sem[sem], cnt)
+                            known[q][sem] = cnt
+                        for k, c in clock.items():
+                            known[q][k] = max(known[q].get(k, 0), c)
+            sem, cnt = nodes[i][4]()
+            event[i] = (sem, cnt, dict(known[q]) if q != "x" else {})
+        for sem, cnt in total.items():
+            if known["g"].get(sem, 0) < cnt:
+                g.wait_ge(T.sem[sem], cnt)
+
+    v, s, t = g.vector, g.scalar, g.tensor
+
+    def size(ap):
+        n = 1
+        for e in list(ap.shape)[1:]:
+            n *= int(e)
+        return n
+
+    def ind(win, off):
+        return (win.indirect(off), 16 * size(off))
+
+    def cost(out, ins, plain):
+        if isinstance(out, tuple):
+            return T_FIX + out[1] * T_SCAT * T_CYC
+        if isinstance(ins[0], tuple):
+            return T_FIX + ins[0][1] * T_GATH * T_CYC
+        if plain is None:
+            plain = 0.5 if all(SCRATCH[a.name][2] in (BF, U16) for a in [out] + ins) else 1.0
+        return max(64.0, size(out) * plain) * T_CYC
+
+    def ap(x):
+        return x[0] if isinstance(x, tuple) else x
+
+    def ts(rd, wr, out, in0, s1, o1, s2=None, o2=None):
+        if o2 is None:
+            op("v", rd, wr, cost(out, [in0], None), lambda: v.tensor_scalar(ap(out), ap(in0), s1, None, o1))
+        else:
+            op("v", rd, wr, cost(out, [in0], None), lambda: v.tensor_scalar(ap(out), ap(in0), s1, s2, o1, o2))
+
+    def tt(rd, wr, out, a, b, o):
+        op("v", rd, wr, cost(out, [a], 1.0 if "PS" in rd else 2.0), lambda: v.tensor_tensor(ap(out), ap(a), b, o))
+
+    def cp(rd, wr, out, in_):
+        op("v", rd, wr, cost(out, [in_], None), lambda: v.tensor_copy(ap(out), ap(in_)))
+
+    def ms(wr, out, val):
+        op("v", "", wr, cost(out, [out], None), lambda: v.memset(out, val))
+
+    def scan(rd, wr, out, d0, d1, ini, o0, o1):
+        op("v", rd, wr, cost(out, [d0, d1], None), lambda: v.tensor_tensor_scan(out, d0, d1, ini, o0, o1))
+
+    def red(rd, wr, out, in_):
+        op("v", rd, wr, cost(in_, [in_], 1.0), lambda: v.tensor_reduce(out, in_, AxisListType.X, A.add))
+
+    def act(rd, wr, out, in_, f, **kw):
+        op("a", rd, wr, cost(out, [in_], 1.0) + 0.015, lambda: s.activation(ap(out), ap(in_), f, **kw))
+
+    def mm(rd, wr, out, lhsT, rhs, st=True, sp=True):
+        op("t", rd, wr, max(64, size(rhs)) * T_PE, lambda: t.matmul(out, lhsT, rhs, st, sp))
+
+    def iota(wr, out, pat, base, ch=0, exact=False):
+        if exact:
+            op("g", "", wr, 0.13 + 2 * size(out) * T_CYC, lambda: g.iota(out, pat, base, ch))
+        else:
+            op("g", "", wr, 0.13 + 2 * size(out) * T_CYC, lambda: g.iota(out, pat, base, ch, allow_small_or_imprecise_dtypes=True))
+
+    PS = [T["PS%d" % b] for b in range(8)]
+
+    def seg(name, k0, k1):
+        return T[name][:, 16 * k0:16 * k1]
+
+    def col(name, j, k0, k1):
+        return T[name][:, 16 * k0 + j:16 * k1:16]
+
+    def keys(name, k0, k1):
+        return " ".join("%s_%d" % (name, b) for b in range(k0 // 16, (k1 + 15) // 16))
+
+    def E(j):
+        return T.ZE[:, 15 - j:143 - j]
+
+    def fold(b, out, name, k0, k1, rd=None):
+        for j in range(16):
+            mm((rd or keys(name, k0, k1)) + " ZE", "PS%d" % b, out, E(j), col(name, j, k0, k1), j == 0, j == 15)
+
+    def exchange(n, srckey, src, b):
+        snd, key, loc = (T.SNX, "SNX", "loc0") if n % 2 == 0 else (T.SNB, "SNB", "loc1")
+        for d in (1, 2, 3):
+            c0 = 128 * (d - 1)
+            mm(srckey + " PM", "PS%d" % b, PS[b][:, c0:c0 + 128], T.PM[:, c0:c0 + 128], src[:, c0:c0 + 128])
+        act("PS%d" % b, key, snd[:, :], PS[b][:, 0:384], F.Copy)
+        trs, used, arr = [], [], 0
+        for d in sorted((1, 2, 3), key=lambda e: relay_of(T, topo, rank, e) is not None):
+            rl = relay_of(T, topo, rank, d)
+            dst = T.cores[rank ^ d] if rl is None else rl
+            free = [e for e in topo.engines(core, dst) if e not in used]
+            eng = free[:8] if rl is None else free[:4]
+            used += eng
+            rid, pid = topo.addr(dst, core)
+            trs.append(RemoteDMATransfer(dst_ids=[DstId(rid=rid, pnc=pid)], dma_engine_mask=bits(eng),
+                                         remote_sem=T.sem["arr%d" % n], src=snd[:, 128 * (d - 1):128 * d],
+                                         dst=landing(T, n, d) if rl is None else T.O[:, 128 * n:128 * n + 128]))
+            prl = relay_of(T, topo, rank ^ d, d)
+            arr += 8 if prl is None else len(topo.engines(prl, core))
+
+        def send():
+            g.remote_dma_fused(trs, local_sem=T.sem[loc])
+            total[loc] = total.get(loc, 0) + len(used)
+            return loc, total[loc]
+
+        def arrive():
+            total["arr%d" % n] = arr
+            return "arr%d" % n, arr
+        node("g", key, "sent", 0.3, T_REMOTE, send)
+        node("x", "sent", "XG" if n % 2 == 0 else "LG", 0.01, T_REMOTE, arrive)
+
+    dma("s", "", "X", T.X[:, 0:640], T.x0[:, :], 160)
+    dma("a", "", "CI CIb", T.CI[:, 0:288], T.ct[:, :], 144)
+    dma("s", "", "O0", T.O[:, 0:1792], T.obs[:, 0:1792], 448)
+    iota("SI", T.SI[:, 0:8], [[0, 8]], 0, 1, True)
+    iota("RQ", T.RQ[:, :], [[1, 128]], 0)
+    iota("OO", T.OO[:, :], [[16, 432]], 0)
+    iota("RG", T.RG[:, :], [[16, 8], [0, 16]], 0)
+    ms("Z32", T.Z32[:, :], 0.0)
+    dma("s", "Z32", "WA0", T.WA[0:128:16, 0:10240], T.Z32[:, 0:640], 320)
+    for i, m in enumerate((16, 32, 48, 15, 112)):
+        ts("SI", "SI%d" % i, T.SI[:, 8 + i:9 + i], T.SI[:, 0:1], m, A.bitwise_and)
+    cp("SI SI0 SI1 SI2 SI3 SI4", "SF", T.SF[:, 0:13], T.SI[:, 0:13])
+    PF, SC, GC = T.SF[:, 0:1], T.SF[:, 11:12], T.SF[:, 12:13]
+    ts("SF", "SFb", T.SF[:, 16:19], T.SF[:, 8:11], -2.0, A.mult, PF, A.add)
+    for d in (1, 2, 3):
+        ts("RQ SF SFb", "PM", T.PM[:, 128 * (d - 1):128 * d], T.RQ[:, :], -16.0 * d, A.add, T.SF[:, 15 + d:16 + d], A.is_equal)
+    exchange(0, "X", T.X, 4)
+    ms("ONA", T.ONA[:, :], ONE)
+    ts("OO SF", "OO", T.OO[:, :], T.OO[:, :], SC, A.add, 4607.0, A.min)
+    ts("CI", "CTO", T.CTO[:, 0:288], T.CI[:, 0:288], 10240.0, A.is_ge, 20000.0, A.mult)
+    ts("OO", "DU1", T.DU1[:, :], T.OO[:, 0:112], 10240.0, A.add)
+    tt("CTO CI", "CTO", T.CTO[:, 0:288], T.CTO[:, 0:288], T.CI[:, 0:288], A.add)
+    ts("CI", "CIb", T.CI[:, 288:576], T.CI[:, 0:288], 4, A.arith_shift_right)
+    ms("CTOx", T.CTO[:, 288:432], 30000.0)
+    ts("CIb", "CTL", T.CTL[:, 0:288], T.CI[:, 288:576], 640.0, A.is_ge, 160.0, A.mult)
+    ms("CTLx", T.CTL[:, 288:432], float(XN))
+    tt("CTL CIb CTLx", "CTL", T.CTL[:, 0:288], T.CTL[:, 0:288], T.CI[:, 288:576], A.add)
+    ms("Xd", T.X[:, 640:800], 512.0)
+    ms("Xn", T.X[:, XN:1200], 512.0)
+    iota("CP", T.CP[:, :], [[0, 64], [1, 16]], 0)
+    dma("s", "", "CI CIb", T.CI[:, :], T.tv[:, :], 320)
+    dma("s", "CI", "O1", T.O[:, 1792:4608], T.obs[:, 1792:4608], 704)
+
+    def constants():
+        ts("RQ SF", "ID", T.ID[:, :], T.RQ[:, :], PF, A.is_equal)
+        ts("RG SF", "BO", T.BO[:, :], T.RG[:, :], GC, A.is_equal)
+        ms("ZE", T.ZE[:, :], 0.0)
+        ts("ID", "NI", T.NI[:, :], T.ID[:, :], -1.0, A.mult)
+        cp("BO ZE", "ZE", T.ZE[:, 15:143:16], T.BO[:, 0:128:16])
+        for name, x in (("I200", 200.0), ("IXN", float(XN)), ("IF", 1.0), ("I864", 864.0), ("IBG", 18432.0)):
+            act("ID", name, T[name][:, :], T.ID[:, :], F.Copy, scale=x)
+        ts("ID", "M2", T.M2[:, :], T.ID[:, :], 100.0, A.mult)
+        ts("RQ SF", "D16", T.D16[:, :], T.RQ[:, 0:16], SC, A.is_equal, 1024.0, A.mult)
+        tt("BO M2", "M1", T.M1[:, :], T.BO[:, :], T.M2[:, :], A.add)
+        tt("BO M2", "M2", T.M2[:, :], T.BO[:, :], T.M2[:, :], A.subtract)
+        ms("EXP", T.EXP[:, :], 1.0)
+        op("g", "EXP", "EXP", 2.2, lambda: g.affine_select(T.EXP[:, :], T.EXP[:, :], [[1, 64], [0, 16]], A.is_equal, 0.0, 0, -1))
+        iota("PTD", T.PTD[:, :], [[1, 448]], 25 - 256)
+        ms("PTR", T.PTR[:, :], 24.0 - 256)
+        iota("PTR", T.PTR[:, 288:312], [[1, 24]], -256)
+        iota("KI", T.KI[:, 0:4], [[-3, 4]], 48, 1, True)
+        iota("KP", T.KP[:, :], [[0, 40], [1, 16]], 0)
+        iota("TID", T.TID[:, :], [[1, 40], [40, 16]], 64)
+        iota("DI", T.DI[:, :], [[1, 160]], 704)
+        ts("CP", "CP", T.CP[:, :], T.CP[:, :], -14.5, A.add, 2048.0, A.mult)
+        for k in range(8):
+            ms("S%d" % k, T.S[:, k * SW:k * SW + 16], 1024.0)
+        ms("LOGn", T.LOG[:, 384:400], 1024.0)
+        ts("OO", "FN", T.FN[:, :], T.OO[:, 0:16], 16.0, A.mult)
+        ts("SF", "SFd", T.SF[:, 21:22], SC, 4096.0 - 384, A.add)
+        cp("PTD PTR", "PTR", T.PTR[:, 0:K1], T.PTD[:, 0:K1])
+        for j in range(16):
+            act("BO D16", "SEL%d" % j, T.SEL[:, 128 * j:128 * j + 128], T.BO[:, :], F.Copy, scale=T.D16[:, j:j + 1])
+
+    def constants2():
+        ms("Z16", T.Z16[:, :], 0.0)
+        dma("s", "Z16 TC", "WB", T.WB[0:128:16, 0:MW], T.Z16[:, :], 216)
+        ts("KP SF", "DG", T.DG[:, :], T.KP[:, 0:160], SC, A.is_equal)
+        ts("KP", "KP", T.KP[:, :], T.KP[:, :], 0.0, A.not_equal)
+        ts("CI", "LWi", T.LW[:, 0:640], T.CI[:, :], 0.0, A.add)
+        ts("CI", "CI", T.CI[:, :], T.CI[:, :], 4, A.arith_shift_right)
+        cp("CI", "TC", T.TC[:, 0:640], T.CI[:, :])
+        ms("TCx", T.TC[:, 640:800], float(EC))
+        ms("LOx", T.LO[:, 640:800], 0.0)
+        act("TC", "LWj", T.LW[:, 640:1280], T.TC[:, 0:640], F.Copy, scale=-16.0)
+        iota("CI", T.CI[:, 0:512], [[-3, 4], [1, 128]], 48, 0, True)
+        tt("LWi LWj", "LO LW", T.LO[:, 0:640], T.LW[:, 0:640], T.LW[:, 640:1280], A.add)
+        ts("KI", "KI", T.KI[:, 0:4], T.KI[:, 0:4], 15, A.bitwise_and)
+        cp("KI", "W3", T.PB[:, 0:4], T.KI[:, 0:4])
+        ts("SF", "SFc", T.SF[:, 20:21], SC, 40.0, A.mult, 640.0, A.add)
+        ts("SF", "SFe", T.SF[:, 22:23], SC, 0.0, A.not_equal, ONE, A.mult)
+        ts("RQ SFc", "RB", T.RB[:, :], T.RQ[:, 0:40], T.SF[:, 20:21], A.add)
+        ts("RQ SFc", "RB1", T.RB1[:, :], T.RQ[:, 0:40], T.SF[:, 20:21], A.add, 1.0, A.add)
+        ms("FA", T.FA[:, :], 0.0)
+        ts("CI", "CI", T.CI[:, 0:512], T.CI[:, 0:512], 15, A.bitwise_and)
+        for u in range(RO):
+            ts("CI W3", "TRI%d" % u, T.TRI[:, 128 * u:128 * u + 128], T.CI[:, 128 * u:128 * u + 128], T.PB[:, u:u + 1], A.is_gt)
+        for u in range(RO):
+            tt("TRI%d BO" % u, "TRI%d" % u, T.TRI[:, 128 * u:128 * u + 128], T.TRI[:, 128 * u:128 * u + 128], T.BO[:, :], A.mult)
+
+    def constants3():
+        for a, e in CALLS:
+            act("OO", "DU2", T.DU2[:, a:e], T.OO[:, 0:e - a], F.Identity, bias=float(MW))
+        act("Z16 SFe", "ONM", T.ONM[:, :], T.Z16[:, 0:768], F.Identity, bias=T.SF[:, 22:23])
+        ms("ONB", T.ONB[:, :], 1.0)
+        ms("FL", T.FL[:, :], 1.0)
+        ms("CAP", T.CAP[:, :], float(K1))
+        ms("QC0", T.QC[:, 15:16], 0.0)
+        scan("FL CAP", "QC", T.QC[:, 16:16 + C], T.FL[:, :], T.CAP[:, :], 0.0, A.add, A.min)
+        ts("OO", "TH5", T.TH5[:, 0:8], T.OO[:, 0:8], 0.5, A.add)
+        ts("RQ", "OFF", T.OFF[:, 0:2], T.RQ[:, 0:2], 32.0, A.mult)
+        ts("RQ", "OFFb", T.OFF[:, 2:7], T.RQ[:, 2:7], 16.0, A.mult, 288.0, A.add)
+        ts("OO", "DM", T.DM[:, 0:7], T.OO[:, 0:7], 2.0, A.mult, 64.0, A.add)
+
+    def camera_flags(u):
+        st = (72 * u) % C
+        src = [(T.FL, "FL", 0, T.ID, "ID", 72), (T.QC, "QC", 16, T.NI, "NI", 72), (T.QC, "QC QC0", 15, T.ID, "ID", 72),
+               (T.MC, "MC", 0, T.BO, "BO", st), (T.MC, "MC", 288, T.BO, "BO", st),
+               (T.M16, "M16", 0, T.BO, "BO", st), (T.M16, "M16", 288, T.BO, "BO", st)]
+        mm("Z16 ID", "PS4", PS[4][:, 0:C], T.ID[:, :], T.Z16[:, 0:C], True, False)
+        for i, (buf, key, c0, m, mk, sh) in enumerate(src):
+            last = i == len(src) - 1
+            mm(key + " " + mk, "PS4", PS[4][:, 0:C - sh], m[:, :], buf[:, c0 + sh:c0 + C], False, last and sh == 0)
+            if sh:
+                mm(key + " " + mk, "PS4", PS[4][:, C - sh:C], m[:, :], buf[:, c0:c0 + sh], False, last)
+        ts("PS4", "FL", T.FL[:, :], PS[4][:, 0:C], 0.5, A.is_gt)
+
+    def kills():
+        src = [(T.MC, "MC", 288), (T.MC, "MCb", 576), (T.M16, "M16", 288), (T.M16, "M16", 576)]
+        for i, (buf, key, c0) in enumerate(src):
+            mm(key + " IXN", "PS5", PS[5][:, 0:C], T.IXN[:, :], buf[:, c0:c0 + C], i == 0, i == 3)
+        tt("PS5 CTL", "CTL", T.CTL[:, 0:C], T.CTL[:, 0:C], PS[5][:, 0:C], A.max)
+
+    def camera_list(u):
+        st = 72 * u
+        scan("FL CAP", "QC", T.QC[:, 16:16 + C], T.FL[:, :], T.CAP[:, :], 0.0, A.add, A.min)
+        qa, qn = T.QC[:, 15 + C - st:16 + C - st], T.QC[:, 15 + C:16 + C]
+        ts("QC", "NP", T.NP[:, 0:st], T.QC[:, 16 + C - st:16 + C], qa, A.subtract)
+        ts("QC", "NPb", T.NP[:, st:C], T.QC[:, 16:16 + C - st], qn, A.add, qa, A.subtract)
+        for m in range(2, 7):
+            act("NP NPb TH5", "ACC%d " % m + keys("PG", 32 * (m - 2), 32 * (m - 1)), T.PG[:, 512 * (m - 2):512 * (m - 2) + C - 16 * m], T.NP[:, 16 * m:C], F.Sign, bias=T.TH5[:, m:m + 1],
+                scale=-1.0, accum_out=T.ACC[:, m:m + 1])
+        ts("QC OO", "W1", T.W1[:, 0:7], T.OO[:, 0:7], qn, A.is_ge)
+        tt("W1 DM", "W1", T.W1[:, 0:7], T.W1[:, 0:7], T.DM[:, 0:7], A.mult)
+        tt("W1 OFF OFFb", "W1", T.W1[:, 0:7], T.W1[:, 0:7], T.OFF[:, 0:7], A.add)
+        for m in range(2):
+            jk = (T.JK, T.FG)[m % 2]
+            ts("NP NPb TH5", "JK%d" % (m % 2), jk[:, 0:C], T.NP[:, 0:C], T.TH5[:, m:m + 1], A.is_le, 2.0, A.mult)
+            red("JK%d" % (m % 2), "ACC%d" % m, T.ACC[:, m:m + 1], jk[:, 16 * m:C])
+        kills()
+        tt("W1 " + " ".join("ACC%d" % m for m in range(7)), "W2", T.W2[:, 0:7], T.W1[:, 0:7], T.ACC[:, 0:7], A.add)
+        ts("W2", "WL", T.WL[:, 0:7], T.W2[:, 0:7], 0.5, A.mult)
+
+    def passes(name, k0, k1, between):
+        n, key = k1 - k0, keys(name, k0, k1)
+        between = list(between)
+        for k in range(8):
+            d1 = T.CP[:, 0:16 * n] if k == 0 else T.S[:, (k - 1) * SW + 15:(k - 1) * SW + 15 + 16 * n]
+            scan(key + (" CP" if k == 0 else " S%d" % (k - 1)), "S%d" % k, T.S[:, k * SW + 16:k * SW + 16 + 16 * n],
+                 seg(name, k0, k1), d1, 1024.0, A.min, A.max)
+            if between:
+                f = between.pop(0)
+                if f:
+                    f()
+        for f in between:
+            if f:
+                f()
+
+    def move(on_scalar, rd, wr, out, in_):
+        if on_scalar:
+            act(rd, wr, out, in_, F.Copy)
+        else:
+            cp(rd, wr, out, in_)
+
+    def pick_places(nk, chunks, low):
+        w = nk // 16
+        fold(6, PS[6][:, 0:w], "UH", 0, w, "UH")
+
+        def f1():
+            ts("PS6", "W1", T.W1[:, 0:w], PS[6][:, 0:w], low, A.max, 0.25, A.add)
+
+        def f2():
+            cp("W1", "KI", T.KI[:, 0:w], T.W1[:, 0:w])
+
+        def f3():
+            for ch, (k0, n) in enumerate(chunks):
+                r = slice(k0 // 16, (k0 + n) // 16)
+                ts("KI", "W3_%d" % ch, T.W3[:, r], T.KI[:, r], float(SW), A.mult, 31.0 - 2 * SW - 16 * k0, A.add)
+
+        def f4():
+            tt("W3_0 W3_1 W3_2 FN", "W2", T.W2[:, 0:w], T.W3[:, 0:w], T.FN[:, 0:w], A.add)
+            cp("W2", "PU", T.PU[:, 0:w], T.W2[:, 0:w])
+        return [f1, f2, f3, f4]
+
+    bank = [0]
+
+    def nextbank():
+        bank[0] = (bank[0] + 1) % 4
+        return bank[0]
+
+    def spread(ch, k0, nk):
+        mm("PC%d ID" % ch, "PS7", PS[7][0:nk, 0:128], T.PC[:, k0:k0 + nk], T.ID[:, :])
+        act("PS7", "PT%d" % ch, T.PT[0:nk, 128 * ch:128 * ch + 128], PS[7][0:nk, 0:128], F.Copy)
+
+    def wide(ch, k0, nk, m, mk, src, out, f, rd=None, **kw):
+        for a in range(0, nk, 32):
+            e = min(nk, a + 32)
+            b, n = nextbank(), 16 * (e - a)
+            mm((rd or keys(src, k0 + a, k0 + e)) + " " + mk, "PS%d" % b, PS[b][:, 0:n], m[:, :], seg(src, k0 + a, k0 + e), True, False)
+            mm("PT%d EXP" % ch, "PS%d" % b, PS[b][:, 0:n], T.PT[0:nk, 128 * ch:128 * ch + 128], T.EXP[0:nk, 16 * a:16 * e], False, True)
+            act("PS%d" % b, keys(out, k0 + a, k0 + e), seg(out, k0 + a, k0 + e), PS[b][:, 0:n], f, **kw)
+
+    def near(name, k0, nk):
+        for a in range(k0, k0 + nk, 32):
+            e = min(k0 + nk, a + 32)
+            k = keys(name, a, e)
+            if name == "PG" and e <= NA:
+                act(k, k, seg(name, a, e), seg(name, a, e), F.Sign, bias=12.5, scale=-1.0)
+            else:
+                ts(k, k, seg(name, a, e), seg(name, a, e), 12.5, A.is_le)
+
+    def port_places(c0, n):
+        ts("PTR SFd", "G1", T.G1[:, 0:n], T.PTR[:, c0:c0 + n], 16.0, A.mult, T.SF[:, 21:22], A.add)
+        ts("CTL", "G2", T.G2[:, 0:n], T.CTL[:, c0:c0 + n], XN - 0.5, A.is_lt)
+        tt("G1 G2", "G1", T.G1[:, 0:n], T.G1[:, 0:n], T.G2[:, 0:n], A.mult)
+        cp("G1", "GU", T.GU[:, 0:n], T.G1[:, 0:n])
+
+    def list_a(u):
+        scan("M32 KP", "FS", T.FS[:, :], T.KP[:, :], T.M32[:, 0:640], 0.0, A.mult, A.max)
+        tt("FS FA", "FB", T.FB[:, :], T.FS[:, 15:640:16], T.FA[:, :], A.max)
+        scan("FB Z16", "PP", T.PP[:, :], T.FB[:, :], T.Z16[:, 0:40], 0.0, A.add, A.add)
+        mm("PP TRI%d" % u, "PS7", PS[7][:, 0:2], T.TRI[:, 128 * u:128 * u + 128], T.PP[:, 38:40])
+        tt("PP RB1", "B1", T.B1[:, :], T.PP[:, :], T.RB1[:, :], A.subtract)
+
+    def list_b():
+        ts("B1 PS7", "B1", T.B1[:, :], T.B1[:, :], PS[7][:, 1:2], A.add)
+        ts("PP PS7", "B2", T.B2[:, :], T.PP[:, :], PS[7][:, 1:2], A.add, K2 + 0.5, A.is_gt)
+        tt("B1 FB", "B1", T.B1[:, :], T.B1[:, :], T.FB[:, :], A.mult)
+        tt("B2 FB", "FA", T.FA[:, :], T.B2[:, :], T.FB[:, :], A.mult)
+        tt("B1 RB", "B1", T.B1[:, :], T.B1[:, :], T.RB[:, :], A.add)
+        cp("B1", "BU", T.BU[:, :], T.B1[:, :])
+        if LA:
+            act("BU TID", "LW", ind(T.LW[:, :], T.BU[:, :]), T.TID[:, :], F.Silu)
+        else:
+            cp("BU TID", "LW", ind(T.LW[:, :], T.BU[:, :]), T.TID[:, :])
+
+    def list_c():
+        tt("LW DG", "L1", T.L1[:, :], T.LW[:, 0:K2], T.DG[:, :], A.mult)
+        scan("L1 KP", "L2", T.L2[:, :], T.KP[:, 0:K2], T.L1[:, :], 0.0, A.mult, A.add)
+        ts("L2", "TL", T.TL[:, 0:10], T.L2[:, 15:K2:16], -63.75, A.add)
+        cp("TL TC TCx", "CU", T.CU[:, :], ind(T.TC[:, :], T.TL[:, 0:10]))
+
+    held, SK = [], " ".join("S%d" % k for k in range(1, 8))
+    for u in range(RO):
+        lb = 400 + 1792 * u
+        lk = "LOG%d" % u
+
+        def tab(buf):
+            return buf[:, 0:K1] if u == 0 else ind(buf[:, :], T.WL[:, 0:7])
+        og = "O" if u == 0 else "OG"
+        parts = [(0, 32), (32, 64), (64, 96), (96, 112)]
+        if u > 0:
+            cp("OO WL", "OU", T.OU[:, :], tab(T.OO))
+            for a, e in parts:
+                move(e <= OA, "O0 O1 OU", keys("OG", a, e), seg("OG", a, e), ind(T.O[:, :], T.OU[:, a:e]))
+        cp("CTL WL", "XO", T.XO[:, :], tab(T.CTL))
+        tt("CTO CTOx DU1 WL", "FO", T.FO[:, :], tab(T.CTO), T.DU1[:, :], A.min)
+        cp("FO", "FU", T.FU[:, :], T.FO[:, :])
+        act("CTL WL", "XF", T.XF[:, :], tab(T.CTL), F.Copy)
+        for h in range(2):
+            act("FU ONA", "WA0 WA8", ind(T.WA[:, 0:12032], T.FU[:, 56 * h:56 * h + 56]), T.ONA[:, :], F.Silu)
+        dma("a", "WA0", "M32", T.M32[:, 0:640], T.WA[0:128:16, 0:10240], 320)
+        dma("s", "Z32", "WA8", T.WA[8:128:16, 0:MW], T.Z32[:, :], 432)
+        if u < RO - 1:
+            dma("s", "Z32", "WA0", T.WA[0:128:16, 0:10240], T.Z32[:, 0:640], 320)
+        if u == 0:
+            constants()
+            constants2()
+            constants3()
+        act("DI", "LW", T.LW[:, 0:K2], T.DI[:, :], F.Copy)
+        for a, e in parts:
+            tt("X Xd Xn XG XO " + ("O0" if u == 0 else keys("OG", a, e)), keys("D", a, e), seg("D", a, e),
+               ind(T.X[:, :], T.XO[:, a:e]), seg(og, a, e), A.subtract)
+        fold(5, PS[5][:, 0:K1], "D", 0, K1)
+
+        def used1():
+            ts("PS5", "UH", T.UH[:, 0:K1], PS[5][:, 0:K1], 4088.0, A.is_lt, 0.5, A.mult)
+            held[:] = pick_places(K1, CH1, 2.5)
+            ts("XF", "LV", T.LV[:, :], T.XF[:, :], XN - 0.5, A.is_lt, 0.5, A.mult)
+
+        def side1():
+            if u > 0:
+                cp("PTD WL", "PTR", ind(T.PTR[:, :], T.WL[:, 0:7]), T.PTD[:, K1 * u:K1 * u + K1])
+
+        def side2():
+            ts("UH", "TH1", T.TH1[:, 0:K1], T.UH[:, 0:K1], -176.0, A.mult, 99.5, A.add)
+            tt("LV UH", "LU", T.LU[:, :], T.LV[:, :], T.UH[:, 0:K1], A.subtract)
+
+        def head1(ch):
+            k0, nk = CH1[ch]
+            cp(SK + " PU", "PC%d" % ch, T.PC[:, k0:k0 + nk], ind(T.S[:, SW:7 * SW + 16 + 16 * nk], T.PU[:, k0 // 16:(k0 + nk) // 16]))
+            spread(ch, k0, nk)
+            wide(ch, k0, nk, T.NI, "NI", "D", "D", F.Abs)
+
+        def count1(ch):
+            k0, nk = CH1[ch]
+            near("D", k0, nk)
+            fold(4, PS[4][:, 0:nk], "D", k0, k0 + nk)
+
+        def fit1(ch):
+            k0, nk = CH1[ch]
+            r, fk = slice(k0, k0 + nk), "FIT%d" % ch
+            tt("PS4 TH1", fk, T.FIT[:, r], PS[4][:, 0:nk], T.TH1[:, r], A.is_gt)
+            mm(fk + " M1", "PS6", PS[6][:, 0:nk], T.M1[:, :], T.FIT[:, r], True, False)
+            mm("LU I200", "PS6", PS[6][:, 0:nk], T.I200[:, :], T.LU[:, r], False, True)
+            mm(fk + " M2", "PS4", PS[4][:, 0:nk], T.M2[:, :], T.FIT[:, r], True, False)
+            mm("UH I200", "PS4", PS[4][:, 0:nk], T.I200[:, :], T.UH[:, r], False, True)
+
+        def log1(ch):
+            k0, nk = CH1[ch]
+            r = slice(k0, k0 + nk)
+            ts("PS6", "NONE%d" % ch, T.NONE[:, r], PS[6][:, 0:nk], 105.5, A.is_lt)
+            ts("PS4", "DIE%d" % ch, T.DIE[:, r], PS[4][:, 0:nk], 105.5, A.is_ge, float(XN), A.mult)
+            for a in range(k0, k0 + nk, 32) if SO else []:
+                e = min(k0 + nk, a + 32)
+                b, n = nextbank(), 16 * (e - a)
+                mm(("O0" if u == 0 else keys("OG", a, e)) + " ID", "PS%d" % b, PS[b][:, 0:n], T.ID[:, :], seg(og, a, e), True, False)
+                mm("PT%d EXP" % ch, "PS%d" % b, PS[b][:, 0:n], T.PT[0:nk, 128 * ch:128 * ch + 128], T.EXP[0:nk, 16 * (a - k0):16 * (e - k0)], False, False)
+                for j in range(16):
+                    mm("NONE%d SEL%d" % (ch, j), "PS%d PEL" % b, PS[b][:, j:n:16], T.SEL[:, 128 * j:128 * j + 128], T.NONE[:, a:e], False, j == 15)
+                dst, key = T.LOG[:, lb + 16 * a:lb + 16 * e], "%s_%d_%d" % (lk, ch, (a - k0) // 32)
+                if EA[a // 32]:
+                    act("PS%d" % b, key, dst, PS[b][:, 0:n], F.Relu)
+                else:
+                    ts("PS%d" % b, key, dst, PS[b][:, 0:n], 0.0, A.max)
+            per = 8 if ch == 0 else 4
+            for j0 in range(0, 16, per) if not SO else []:
+                b = nextbank()
+                for j in range(j0, j0 + per):
+                    o = PS[b][:, nk * (j - j0):nk * (j - j0 + 1)]
+                    mm(("O0" if u == 0 else keys("OG", k0, k0 + nk)) + " ID", "PS%d" % b, o, T.ID[:, :], col(og, j, k0, k0 + nk), True, False)
+                    mm("PC%d ID" % ch, "PS%d" % b, o, T.ID[:, :], T.PC[:, r], False, False)
+                    mm("NONE%d SEL%d" % (ch, j), "PS%d PEL" % b, o, T.SEL[:, 128 * j:128 * j + 128], T.NONE[:, r], False, True)
+                for j in range(j0, j0 + per):
+                    o = PS[b][:, nk * (j - j0):nk * (j - j0 + 1)]
+                    dst = T.LOG[:, lb + 16 * k0 + j:lb + 16 * (k0 + nk):16]
+                    if EA[j0 // 8 if ch == 0 else 2 + j0 // 4 % 2]:
+                        act("PS%d" % b, "%s_%d_%d" % (lk, ch, j), dst, o, F.Relu)
+                    else:
+                        ts("PS%d" % b, "%s_%d_%d" % (lk, ch, j), dst, o, 0.0, A.max)
+        logk = ["LOGn " + " ".join("%s_%d_%d" % (lk, ch, j) for j in range(16)) for ch in range(2)]
+
+        def send_b():
+            move(SA, logk[0] + " GU", "SG", T.SG[:, :], ind(T.LOG[:, 384:lb + 16 * CH1[1][0]], T.GU[:, 0:24]))
+            exchange(2 * u + 1, "SG", T.SG, 7)
+
+        passes("D", 0, 64, [side1, used1, lambda: port_places(0, 24), lambda: held[0](), lambda: held[1](), lambda: held[2](),
+                            lambda: held[3](), side2])
+        head1(0)
+        count1(0)
+        fit1(0)
+        passes("D", CH1[1][0], K1, [])
+        list_a(u)
+        list_b()
+        log1(0)
+        head1(1)
+        list_c()
+        for a in range(0, K2, 32):
+            move(a + 32 <= PA, "PTR CU", keys("PG", a, a + 32), seg("PG", a, a + 32), ind(T.PTR[:, :], T.CU[:, a:a + 32]))
+        send_b()
+        count1(1)
+        act("LO LOx TL", "LO4", T.LO4[:, :], ind(T.LO[:, :], T.TL[:, 0:10]), F.Identity, bias=4096.0)
+        fit1(1)
+        log1(1)
+        tt("DIE0 DIE1 XF WL", "CTL", tab(T.CTL), T.DIE[:, :], T.XF[:, :], A.max)
+        fold(5, PS[5][:, 0:K2], "PG", 0, K2)
+        tt("PS5 LO4", "L1", T.L1[:, :], PS[5][:, 0:K2], T.LO4[:, :], A.add)
+        cp("L1", "IU", T.IU[:, :], T.L1[:, :])
+        win, wk = T.LOG[:, 0:lb + 1792], logk[0] + " " + logk[1] + " LG IU"
+        h0 = CH2[0][1] // 2
+        cp(wk, keys("BG", 0, h0), seg("BG", 0, h0), ind(win, T.IU[:, 0:h0]))
+        for a, e in [(h0, 2 * h0)] + [(k0, k0 + nk) for k0, nk in CH2[1:]]:
+            act(wk, keys("BG", a, e), seg("BG", a, e), ind(win, T.IU[:, a:e]), F.Copy)
+        act("TC TCx TL", "CF", T.CF[:, :], ind(T.TC[:, :], T.TL[:, 0:10]), F.Copy)
+        act("LO LOx TL", "MO", T.MO[:, :], ind(T.LO[:, :], T.TL[:, 0:10]), F.Copy)
+        act("CF", "PEN", T.PEN[:, :], T.CF[:, :], F.Relu, bias=-287.0)
+        fold(5, PS[5][:, 0:K2], "BG", 0, K2)
+        for a in range(0, K2, 32):
+            act(keys("BG", a, a + 32), keys("PG", a, a + 32), seg("PG", a, a + 32), seg("BG", a, a + 32), F.Relu, bias=255.0, scale=-1.0)
+
+        def used2():
+            ts("PS5", "UH", T.UH[:, :], PS[5][:, 0:K2], 10000.0, A.is_lt, 0.5, A.mult)
+            held[:] = pick_places(K2, CH2, 1.5)
+            mm("UH BO", "PS7", PS[7][:, 0:K2], T.BO[:, :], T.UH[:, :])
+            if NA:
+                act("UH", "TH1", T.TH1[:, 0:NA], T.UH[:, 0:NA], F.Identity, scale=48.0, bias=-17.0)
+            act("UH", "TH1", T.TH1[:, NA:K2], T.UH[:, NA:K2], F.Copy, scale=23.0)
+
+        def has2():
+            held[0]()
+            ts("PS7", "NH", T.NH[:, :], PS[7][:, 0:K2], 1.25, A.is_lt, 512.0, A.mult)
+
+        def head2(ch):
+            k0, nk = CH2[ch]
+            r, w = slice(k0, k0 + nk), slice(k0 // 16, (k0 + nk) // 16)
+            ts(SK + " PU", "PC%d" % ch, T.PC[:, r], ind(T.S[:, SW:7 * SW + 16 + 16 * nk], T.PU[:, w]), 255.0, A.min)
+            spread(ch, k0, nk)
+            tt("PC%d NH" % ch, "XNW%d" % ch, T.XNW[:, r], T.PC[:, r], T.NH[:, r], A.max)
+            tt("X Xd TL XNW%d" % ch, "NE%d" % ch, T.NE[:, r], ind(T.X[:, 0:800], T.TL[:, w]), T.XNW[:, r], A.not_equal)
+            mm("NE%d BO" % ch, "PS6", PS[6][:, 0:nk], T.BO[:, :], T.NE[:, r])
+            wide(ch, k0, nk, T.ID, "ID", "PG", "PG", F.Abs, bias=-255.0)
+            act("PS6", "SN%d" % ch, T.SN[:, r], PS[6][:, 0:nk], F.Relu, bias=1.0, scale=-1.0)
+            act("SN%d" % ch, "DL%d" % ch, T.DL[:, r], T.SN[:, r], F.Identity, bias=288.0, scale=288.0 - 18432)
+            mm("CF IF", "PS5", PS[5][:, 0:nk], T.IF[:, :], T.CF[:, r], True, False)
+            mm("MO I864", "PS5", PS[5][:, 0:nk], T.I864[:, :], T.MO[:, r], False, False)
+            mm("PEN IBG", "PS5", PS[5][:, 0:nk], T.IBG[:, :], T.PEN[:, r], False, False)
+            mm("SN%d IBG" % ch, "PS5", PS[5][:, 0:nk], T.IBG[:, :], T.SN[:, r], False, True)
+
+        def count2(ch):
+            k0, nk = CH2[ch]
+            r = slice(k0, k0 + nk)
+            near("PG", k0, nk)
+            fold(4, PS[4][:, 0:nk], "PG", k0, k0 + nk)
+
+        def marks(ch):
+            k0, nk = CH2[ch]
+            r = slice(k0, k0 + nk)
+            tt("PS4 TH1", "REJ%d" % ch, T.REJ[:, r], PS[4][:, 0:nk], T.TH1[:, r], A.is_lt)
+            dl = "DL%d" % ch
+            tt(dl + " REJ%d" % ch, dl, T.DL[:, r], T.DL[:, r], T.REJ[:, r], A.mult)
+            tt(dl + " PS5", dl, T.DL[:, r], T.DL[:, r], PS[5][:, 0:nk], A.add)
+            tt(dl + " DU2", dl, T.DL[:, r], T.DL[:, r], T.DU2[:, r], A.min)
+            cp(dl, "MU%d" % ch, T.MU[:, r], T.DL[:, r])
+            for a, e in CALLS:
+                if k0 <= a < k0 + nk and e <= MA:
+                    act("MU%d ONM" % ch, "WA0 WA8", ind(T.WA[:, :], T.MU[:, a:e]), T.ONM[:, 0:16 * (e - a)], F.Silu)
+                elif k0 <= a < k0 + nk:
+                    cp("MU%d ONB" % ch, "WB", ind(T.WB[:, :], T.MU[:, a:e]), T.ONB[:, 0:16 * (e - a)])
+
+        def every(name):
+            return " ".join("%s%d" % (name, ch) for ch in range(len(CH2)))
+        for ch, (k0, nk) in enumerate(CH2):
+            passes("BG", k0, k0 + nk, [] if ch else [used2, has2, lambda: held[1](), lambda: held[2](), lambda: held[3]()])
+            head2(ch)
+            if ch == 0:
+                tt("TH1 NH", "TH1", T.TH1[:, :], T.TH1[:, :], T.NH[:, :], A.subtract)
+            count2(ch)
+            marks(ch)
+        dma("a", "WA8", "M32", T.M32[:, :], T.WA[8:128:16, 0:MW], 432)
+        cp(every("XNW") + " TL", "X Xd", ind(T.X[:, 0:800], T.TL[:, 0:10]), T.XNW[:, :])
+        dma("s", "WB", "M16", T.M16[:, :], T.WB[0:128:16, 0:MW], 216)
+        if u < RO - 1:
+            exchange(2 * u + 2, "X", T.X, 7)
+            dma("s", "Z16", "WB", T.WB[0:128:16, 0:MW], T.Z16[:, :], 216)
+        else:
+            dma("s", "X", "", T.yx[:, :], T.X[:, 0:640], 160)
+        ts(every("REJ"), "L2", T.L2[:, :], T.REJ[:, :], float(EC), A.mult)
+        tt("L2 CF TL", "TC TCx", ind(T.TC[:, :], T.TL[:, 0:10]), T.L2[:, :], T.CF[:, :], A.max)
+        if u == RO - 1:
+            ts("TC", "FS", T.FS[:, :], T.TC[:, 0:640], EC - 0.5, A.is_lt)
+            ts("FA", "FB", T.FB[:, :], T.FA[:, :], 32.0, A.mult)
+            for a in range(16):
+                mm("FS ZE", "PS6", PS[6][:, 0:40], E(a), T.FS[:, 40 * a:40 * a + 40], a == 0, False)
+            mm("FB ID", "PS6", PS[6][:, 0:40], T.ID[:, :], T.FB[:, :], False, True)
+            cp("PS6", "YT", T.YT[:, :], PS[6][:, 0:40])
+            dma("s", "YT", "", T.yt[:, :], T.YT[:, :], 20)
+        act("M32", "MC", T.MC[:, 0:576], T.M32[:, 0:576], F.Copy)
+        act("M32", "MCb", T.MC[:, 576:864], T.M32[:, 576:864], F.Copy)
+        camera_flags(u + 1)
+        if u < RO - 1:
+            camera_list(u + 1)
+    kills()
+    port_places(272, 16)
+    cp(wk + " GU", "SG", T.SG[:, 0:256], ind(T.LOG[:, 384:400 + RO * 1792], T.GU[:, 0:16]))
+    ts("CTL", "JK0", T.JK[:, :], T.CTL[:, 0:C], XN - 0.5, A.is_lt)
+    ts("FL", "JK1", T.FG[:, :], T.FL[:, :], 32.0, A.mult)
+    ts("SG", "SNB", T.SNB[:, 0:256], T.SG[:, 0:256], 600.0, A.is_gt, 512.0, A.mult)
+    ts("SG", "SG", T.SG[:, 0:256], T.SG[:, 0:256], 255.0, A.min)
+    tt("SG SNB", "SG", T.SG[:, 0:256], T.SG[:, 0:256], T.SNB[:, 0:256], A.max)
+    dma("s", "SG", "", T.yb[:, :], T.SG[:, 0:256], 64)
+    mm("JK0 BO", "PS6", PS[6][:, 0:C], T.BO[:, :], T.JK[:, :], True, False)
+    mm("JK1 ID", "PS6", PS[6][:, 0:C], T.ID[:, :], T.FG[:, :], False, True)
+    act("PS6", "M32", T.M32[:, 0:C], PS[6][:, 0:C], F.Copy)
+    dma("a", "M32", "", T.yc[:, :], T.M32[0:128:16, 0:C], 9)
+    emit()

@@ -11,9 +11,10 @@ SW = 1040
 ONE = 1.278465
 CH1 = [(0, 64), (64, 48)]
 CH2 = [(0, 64), (64, 64), (128, 32)]
-T_CYC, T_GATH, T_SCAT, T_FIX, T_PE, T_HOP, T_DMA, T_KB, T_REMOTE = 0.001, 1.5, 3.5, 0.05, 0.0006, 0.08, 2.0, 288.0, 2.5
+T_CYC, T_GATH, T_SCAT, T_FIX, T_PE, T_HOP, T_DMA, T_KB, T_REMOTE = 0.001, 1.5, 3.5, 0.05, 0.0007, 0.13, 2.0, 288.0, 2.5
 LA, NA, SO, EA, SA = True, 0, True, (1, 1, 0, 1), False
-MA, PA, OA = 96, 96, 64
+MA, PA, OA = 96, 128, 96
+T_OWN = (0.13, 0.0)
 PLAN, TURNS = {}, 6
 CUTS = sorted(set([k0 for k0, nk in CH2] + [MA, K2] + list(range(0, MA, 48))))
 CALLS = list(zip(CUTS[:-1], CUTS[1:]))
@@ -23,7 +24,7 @@ SB = {
     "M32": (864, F32), "M16": (864, BF), "MC": (864, BF), "Z32": (864, F32), "Z16": (864, BF),
     "CTL": (432, F32), "CTO": (432, F32), "OO": (432, F32), "PTR": (432, BF), "PTD": (448, BF),
     "TC": (800, F32), "LO": (800, BF), "LW": (1280, F32), "TID": (640, F32), "DI": (160, F32), "X": (1200, BF),
-    "EXP": (1024, BF), "SEL": (2048, BF), "CP": (1024, BF), "D": (1792, BF), "BG": (2560, BF), "S": (8 * SW, BF), "KP": (640, BF), "DG": (160, BF),
+    "EXP": (1024, BF), "SEL": (2048, BF), "CP": (1024, BF), "D": (1792, BF), "BG": (2560, BF), "S": (7 * SW, BF), "SS": (7 * SW, BF), "KP": (640, BF), "DG": (160, BF),
     "ID": (128, BF), "NI": (128, BF), "BO": (128, BF), "M1": (128, BF), "M2": (128, BF), "I200": (128, BF),
     "IXN": (128, BF), "PM": (384, BF), "TRI": (512, BF), "ZE": (144, BF), "RQ": (128, F32), "RG": (128, F32),
     "SI": (16, I32), "SF": (32, F32), "D16": (16, F32), "CI": (640, I32),
@@ -135,7 +136,7 @@ def rank_program(g, core, T, topo):
         for i in range(n - 1, -1, -1):
             level[i] += nodes[i][2]
             for d in nodes[i][3]:
-                level[d] = max(level[d], level[i] + (T_HOP if nodes[d][0] != nodes[i][0] else 0.0))
+                level[d] = max(level[d], level[i] + (T_HOP if nodes[d][0] != nodes[i][0] else T_OWN[nodes[i][0] == "t"]))
         after = [[] for _ in range(n)]
         for i in range(n):
             for d in nodes[i][3]:
@@ -147,7 +148,7 @@ def rank_program(g, core, T, topo):
                 q, busy, lat = nodes[i][0], nodes[i][1], nodes[i][2]
                 at = 0.0
                 for d in (after[i] if back else nodes[i][3]):
-                    at = max(at, at0[d] + (nodes[d][1] + lat - busy if back else nodes[d][2]) + (T_HOP if nodes[d][0] != q else 0.0))
+                    at = max(at, at0[d] + (nodes[d][1] + lat - busy if back else nodes[d][2]) + (T_HOP if nodes[d][0] != q else T_OWN[q == "t"]))
                 if back and not after[i]:
                     at = lat - busy
                 row = slots[q]
@@ -352,10 +353,12 @@ def rank_program(g, core, T, topo):
         iota("TID", T.TID[:, :], [[1, 40], [40, 16]], 64)
         iota("DI", T.DI[:, :], [[1, 160]], 704)
         ts("CP", "CP", T.CP[:, :], T.CP[:, :], -14.5, A.add, 2048.0, A.mult)
-        for k in range(8):
+        for k in range(7):
             ms("S%d" % k, T.S[:, k * SW:k * SW + 16], 1024.0)
+            ms("SS%d SS%d" % (k, (k + 6) % 7), T.SS[:, max(k * SW - 256, 0):k * SW + 16], 1024.0)
         ms("LOGn", T.LOG[:, 384:400], 1024.0)
-        ts("OO", "FN", T.FN[:, :], T.OO[:, 0:16], 16.0, A.mult)
+        for c0 in (0, 4, 8):
+            ts("OO", "FN", T.FN[:, c0:c0 + 4], T.OO[:, 0:4], 16.0, A.mult)
         ts("SF", "SFd", T.SF[:, 21:22], SC, 4096.0 - 384, A.add)
         cp("PTD PTR", "PTR", T.PTR[:, 0:K1], T.PTD[:, 0:K1])
         for j in range(16):
@@ -440,12 +443,20 @@ def rank_program(g, core, T, topo):
         tt("W1 " + " ".join("ACC%d" % m for m in range(7)), "W2", T.W2[:, 0:7], T.W1[:, 0:7], T.ACC[:, 0:7], A.add)
         ts("W2", "WL", T.WL[:, 0:7], T.W2[:, 0:7], 0.5, A.mult)
 
+    def sbuf(k0):
+        return "SS" if k0 == 64 else "S"
+
+    def finals(k0, nk):
+        sb = sbuf(k0)
+        return " ".join("%s%d" % (sb, k) for k in range(7)), T[sb][:, 0:6 * SW + 16 + 16 * nk]
+
     def passes(name, k0, k1, between):
         n, key = k1 - k0, keys(name, k0, k1)
         between = list(between)
         for k in range(8):
-            d1 = T.CP[:, 0:16 * n] if k == 0 else T.S[:, (k - 1) * SW + 15:(k - 1) * SW + 15 + 16 * n]
-            scan(key + (" CP" if k == 0 else " S%d" % (k - 1)), "S%d" % k, T.S[:, k * SW + 16:k * SW + 16 + 16 * n],
+            sb, a, b = sbuf(k0), (k + 5) % 7, (k + 6) % 7
+            d1 = T.CP[:, 0:16 * n] if k == 0 else T[sb][:, a * SW + 15:a * SW + 15 + 16 * n]
+            scan(key + (" CP" if k == 0 else " %s%d" % (sb, a)), "%s%d" % (sb, b), T[sb][:, b * SW + 16:b * SW + 16 + 16 * n],
                  seg(name, k0, k1), d1, 1024.0, A.min, A.max)
             if between:
                 f = between.pop(0)
@@ -461,25 +472,15 @@ def rank_program(g, core, T, topo):
         else:
             cp(rd, wr, out, in_)
 
-    def pick_places(nk, chunks, low):
-        w = nk // 16
-        fold(6, PS[6][:, 0:w], "UH", 0, w, "UH")
-
-        def f1():
-            ts("PS6", "W1", T.W1[:, 0:w], PS[6][:, 0:w], low, A.max, 0.25, A.add)
-
-        def f2():
-            cp("W1", "KI", T.KI[:, 0:w], T.W1[:, 0:w])
-
-        def f3():
-            for ch, (k0, n) in enumerate(chunks):
-                r = slice(k0 // 16, (k0 + n) // 16)
-                ts("KI", "W3_%d" % ch, T.W3[:, r], T.KI[:, r], float(SW), A.mult, 31.0 - 2 * SW - 16 * k0, A.add)
-
-        def f4():
-            tt("W3_0 W3_1 W3_2 FN", "W2", T.W2[:, 0:w], T.W3[:, 0:w], T.FN[:, 0:w], A.add)
-            cp("W2", "PU", T.PU[:, 0:w], T.W2[:, 0:w])
-        return [f1, f2, f3, f4]
+    def pick_places(k0, k1, low, uh, pu):
+        w0, w1 = k0 // 16, k1 // 16
+        w, r = w1 - w0, slice(w0, w1)
+        fold(6, PS[6][:, 0:w], "UH", w0, w1, uh)
+        ts("PS6", "W1", T.W1[:, 0:w], PS[6][:, 0:w], low, A.max, 0.25, A.add)
+        cp("W1", "KI", T.KI[:, 0:w], T.W1[:, 0:w])
+        ts("KI", "W3", T.W3[:, 0:w], T.KI[:, 0:w], float(SW), A.mult, 31.0 - 2 * SW, A.add)
+        tt("W3 FN", "W2", T.W2[:, 0:w], T.W3[:, 0:w], T.FN[:, r], A.add)
+        cp("W2", pu, T.PU[:, r], T.W2[:, 0:w])
 
     bank = [0]
 
@@ -539,7 +540,6 @@ def rank_program(g, core, T, topo):
         ts("L2", "TL", T.TL[:, 0:10], T.L2[:, 15:K2:16], -63.75, A.add)
         cp("TL TC TCx", "CU", T.CU[:, :], ind(T.TC[:, :], T.TL[:, 0:10]))
 
-    held, SK = [], " ".join("S%d" % k for k in range(1, 8))
     for u in range(RO):
         lb = 400 + 1792 * u
         lk = "LOG%d" % u
@@ -559,7 +559,7 @@ def rank_program(g, core, T, topo):
         for h in range(2):
             act("FU ONA", "WA0 WA8", ind(T.WA[:, 0:12032], T.FU[:, 56 * h:56 * h + 56]), T.ONA[:, :], F.Silu)
         dma("a", "WA0", "M32", T.M32[:, 0:640], T.WA[0:128:16, 0:10240], 320)
-        dma("s", "Z32", "WA8", T.WA[8:128:16, 0:MW], T.Z32[:, :], 432)
+        dma("s", "Z32 M32", "WA8", T.WA[8:128:16, 0:MW], T.Z32[:, :], 432)
         if u < RO - 1:
             dma("s", "Z32", "WA0", T.WA[0:128:16, 0:10240], T.Z32[:, 0:640], 320)
         if u == 0:
@@ -573,8 +573,8 @@ def rank_program(g, core, T, topo):
         fold(5, PS[5][:, 0:K1], "D", 0, K1)
 
         def used1():
-            ts("PS5", "UH", T.UH[:, 0:K1], PS[5][:, 0:K1], 4088.0, A.is_lt, 0.5, A.mult)
-            held[:] = pick_places(K1, CH1, 2.5)
+            ts("PS5", "UH0 UH1", T.UH[:, 0:K1], PS[5][:, 0:K1], 4088.0, A.is_lt, 0.5, A.mult)
+            pick_places(0, K1, 2.5, "UH0 UH1", "PU0 PU1")
             ts("XF", "LV", T.LV[:, :], T.XF[:, :], XN - 0.5, A.is_lt, 0.5, A.mult)
 
         def side1():
@@ -582,12 +582,12 @@ def rank_program(g, core, T, topo):
                 cp("PTD WL", "PTR", ind(T.PTR[:, :], T.WL[:, 0:7]), T.PTD[:, K1 * u:K1 * u + K1])
 
         def side2():
-            ts("UH", "TH1", T.TH1[:, 0:K1], T.UH[:, 0:K1], -176.0, A.mult, 99.5, A.add)
-            tt("LV UH", "LU", T.LU[:, :], T.LV[:, :], T.UH[:, 0:K1], A.subtract)
+            act("UH0 UH1", "TH0 TH1", T.TH1[:, 0:K1], T.UH[:, 0:K1], F.Identity, scale=-176.0, bias=99.5)
+            tt("LV UH0 UH1", "LU", T.LU[:, :], T.LV[:, :], T.UH[:, 0:K1], A.subtract)
 
         def head1(ch):
             k0, nk = CH1[ch]
-            cp(SK + " PU", "PC%d" % ch, T.PC[:, k0:k0 + nk], ind(T.S[:, SW:7 * SW + 16 + 16 * nk], T.PU[:, k0 // 16:(k0 + nk) // 16]))
+            cp(finals(k0, nk)[0] + " PU0 PU1", "PC%d" % ch, T.PC[:, k0:k0 + nk], ind(finals(k0, nk)[1], T.PU[:, k0 // 16:(k0 + nk) // 16]))
             spread(ch, k0, nk)
             wide(ch, k0, nk, T.NI, "NI", "D", "D", F.Abs)
 
@@ -599,11 +599,11 @@ def rank_program(g, core, T, topo):
         def fit1(ch):
             k0, nk = CH1[ch]
             r, fk = slice(k0, k0 + nk), "FIT%d" % ch
-            tt("PS4 TH1", fk, T.FIT[:, r], PS[4][:, 0:nk], T.TH1[:, r], A.is_gt)
+            tt("PS4 TH0 TH1", fk, T.FIT[:, r], PS[4][:, 0:nk], T.TH1[:, r], A.is_gt)
             mm(fk + " M1", "PS6", PS[6][:, 0:nk], T.M1[:, :], T.FIT[:, r], True, False)
             mm("LU I200", "PS6", PS[6][:, 0:nk], T.I200[:, :], T.LU[:, r], False, True)
             mm(fk + " M2", "PS4", PS[4][:, 0:nk], T.M2[:, :], T.FIT[:, r], True, False)
-            mm("UH I200", "PS4", PS[4][:, 0:nk], T.I200[:, :], T.UH[:, r], False, True)
+            mm("UH0 UH1 I200", "PS4", PS[4][:, 0:nk], T.I200[:, :], T.UH[:, r], False, True)
 
         def log1(ch):
             k0, nk = CH1[ch]
@@ -643,8 +643,7 @@ def rank_program(g, core, T, topo):
             move(SA, logk[0] + " GU", "SG", T.SG[:, :], ind(T.LOG[:, 384:lb + 16 * CH1[1][0]], T.GU[:, 0:24]))
             exchange(2 * u + 1, "SG", T.SG, 7)
 
-        passes("D", 0, 64, [side1, used1, lambda: port_places(0, 24), lambda: held[0](), lambda: held[1](), lambda: held[2](),
-                            lambda: held[3](), side2])
+        passes("D", 0, 64, [side1, used1, lambda: port_places(0, 24), side2])
         head1(0)
         count1(0)
         fit1(0)
@@ -662,39 +661,39 @@ def rank_program(g, core, T, topo):
         fit1(1)
         log1(1)
         tt("DIE0 DIE1 XF WL", "CTL", tab(T.CTL), T.DIE[:, :], T.XF[:, :], A.max)
-        fold(5, PS[5][:, 0:K2], "PG", 0, K2)
-        tt("PS5 LO4", "L1", T.L1[:, :], PS[5][:, 0:K2], T.LO4[:, :], A.add)
-        cp("L1", "IU", T.IU[:, :], T.L1[:, :])
-        win, wk = T.LOG[:, 0:lb + 1792], logk[0] + " " + logk[1] + " LG IU"
+        halves = [(0, 64), (64, K2)]
+        for h, (a, e) in enumerate(halves):
+            b = nextbank()
+            fold(b, PS[b][:, 0:e - a], "PG", a, e)
+            tt("PS%d LO4" % b, "L1", T.L1[:, a:e], PS[b][:, 0:e - a], T.LO4[:, a:e], A.add)
+            cp("L1", "IU%d" % h, T.IU[:, a:e], T.L1[:, a:e])
+        win, wk = T.LOG[:, 0:lb + 1792], logk[0] + " " + logk[1] + " LG"
         h0 = CH2[0][1] // 2
-        cp(wk, keys("BG", 0, h0), seg("BG", 0, h0), ind(win, T.IU[:, 0:h0]))
+        cp(wk + " IU0", keys("BG", 0, h0), seg("BG", 0, h0), ind(win, T.IU[:, 0:h0]))
         for a, e in [(h0, 2 * h0)] + [(k0, k0 + nk) for k0, nk in CH2[1:]]:
-            act(wk, keys("BG", a, e), seg("BG", a, e), ind(win, T.IU[:, a:e]), F.Copy)
+            act(wk + " IU%d" % min(a // 64, 1), keys("BG", a, e), seg("BG", a, e), ind(win, T.IU[:, a:e]), F.Copy)
         act("TC TCx TL", "CF", T.CF[:, :], ind(T.TC[:, :], T.TL[:, 0:10]), F.Copy)
         act("LO LOx TL", "MO", T.MO[:, :], ind(T.LO[:, :], T.TL[:, 0:10]), F.Copy)
         act("CF", "PEN", T.PEN[:, :], T.CF[:, :], F.Relu, bias=-287.0)
-        fold(5, PS[5][:, 0:K2], "BG", 0, K2)
         for a in range(0, K2, 32):
             act(keys("BG", a, a + 32), keys("PG", a, a + 32), seg("PG", a, a + 32), seg("BG", a, a + 32), F.Relu, bias=255.0, scale=-1.0)
 
-        def used2():
-            ts("PS5", "UH", T.UH[:, :], PS[5][:, 0:K2], 10000.0, A.is_lt, 0.5, A.mult)
-            held[:] = pick_places(K2, CH2, 1.5)
-            mm("UH BO", "PS7", PS[7][:, 0:K2], T.BO[:, :], T.UH[:, :])
-            if NA:
-                act("UH", "TH1", T.TH1[:, 0:NA], T.UH[:, 0:NA], F.Identity, scale=48.0, bias=-17.0)
-            act("UH", "TH1", T.TH1[:, NA:K2], T.UH[:, NA:K2], F.Copy, scale=23.0)
-
-        def has2():
-            held[0]()
-            ts("PS7", "NH", T.NH[:, :], PS[7][:, 0:K2], 1.25, A.is_lt, 512.0, A.mult)
+        for h, (a, e) in enumerate(halves):
+            b, uh, th = nextbank(), "UH%d" % h, "TH%d" % h
+            fold(b, PS[b][:, 0:e - a], "BG", a, e)
+            ts("PS%d" % b, uh, T.UH[:, a:e], PS[b][:, 0:e - a], 10000.0, A.is_lt, 0.5, A.mult)
+            pick_places(a, e, 1.5, uh, "PU%d" % h)
+            mm(uh + " BO", "PS7", PS[7][:, 0:e - a], T.BO[:, :], T.UH[:, a:e])
+            act(uh, th, T.TH1[:, a:e], T.UH[:, a:e], F.Copy, scale=23.0)
+            ts("PS7", "NH%d" % h, T.NH[:, a:e], PS[7][:, 0:e - a], 1.25, A.is_lt, 512.0, A.mult)
+            tt(th + " NH%d" % h, th, T.TH1[:, a:e], T.TH1[:, a:e], T.NH[:, a:e], A.subtract)
 
         def head2(ch):
             k0, nk = CH2[ch]
             r, w = slice(k0, k0 + nk), slice(k0 // 16, (k0 + nk) // 16)
-            ts(SK + " PU", "PC%d" % ch, T.PC[:, r], ind(T.S[:, SW:7 * SW + 16 + 16 * nk], T.PU[:, w]), 255.0, A.min)
+            ts(finals(k0, nk)[0] + " PU%d" % min(ch, 1), "PC%d" % ch, T.PC[:, r], ind(finals(k0, nk)[1], T.PU[:, w]), 255.0, A.min)
             spread(ch, k0, nk)
-            tt("PC%d NH" % ch, "XNW%d" % ch, T.XNW[:, r], T.PC[:, r], T.NH[:, r], A.max)
+            tt("PC%d NH%d" % (ch, min(ch, 1)), "XNW%d" % ch, T.XNW[:, r], T.PC[:, r], T.NH[:, r], A.max)
             tt("X Xd TL XNW%d" % ch, "NE%d" % ch, T.NE[:, r], ind(T.X[:, 0:800], T.TL[:, w]), T.XNW[:, r], A.not_equal)
             mm("NE%d BO" % ch, "PS6", PS[6][:, 0:nk], T.BO[:, :], T.NE[:, r])
             wide(ch, k0, nk, T.ID, "ID", "PG", "PG", F.Abs, bias=-255.0)
@@ -714,7 +713,7 @@ def rank_program(g, core, T, topo):
         def marks(ch):
             k0, nk = CH2[ch]
             r = slice(k0, k0 + nk)
-            tt("PS4 TH1", "REJ%d" % ch, T.REJ[:, r], PS[4][:, 0:nk], T.TH1[:, r], A.is_lt)
+            tt("PS4 TH%d" % min(ch, 1), "REJ%d" % ch, T.REJ[:, r], PS[4][:, 0:nk], T.TH1[:, r], A.is_lt)
             dl = "DL%d" % ch
             tt(dl + " REJ%d" % ch, dl, T.DL[:, r], T.DL[:, r], T.REJ[:, r], A.mult)
             tt(dl + " PS5", dl, T.DL[:, r], T.DL[:, r], PS[5][:, 0:nk], A.add)
@@ -729,10 +728,8 @@ def rank_program(g, core, T, topo):
         def every(name):
             return " ".join("%s%d" % (name, ch) for ch in range(len(CH2)))
         for ch, (k0, nk) in enumerate(CH2):
-            passes("BG", k0, k0 + nk, [] if ch else [used2, has2, lambda: held[1](), lambda: held[2](), lambda: held[3]()])
+            passes("BG", k0, k0 + nk, [])
             head2(ch)
-            if ch == 0:
-                tt("TH1 NH", "TH1", T.TH1[:, :], T.TH1[:, :], T.NH[:, :], A.subtract)
             count2(ch)
             marks(ch)
         dma("a", "WA8", "M32", T.M32[:, :], T.WA[8:128:16, 0:MW], 432)

@@ -3,43 +3,75 @@ from concourse.bass import DstId, RemoteDMATransfer
 A = AluOpType
 F = ActivationFunctionType
 BF, F32, I32, U16 = "bfloat16", "float32", "int32", "uint16"
-C, NT, K1, K2, RO = 288, 640, 112, 160, 4
+C, NT, K1, K2, RO, SC = 288, 640, 112, 160, 4, 72
 XN = 1184
 EC = 312
 MW = 13824
 SW = 1040
 ONE = 1.278465
-CH1 = [(0, 64), (64, 48)]
-CH2 = [(0, 64), (64, 64), (128, 32)]
-T_CYC, T_GATH, T_SCAT, T_FIX, T_PE, T_HOP, T_DMA, T_KB, T_REMOTE = 0.001, 1.5, 3.5, 0.05, 0.0007, 0.13, 2.0, 288.0, 2.5
-LA, NA, SO, EA, SA = True, 0, True, (1, 1, 0, 1), False
-MA, PA, OA = 96, 128, 96
-T_OWN = (0.13, 0.0)
-PLAN, TURNS = {}, 6
-CUTS = sorted(set([k0 for k0, nk in CH2] + [MA, K2] + list(range(0, MA, 48))))
+BIG = 16384.0
+
+
+def sure_cameras():
+    out, reach = [], 0
+    for u in range(RO):
+        n = max(min(K1 - (reach - SC * u), C - reach), 0)
+        out.append((reach, n if u == 0 else n // 32 * 32))
+        reach = min(reach + K1, C)
+    return out
+
+
+SURE = sure_cameras()
+CH1 = [(32, 64, 16), (64, 32, 16), (32, 32, 32, 16), (32, 64, 16)]
+CH2 = (64, 64, 32)
+UG1 = [(1, 3), (1, 3), (1, 4), (1, 3)]
+UG2 = (1, 3)
+IG2 = (1, 2, 3)
+TIMES = (0.0009, 1.56, 3.8, 0.05, 0.0005, 0.17, 1.5, 200.0, 1.9)
+T_CYC, T_GATH, T_SCAT, T_FIX, T_PE, T_HOP, T_DMA, T_KB, T_REMOTE = TIMES
+ON = dict(LW=0, SG=0, PC1=0, PC2=1, XOLD=1, CLIP=(1, 1, 1, 1), LOG=(1, 1, 1, 1), OG=(1, 1, 1, 1), PG=(1, 0, 1, 0, 1), BG=(0, 1, 1, 1, 1))
+MA = 96
+MCALL = 16
+PLAN = {}
+TURNS = 3
+ROUNDS = 6
+STEPS = 1500
+TABU = 10
+JITTER = 0.02
+SEED = 1
+WORTH = ((0.92, 0.2), (1.15, 0.06))
+
+
+def spans(sizes):
+    return [(sum(sizes[:i]), n) for i, n in enumerate(sizes)]
+
+
+CUTS = sorted(set([k0 for k0, nk in spans(CH2)] + [MA, K2] + list(range(0, K2, MCALL))))
 CALLS = list(zip(CUTS[:-1], CUTS[1:]))
+SCALED = dict(I50=50.0, N50=-50.0, IXN=float(XN), I864=864.0, NBG=-BIG, I288=288.0, I23=23.0 * 8192, N19=-524288.0,
+              ISW=float(SW), I16=16.0, NI=-1.0)
 SB = {
-    "WA": (MW + 768, F32), "WB": (MW + 1024, BF), "ONA": (896, F32), "ONM": (768, F32), "ONB": (1024, BF),
-    "O": (4608, BF), "LOG": (400 + RO * 1792, BF), "OG": (1792, BF), "PG": (2560, BF), "FS": (640, BF), "FN": (16, F32),
+    "WA": (MW + 864, F32), "WB": (MW + 864, BF), "ONA": (512, F32), "ONM": (512, F32), "ONB": (512, BF),
+    "O": (4608, BF), "LOG": (400 + RO * 1792, BF), "OG": (1792, BF), "PG": (2560, BF), "FS": (640, BF), "FN": (64, BF),
     "M32": (864, F32), "M16": (864, BF), "MC": (864, BF), "Z32": (864, F32), "Z16": (864, BF),
     "CTL": (432, F32), "CTO": (432, F32), "OO": (432, F32), "PTR": (432, BF), "PTD": (448, BF),
     "TC": (800, F32), "LO": (800, BF), "LW": (1280, F32), "TID": (640, F32), "DI": (160, F32), "X": (1200, BF),
     "EXP": (1024, BF), "SEL": (2048, BF), "CP": (1024, BF), "D": (1792, BF), "BG": (2560, BF), "S": (7 * SW, BF), "SS": (7 * SW, BF), "KP": (640, BF), "DG": (160, BF),
-    "ID": (128, BF), "NI": (128, BF), "BO": (128, BF), "M1": (128, BF), "M2": (128, BF), "I200": (128, BF),
-    "IXN": (128, BF), "PM": (384, BF), "TRI": (512, BF), "ZE": (144, BF), "RQ": (128, F32), "RG": (128, F32),
+    "ID": (128, BF), "BO": (128, BF), "M1": (128, BF), "M2": (128, BF), "II": (128 * len(SCALED), BF),
+    "PM": (384, BF), "TRI": (512, BF), "ZE": (288, BF), "RQ": (128, F32), "RG": (128, F32),
     "SI": (16, I32), "SF": (32, F32), "D16": (16, F32), "CI": (640, I32),
     "SNX": (384, BF), "SNB": (384, BF), "SG": (384, BF),
-    "DU1": (112, F32), "DU2": (160, F32), "RB": (40, F32), "RB1": (40, F32), "OFF": (16, F32), "DM": (16, F32),
+    "DU1": (112, F32), "DU2": (160, F32), "KIU": (160, F32), "OFF": (32, F32), "DM": (16, F32),
     "TH5": (16, F32), "PB": (16, F32), "FL": (288, BF), "QC": (304, BF), "NP": (288, BF), "CAP": (288, BF),
     "JK": (288, BF), "FG": (288, BF), "ACC": (8, F32), "W1": (16, F32), "W2": (16, F32), "W3": (16, F32),
     "WL": (8, U16), "XO": (112, U16), "OU": (112, U16), "FU": (112, U16), "XF": (112, F32), "FO": (112, F32),
-    "UH": (160, BF), "TH1": (160, F32), "LV": (112, BF), "LU": (112, BF), "FIT": (112, BF), "NONE": (112, BF),
-    "DIE": (112, F32), "KI": (16, I32), "PU": (16, U16), "PC": (160, BF), "PT": (384, BF),
-    "G1": (32, F32), "G2": (32, F32), "GU": (32, U16),
-    "FB": (40, BF), "FA": (40, BF), "PP": (40, BF), "B1": (40, F32), "B2": (40, F32), "BU": (40, U16),
-    "L1": (160, F32), "L2": (160, F32), "TL": (16, U16), "CF": (160, F32), "CU": (160, U16), "LO4": (160, F32),
-    "IU": (160, U16), "MO": (160, BF), "PEN": (160, BF), "IF": (128, F32), "I864": (128, BF), "IBG": (128, BF), "NH": (160, BF), "XNW": (160, BF), "NE": (160, BF),
-    "SN": (160, BF), "DL": (160, F32), "REJ": (160, F32), "MU": (160, U16), "YT": (40, F32),
+    "UH": (160, BF), "LV": (112, BF), "FIT": (112, BF), "NONE": (112, BF),
+    "DIE": (112, F32), "KI": (16, I32), "KB": (16, BF), "PU": (16, U16), "PC": (160, BF), "PT": (512, BF),
+    "DEAD": (32, BF), "GU": (32, U16),
+    "FB": (40, BF), "FA": (40, BF), "PP": (40, BF), "NG": (40, BF), "B1": (40, F32), "B2": (40, BF), "BU": (40, U16),
+    "L1": (160, F32), "L2": (160, F32), "TL": (16, U16), "CF": (160, F32), "CU": (160, U16),
+    "IU": (160, U16), "MO": (160, BF), "PEN": (160, BF), "IF": (128, F32), "NH": (160, BF), "XOLD": (160, BF), "NE": (160, BF),
+    "SN": (160, BF), "P0": (160, F32), "P1": (160, F32), "MU": (160, U16), "YT": (40, F32),
 }
 SCRATCH = {k: ("sbuf", [128, v[0]], v[1]) for k, v in SB.items()}
 for _b in range(8):
@@ -58,6 +90,18 @@ def relay_of(T, topo, r, d):
     return can[far.index(d) % len(can)]
 
 
+def share(T, topo, r, d):
+    rl = relay_of(T, topo, r, d)
+    if rl is None:
+        return topo.engines(T.cores[r], T.cores[r ^ d])
+    far = [e for e in (1, 2, 3) if relay_of(T, topo, r, e) is not None]
+    eng = topo.engines(T.cores[r], rl)
+    n = 1
+    while 2 * n * len(far) <= len(eng):
+        n *= 2
+    return eng[n * far.index(d):n * far.index(d) + n]
+
+
 def bits(engines):
     return sum(1 << e for e in engines)
 
@@ -74,10 +118,240 @@ def relay_program(g, core, T, topo):
                 rid, pid = topo.addr(dst, core)
                 eng = topo.engines(core, dst)
                 for n in range(2 * RO):
-                    g.wait_ge(T.sem["arr%d" % n], 4)
+                    g.wait_ge(T.sem["arr%d" % n], len(share(T, topo, r, d)))
                     g.remote_dma(landing(T, n, d), T.O[:, 128 * n:128 * n + 128], T.sem["arr%d" % n], T.sem.loc0,
                                  pid, rid, bits(eng))
                 g.wait_ge(T.sem.loc0, 2 * RO * len(eng))
+
+
+READS, FOLLOWS, SHARES, AFTER = 3, 2, 1, 0
+
+
+def waits(kind, q, qd):
+    return kind == READS or kind == FOLLOWS and not q == qd == "t" or kind == SHARES and q != qd
+
+
+def plan(nodes, users):
+    n = len(nodes)
+    queue, busy, lat = [x[0] for x in nodes], [x[1] for x in nodes], [x[2] for x in nodes]
+    comp = [x[5] for x in nodes]
+    either = [i for i in range(n) if nodes[i][6]]
+
+    def links(extra):
+        pre, post = [[] for _ in range(n)], [[] for _ in range(n)]
+        for i in range(n):
+            for d, kind in list(nodes[i][3].items()) + list(extra.get(i, {}).items()):
+                w = waits(kind, queue[i] if comp[i] else None, queue[d] if comp[d] else None)
+                pre[i].append((d, lat[d] + T_HOP if w else busy[d], w))
+                post[d].append((i, lat[d] - busy[d] + T_HOP if w else 0.0))
+        return pre, post
+
+    def place(seq, edges, back):
+        at0, slots = [0.0] * n, {q: [] for q in "vatgsx"}
+        for i in seq:
+            b = busy[i]
+            if back:
+                at = max([lat[i] - b] + [at0[e[0]] + busy[e[0]] + e[1] for e in edges[i]])
+            else:
+                at = max([0.0] + [at0[e[0]] + e[1] for e in edges[i]])
+            row = slots[queue[i]]
+            lo = len(row)
+            while lo and row[lo - 1][1] > at:
+                lo -= 1
+            while lo < len(row) and at + b > row[lo][0] + 1e-9:
+                at = max(at, row[lo][1])
+                lo += 1
+            row.insert(lo, (at, at + b))
+            at0[i] = at
+        return at0
+
+    def worth(start, pre):
+        seq, out = sorted(range(n), key=lambda k: start[k]), 0.0
+        for speed, hop in WORTH:
+            free, at = {q: 0.0 for q in "vatgsx"}, [0.0] * n
+            for i in seq:
+                x = max([free[queue[i]]] + [at[d] + hop for d, gap, w in pre[i] if w])
+                f = speed if comp[i] else 1.0
+                free[queue[i]] = x + busy[i] * f
+                at[i] = x + lat[i] * f
+            out += max(at)
+        return out
+
+    def backwards(start, post):
+        late = place(sorted(range(n), key=lambda k: -start[k] - busy[k]), post, True)
+        return [-late[k] - busy[k] for k in range(n)]
+
+    def settle(start, pre, post, turns):
+        best = (worth(start, pre), start)
+        for _ in range(turns):
+            late = backwards(start, post)
+            start = place(sorted(range(n), key=lambda k: late[k]), pre, False)
+            best = min(best, (worth(start, pre), start))
+        return best
+
+    def banks(start, post):
+        bank, extra, last = {}, {}, [(-1e9 - b, None) for b in range(8)]
+        post, start = [[e[0] for e in p] for p in post], list(start)
+        for k in sorted(users, key=lambda k: start[users[k][0]]):
+            first = users[k][0]
+            for b in sorted(range(8), key=lambda b: last[b][0]):
+                old = users[last[b][1]] if last[b][1] is not None else []
+                seen, todo = {first}, [first] if last[b][0] > start[first] else []
+                while todo:
+                    for e in post[todo.pop()]:
+                        if e not in seen and start[e] <= last[b][0]:
+                            seen.add(e)
+                            todo.append(e)
+                if not seen.intersection(old):
+                    break
+            else:
+                raise ValueError("more than eight products at a time")
+            extra[first] = {i: FOLLOWS for i in old}
+            for i in old:
+                post[i].append(first)
+            todo = [i for i in old if start[i] >= start[first]]
+            while todo:
+                d = todo.pop()
+                for e in post[d]:
+                    if start[e] <= start[d]:
+                        start[e] = start[d] + 1e-3
+                        todo.append(e)
+            bank[k], last[b] = b, (0.0, k)
+            last = [(max(start[i] + lat[i] for i in users[x[1]]), x[1]) if x[1] is not None else x for x in last]
+        return bank, extra
+
+    def swap(i):
+        other = nodes[i][6] if queue[i] == nodes[i][0] else nodes[i][:2]
+        queue[i], busy[i], lat[i] = other[0], other[1], other[1]
+
+    seed = [SEED]
+
+    def draw():
+        seed[0] = (seed[0] * 1103515245 + 12345) % 2147483648
+        return seed[0] / 2147483648
+
+    def improve(start, extra, turns):
+        seq = sorted(range(n), key=lambda k: start[k])
+        full, anc = [dict(nodes[i][3]) for i in range(n)], [0] * n
+        for i, more in extra.items():
+            for d, kind in more.items():
+                full[i][d] = max(kind, full[i].get(d, AFTER))
+        for i in seq:
+            deep = 0
+            for d in full[i]:
+                deep |= anc[d]
+            for d in full[i]:
+                anc[i] |= 1 << d
+            anc[i] |= deep
+            full[i] = {d: kind for d, kind in full[i].items() if not (deep >> d & 1 and comp[d])}
+        needing = [[] for _ in range(n)]
+        for i in range(n):
+            for d in full[i]:
+                needing[d].append(i)
+
+        def gap(d, i):
+            return lat[d] + T_HOP if waits(full[i][d], queue[i] if comp[i] else None, queue[d] if comp[d] else None) else busy[d]
+        pre = [[(d, gap(d, i)) for d in full[i]] for i in range(n)]
+        post = [[(i, gap(d, i)) for i in needing[d]] for d in range(n)]
+        best, tabu = None, {}
+        head, tail, dep, need = [0.0] * (n + 1), [0.0] * (n + 1), [0.0] * n, [0.0] * n
+        before, behind = [n] * (n + 1), [n] * (n + 1)
+        span = busy + [0.0]
+        for turn in range(turns + 1):
+            last = {q: n for q in "vatgsx"}
+            for i in seq:
+                x = 0.0
+                for d, w in pre[i]:
+                    if head[d] + w > x:
+                        x = head[d] + w
+                dep[i] = x
+                p = last[queue[i]]
+                before[i], behind[p], last[queue[i]] = p, i, i
+                head[i] = x if x > head[p] + span[p] else head[p] + span[p]
+            for p in last.values():
+                behind[p] = n
+            for i in reversed(seq):
+                x = lat[i]
+                for e, w in post[i]:
+                    if tail[e] + w > x:
+                        x = tail[e] + w
+                need[i] = x
+                y = span[i] + tail[behind[i]]
+                tail[i] = x if x > y else y
+            length = max(tail)
+            if best is None or length < best[0] - 1e-9:
+                best = (length, head[:n], list(queue))
+            pick = None
+            for at, i in enumerate(seq):
+                if head[i] + tail[i] < length - 1e-6:
+                    continue
+                j = behind[i]
+                if j < n and head[j] < head[i] + span[i] + 1e-6 and head[j] + tail[j] > length - 1e-6 and not anc[j] >> i & 1:
+                    p = before[i]
+                    hj = max(dep[j], head[p] + span[p])
+                    ti = max(need[i], span[i] + tail[behind[j]])
+                    x = max(hj + max(need[j], span[j] + ti), max(dep[i], hj + span[j]) + ti) + JITTER * draw()
+                    if (tabu.get((j, i), -1) < turn or x < best[0]) and (pick is None or x < pick[0]):
+                        pick = (x, i, j)
+                if nodes[i][6] and tabu.get(i, -1) < turn:
+                    q, b = nodes[i][6] if queue[i] == nodes[i][0] else nodes[i][:2]
+                    p = next((k for k in seq[at::-1] if queue[k] == q), n)
+                    e = behind[p] if p < n else next((k for k in seq if queue[k] == q), n)
+                    x = max(dep[i], head[p] + span[p]) + max(need[i] + b - span[i], b + tail[e]) + JITTER * draw()
+                    if pick is None or x < pick[0]:
+                        pick = (x, i, None)
+            if pick is None:
+                break
+            x, i, j = pick
+            if j is None:
+                swap(i)
+                span[i] = busy[i]
+                for x in [i] + needing[i]:
+                    pre[x] = [(d, gap(d, x)) for d in full[x]]
+                for x in [i] + list(full[i]):
+                    post[x] = [(e, gap(x, e)) for e in needing[x]]
+                tabu[i] = turn + TABU * 4
+            else:
+                a, e = seq.index(i), seq.index(j)
+                late, early = {i}, []
+                for k in seq[a + 1:e]:
+                    if before[k] in late or any(d in late for d in full[k]):
+                        late.add(k)
+                    else:
+                        early.append(k)
+                seq[a:e + 1] = early + [j] + [k for k in seq[a:e] if k in late]
+                tabu[(i, j)] = turn + TABU + int(TABU * draw())
+        for i in either:
+            if queue[i] != best[2][i]:
+                swap(i)
+        return best[1]
+
+    pre, post = links({})
+    level = [0.0] * n
+    for i in range(n - 1, -1, -1):
+        level[i] = max([lat[i]] + [level[e[0]] + busy[i] + e[1] for e in post[i]])
+    start = settle(place(sorted(range(n), key=lambda k: -level[k]), pre, False), pre, post, TURNS)[1]
+    best = None
+    for turn in range(ROUNDS):
+        bank, extra = banks(backwards(start, post), links({})[1])
+        pre, post = links(extra)
+        key, left = list(start), [len(p) for p in pre]
+        todo = [i for i in range(n) if not left[i]]
+        while todo:
+            d = todo.pop()
+            for e in post[d]:
+                key[e[0]] = max(key[e[0]], key[d] + 1e-6)
+                left[e[0]] -= 1
+                if not left[e[0]]:
+                    todo.append(e[0])
+        start = settle(place(sorted(range(n), key=lambda k: key[k]), pre, False), pre, post, TURNS)[1]
+        start = improve(start, extra, STEPS)
+        pre, post = links(extra)
+        got = settle(start, pre, post, TURNS)
+        start = got[1]
+        if best is None or got[0] < best[0]:
+            best = got + (bank, extra, list(queue))
+    PLAN.update(worth=best[0], start=best[1], bank=best[2], extra=best[3], queue=best[4])
 
 
 def rank_program(g, core, T, topo):
@@ -85,38 +359,46 @@ def rank_program(g, core, T, topo):
     if rank is None:
         relay_program(g, core, T, topo)
         return
+    if not PLAN:
+        record(g, core, T, topo, rank)
+    record(g, core, T, topo, rank)
+
+
+def record(g, core, T, topo, rank):
     Q = {"v": g.vector, "a": g.scalar, "t": g.tensor, "g": g, "s": g.sync}
     own = {"v": "cv", "a": "ca", "t": "ct", "g": "cg"}
     total = {}
     known = {q: {} for q in Q}
-    writer, readers = {}, {}
+    writer, readers, users = {}, {}, {}
     nodes = []
 
-    def node(q, rd, wr, busy, lat, issue):
-        deps = set()
+    def node(q, rd, wr, busy, lat, issue, comp=False, other=None):
+        deps = {}
         rd, wr = rd.split(), wr.split()
-        for k in rd:
-            if k in writer:
-                deps.add(writer[k])
-            if k.startswith("PS"):
-                deps.update(e for e in readers.get(k, []) if nodes[e][0] != q)
         for k in wr:
+            for e in ([writer[k]] if k in writer else []) + readers.get(k, []):
+                deps[e] = max(deps.get(e, AFTER), AFTER if k == "order" else FOLLOWS)
+        for k in rd:
+            if k.startswith("PS"):
+                deps.update((e, max(deps.get(e, AFTER), SHARES)) for e in readers.get(k, []))
             if k in writer:
-                deps.add(writer[k])
-            deps.update(readers.get(k, []))
-        nodes.append((q, busy, lat, sorted(deps), issue))
+                deps[writer[k]] = READS
+        nodes.append((q, busy, lat, deps, issue, comp, other))
+        for k in rd + wr:
+            if k.startswith("PS"):
+                users.setdefault(k, []).append(len(nodes) - 1)
         for k in rd:
             readers.setdefault(k, []).append(len(nodes) - 1)
         for k in wr:
             writer[k] = len(nodes) - 1
             readers[k] = []
 
-    def op(q, rd, wr, dur, call):
+    def op(q, rd, wr, dur, call, other=None):
         def issue():
             total[own[q]] = total.get(own[q], 0) + 1
             call().then_inc(T.sem[own[q]], 1)
             return own[q], total[own[q]]
-        node(q, rd, wr, dur, dur, issue)
+        node(q, rd, wr, dur, dur, issue, True, other)
 
     ndma = [0]
 
@@ -131,57 +413,19 @@ def rank_program(g, core, T, topo):
         node(q, rd, wr, 0.06, T_DMA + kb / T_KB, issue)
 
     def emit():
-        n = len(nodes)
-        level = [0.0] * n
-        for i in range(n - 1, -1, -1):
-            level[i] += nodes[i][2]
-            for d in nodes[i][3]:
-                level[d] = max(level[d], level[i] + (T_HOP if nodes[d][0] != nodes[i][0] else T_OWN[nodes[i][0] == "t"]))
-        after = [[] for _ in range(n)]
-        for i in range(n):
-            for d in nodes[i][3]:
-                after[d].append(i)
-
-        def place(seq, back):
-            at0, slots = [0.0] * n, {q: [] for q in list(Q) + ["x"]}
-            for i in seq:
-                q, busy, lat = nodes[i][0], nodes[i][1], nodes[i][2]
-                at = 0.0
-                for d in (after[i] if back else nodes[i][3]):
-                    at = max(at, at0[d] + (nodes[d][1] + lat - busy if back else nodes[d][2]) + (T_HOP if nodes[d][0] != q else T_OWN[q == "t"]))
-                if back and not after[i]:
-                    at = lat - busy
-                row = slots[q]
-                lo, hi = 0, len(row)
-                while lo < hi:
-                    mid = (lo + hi) // 2
-                    if row[mid][1] <= at:
-                        lo = mid + 1
-                    else:
-                        hi = mid
-                while lo < len(row) and at + busy > row[lo][0] + 1e-9:
-                    at = max(at, row[lo][1])
-                    lo += 1
-                row.insert(lo, (at, at + busy))
-                at0[i] = at
-            return at0
-        if "start" not in PLAN:
-            start = place(sorted(range(n), key=lambda k: (-level[k], k)), False)
-            best = (max(start), start)
-            for _ in range(TURNS):
-                late = place(sorted(range(n), key=lambda k: (-start[k] - nodes[k][1], -k)), True)
-                start = place(sorted(range(n), key=lambda k: (-late[k] - nodes[k][1], k)), False)
-                if max(start) < best[0]:
-                    best = (max(start), start)
-            PLAN["start"] = best[1]
-        start = PLAN["start"]
+        if not PLAN:
+            plan(nodes, users)
+            return
+        n, start = len(nodes), PLAN["start"]
         event = [None] * n
-        for i in sorted(range(n), key=lambda k: (start[k], k)):
-            q = nodes[i][0]
+        for i in sorted(range(n), key=lambda k: start[k]):
+            q, deps = nodes[i][0], dict(PLAN["extra"].get(i, {}))
+            for d, kind in nodes[i][3].items():
+                deps[d] = max(kind, deps.get(d, AFTER))
             if q != "x":
-                for d in sorted(nodes[i][3], key=lambda k: -event[k][1]):
+                for d in sorted(deps, key=lambda k: (-event[k][1], k)):
                     sem, cnt, clock = event[d]
-                    if not (q == "t" and sem == "ct"):
+                    if waits(deps[d], q if nodes[i][5] else None, nodes[d][0] if nodes[d][5] else None):
                         if known[q].get(sem, 0) < cnt:
                             Q[q].wait_ge(T.sem[sem], cnt)
                             known[q][sem] = cnt
@@ -240,8 +484,17 @@ def rank_program(g, core, T, topo):
     def act(rd, wr, out, in_, f, **kw):
         op("a", rd, wr, cost(out, [in_], 1.0) + 0.015, lambda: s.activation(ap(out), ap(in_), f, **kw))
 
+    def group(rd, wr, calls):
+        def issue():
+            for c in calls:
+                t.matmul(*c).then_inc(T.sem.ct, 1)
+            total["ct"] = total.get("ct", 0) + len(calls)
+            return "ct", total["ct"]
+        dur = sum(max(64, size(c[2])) * T_PE * (4 if SCRATCH[c[2].name][2] == F32 else 1) for c in calls)
+        node("t", rd, wr, dur, dur, issue, True)
+
     def mm(rd, wr, out, lhsT, rhs, st=True, sp=True):
-        op("t", rd, wr, max(64, size(rhs)) * T_PE, lambda: t.matmul(out, lhsT, rhs, st, sp))
+        group(rd, wr, [(out, lhsT, rhs, st, sp)])
 
     def iota(wr, out, pat, base, ch=0, exact=False):
         if exact:
@@ -249,10 +502,36 @@ def rank_program(g, core, T, topo):
         else:
             op("g", "", wr, 0.13 + 2 * size(out) * T_CYC, lambda: g.iota(out, pat, base, ch, allow_small_or_imprecise_dtypes=True))
 
-    PS = [T["PS%d" % b] for b in range(8)]
+    def either(on_scalar, rd, wr, out, in_, on_a, on_v):
+        q = PLAN["queue"][len(nodes)] if PLAN else "va"[on_scalar]
+        da, dv = cost(out, [in_], 1.0) + 0.015, cost(out, [in_], None)
+        op(q, rd, wr, da if q == "a" else dv, on_a if q == "a" else on_v, ("v", dv) if q == "a" else ("a", da))
 
-    def seg(name, k0, k1):
-        return T[name][:, 16 * k0:16 * k1]
+    def move(on_scalar, rd, wr, out, in_, f=F.Copy):
+        either(on_scalar, rd, wr, out, in_, lambda: s.activation(ap(out), ap(in_), f), lambda: v.tensor_copy(ap(out), ap(in_)))
+
+    def relu(rd, wr, out, in_, plus):
+        either(1, rd, wr, out, in_, lambda: s.activation(out, in_, F.Relu, bias=plus), lambda: v.tensor_scalar(out, in_, plus, 0.0, A.add, A.max))
+
+    PS = []
+
+    def small():
+        PS.append(T["PS%d" % (PLAN["bank"]["PS%d" % len(PS)] if PLAN else 0)])
+        return len(PS) - 1
+    nextbank = small
+
+    def mat(name):
+        if name in SCALED:
+            i = list(SCALED).index(name)
+            return T.II[:, 128 * i:128 * i + 128]
+        return T[name][:, :]
+
+    def mms(b, n, terms, st=True, sp=True, c0=0):
+        for i, (m, rd, x) in enumerate(terms):
+            mm(rd + " " + m, "PS%d" % b, PS[b][:, c0:c0 + n], mat(m), x, st and i == 0, sp and i == len(terms) - 1)
+
+    def seg(name, k0, k1, c0=0):
+        return T[name][:, 16 * (c0 + k0):16 * (c0 + k1)]
 
     def col(name, j, k0, k1):
         return T[name][:, 16 * k0 + j:16 * k1:16]
@@ -260,46 +539,47 @@ def rank_program(g, core, T, topo):
     def keys(name, k0, k1):
         return " ".join("%s_%d" % (name, b) for b in range(k0 // 16, (k1 + 15) // 16))
 
-    def E(j):
-        return T.ZE[:, 15 - j:143 - j]
+    def E(j, z=0):
+        return T.ZE[:, z + 15 - j:z + 143 - j]
 
-    def fold(b, out, name, k0, k1, rd=None):
-        for j in range(16):
-            mm((rd or keys(name, k0, k1)) + " ZE", "PS%d" % b, out, E(j), col(name, j, k0, k1), j == 0, j == 15)
+    def fold(b, name, k0, k1, rd=None, st=True, sp=True, z=0):
+        group((rd or keys(name, k0, k1)) + " ZE ZS", "PS%d" % b,
+              [(PS[b][:, 0:k1 - k0], E(j, z), col(name, j, k0, k1), st and j == 0, sp and j == 15) for j in range(16)])
 
-    def exchange(n, srckey, src, b):
+    def exchange(n, srckey, src, after=""):
         snd, key, loc = (T.SNX, "SNX", "loc0") if n % 2 == 0 else (T.SNB, "SNB", "loc1")
-        for d in (1, 2, 3):
-            c0 = 128 * (d - 1)
-            mm(srckey + " PM", "PS%d" % b, PS[b][:, c0:c0 + 128], T.PM[:, c0:c0 + 128], src[:, c0:c0 + 128])
-        act("PS%d" % b, key, snd[:, :], PS[b][:, 0:384], F.Copy)
-        trs, used, arr = [], [], 0
-        for d in sorted((1, 2, 3), key=lambda e: relay_of(T, topo, rank, e) is not None):
-            rl = relay_of(T, topo, rank, d)
-            dst = T.cores[rank ^ d] if rl is None else rl
-            free = [e for e in topo.engines(core, dst) if e not in used]
-            eng = free[:8] if rl is None else free[:4]
-            used += eng
-            rid, pid = topo.addr(dst, core)
-            trs.append(RemoteDMATransfer(dst_ids=[DstId(rid=rid, pnc=pid)], dma_engine_mask=bits(eng),
-                                         remote_sem=T.sem["arr%d" % n], src=snd[:, 128 * (d - 1):128 * d],
-                                         dst=landing(T, n, d) if rl is None else T.O[:, 128 * n:128 * n + 128]))
-            prl = relay_of(T, topo, rank ^ d, d)
-            arr += 8 if prl is None else len(topo.engines(prl, core))
+        b = small()
+        group(srckey + " PM1 PM2 PM3", "PS%d" % b, [(PS[b][:, c0:c0 + 128], T.PM[:, c0:c0 + 128], src[:, c0:c0 + 128], True, True) for c0 in (0, 128, 256)])
+        move(1, "PS%d" % b, key, snd[:, :], PS[b][:, 0:384])
+        arr = 0
+        for far in (True, False):
+            trs, used = [], 0
+            for d in (1, 2, 3):
+                rl = relay_of(T, topo, rank, d)
+                if (rl is not None) == far:
+                    eng = share(T, topo, rank, d)
+                    used += len(eng)
+                    rid, pid = topo.addr(T.cores[rank ^ d] if rl is None else rl, core)
+                    trs.append(RemoteDMATransfer(dst_ids=[DstId(rid=rid, pnc=pid)], dma_engine_mask=bits(eng),
+                                                 remote_sem=T.sem["arr%d" % n], src=snd[:, 128 * (d - 1):128 * d],
+                                                 dst=landing(T, n, d) if rl is None else T.O[:, 128 * n:128 * n + 128]))
+                    prl = relay_of(T, topo, rank ^ d, d)
+                    arr += len(topo.engines(T.cores[rank ^ d] if prl is None else prl, core))
 
-        def send():
-            g.remote_dma_fused(trs, local_sem=T.sem[loc])
-            total[loc] = total.get(loc, 0) + len(used)
-            return loc, total[loc]
+            def send(trs=trs, used=used):
+                g.remote_dma_fused(trs, local_sem=T.sem[loc])
+                total[loc] = total.get(loc, 0) + used
+                return loc, total[loc]
+            node("g", key + after, "order" + (" sent%d" % n if far else ""), 0.3, T_REMOTE, send)
 
         def arrive():
             total["arr%d" % n] = arr
             return "arr%d" % n, arr
-        node("g", key, "sent", 0.3, T_REMOTE, send)
-        node("x", "sent", "XG" if n % 2 == 0 else "LG", 0.01, T_REMOTE, arrive)
+        node("x", "sent%d" % n, "XG" if n % 2 == 0 else "LG", 0.01, T_REMOTE + (4.0 if n == 0 else 0.0), arrive)
 
-    dma("s", "", "X", T.X[:, 0:640], T.x0[:, :], 160)
+    dma("s", "", "Xb", T.X[:, 0:384], T.x0[:, 0:384], 96)
     dma("a", "", "CI CIb", T.CI[:, 0:288], T.ct[:, :], 144)
+    dma("s", "", "X", T.X[:, 384:640], T.x0[:, 384:640], 64)
     dma("s", "", "O0", T.O[:, 0:1792], T.obs[:, 0:1792], 448)
     iota("SI", T.SI[:, 0:8], [[0, 8]], 0, 1, True)
     iota("RQ", T.RQ[:, :], [[1, 128]], 0)
@@ -310,13 +590,13 @@ def rank_program(g, core, T, topo):
     for i, m in enumerate((16, 32, 48, 15, 112)):
         ts("SI", "SI%d" % i, T.SI[:, 8 + i:9 + i], T.SI[:, 0:1], m, A.bitwise_and)
     cp("SI SI0 SI1 SI2 SI3 SI4", "SF", T.SF[:, 0:13], T.SI[:, 0:13])
-    PF, SC, GC = T.SF[:, 0:1], T.SF[:, 11:12], T.SF[:, 12:13]
+    PF, P16, GC = T.SF[:, 0:1], T.SF[:, 11:12], T.SF[:, 12:13]
     ts("SF", "SFb", T.SF[:, 16:19], T.SF[:, 8:11], -2.0, A.mult, PF, A.add)
     for d in (1, 2, 3):
-        ts("RQ SF SFb", "PM", T.PM[:, 128 * (d - 1):128 * d], T.RQ[:, :], -16.0 * d, A.add, T.SF[:, 15 + d:16 + d], A.is_equal)
-    exchange(0, "X", T.X, 4)
+        ts("RQ SF SFb", "PM%d" % d, T.PM[:, 128 * (d - 1):128 * d], T.RQ[:, :], -16.0 * d, A.add, T.SF[:, 15 + d:16 + d], A.is_equal)
+    exchange(0, "Xb", T.X)
     ms("ONA", T.ONA[:, :], ONE)
-    ts("OO SF", "OO", T.OO[:, :], T.OO[:, :], SC, A.add, 4607.0, A.min)
+    ts("OO SF", "OO", T.OO[:, :], T.OO[:, :], P16, A.add, 4607.0, A.min)
     ts("CI", "CTO", T.CTO[:, 0:288], T.CI[:, 0:288], 10240.0, A.is_ge, 20000.0, A.mult)
     ts("OO", "DU1", T.DU1[:, :], T.OO[:, 0:112], 10240.0, A.add)
     tt("CTO CI", "CTO", T.CTO[:, 0:288], T.CTO[:, 0:288], T.CI[:, 0:288], A.add)
@@ -331,16 +611,20 @@ def rank_program(g, core, T, topo):
     dma("s", "", "CI CIb", T.CI[:, :], T.tv[:, :], 320)
     dma("s", "CI", "O1", T.O[:, 1792:4608], T.obs[:, 1792:4608], 704)
 
+    def sbuf(ch):
+        return "SS" if ch % 2 else "S"
+
     def constants():
         ts("RQ SF", "ID", T.ID[:, :], T.RQ[:, :], PF, A.is_equal)
         ts("RG SF", "BO", T.BO[:, :], T.RG[:, :], GC, A.is_equal)
-        ms("ZE", T.ZE[:, :], 0.0)
-        ts("ID", "NI", T.NI[:, :], T.ID[:, :], -1.0, A.mult)
+        ms("ZE", T.ZE[:, 0:144], 0.0)
         cp("BO ZE", "ZE", T.ZE[:, 15:143:16], T.BO[:, 0:128:16])
-        for name, x in (("I200", 200.0), ("IXN", float(XN)), ("IF", 1.0), ("I864", 864.0), ("IBG", 18432.0)):
-            act("ID", name, T[name][:, :], T.ID[:, :], F.Copy, scale=x)
+        act("ZE", "ZS", T.ZE[:, 144:288], T.ZE[:, 0:144], F.Copy, scale=-32768.0)
+        for name, x in SCALED.items():
+            act("ID", name, mat(name), T.ID[:, :], F.Copy, scale=x)
+        act("ID", "IF", T.IF[:, :], T.ID[:, :], F.Copy)
         ts("ID", "M2", T.M2[:, :], T.ID[:, :], 100.0, A.mult)
-        ts("RQ SF", "D16", T.D16[:, :], T.RQ[:, 0:16], SC, A.is_equal, 1024.0, A.mult)
+        ts("RQ SF", "D16", T.D16[:, :], T.RQ[:, 0:16], P16, A.is_equal, 1024.0, A.mult)
         tt("BO M2", "M1", T.M1[:, :], T.BO[:, :], T.M2[:, :], A.add)
         tt("BO M2", "M2", T.M2[:, :], T.BO[:, :], T.M2[:, :], A.subtract)
         ms("EXP", T.EXP[:, :], 1.0)
@@ -353,419 +637,385 @@ def rank_program(g, core, T, topo):
         iota("TID", T.TID[:, :], [[1, 40], [40, 16]], 64)
         iota("DI", T.DI[:, :], [[1, 160]], 704)
         ts("CP", "CP", T.CP[:, :], T.CP[:, :], -14.5, A.add, 2048.0, A.mult)
-        for k in range(7):
-            ms("S%d" % k, T.S[:, k * SW:k * SW + 16], 1024.0)
-            ms("SS%d SS%d" % (k, (k + 6) % 7), T.SS[:, max(k * SW - 256, 0):k * SW + 16], 1024.0)
+        for ch in range(2):
+            sb, gap = sbuf(ch), SW - 16 - 16 * CH1[0][ch]
+            for k in range(7):
+                ms("%s%d %s%d" % (sb, k, sb, (k + 6) % 7), T[sb][:, max(k * SW - gap, 8):k * SW + 16], 1024.0)
+            ms(sb + "n", T[sb][:, 0:8], 512.0)
         ms("LOGn", T.LOG[:, 384:400], 1024.0)
-        for c0 in (0, 4, 8):
-            ts("OO", "FN", T.FN[:, c0:c0 + 4], T.OO[:, 0:4], 16.0, A.mult)
-        ts("SF", "SFd", T.SF[:, 21:22], SC, 4096.0 - 384, A.add)
-        cp("PTD PTR", "PTR", T.PTR[:, 0:K1], T.PTD[:, 0:K1])
+        for i, sizes in enumerate(CH1 + [CH2]):
+            for k0, nk in spans(sizes):
+                if i == 0 or sizes != (CH1 + [CH2])[i - 1]:
+                    c0 = 10 * fn_of(i) + k0 // 16
+                    act("OO", keys("FN", 16 * c0, 16 * c0 + nk), T.FN[:, c0:c0 + nk // 16], T.OO[:, 0:nk // 16], F.Copy)
+        ts("SF", "SFd", T.SF[:, 21:22], P16, 4096.0 - 384, A.add)
         for j in range(16):
             act("BO D16", "SEL%d" % j, T.SEL[:, 128 * j:128 * j + 128], T.BO[:, :], F.Copy, scale=T.D16[:, j:j + 1])
 
+    def fn_of(i):
+        while 0 < i < RO and CH1[i] == CH1[i - 1]:
+            i -= 1
+        return i
+
     def constants2():
         ms("Z16", T.Z16[:, :], 0.0)
-        dma("s", "Z16 TC", "WB", T.WB[0:128:16, 0:MW], T.Z16[:, :], 216)
-        ts("KP SF", "DG", T.DG[:, :], T.KP[:, 0:160], SC, A.is_equal)
-        ts("KP", "KP", T.KP[:, :], T.KP[:, :], 0.0, A.not_equal)
+        dma("s", "Z16 TC", "WB", T.WB[0:128:16, 864:864 + MW], T.Z16[:, :], 216)
+        ts("KP SF", "DG", T.DG[:, :], T.KP[:, 0:160], P16, A.is_equal)
         ts("CI", "LWi", T.LW[:, 0:640], T.CI[:, :], 0.0, A.add)
         ts("CI", "CI", T.CI[:, :], T.CI[:, :], 4, A.arith_shift_right)
         cp("CI", "TC", T.TC[:, 0:640], T.CI[:, :])
         ms("TCx", T.TC[:, 640:800], float(EC))
         ms("LOx", T.LO[:, 640:800], 0.0)
         act("TC", "LWj", T.LW[:, 640:1280], T.TC[:, 0:640], F.Copy, scale=-16.0)
-        iota("CI", T.CI[:, 0:512], [[-3, 4], [1, 128]], 48, 0, True)
         tt("LWi LWj", "LO LW", T.LO[:, 0:640], T.LW[:, 0:640], T.LW[:, 640:1280], A.add)
         ts("KI", "KI", T.KI[:, 0:4], T.KI[:, 0:4], 15, A.bitwise_and)
-        cp("KI", "W3", T.PB[:, 0:4], T.KI[:, 0:4])
-        ts("SF", "SFc", T.SF[:, 20:21], SC, 40.0, A.mult, 640.0, A.add)
-        ts("SF", "SFe", T.SF[:, 22:23], SC, 0.0, A.not_equal, ONE, A.mult)
-        ts("RQ SFc", "RB", T.RB[:, :], T.RQ[:, 0:40], T.SF[:, 20:21], A.add)
-        ts("RQ SFc", "RB1", T.RB1[:, :], T.RQ[:, 0:40], T.SF[:, 20:21], A.add, 1.0, A.add)
-        ms("FA", T.FA[:, :], 0.0)
-        ts("CI", "CI", T.CI[:, 0:512], T.CI[:, 0:512], 15, A.bitwise_and)
+        cp("KI", "PB", T.PB[:, 0:4], T.KI[:, 0:4])
+        ts("PB", "PBb", T.PB[:, 4:8], T.PB[:, 0:4], -40.0, A.mult, 1280.0, A.add)
         for u in range(RO):
-            ts("CI W3", "TRI%d" % u, T.TRI[:, 128 * u:128 * u + 128], T.CI[:, 128 * u:128 * u + 128], T.PB[:, u:u + 1], A.is_gt)
+            act("RQ PBb", "KIU%d" % u, T.KIU[:, 40 * u:40 * u + 40], T.RQ[:, 0:40], F.Identity, scale=-1.0, bias=T.PB[:, 4 + u:5 + u])
+        ts("SF", "SFe", T.SF[:, 22:23], P16, 0.0, A.not_equal, ONE, A.mult)
+        ms("FA", T.FA[:, :], 1.0)
+        ms("NG", T.NG[:, :], -1.0)
+        for u in range(RO):
+            ts("KP PB", "TRI%d" % u, T.TRI[:, 128 * u:128 * u + 128], T.KP[:, 16 - 3 * u:144 - 3 * u], T.PB[:, u:u + 1], A.is_gt)
+        ts("KP", "KP", T.KP[:, :], T.KP[:, :], 0.0, A.not_equal)
         for u in range(RO):
             tt("TRI%d BO" % u, "TRI%d" % u, T.TRI[:, 128 * u:128 * u + 128], T.TRI[:, 128 * u:128 * u + 128], T.BO[:, :], A.mult)
 
+    VC = 2
+
+    def listed(u):
+        s0, ns = SURE[u]
+        wrap = s0 + K1 > C
+        return (0, C, True) if wrap else (SC * u, s0 + K1, False)
+
     def constants3():
-        for a, e in CALLS:
-            act("OO", "DU2", T.DU2[:, a:e], T.OO[:, 0:e - a], F.Identity, bias=float(MW))
-        act("Z16 SFe", "ONM", T.ONM[:, :], T.Z16[:, 0:768], F.Identity, bias=T.SF[:, 22:23])
+        iota("DU2", T.DU2[:, :], [[0, 5], [16, 32]], 0)
+        act("DU2 SF", "DU2", T.DU2[:, :], T.DU2[:, :], F.Identity, bias=P16)
+        act("Z16 SFe", "ONM", T.ONM[:, :], T.Z16[:, 0:512], F.Identity, bias=T.SF[:, 22:23])
         ms("ONB", T.ONB[:, :], 1.0)
         ms("FL", T.FL[:, :], 1.0)
         ms("CAP", T.CAP[:, :], float(K1))
         ms("QC0", T.QC[:, 15:16], 0.0)
         scan("FL CAP", "QC", T.QC[:, 16:16 + C], T.FL[:, :], T.CAP[:, :], 0.0, A.add, A.min)
         ts("OO", "TH5", T.TH5[:, 0:8], T.OO[:, 0:8], 0.5, A.add)
-        ts("RQ", "OFF", T.OFF[:, 0:2], T.RQ[:, 0:2], 32.0, A.mult)
-        ts("RQ", "OFFb", T.OFF[:, 2:7], T.RQ[:, 2:7], 16.0, A.mult, 288.0, A.add)
+        for u in range(1, RO):
+            lo, hi, wrap = listed(u)
+            n = hi - lo - SURE[u][1]
+            act("RQ", "OFFa%d" % u, T.OFF[:, 8 * u:8 * u + VC], T.RQ[:, 0:VC], F.Identity, scale=32.0, bias=2.0 * lo)
+            act("RQ", "OFFb%d" % u, T.OFF[:, 8 * u + VC:8 * u + 8], T.RQ[:, VC:8], F.Identity, scale=16.0, bias=2.0 * lo + n)
         ts("OO", "DM", T.DM[:, 0:7], T.OO[:, 0:7], 2.0, A.mult, 64.0, A.add)
 
-    def camera_flags(u):
-        st = (72 * u) % C
-        src = [(T.FL, "FL", 0, T.ID, "ID", 72), (T.QC, "QC", 16, T.NI, "NI", 72), (T.QC, "QC QC0", 15, T.ID, "ID", 72),
-               (T.MC, "MC", 0, T.BO, "BO", st), (T.MC, "MC", 288, T.BO, "BO", st),
-               (T.M16, "M16", 0, T.BO, "BO", st), (T.M16, "M16", 288, T.BO, "BO", st)]
-        mm("Z16 ID", "PS4", PS[4][:, 0:C], T.ID[:, :], T.Z16[:, 0:C], True, False)
-        for i, (buf, key, c0, m, mk, sh) in enumerate(src):
+    def camera_flags(u, scale=1.0):
+        st, b = (SC * u) % C, small()
+        src = [(T.FL, "FL", 0, "ID", SC), (T.QC, "QC", 16, "NI", SC), (T.QC, "QC QC0", 15, "ID", SC),
+               (T.MC, "MC", 0, "BO", st), (T.MC, "MC", 288, "BO", st), (T.M16, "M16", 0, "BO", st), (T.M16, "M16", 288, "BO", st)]
+        mms(b, C, [("ID", "Z16", T.Z16[:, 0:C])], True, False)
+        for i, (buf, key, c0, m, sh) in enumerate(src):
             last = i == len(src) - 1
-            mm(key + " " + mk, "PS4", PS[4][:, 0:C - sh], m[:, :], buf[:, c0 + sh:c0 + C], False, last and sh == 0)
+            mms(b, C - sh, [(m, key, buf[:, c0 + sh:c0 + C])], False, last and sh == 0)
             if sh:
-                mm(key + " " + mk, "PS4", PS[4][:, C - sh:C], m[:, :], buf[:, c0:c0 + sh], False, last)
-        ts("PS4", "FL", T.FL[:, :], PS[4][:, 0:C], 0.5, A.is_gt)
+                mms(b, sh, [(m, key, buf[:, c0:c0 + sh])], False, last, C - sh)
+        ts("PS%d" % b, "FL", T.FL[:, :], PS[b][:, 0:C], 0.5, A.is_gt, scale, A.mult)
 
-    def kills():
-        src = [(T.MC, "MC", 288), (T.MC, "MCb", 576), (T.M16, "M16", 288), (T.M16, "M16", 576)]
-        for i, (buf, key, c0) in enumerate(src):
-            mm(key + " IXN", "PS5", PS[5][:, 0:C], T.IXN[:, :], buf[:, c0:c0 + C], i == 0, i == 3)
-        tt("PS5 CTL", "CTL", T.CTL[:, 0:C], T.CTL[:, 0:C], PS[5][:, 0:C], A.max)
+    def killed(m, c0, n):
+        return [(m, key, buf[:, r + c0:r + c0 + n]) for buf, key, r in ((T.MC, "MC", 288), (T.MC, "MCb", 576), (T.M16, "M16", 288), (T.M16, "M16", 576))]
+
+    def kills(u):
+        s0, ns = SURE[u]
+        if ns:
+            b = small()
+            mms(b, ns, [("IF", "CTL", T.CTL[:, s0:s0 + ns])] + killed("IXN", s0, ns))
+            ts("PS%d" % b, keys("XO", 0, ns), T.XO[:, 0:ns], PS[b][:, 0:ns], float(XN), A.min)
+        b = small()
+        mms(b, C, killed("IXN", 0, C))
+        tt("PS%d CTL" % b, "CTL", T.CTL[:, 0:C], T.CTL[:, 0:C], PS[b][:, 0:C], A.max)
 
     def camera_list(u):
-        st = 72 * u
+        st, (s0, ns), (lo, hi, wrap) = SC * u, SURE[u], listed(u)
+        w, n = (K1 - ns) // 16, hi - lo - ns
         scan("FL CAP", "QC", T.QC[:, 16:16 + C], T.FL[:, :], T.CAP[:, :], 0.0, A.add, A.min)
         qa, qn = T.QC[:, 15 + C - st:16 + C - st], T.QC[:, 15 + C:16 + C]
-        ts("QC", "NP", T.NP[:, 0:st], T.QC[:, 16 + C - st:16 + C], qa, A.subtract)
-        ts("QC", "NPb", T.NP[:, st:C], T.QC[:, 16:16 + C - st], qn, A.add, qa, A.subtract)
-        for m in range(2, 7):
-            act("NP NPb TH5", "ACC%d " % m + keys("PG", 32 * (m - 2), 32 * (m - 1)), T.PG[:, 512 * (m - 2):512 * (m - 2) + C - 16 * m], T.NP[:, 16 * m:C], F.Sign, bias=T.TH5[:, m:m + 1],
-                scale=-1.0, accum_out=T.ACC[:, m:m + 1])
-        ts("QC OO", "W1", T.W1[:, 0:7], T.OO[:, 0:7], qn, A.is_ge)
-        tt("W1 DM", "W1", T.W1[:, 0:7], T.W1[:, 0:7], T.DM[:, 0:7], A.mult)
-        tt("W1 OFF OFFb", "W1", T.W1[:, 0:7], T.W1[:, 0:7], T.OFF[:, 0:7], A.add)
-        for m in range(2):
+        a = s0 - lo
+        if wrap:
+            ts("QC", "NP", T.NP[:, 0:st], T.QC[:, 16 + C - st:16 + C], qa, A.subtract)
+            ts("QC", "NPb", T.NP[:, st:a], T.QC[:, 16:16 + a - st], qn, A.add, qa, A.subtract)
+            if ns:
+                ts("QC", "W3", T.W3[:, 0:1], qn, qa, A.subtract, -float(ns), A.add)
+                ts("QC W3", "NPc", T.NP[:, a:n], T.QC[:, 16 + s0 + ns - st:16 + C - st], T.W3[:, 0:1], A.add)
+        else:
+            cp("QC", "NPb", T.NP[:, 0:a], T.QC[:, 16:16 + a])
+            ts("QC", "NPc", T.NP[:, a:n], T.QC[:, 16 + a + ns:16 + n + ns], -float(ns), A.add)
+        for m in range(VC, w):
+            act("NP NPb NPc TH5", "ACC%d " % m + keys("PG", 32 * (m - VC), 32 * (m - VC + 1)), T.PG[:, 512 * (m - VC):512 * (m - VC) + n - 16 * m],
+                T.NP[:, 16 * m:n], F.Sign, bias=T.TH5[:, m:m + 1], scale=-1.0, accum_out=T.ACC[:, m:m + 1])
+        off, offk = T.OFF[:, 8 * u:8 * u + w], "OFFa%d OFFb%d" % (u, u)
+        if wrap:
+            ts("QC OO", "W1", T.W1[:, 0:w], T.OO[:, 0:w], float(ns), A.add, qn, A.is_ge)
+            tt("W1 DM", "W1", T.W1[:, 0:w], T.W1[:, 0:w], T.DM[:, 0:w], A.mult)
+            tt("W1 " + offk, "W1", T.W1[:, 0:w], T.W1[:, 0:w], off, A.add)
+            off, offk = T.W1[:, 0:w], "W1"
+        if ns:
+            ts("NPb OO", "W1b", T.W1[:, 8:8 + w], T.OO[:, 0:w], T.NP[:, a - 1:a], A.is_ge, 2.0 * ns, A.mult)
+            tt("W1b " + offk, "W1", T.W1[:, 0:w], T.W1[:, 8:8 + w], off, A.add)
+        for m in range(VC):
             jk = (T.JK, T.FG)[m % 2]
-            ts("NP NPb TH5", "JK%d" % (m % 2), jk[:, 0:C], T.NP[:, 0:C], T.TH5[:, m:m + 1], A.is_le, 2.0, A.mult)
-            red("JK%d" % (m % 2), "ACC%d" % m, T.ACC[:, m:m + 1], jk[:, 16 * m:C])
-        kills()
-        tt("W1 " + " ".join("ACC%d" % m for m in range(7)), "W2", T.W2[:, 0:7], T.W1[:, 0:7], T.ACC[:, 0:7], A.add)
-        ts("W2", "WL", T.WL[:, 0:7], T.W2[:, 0:7], 0.5, A.mult)
+            ts("NP NPb NPc TH5", "JK%d" % (m % 2), jk[:, 0:n], T.NP[:, 0:n], T.TH5[:, m:m + 1], A.is_le, 2.0, A.mult)
+            red("JK%d" % (m % 2), "ACC%d" % m, T.ACC[:, m:m + 1], jk[:, 16 * m:n])
+        tt("W1 " + " ".join("ACC%d" % m for m in range(w)), "W2", T.W2[:, 0:w], T.W1[:, 0:w], T.ACC[:, 0:w], A.add)
+        ts("W2", "WL", T.WL[:, 0:w], T.W2[:, 0:w], 0.5, A.mult)
 
-    def sbuf(k0):
-        return "SS" if k0 == 64 else "S"
+    def finals(ch, nk):
+        sb = sbuf(ch)
+        return sb + "n " + " ".join("%s%d" % (sb, k) for k in range(7)), T[sb][:, 0:6 * SW + 16 + 16 * nk]
 
-    def finals(k0, nk):
-        sb = sbuf(k0)
-        return " ".join("%s%d" % (sb, k) for k in range(7)), T[sb][:, 0:6 * SW + 16 + 16 * nk]
-
-    def passes(name, k0, k1, between):
-        n, key = k1 - k0, keys(name, k0, k1)
-        between = list(between)
+    def passes(name, ch, k0, n):
+        key = keys(name, k0, k0 + n)
         for k in range(8):
-            sb, a, b = sbuf(k0), (k + 5) % 7, (k + 6) % 7
+            sb, a, b = sbuf(ch), (k + 5) % 7, (k + 6) % 7
             d1 = T.CP[:, 0:16 * n] if k == 0 else T[sb][:, a * SW + 15:a * SW + 15 + 16 * n]
             scan(key + (" CP" if k == 0 else " %s%d" % (sb, a)), "%s%d" % (sb, b), T[sb][:, b * SW + 16:b * SW + 16 + 16 * n],
-                 seg(name, k0, k1), d1, 1024.0, A.min, A.max)
-            if between:
-                f = between.pop(0)
-                if f:
-                    f()
-        for f in between:
-            if f:
-                f()
+                 seg(name, k0, k0 + n), d1, 1024.0, A.min, A.max)
 
-    def move(on_scalar, rd, wr, out, in_):
-        if on_scalar:
-            act(rd, wr, out, in_, F.Copy)
-        else:
-            cp(rd, wr, out, in_)
+    def pucol(k0):
+        return k0 // 16 + k0 // 16 % 2
 
-    def pick_places(k0, k1, low, uh, pu):
+    def pick_places(chunks, fn, plus):
+        k0, k1 = chunks[0][0], chunks[-1][0] + chunks[-1][1]
         w0, w1 = k0 // 16, k1 // 16
-        w, r = w1 - w0, slice(w0, w1)
-        fold(6, PS[6][:, 0:w], "UH", w0, w1, uh)
-        ts("PS6", "W1", T.W1[:, 0:w], PS[6][:, 0:w], low, A.max, 0.25, A.add)
-        cp("W1", "KI", T.KI[:, 0:w], T.W1[:, 0:w])
-        ts("KI", "W3", T.W3[:, 0:w], T.KI[:, 0:w], float(SW), A.mult, 31.0 - 2 * SW, A.add)
-        tt("W3 FN", "W2", T.W2[:, 0:w], T.W3[:, 0:w], T.FN[:, r], A.add)
-        cp("W2", pu, T.PU[:, r], T.W2[:, 0:w])
+        b, b2, w = small(), small(), w1 - w0
+        fold(b, "UH", w0, w1, keys("UH", k0, k1))
+        ts("PS%d" % b, "KB", T.KB[:, 0:w], PS[b][:, 0:w], 0.25, A.mult, 128.25 + 4 * plus, A.add)
+        mms(b2, w, [("I16", keys("FN", 16 * (fn + w0), 16 * (fn + w1)), T.FN[:, fn + w0:fn + w1]), ("ISW", "KB", T.KB[:, 0:w])])
+        cuts = [w0] + [a // 16 for a, nk in chunks[1:] if a // 16 % 2] + [w1]
+        for a, e in zip(cuts[:-1], cuts[1:]):
+            ts("PS%d" % b2, keys("PU", 16 * a, 16 * e), T.PU[:, pucol(16 * a):pucol(16 * a) + e - a], PS[b2][:, a - w0:e - w0],
+               31.0 - 130 * SW, A.add, 0.0, A.max)
 
-    bank = [0]
-
-    def nextbank():
-        bank[0] = (bank[0] + 1) % 4
-        return bank[0]
+    def median(ch, k0, nk):
+        return finals(ch, nk)[0] + " " + keys("PU", k0, k0 + nk), ind(finals(ch, nk)[1], T.PU[:, pucol(k0):pucol(k0) + nk // 16])
 
     def spread(ch, k0, nk):
-        mm("PC%d ID" % ch, "PS7", PS[7][0:nk, 0:128], T.PC[:, k0:k0 + nk], T.ID[:, :])
-        act("PS7", "PT%d" % ch, T.PT[0:nk, 128 * ch:128 * ch + 128], PS[7][0:nk, 0:128], F.Copy)
+        b = small()
+        mm("PC%d ID" % ch, "PS%d" % b, PS[b][0:nk, 0:128], T.PC[:, k0:k0 + nk], T.ID[:, :])
+        move(1, "PS%d" % b, "PT%d" % ch, T.PT[0:nk, 128 * ch:128 * ch + 128], PS[b][0:nk, 0:128])
 
-    def wide(ch, k0, nk, m, mk, src, out, f, rd=None, **kw):
-        for a in range(0, nk, 32):
-            e = min(nk, a + 32)
+    def wide(ch, k0, nk, m, src):
+        for a in range(k0, k0 + nk, 32):
+            e = min(k0 + nk, a + 32)
             b, n = nextbank(), 16 * (e - a)
-            mm((rd or keys(src, k0 + a, k0 + e)) + " " + mk, "PS%d" % b, PS[b][:, 0:n], m[:, :], seg(src, k0 + a, k0 + e), True, False)
-            mm("PT%d EXP" % ch, "PS%d" % b, PS[b][:, 0:n], T.PT[0:nk, 128 * ch:128 * ch + 128], T.EXP[0:nk, 16 * a:16 * e], False, True)
-            act("PS%d" % b, keys(out, k0 + a, k0 + e), seg(out, k0 + a, k0 + e), PS[b][:, 0:n], f, **kw)
+            mms(b, n, [(m,) + src(a, e)], True, False)
+            mm("PT%d EXP" % ch, "PS%d" % b, PS[b][:, 0:n], T.PT[0:nk, 128 * ch:128 * ch + 128], T.EXP[0:nk, 16 * (a - k0):16 * (e - k0)], False, True)
+            yield a, e, b
 
     def near(name, k0, nk):
         for a in range(k0, k0 + nk, 32):
             e = min(k0 + nk, a + 32)
-            k = keys(name, a, e)
-            if name == "PG" and e <= NA:
-                act(k, k, seg(name, a, e), seg(name, a, e), F.Sign, bias=12.5, scale=-1.0)
-            else:
-                ts(k, k, seg(name, a, e), seg(name, a, e), 12.5, A.is_le)
+            ts(keys(name, a, e), keys(name, a, e), seg(name, a, e), seg(name, a, e), 12.5, A.is_le)
 
-    def port_places(c0, n):
-        ts("PTR SFd", "G1", T.G1[:, 0:n], T.PTR[:, c0:c0 + n], 16.0, A.mult, T.SF[:, 21:22], A.add)
-        ts("CTL", "G2", T.G2[:, 0:n], T.CTL[:, c0:c0 + n], XN - 0.5, A.is_lt)
-        tt("G1 G2", "G1", T.G1[:, 0:n], T.G1[:, 0:n], T.G2[:, 0:n], A.mult)
-        cp("G1", "GU", T.GU[:, 0:n], T.G1[:, 0:n])
+    def port_places(c0, n, more):
+        b = small()
+        act("CTL", "DEAD", T.DEAD[:, 0:n], T.CTL[:, c0:c0 + n], F.Relu, bias=1.0 - XN)
+        mms(b, n, [("NBG", "DEAD", T.DEAD[:, 0:n]), ("I16", "PTR", T.PTR[:, c0:c0 + n])] + more)
+        ts("PS%d SFd" % b, "GU", T.GU[:, 0:n], PS[b][:, 0:n], T.SF[:, 21:22], A.add, 0.0, A.max)
 
-    def list_a(u):
+    def track_list(u):
+        b = small()
         scan("M32 KP", "FS", T.FS[:, :], T.KP[:, :], T.M32[:, 0:640], 0.0, A.mult, A.max)
-        tt("FS FA", "FB", T.FB[:, :], T.FS[:, 15:640:16], T.FA[:, :], A.max)
-        scan("FB Z16", "PP", T.PP[:, :], T.FB[:, :], T.Z16[:, 0:40], 0.0, A.add, A.add)
-        mm("PP TRI%d" % u, "PS7", PS[7][:, 0:2], T.TRI[:, 128 * u:128 * u + 128], T.PP[:, 38:40])
-        tt("PP RB1", "B1", T.B1[:, :], T.PP[:, :], T.RB1[:, :], A.subtract)
-
-    def list_b():
-        ts("B1 PS7", "B1", T.B1[:, :], T.B1[:, :], PS[7][:, 1:2], A.add)
-        ts("PP PS7", "B2", T.B2[:, :], T.PP[:, :], PS[7][:, 1:2], A.add, K2 + 0.5, A.is_gt)
-        tt("B1 FB", "B1", T.B1[:, :], T.B1[:, :], T.FB[:, :], A.mult)
-        tt("B2 FB", "FA", T.FA[:, :], T.B2[:, :], T.FB[:, :], A.mult)
-        tt("B1 RB", "B1", T.B1[:, :], T.B1[:, :], T.RB[:, :], A.add)
-        cp("B1", "BU", T.BU[:, :], T.B1[:, :])
-        if LA:
-            act("BU TID", "LW", ind(T.LW[:, :], T.BU[:, :]), T.TID[:, :], F.Silu)
-        else:
-            cp("BU TID", "LW", ind(T.LW[:, :], T.BU[:, :]), T.TID[:, :])
-
-    def list_c():
+        tt("FS FA", "FB", T.FB[:, :], T.FA[:, :], T.FS[:, 15:640:16], A.is_gt)
+        scan("FB NG", "PP", T.PP[:, :], T.FB[:, :], T.NG[:, :], 0.0, A.add, A.add)
+        tt("FB KIU%d" % u, "B1", T.B1[:, :], T.FB[:, :], T.KIU[:, 40 * u:40 * u + 40], A.mult)
+        mm("PP TRI%d" % u, "PS%d" % b, PS[b][:, 0:2], T.TRI[:, 128 * u:128 * u + 128], T.PP[:, 38:40])
+        tt("PP B1", "B1", T.B1[:, :], T.B1[:, :], T.PP[:, :], A.subtract)
+        ts("B1 PS%d" % b, "BU", T.BU[:, :], T.B1[:, :], PS[b][:, 1:2], A.subtract, -1.0, A.add)
+        ts("PP PS%d" % b, "B2", T.B2[:, :], T.PP[:, :], PS[b][:, 1:2], A.add, -K2 - 0.5, A.is_gt)
+        tt("B2 FB", "FA", T.FA[:, :], T.B2[:, :], T.FB[:, :], A.max)
+        move(ON["LW"], "BU TID", "LW", ind(T.LW[:, :], T.BU[:, :]), T.TID[:, :], F.Silu)
         tt("LW DG", "L1", T.L1[:, :], T.LW[:, 0:K2], T.DG[:, :], A.mult)
         scan("L1 KP", "L2", T.L2[:, :], T.KP[:, 0:K2], T.L1[:, :], 0.0, A.mult, A.add)
         ts("L2", "TL", T.TL[:, 0:10], T.L2[:, 15:K2:16], -63.75, A.add)
         cp("TL TC TCx", "CU", T.CU[:, :], ind(T.TC[:, :], T.TL[:, 0:10]))
 
+    def groups(chunks, ends):
+        return [chunks[a:e] for a, e in zip((0,) + tuple(ends[:-1]), ends)]
+
     for u in range(RO):
         lb = 400 + 1792 * u
-        lk = "LOG%d" % u
+        s0, ns = SURE[u]
+        ch1 = spans(CH1[u])
+        both = [(0, ns, lambda buf: buf[:, s0:s0 + ns], ""), (ns, K1, lambda buf: ind(buf[:, :], T.WL[:, 0:(K1 - ns) // 16]), " WL")]
+        both = [p for p in both if p[1] > p[0]]
+        parts = [(a, min(a + 32, K1)) for a in range(0, K1, 32)]
 
-        def tab(buf):
-            return buf[:, 0:K1] if u == 0 else ind(buf[:, :], T.WL[:, 0:7])
-        og = "O" if u == 0 else "OG"
-        parts = [(0, 32), (32, 64), (64, 96), (96, 112)]
-        if u > 0:
-            cp("OO WL", "OU", T.OU[:, :], tab(T.OO))
+        def obs(a, e):
+            return ("O0 O1" if u else "O0", seg("O", a, e, s0)) if e <= ns else (keys("OG", a, e), seg("OG", a, e))
+        if ns < K1:
+            cp("OO WL", "OU", T.OU[:, ns:K1], both[-1][2](T.OO))
             for a, e in parts:
-                move(e <= OA, "O0 O1 OU", keys("OG", a, e), seg("OG", a, e), ind(T.O[:, :], T.OU[:, a:e]))
-        cp("CTL WL", "XO", T.XO[:, :], tab(T.CTL))
-        tt("CTO CTOx DU1 WL", "FO", T.FO[:, :], tab(T.CTO), T.DU1[:, :], A.min)
-        cp("FO", "FU", T.FU[:, :], T.FO[:, :])
-        act("CTL WL", "XF", T.XF[:, :], tab(T.CTL), F.Copy)
-        for h in range(2):
-            act("FU ONA", "WA0 WA8", ind(T.WA[:, 0:12032], T.FU[:, 56 * h:56 * h + 56]), T.ONA[:, :], F.Silu)
+                if a >= ns:
+                    move(ON["OG"][a // 32], "O0 O1 OU", keys("OG", a, e), seg("OG", a, e), ind(T.O[:, :], T.OU[:, a:e]))
+        for a, e, tab, wl in both:
+            if wl or u == 0:
+                cp("CTL" + wl, keys("XO", a, e), T.XO[:, a:e], tab(T.CTL))
+            tt("CTO CTOx DU1" + wl, keys("FO", a, e), T.FO[:, a:e], tab(T.CTO), T.DU1[:, a:e], A.min)
+            cp(keys("FO", a, e), keys("FU", a, e), T.FU[:, a:e], T.FO[:, a:e])
+            if wl:
+                move(1, "CTL WL", "XF", T.XF[:, a:e], tab(T.CTL))
+            act("XF" if wl else "CTL", keys("LV", a, e), T.LV[:, a:e], T.XF[:, a:e] if wl else tab(T.CTL), F.Sign, scale=-1.0, bias=XN - 0.5)
+        for a, e in parts:
+            act(keys("FU", a, e) + " ONA", "WA0 WA8", ind(T.WA[:, 0:12032], T.FU[:, a:e]), T.ONA[:, 0:16 * (e - a)], F.Silu)
         dma("a", "WA0", "M32", T.M32[:, 0:640], T.WA[0:128:16, 0:10240], 320)
-        dma("s", "Z32 M32", "WA8", T.WA[8:128:16, 0:MW], T.Z32[:, :], 432)
+        dma("s", "Z32 M32", "WA8", T.WA[8:128:16, 864:864 + MW], T.Z32[:, :], 432)
         if u < RO - 1:
             dma("s", "Z32", "WA0", T.WA[0:128:16, 0:10240], T.Z32[:, 0:640], 320)
         if u == 0:
             constants()
             constants2()
             constants3()
-        act("DI", "LW", T.LW[:, 0:K2], T.DI[:, :], F.Copy)
+        move(1, "DI", "LW", T.LW[:, 0:K2], T.DI[:, :])
+        for a, e, tab, wl in both:
+            cp("PTD" + wl, "PTR", tab(T.PTR), T.PTD[:, K1 * u + a:K1 * u + e])
+        port_places(0, 24, [])
         for a, e in parts:
-            tt("X Xd Xn XG XO " + ("O0" if u == 0 else keys("OG", a, e)), keys("D", a, e), seg("D", a, e),
-               ind(T.X[:, :], T.XO[:, a:e]), seg(og, a, e), A.subtract)
-        fold(5, PS[5][:, 0:K1], "D", 0, K1)
+            tt("X Xb Xd Xn XG " + keys("XO", a, e) + " " + obs(a, e)[0], keys("D", a, e) + " " + keys("XR", a, e), seg("D", a, e),
+               ind(T.X[:, :], T.XO[:, a:e]), obs(a, e)[1], A.subtract)
+        for grp in groups(ch1, UG1[u]):
+            a, e, b = grp[0][0], grp[-1][0] + grp[-1][1], small()
+            fold(b, "D", a, e)
+            ts("PS%d" % b, keys("UH", a, e), T.UH[:, a:e], PS[b][:, 0:e - a], 4088.0, A.is_lt, 2.0, A.mult)
+            pick_places(grp, 10 * fn_of(u), 0)
+        track_list(u)
+        for a in range(0, K2, 32):
+            move(ON["PG"][a // 32], "PTR CU", keys("PG", a, a + 32), seg("PG", a, a + 32), ind(T.PTR[:, :], T.CU[:, a:a + 32]))
+        act("LO LOx TL", "MO", T.MO[:, :], ind(T.LO[:, :], T.TL[:, 0:10]), F.Identity, bias=1.0)
+        logk = "LOGn"
+        border = 0 if u and not listed(u)[2] else (ns if u else 0) + 24
 
-        def used1():
-            ts("PS5", "UH0 UH1", T.UH[:, 0:K1], PS[5][:, 0:K1], 4088.0, A.is_lt, 0.5, A.mult)
-            pick_places(0, K1, 2.5, "UH0 UH1", "PU0 PU1")
-            ts("XF", "LV", T.LV[:, :], T.XF[:, :], XN - 0.5, A.is_lt, 0.5, A.mult)
-
-        def side1():
-            if u > 0:
-                cp("PTD WL", "PTR", ind(T.PTR[:, :], T.WL[:, 0:7]), T.PTD[:, K1 * u:K1 * u + K1])
-
-        def side2():
-            act("UH0 UH1", "TH0 TH1", T.TH1[:, 0:K1], T.UH[:, 0:K1], F.Identity, scale=-176.0, bias=99.5)
-            tt("LV UH0 UH1", "LU", T.LU[:, :], T.LV[:, :], T.UH[:, 0:K1], A.subtract)
-
-        def head1(ch):
-            k0, nk = CH1[ch]
-            cp(finals(k0, nk)[0] + " PU0 PU1", "PC%d" % ch, T.PC[:, k0:k0 + nk], ind(finals(k0, nk)[1], T.PU[:, k0 // 16:(k0 + nk) // 16]))
+        def send_b(end):
+            move(ON["SG"], logk + " GU", "SG", T.SG[:, :], ind(T.LOG[:, 384:lb + 16 * end], T.GU[:, 0:24]))
+            exchange(2 * u + 1, "SG", T.SG, " " + keys("XR", 0, K1))
+        if not border:
+            send_b(0)
+        for ch, (k0, nk) in enumerate(ch1):
+            r, k1 = slice(k0, k0 + nk), k0 + nk
+            passes("D", ch, k0, nk)
+            move(ON["PC1"], median(ch, k0, nk)[0], "PC%d" % ch, T.PC[:, r], median(ch, k0, nk)[1])
             spread(ch, k0, nk)
-            wide(ch, k0, nk, T.NI, "NI", "D", "D", F.Abs)
-
-        def count1(ch):
-            k0, nk = CH1[ch]
-            near("D", k0, nk)
-            fold(4, PS[4][:, 0:nk], "D", k0, k0 + nk)
-
-        def fit1(ch):
-            k0, nk = CH1[ch]
-            r, fk = slice(k0, k0 + nk), "FIT%d" % ch
-            tt("PS4 TH0 TH1", fk, T.FIT[:, r], PS[4][:, 0:nk], T.TH1[:, r], A.is_gt)
-            mm(fk + " M1", "PS6", PS[6][:, 0:nk], T.M1[:, :], T.FIT[:, r], True, False)
-            mm("LU I200", "PS6", PS[6][:, 0:nk], T.I200[:, :], T.LU[:, r], False, True)
-            mm(fk + " M2", "PS4", PS[4][:, 0:nk], T.M2[:, :], T.FIT[:, r], True, False)
-            mm("UH0 UH1 I200", "PS4", PS[4][:, 0:nk], T.I200[:, :], T.UH[:, r], False, True)
-
-        def log1(ch):
-            k0, nk = CH1[ch]
-            r = slice(k0, k0 + nk)
-            ts("PS6", "NONE%d" % ch, T.NONE[:, r], PS[6][:, 0:nk], 105.5, A.is_lt)
-            ts("PS4", "DIE%d" % ch, T.DIE[:, r], PS[4][:, 0:nk], 105.5, A.is_ge, float(XN), A.mult)
-            for a in range(k0, k0 + nk, 32) if SO else []:
-                e = min(k0 + nk, a + 32)
-                b, n = nextbank(), 16 * (e - a)
-                mm(("O0" if u == 0 else keys("OG", a, e)) + " ID", "PS%d" % b, PS[b][:, 0:n], T.ID[:, :], seg(og, a, e), True, False)
-                mm("PT%d EXP" % ch, "PS%d" % b, PS[b][:, 0:n], T.PT[0:nk, 128 * ch:128 * ch + 128], T.EXP[0:nk, 16 * (a - k0):16 * (e - k0)], False, False)
-                for j in range(16):
-                    mm("NONE%d SEL%d" % (ch, j), "PS%d PEL" % b, PS[b][:, j:n:16], T.SEL[:, 128 * j:128 * j + 128], T.NONE[:, a:e], False, j == 15)
-                dst, key = T.LOG[:, lb + 16 * a:lb + 16 * e], "%s_%d_%d" % (lk, ch, (a - k0) // 32)
-                if EA[a // 32]:
-                    act("PS%d" % b, key, dst, PS[b][:, 0:n], F.Relu)
+            for a, e, b in wide(ch, k0, nk, "NI", lambda a, e: (keys("D", a, e), seg("D", a, e))):
+                act("PS%d" % b, keys("D", a, e), seg("D", a, e), PS[b][:, 0:16 * (e - a)], F.Abs)
+            for a, e, b in wide(ch, k0, nk, "ID", obs):
+                if ON["CLIP"][a // 32]:
+                    act("PS%d" % b, keys("OG", a, e), seg("OG", a, e), PS[b][:, 0:16 * (e - a)], F.Relu, scale=-1.0, bias=255.0)
                 else:
-                    ts("PS%d" % b, key, dst, PS[b][:, 0:n], 0.0, A.max)
-            per = 8 if ch == 0 else 4
-            for j0 in range(0, 16, per) if not SO else []:
-                b = nextbank()
-                for j in range(j0, j0 + per):
-                    o = PS[b][:, nk * (j - j0):nk * (j - j0 + 1)]
-                    mm(("O0" if u == 0 else keys("OG", k0, k0 + nk)) + " ID", "PS%d" % b, o, T.ID[:, :], col(og, j, k0, k0 + nk), True, False)
-                    mm("PC%d ID" % ch, "PS%d" % b, o, T.ID[:, :], T.PC[:, r], False, False)
-                    mm("NONE%d SEL%d" % (ch, j), "PS%d PEL" % b, o, T.SEL[:, 128 * j:128 * j + 128], T.NONE[:, r], False, True)
-                for j in range(j0, j0 + per):
-                    o = PS[b][:, nk * (j - j0):nk * (j - j0 + 1)]
-                    dst = T.LOG[:, lb + 16 * k0 + j:lb + 16 * (k0 + nk):16]
-                    if EA[j0 // 8 if ch == 0 else 2 + j0 // 4 % 2]:
-                        act("PS%d" % b, "%s_%d_%d" % (lk, ch, j), dst, o, F.Relu)
-                    else:
-                        ts("PS%d" % b, "%s_%d_%d" % (lk, ch, j), dst, o, 0.0, A.max)
-        logk = ["LOGn " + " ".join("%s_%d_%d" % (lk, ch, j) for j in range(16)) for ch in range(2)]
-
-        def send_b():
-            move(SA, logk[0] + " GU", "SG", T.SG[:, :], ind(T.LOG[:, 384:lb + 16 * CH1[1][0]], T.GU[:, 0:24]))
-            exchange(2 * u + 1, "SG", T.SG, 7)
-
-        passes("D", 0, 64, [side1, used1, lambda: port_places(0, 24), side2])
-        head1(0)
-        count1(0)
-        fit1(0)
-        passes("D", CH1[1][0], K1, [])
-        list_a(u)
-        list_b()
-        log1(0)
-        head1(1)
-        list_c()
+                    ts("PS%d" % b, keys("OG", a, e), seg("OG", a, e), PS[b][:, 0:16 * (e - a)], 255.0, A.min)
+            near("D", k0, nk)
+            b, uh = small(), keys("UH", k0, k1)
+            mms(b, nk, [("I50", uh, T.UH[:, r])], True, False)
+            fold(b, "D", k0, k1, st=False)
+            ts("PS%d" % b, "FIT%d" % ch, T.FIT[:, r], PS[b][:, 0:nk], 111.5, A.is_gt)
+            b, b2 = small(), small()
+            mms(b, nk, [("I50", keys("LV", k0, k1), T.LV[:, r]), ("N50", uh, T.UH[:, r]), ("M1", "FIT%d" % ch, T.FIT[:, r])])
+            ts("PS%d" % b, "NONE%d" % ch, T.NONE[:, r], PS[b][:, 0:nk], 55.5, A.is_lt)
+            mms(b2, nk, [("I50", uh, T.UH[:, r]), ("M2", "FIT%d" % ch, T.FIT[:, r])])
+            ts("PS%d" % b2, keys("DIE", k0, k1), T.DIE[:, r], PS[b2][:, 0:nk], 105.5, A.is_ge, float(XN), A.mult)
+            for a in range(k0, k1, 32):
+                e = min(k1, a + 32)
+                b, n, clip = nextbank(), 16 * (e - a), ON["CLIP"][a // 32]
+                mms(b, n, [("NI" if clip else "ID", keys("OG", a, e), seg("OG", a, e))], True, False)
+                group("NONE%d " % ch + " ".join("SEL%d" % j for j in range(16)), "PS%d" % b,
+                      [(PS[b][:, j:n:16], T.SEL[:, 128 * j:128 * j + 128], T.NONE[:, a:e], False, j == 15) for j in range(16)])
+                key = "LOG%d_%d" % (u, a)
+                logk += " " + key
+                relu("PS%d" % b, key, T.LOG[:, lb + 16 * a:lb + 16 * e], PS[b][:, 0:n], 255.0 * clip)
+            if k0 < border <= k1:
+                send_b(k1)
+        for a, e, tab, wl in both:
+            tt(keys("DIE", a, e) + (" XF WL" if wl else " CTL"), "CTL", tab(T.CTL), T.DIE[:, a:e], T.XF[:, a:e] if wl else tab(T.CTL), A.max)
+        ch2 = spans(CH2)
+        for grp in groups(ch2, IG2):
+            a, e, b = grp[0][0], grp[-1][0] + grp[-1][1], small()
+            mms(b, e - a, [("ID", "MO", T.MO[:, a:e])], True, False)
+            fold(b, "PG", a, e, st=False)
+            ts("PS%d" % b, keys("IU", a, e), T.IU[:, a:e], PS[b][:, 0:e - a], 4095.0, A.add)
+        win, wk = T.LOG[:, 0:lb + 1792], logk + " LG"
         for a in range(0, K2, 32):
-            move(a + 32 <= PA, "PTR CU", keys("PG", a, a + 32), seg("PG", a, a + 32), ind(T.PTR[:, :], T.CU[:, a:a + 32]))
-        send_b()
-        count1(1)
-        act("LO LOx TL", "LO4", T.LO4[:, :], ind(T.LO[:, :], T.TL[:, 0:10]), F.Identity, bias=4096.0)
-        fit1(1)
-        log1(1)
-        tt("DIE0 DIE1 XF WL", "CTL", tab(T.CTL), T.DIE[:, :], T.XF[:, :], A.max)
-        halves = [(0, 64), (64, K2)]
-        for h, (a, e) in enumerate(halves):
-            b = nextbank()
-            fold(b, PS[b][:, 0:e - a], "PG", a, e)
-            tt("PS%d LO4" % b, "L1", T.L1[:, a:e], PS[b][:, 0:e - a], T.LO4[:, a:e], A.add)
-            cp("L1", "IU%d" % h, T.IU[:, a:e], T.L1[:, a:e])
-        win, wk = T.LOG[:, 0:lb + 1792], logk[0] + " " + logk[1] + " LG"
-        h0 = CH2[0][1] // 2
-        cp(wk + " IU0", keys("BG", 0, h0), seg("BG", 0, h0), ind(win, T.IU[:, 0:h0]))
-        for a, e in [(h0, 2 * h0)] + [(k0, k0 + nk) for k0, nk in CH2[1:]]:
-            act(wk + " IU%d" % min(a // 64, 1), keys("BG", a, e), seg("BG", a, e), ind(win, T.IU[:, a:e]), F.Copy)
-        act("TC TCx TL", "CF", T.CF[:, :], ind(T.TC[:, :], T.TL[:, 0:10]), F.Copy)
-        act("LO LOx TL", "MO", T.MO[:, :], ind(T.LO[:, :], T.TL[:, 0:10]), F.Copy)
+            move(ON["BG"][a // 32], wk + " " + keys("IU", a, a + 32), keys("BG", a, a + 32), seg("BG", a, a + 32), ind(win, T.IU[:, a:a + 32]))
+        move(1, "TC TCx TL", "CF", T.CF[:, :], ind(T.TC[:, :], T.TL[:, 0:10]))
         act("CF", "PEN", T.PEN[:, :], T.CF[:, :], F.Relu, bias=-287.0)
-        for a in range(0, K2, 32):
-            act(keys("BG", a, a + 32), keys("PG", a, a + 32), seg("PG", a, a + 32), seg("BG", a, a + 32), F.Relu, bias=255.0, scale=-1.0)
-
-        for h, (a, e) in enumerate(halves):
-            b, uh, th = nextbank(), "UH%d" % h, "TH%d" % h
-            fold(b, PS[b][:, 0:e - a], "BG", a, e)
-            ts("PS%d" % b, uh, T.UH[:, a:e], PS[b][:, 0:e - a], 10000.0, A.is_lt, 0.5, A.mult)
-            pick_places(a, e, 1.5, uh, "PU%d" % h)
-            mm(uh + " BO", "PS7", PS[7][:, 0:e - a], T.BO[:, :], T.UH[:, a:e])
-            act(uh, th, T.TH1[:, a:e], T.UH[:, a:e], F.Copy, scale=23.0)
-            ts("PS7", "NH%d" % h, T.NH[:, a:e], PS[7][:, 0:e - a], 1.25, A.is_lt, 512.0, A.mult)
-            tt(th + " NH%d" % h, th, T.TH1[:, a:e], T.TH1[:, a:e], T.NH[:, a:e], A.subtract)
-
-        def head2(ch):
-            k0, nk = CH2[ch]
-            r, w = slice(k0, k0 + nk), slice(k0 // 16, (k0 + nk) // 16)
-            ts(finals(k0, nk)[0] + " PU%d" % min(ch, 1), "PC%d" % ch, T.PC[:, r], ind(finals(k0, nk)[1], T.PU[:, w]), 255.0, A.min)
+        move(ON["XOLD"], "X Xb Xd TL", "XOLD", T.XOLD[:, :], ind(T.X[:, 0:800], T.TL[:, 0:10]))
+        for grp in groups(ch2, UG2):
+            a, e, b = grp[0][0], grp[-1][0] + grp[-1][1], small()
+            fold(b, "BG", a, e)
+            act("PS%d" % b, keys("UH", a, e), T.UH[:, a:e], PS[b][:, 0:e - a], F.Sign, scale=-1.0, bias=10000.0)
+            pick_places(grp, 10 * RO, 1)
+            b = small()
+            mms(b, e - a, [("BO", keys("UH", a, e), T.UH[:, a:e])])
+            act("PS%d" % b, keys("NH", a, e), T.NH[:, a:e], PS[b][:, 0:e - a], F.Relu, scale=-1.0, bias=5.0 - 16)
+        for ch, (k0, nk) in enumerate(ch2):
+            r, k1 = slice(k0, k0 + nk), k0 + nk
+            passes("BG", ch, k0, nk)
+            mk, med = median(ch, k0, nk)
+            move(ON["PC2"], mk, "PC%d" % ch, T.PC[:, r], med)
+            tt(mk + " XOLD", "NE%d" % ch, T.NE[:, r], med, T.XOLD[:, r], A.not_equal)
             spread(ch, k0, nk)
-            tt("PC%d NH%d" % (ch, min(ch, 1)), "XNW%d" % ch, T.XNW[:, r], T.PC[:, r], T.NH[:, r], A.max)
-            tt("X Xd TL XNW%d" % ch, "NE%d" % ch, T.NE[:, r], ind(T.X[:, 0:800], T.TL[:, w]), T.XNW[:, r], A.not_equal)
-            mm("NE%d BO" % ch, "PS6", PS[6][:, 0:nk], T.BO[:, :], T.NE[:, r])
-            wide(ch, k0, nk, T.ID, "ID", "PG", "PG", F.Abs, bias=-255.0)
-            act("PS6", "SN%d" % ch, T.SN[:, r], PS[6][:, 0:nk], F.Relu, bias=1.0, scale=-1.0)
-            act("SN%d" % ch, "DL%d" % ch, T.DL[:, r], T.SN[:, r], F.Identity, bias=288.0, scale=288.0 - 18432)
-            mm("CF IF", "PS5", PS[5][:, 0:nk], T.IF[:, :], T.CF[:, r], True, False)
-            mm("MO I864", "PS5", PS[5][:, 0:nk], T.I864[:, :], T.MO[:, r], False, False)
-            mm("PEN IBG", "PS5", PS[5][:, 0:nk], T.IBG[:, :], T.PEN[:, r], False, False)
-            mm("SN%d IBG" % ch, "PS5", PS[5][:, 0:nk], T.IBG[:, :], T.SN[:, r], False, True)
-
-        def count2(ch):
-            k0, nk = CH2[ch]
-            r = slice(k0, k0 + nk)
+            for a, e, b in wide(ch, k0, nk, "NI", lambda a, e: (keys("BG", a, e), seg("BG", a, e))):
+                act("PS%d" % b, keys("PG", a, e), seg("PG", a, e), PS[b][:, 0:16 * (e - a)], F.Abs)
+            b = small()
+            mms(b, nk, [("BO", "NE%d" % ch, T.NE[:, r])])
+            act("PS%d" % b, "SN%d" % ch, T.SN[:, r], PS[b][:, 0:nk], F.Relu, bias=1.0, scale=-1.0)
+            port = [("IF", "CF", T.CF[:, r]), ("I864", "MO", T.MO[:, r]), ("NBG", "PEN", T.PEN[:, r])]
+            b, b2 = small(), small()
+            mms(b, nk, port + [("I288", "SN%d" % ch, T.SN[:, r])])
+            act("PS%d" % b, "P1%d" % ch, T.P1[:, r], PS[b][:, 0:nk], F.Identity, bias=288.0)
+            mms(b2, nk, port + [("NBG", "SN%d" % ch, T.SN[:, r])])
+            tt("PS%d DU2" % b2, "P0%d" % ch, T.P0[:, r], PS[b2][:, 0:nk], T.DU2[:, r], A.max)
             near("PG", k0, nk)
-            fold(4, PS[4][:, 0:nk], "PG", k0, k0 + nk)
-
-        def marks(ch):
-            k0, nk = CH2[ch]
-            r = slice(k0, k0 + nk)
-            tt("PS4 TH%d" % min(ch, 1), "REJ%d" % ch, T.REJ[:, r], PS[4][:, 0:nk], T.TH1[:, r], A.is_lt)
-            dl = "DL%d" % ch
-            tt(dl + " REJ%d" % ch, dl, T.DL[:, r], T.DL[:, r], T.REJ[:, r], A.mult)
-            tt(dl + " PS5", dl, T.DL[:, r], T.DL[:, r], PS[5][:, 0:nk], A.add)
-            tt(dl + " DU2", dl, T.DL[:, r], T.DL[:, r], T.DU2[:, r], A.min)
-            cp(dl, "MU%d" % ch, T.MU[:, r], T.DL[:, r])
+            b = small()
+            mms(b, nk, [("I23", keys("UH", k0, k1), T.UH[:, r]), ("I23", "ONB", T.ONB[:, 0:nk]), ("N19", keys("NH", k0, k1), T.NH[:, r])], True, False)
+            fold(b, "PG", k0, k1, st=False, z=144)
+            tt("PS%d P1%d" % (b, ch), "P1%d" % ch, T.P1[:, r], PS[b][:, 0:nk], T.P1[:, r], A.min)
+            tt("P0%d P1%d" % (ch, ch), "P1%d" % ch, T.P1[:, r], T.P1[:, r], T.P0[:, r], A.max)
+            cp("P1%d" % ch, "MU%d" % ch, T.MU[:, r], T.P1[:, r])
+            ts("PS%d" % b, "P0%d" % ch, T.P0[:, r], PS[b][:, 0:nk], 0.0, A.is_gt, float(EC), A.mult)
             for a, e in CALLS:
-                if k0 <= a < k0 + nk and e <= MA:
+                if k0 <= a < k1 and e <= MA:
                     act("MU%d ONM" % ch, "WA0 WA8", ind(T.WA[:, :], T.MU[:, a:e]), T.ONM[:, 0:16 * (e - a)], F.Silu)
-                elif k0 <= a < k0 + nk:
+                elif k0 <= a < k1:
                     cp("MU%d ONB" % ch, "WB", ind(T.WB[:, :], T.MU[:, a:e]), T.ONB[:, 0:16 * (e - a)])
 
         def every(name):
             return " ".join("%s%d" % (name, ch) for ch in range(len(CH2)))
-        for ch, (k0, nk) in enumerate(CH2):
-            passes("BG", k0, k0 + nk, [])
-            head2(ch)
-            count2(ch)
-            marks(ch)
-        dma("a", "WA8", "M32", T.M32[:, :], T.WA[8:128:16, 0:MW], 432)
-        cp(every("XNW") + " TL", "X Xd", ind(T.X[:, 0:800], T.TL[:, 0:10]), T.XNW[:, :])
-        dma("s", "WB", "M16", T.M16[:, :], T.WB[0:128:16, 0:MW], 216)
+        dma("a", "WA8", "M32", T.M32[:, :], T.WA[8:128:16, 864:864 + MW], 432)
+        cp(every("PC") + " TL", "X Xb Xd", ind(T.X[:, 0:800], T.TL[:, 0:10]), T.PC[:, :])
+        dma("s", "WB", "M16", T.M16[:, :], T.WB[0:128:16, 864:864 + MW], 216)
         if u < RO - 1:
-            exchange(2 * u + 2, "X", T.X, 7)
-            dma("s", "Z16", "WB", T.WB[0:128:16, 0:MW], T.Z16[:, :], 216)
+            exchange(2 * u + 2, "X", T.X)
+            dma("s", "Z16", "WB", T.WB[0:128:16, 864:864 + MW], T.Z16[:, :], 216)
         else:
             dma("s", "X", "", T.yx[:, :], T.X[:, 0:640], 160)
-        ts(every("REJ"), "L2", T.L2[:, :], T.REJ[:, :], float(EC), A.mult)
-        tt("L2 CF TL", "TC TCx", ind(T.TC[:, :], T.TL[:, 0:10]), T.L2[:, :], T.CF[:, :], A.max)
+        tt(every("P0") + " CF TL", "TC TCx", ind(T.TC[:, :], T.TL[:, 0:10]), T.P0[:, :], T.CF[:, :], A.max)
         if u == RO - 1:
+            b = small()
             ts("TC", "FS", T.FS[:, :], T.TC[:, 0:640], EC - 0.5, A.is_lt)
-            ts("FA", "FB", T.FB[:, :], T.FA[:, :], 32.0, A.mult)
-            for a in range(16):
-                mm("FS ZE", "PS6", PS[6][:, 0:40], E(a), T.FS[:, 40 * a:40 * a + 40], a == 0, False)
-            mm("FB ID", "PS6", PS[6][:, 0:40], T.ID[:, :], T.FB[:, :], False, True)
-            cp("PS6", "YT", T.YT[:, :], PS[6][:, 0:40])
+            ts("FA", "FB", T.FB[:, :], T.FA[:, :], -32.0, A.mult, 32.0, A.add)
+            group("FS ZE", "PS%d" % b, [(PS[b][:, 0:40], E(a), T.FS[:, 40 * a:40 * a + 40], a == 0, False) for a in range(16)])
+            mms(b, 40, [("ID", "FB", T.FB[:, :])], False, True)
+            cp("PS%d" % b, "YT", T.YT[:, :], PS[b][:, 0:40])
             dma("s", "YT", "", T.yt[:, :], T.YT[:, :], 20)
-        act("M32", "MC", T.MC[:, 0:576], T.M32[:, 0:576], F.Copy)
-        act("M32", "MCb", T.MC[:, 576:864], T.M32[:, 576:864], F.Copy)
-        camera_flags(u + 1)
+        move(1, "M32", "MC", T.MC[:, 0:576], T.M32[:, 0:576])
+        move(1, "M32", "MCb", T.MC[:, 576:864], T.M32[:, 576:864])
         if u < RO - 1:
+            kills(u + 1)
+            camera_flags(u + 1)
             camera_list(u + 1)
-    kills()
-    port_places(272, 16)
-    cp(wk + " GU", "SG", T.SG[:, 0:256], ind(T.LOG[:, 384:400 + RO * 1792], T.GU[:, 0:16]))
-    ts("CTL", "JK0", T.JK[:, :], T.CTL[:, 0:C], XN - 0.5, A.is_lt)
-    ts("FL", "JK1", T.FG[:, :], T.FL[:, :], 32.0, A.mult)
-    ts("SG", "SNB", T.SNB[:, 0:256], T.SG[:, 0:256], 600.0, A.is_gt, 512.0, A.mult)
-    ts("SG", "SG", T.SG[:, 0:256], T.SG[:, 0:256], 255.0, A.min)
-    tt("SG SNB", "SG", T.SG[:, 0:256], T.SG[:, 0:256], T.SNB[:, 0:256], A.max)
+    port_places(272, 16, killed("NBG", 272, 16))
+    ts(wk + " GU", "SG", T.SG[:, 0:256], ind(T.LOG[:, 384:400 + RO * 1792], T.GU[:, 0:16]), 512.0, A.min)
     dma("s", "SG", "", T.yb[:, :], T.SG[:, 0:256], 64)
-    mm("JK0 BO", "PS6", PS[6][:, 0:C], T.BO[:, :], T.JK[:, :], True, False)
-    mm("JK1 ID", "PS6", PS[6][:, 0:C], T.ID[:, :], T.FG[:, :], False, True)
-    act("PS6", "M32", T.M32[:, 0:C], PS[6][:, 0:C], F.Copy)
+    camera_flags(RO, 32.0)
+    b, b2 = small(), small()
+    mms(b, C, [("IF", "CTL", T.CTL[:, 0:C])] + killed("IXN", 0, C))
+    ts("PS%d" % b, "JK0", T.JK[:, :], PS[b][:, 0:C], XN - 0.5, A.is_lt)
+    mms(b2, C, [("BO", "JK0", T.JK[:, :]), ("ID", "FL", T.FL[:, :])])
+    act("PS%d" % b2, "M32", T.M32[:, 0:C], PS[b2][:, 0:C], F.Copy)
     dma("a", "M32", "", T.yc[:, :], T.M32[0:128:16, 0:C], 9)
     emit()

@@ -27,37 +27,40 @@ CH2 = (64, 64, 32)
 UG1 = [(1, 3), (1, 3), (1, 4), (1, 3)]
 UG2 = (1, 3)
 IG2 = (1, 2, 3)
-TIMES = (0.0009, 1.56, 3.8, 0.05, 0.0005, 0.17, 1.5, 200.0, 1.9)
-T_CYC, T_GATH, T_SCAT, T_FIX, T_PE, T_HOP, T_DMA, T_KB, T_REMOTE = TIMES
+TIMES = (0.0009, 1.56, 3.8, 0.05, 0.00046, 0.2, 1.5, 200.0, 1.9, 2.0)
+T_CYC, T_GATH, T_SCAT, T_FIX, T_PE, T_HOP, T_DMA, T_KB, T_REMOTE, T_FIRST = TIMES
+HALVES = 32
+FCALLS = [(32, 32, 32, 16), (32, 32, 32, 16), (32, 32, 32, 16), (32, 32, 32, 16)]
+MCALLS = (16, 16, 16, 16, 16, 16, 16, 16, 32)
 ON = dict(LW=0, SG=0, PC1=0, PC2=1, XOLD=1, CLIP=(1, 1, 1, 1), LOG=(1, 1, 1, 1), OG=(1, 1, 1, 1), PG=(1, 0, 1, 0, 1), BG=(0, 1, 1, 1, 1))
-MA = 96
-MCALL = 16
+MA = 80
 PLAN = {}
 TURNS = 3
-ROUNDS = 6
-STEPS = 1500
-TABU = 10
-JITTER = 0.02
+ROUNDS = 10
+STEPS = 500
+STRETCH = 100
+PATIENCE = 500
+TABU = 14
+JITTER = 0.1
 SEED = 1
-WORTH = ((0.92, 0.2), (1.15, 0.06))
+WORTH = ((0.92, 0.2), (1.3, 0.2))
 
 
 def spans(sizes):
     return [(sum(sizes[:i]), n) for i, n in enumerate(sizes)]
 
 
-CUTS = sorted(set([k0 for k0, nk in spans(CH2)] + [MA, K2] + list(range(0, K2, MCALL))))
-CALLS = list(zip(CUTS[:-1], CUTS[1:]))
+CALLS = [(a, a + n) for a, n in spans(MCALLS)]
 SCALED = dict(I50=50.0, N50=-50.0, IXN=float(XN), I864=864.0, NBG=-BIG, I288=288.0, I23=23.0 * 8192, N19=-524288.0,
-              ISW=float(SW), I16=16.0, NI=-1.0)
+              ISW=float(SW), I16=16.0, NI=-1.0, N18=-262144.0, I32=32.0)
 SB = {
-    "WA": (MW + 864, F32), "WB": (MW + 864, BF), "ONA": (512, F32), "ONM": (512, F32), "ONB": (512, BF),
+    "WA": (MW + 864, F32), "WB": (MW + 864, BF), "ONA": (16 * max(max(f) for f in FCALLS), F32), "ONM": (512, F32), "ONB": (512, BF),
     "O": (4608, BF), "LOG": (400 + RO * 1792, BF), "OG": (1792, BF), "PG": (2560, BF), "FS": (640, BF), "FN": (64, BF),
     "M32": (864, F32), "M16": (864, BF), "MC": (864, BF), "Z32": (864, F32), "Z16": (864, BF),
     "CTL": (432, F32), "CTO": (432, F32), "OO": (432, F32), "PTR": (432, BF), "PTD": (448, BF),
     "TC": (800, F32), "LO": (800, BF), "LW": (1280, F32), "TID": (640, F32), "DI": (160, F32), "X": (1200, BF),
-    "EXP": (1024, BF), "SEL": (2048, BF), "CP": (1024, BF), "D": (1792, BF), "BG": (2560, BF), "S": (7 * SW, BF), "SS": (7 * SW, BF), "KP": (640, BF), "DG": (160, BF),
-    "ID": (128, BF), "BO": (128, BF), "M1": (128, BF), "M2": (128, BF), "II": (128 * len(SCALED), BF),
+    "SEL": (2048, BF), "CP": (1024, BF), "D": (1792, BF), "BG": (2560, BF), "S": (7 * SW, BF), "SS": (7 * SW, BF), "KP": (640, BF), "DG": (160, BF),
+    "ID": (128, BF), "BO": (128, BF), "II": (128 * len(SCALED), BF),
     "PM": (384, BF), "TRI": (512, BF), "ZE": (288, BF), "RQ": (128, F32), "RG": (128, F32),
     "SI": (16, I32), "SF": (32, F32), "D16": (16, F32), "CI": (640, I32),
     "SNX": (384, BF), "SNB": (384, BF), "SG": (384, BF),
@@ -66,7 +69,7 @@ SB = {
     "JK": (288, BF), "FG": (288, BF), "ACC": (8, F32), "W1": (16, F32), "W2": (16, F32), "W3": (16, F32),
     "WL": (8, U16), "XO": (112, U16), "OU": (112, U16), "FU": (112, U16), "XF": (112, F32), "FO": (112, F32),
     "UH": (160, BF), "LV": (112, BF), "FIT": (112, BF), "NONE": (112, BF),
-    "DIE": (112, F32), "KI": (16, I32), "KB": (16, BF), "PU": (16, U16), "PC": (160, BF), "PT": (512, BF),
+    "DIE": (112, F32), "KI": (16, I32), "KB": (16, BF), "PU": (16, U16), "PC": (160, BF),
     "DEAD": (32, BF), "GU": (32, U16),
     "FB": (40, BF), "FA": (40, BF), "PP": (40, BF), "NG": (40, BF), "B1": (40, F32), "B2": (40, BF), "BU": (40, U16),
     "L1": (160, F32), "L2": (160, F32), "TL": (16, U16), "CF": (160, F32), "CU": (160, U16),
@@ -253,78 +256,98 @@ def plan(nodes, users):
             return lat[d] + T_HOP if waits(full[i][d], queue[i] if comp[i] else None, queue[d] if comp[d] else None) else busy[d]
         pre = [[(d, gap(d, i)) for d in full[i]] for i in range(n)]
         post = [[(i, gap(d, i)) for i in needing[d]] for d in range(n)]
-        best, tabu = None, {}
         head, tail, dep, need = [0.0] * (n + 1), [0.0] * (n + 1), [0.0] * n, [0.0] * n
-        before, behind = [n] * (n + 1), [n] * (n + 1)
+        before, behind, beside = [n] * (n + 1), [n] * (n + 1), [n] * n
         span = busy + [0.0]
-        for turn in range(turns + 1):
-            last = {q: n for q in "vatgsx"}
-            for i in seq:
+
+        def ways(part, last, following):
+            last = dict(last)
+            for i in part:
                 x = 0.0
                 for d, w in pre[i]:
                     if head[d] + w > x:
                         x = head[d] + w
                 dep[i] = x
-                p = last[queue[i]]
-                before[i], behind[p], last[queue[i]] = p, i, i
-                head[i] = x if x > head[p] + span[p] else head[p] + span[p]
-            for p in last.values():
-                behind[p] = n
-            for i in reversed(seq):
+                q = queue[i]
+                p = last[q]
+                beside[i] = last["a" if q == "v" else "v"]
+                before[i], behind[p], last[q] = p, i, i
+                y = head[p] + span[p]
+                head[i] = x if x > y else y
+            for q, p in last.items():
+                behind[p] = following[q]
+            length = 0.0
+            for i in reversed(part):
                 x = lat[i]
                 for e, w in post[i]:
                     if tail[e] + w > x:
                         x = tail[e] + w
                 need[i] = x
                 y = span[i] + tail[behind[i]]
-                tail[i] = x if x > y else y
-            length = max(tail)
-            if best is None or length < best[0] - 1e-9:
-                best = (length, head[:n], list(queue))
-            pick = None
-            for at, i in enumerate(seq):
-                if head[i] + tail[i] < length - 1e-6:
-                    continue
-                j = behind[i]
-                if j < n and head[j] < head[i] + span[i] + 1e-6 and head[j] + tail[j] > length - 1e-6 and not anc[j] >> i & 1:
-                    p = before[i]
-                    hj = max(dep[j], head[p] + span[p])
-                    ti = max(need[i], span[i] + tail[behind[j]])
-                    x = max(hj + max(need[j], span[j] + ti), max(dep[i], hj + span[j]) + ti) + JITTER * draw()
-                    if (tabu.get((j, i), -1) < turn or x < best[0]) and (pick is None or x < pick[0]):
-                        pick = (x, i, j)
-                if nodes[i][6] and tabu.get(i, -1) < turn:
-                    q, b = nodes[i][6] if queue[i] == nodes[i][0] else nodes[i][:2]
-                    p = next((k for k in seq[at::-1] if queue[k] == q), n)
-                    e = behind[p] if p < n else next((k for k in seq if queue[k] == q), n)
-                    x = max(dep[i], head[p] + span[p]) + max(need[i] + b - span[i], b + tail[e]) + JITTER * draw()
-                    if pick is None or x < pick[0]:
-                        pick = (x, i, None)
-            if pick is None:
-                break
-            x, i, j = pick
-            if j is None:
-                swap(i)
-                span[i] = busy[i]
-                for x in [i] + needing[i]:
-                    pre[x] = [(d, gap(d, x)) for d in full[x]]
-                for x in [i] + list(full[i]):
-                    post[x] = [(e, gap(x, e)) for e in needing[x]]
-                tabu[i] = turn + TABU * 4
-            else:
-                a, e = seq.index(i), seq.index(j)
-                late, early = {i}, []
-                for k in seq[a + 1:e]:
-                    if before[k] in late or any(d in late for d in full[k]):
-                        late.add(k)
-                    else:
-                        early.append(k)
-                seq[a:e + 1] = early + [j] + [k for k in seq[a:e] if k in late]
-                tabu[(i, j)] = turn + TABU + int(TABU * draw())
-        for i in either:
-            if queue[i] != best[2][i]:
-                swap(i)
-        return best[1]
+                tail[i] = x = x if x > y else y
+                if head[i] + x > length:
+                    length = head[i] + x
+            return length
+
+        def turn_over(i):
+            swap(i)
+            span[i] = busy[i]
+            for x in [i] + needing[i]:
+                pre[x] = [(d, gap(d, x)) for d in full[x]]
+            for x in [i] + list(full[i]):
+                post[x] = [(e, gap(x, e)) for e in needing[x]]
+        none = {q: n for q in "vatgsx"}
+        for lo in range(-int(STRETCH * draw() / 2), n, STRETCH // 2):
+            ways(seq, none, none)
+            seq.sort(key=lambda k: head[k])
+            lo, hi = max(lo, 0), min(lo + STRETCH, n)
+            part, last, following = seq[lo:hi], dict(none), dict(none)
+            last.update((queue[k], k) for k in seq[:lo])
+            following.update((queue[k], k) for k in reversed(seq[hi:]))
+            inside, best, tabu = set(part), None, {}
+            for turn in range(turns + 1):
+                length = ways(part, last, following)
+                if best is None or length < best[0] - 1e-9:
+                    best = (length, list(part), list(queue), turn)
+                if turn > best[3] + PATIENCE:
+                    break
+                pick = None
+                for i in [k for k in part if head[k] + tail[k] > length - 1e-6]:
+                    j = behind[i]
+                    if j in inside and head[j] < head[i] + span[i] + 1e-6 and head[j] + tail[j] > length - 1e-6 and not anc[j] >> i & 1:
+                        p = before[i]
+                        hj = max(dep[j], head[p] + span[p])
+                        ti = max(need[i], span[i] + tail[behind[j]])
+                        x = max(hj + max(need[j], span[j] + ti), max(dep[i], hj + span[j]) + ti) + JITTER * draw()
+                        if (tabu.get((j, i), -1) < turn or x < best[0]) and (pick is None or x < pick[0]):
+                            pick = (x, i, j)
+                    if nodes[i][6] and tabu.get(i, -1) < turn:
+                        b, p = (nodes[i][6] if queue[i] == nodes[i][0] else nodes[i])[1], beside[i]
+                        x = max(dep[i], head[p] + span[p]) + max(need[i] + b - span[i], b + tail[behind[p]]) + JITTER * draw()
+                        if p < n and (pick is None or x < pick[0]):
+                            pick = (x, i, None)
+                if pick is None:
+                    break
+                x, i, j = pick
+                if j is None:
+                    turn_over(i)
+                    tabu[i] = turn + TABU * 4
+                else:
+                    a, e = part.index(i), part.index(j)
+                    late, early = {i}, []
+                    for k in part[a + 1:e]:
+                        if before[k] in late or any(d in late for d in full[k]):
+                            late.add(k)
+                        else:
+                            early.append(k)
+                    part[a:e + 1] = early + [j] + [k for k in part[a:e] if k in late]
+                    tabu[(i, j)] = turn + TABU + int(TABU * draw())
+            seq[lo:hi] = best[1]
+            for i in either:
+                if queue[i] != best[2][i]:
+                    turn_over(i)
+        ways(seq, none, none)
+        return head[:n]
 
     pre, post = links({})
     level = [0.0] * n
@@ -506,12 +529,31 @@ def record(g, core, T, topo, rank):
         q = PLAN["queue"][len(nodes)] if PLAN else "va"[on_scalar]
         da, dv = cost(out, [in_], 1.0) + 0.015, cost(out, [in_], None)
         op(q, rd, wr, da if q == "a" else dv, on_a if q == "a" else on_v, ("v", dv) if q == "a" else ("a", da))
+        return int(q == "a")
+
+    def under(rd, wr, out, in_, x, sign=1.0):
+        return either(1, rd, wr, out, in_, lambda: s.activation(out, in_, F.Sign, scale=-sign, bias=sign * x),
+                      lambda: v.tensor_scalar(out, in_, x, 2.0, A.is_lt if sign > 0 else A.is_gt, A.mult))
+
+    def linear(rd, wr, out, in_, scale, plus):
+        either(1, rd, wr, out, in_, lambda: s.activation(ap(out), ap(in_), F.Identity, scale=scale, bias=plus),
+               lambda: v.tensor_scalar(ap(out), ap(in_), scale, plus, A.mult, A.add))
 
     def move(on_scalar, rd, wr, out, in_, f=F.Copy):
         either(on_scalar, rd, wr, out, in_, lambda: s.activation(ap(out), ap(in_), f), lambda: v.tensor_copy(ap(out), ap(in_)))
 
     def relu(rd, wr, out, in_, plus):
         either(1, rd, wr, out, in_, lambda: s.activation(out, in_, F.Relu, bias=plus), lambda: v.tensor_scalar(out, in_, plus, 0.0, A.add, A.max))
+
+    def below(rd, wr, out, in_, x):
+        either(1, rd, wr, out, in_, lambda: s.activation(out, in_, F.Relu, scale=-1.0, bias=x), lambda: v.tensor_scalar(out, in_, x, None, A.is_lt))
+
+    def upper(rd, wr, out, in_):
+        return either(1, rd, wr, out, in_, lambda: s.activation(out, in_, F.Relu, scale=-1.0, bias=255.0), lambda: v.tensor_scalar(out, in_, 255.0, None, A.min))
+
+    def dies(rd, wr, out, in_, x):
+        either(1, rd, wr, out, in_, lambda: s.activation(out, in_, F.Relu, scale=float(XN), bias=-x * XN),
+               lambda: v.tensor_scalar(out, in_, x, float(XN), A.is_gt, A.mult))
 
     PS = []
 
@@ -529,6 +571,11 @@ def record(g, core, T, topo, rank):
     def mms(b, n, terms, st=True, sp=True, c0=0):
         for i, (m, rd, x) in enumerate(terms):
             mm(rd + " " + m, "PS%d" % b, PS[b][:, c0:c0 + n], mat(m), x, st and i == 0, sp and i == len(terms) - 1)
+
+    def opening(b, n, terms, lack, m):
+        calls = [(PS[b][:, 0:n], mat(x[0]), x[2], i == 0, False) for i, x in enumerate(terms)]
+        calls += [(PS[b][:, a:e], mat(m), T.ONB[:, a:e], False, False) for a, e in lack]
+        group(" ".join(x[0] + " " + x[1] for x in terms) + " ONB " + m, "PS%d" % b, calls)
 
     def seg(name, k0, k1, c0=0):
         return T[name][:, 16 * (c0 + k0):16 * (c0 + k1)]
@@ -570,12 +617,13 @@ def record(g, core, T, topo, rank):
                 g.remote_dma_fused(trs, local_sem=T.sem[loc])
                 total[loc] = total.get(loc, 0) + used
                 return loc, total[loc]
-            node("g", key + after, "order" + (" sent%d" % n if far else ""), 0.3, T_REMOTE, send)
+            node("g", key + after, "order sent%d%d" % (n, far), 0.3 + (T_FIRST if n == 0 and far else 0.0), T_REMOTE + (T_FIRST if n == 0 and far else 0.0), send)
 
         def arrive():
             total["arr%d" % n] = arr
             return "arr%d" % n, arr
-        node("x", "sent%d" % n, "XG" if n % 2 == 0 else "LG", 0.01, T_REMOTE + (4.0 if n == 0 else 0.0), arrive)
+        node("x", "sent%d1" % n, "handed%d" % n, 0.01, T_REMOTE + (T_FIRST if n == 0 else 0.0), arrive)
+        node("x", "handed%d sent%d0" % (n, n), "XG" if n % 2 == 0 else "LG", 0.01, 0.01 - T_HOP, arrive)
 
     dma("s", "", "Xb", T.X[:, 0:384], T.x0[:, 0:384], 96)
     dma("a", "", "CI CIb", T.CI[:, 0:288], T.ct[:, :], 144)
@@ -614,23 +662,24 @@ def record(g, core, T, topo, rank):
     def sbuf(ch):
         return "SS" if ch % 2 else "S"
 
+    def part(sb, k, a, e):
+        return " ".join("%s%d_%d" % (sb, k, i) for i in range(a // 8, (e + 7) // 8))
+
+    def fill(wr, out, val):
+        either(0, "O0", wr, out, out, lambda: s.activation(out, T.O[:, 0:size(out)], F.Identity, scale=0.0, bias=val), lambda: v.memset(out, val))
+
     def constants():
         ts("RQ SF", "ID", T.ID[:, :], T.RQ[:, :], PF, A.is_equal)
         ts("RG SF", "BO", T.BO[:, :], T.RG[:, :], GC, A.is_equal)
         ms("ZE", T.ZE[:, 0:144], 0.0)
         cp("BO ZE", "ZE", T.ZE[:, 15:143:16], T.BO[:, 0:128:16])
-        act("ZE", "ZS", T.ZE[:, 144:288], T.ZE[:, 0:144], F.Copy, scale=-32768.0)
+        act("ZE", "ZS", T.ZE[:, 144:288], T.ZE[:, 0:144], F.Copy, scale=-BIG)
         for name, x in SCALED.items():
             act("ID", name, mat(name), T.ID[:, :], F.Copy, scale=x)
         act("ID", "IF", T.IF[:, :], T.ID[:, :], F.Copy)
-        ts("ID", "M2", T.M2[:, :], T.ID[:, :], 100.0, A.mult)
-        ts("RQ SF", "D16", T.D16[:, :], T.RQ[:, 0:16], P16, A.is_equal, 1024.0, A.mult)
-        tt("BO M2", "M1", T.M1[:, :], T.BO[:, :], T.M2[:, :], A.add)
-        tt("BO M2", "M2", T.M2[:, :], T.BO[:, :], T.M2[:, :], A.subtract)
-        ms("EXP", T.EXP[:, :], 1.0)
-        op("g", "EXP", "EXP", 2.2, lambda: g.affine_select(T.EXP[:, :], T.EXP[:, :], [[1, 64], [0, 16]], A.is_equal, 0.0, 0, -1))
+        ts("RQ SF", "D16", T.D16[:, :], T.RQ[:, 0:16], P16, A.is_equal, 512.0, A.mult)
         iota("PTD", T.PTD[:, :], [[1, 448]], 25 - 256)
-        ms("PTR", T.PTR[:, :], 24.0 - 256)
+        fill("PTR", T.PTR[:, :], 24.0 - 256)
         iota("PTR", T.PTR[:, 288:312], [[1, 24]], -256)
         iota("KI", T.KI[:, 0:4], [[-3, 4]], 48, 1, True)
         iota("KP", T.KP[:, :], [[0, 40], [1, 16]], 0)
@@ -640,9 +689,9 @@ def record(g, core, T, topo, rank):
         for ch in range(2):
             sb, gap = sbuf(ch), SW - 16 - 16 * CH1[0][ch]
             for k in range(7):
-                ms("%s%d %s%d" % (sb, k, sb, (k + 6) % 7), T[sb][:, max(k * SW - gap, 8):k * SW + 16], 1024.0)
-            ms(sb + "n", T[sb][:, 0:8], 512.0)
-        ms("LOGn", T.LOG[:, 384:400], 1024.0)
+                fill("%s%d " % (sb, k) + (part(sb, k - 1, CH1[0][ch], 64) if k else ""), T[sb][:, max(k * SW - gap, 8):k * SW + 16], 1024.0)
+            fill(sb + "n", T[sb][:, 0:8], 512.0)
+        fill("LOGn", T.LOG[:, 384:400], 1024.0)
         for i, sizes in enumerate(CH1 + [CH2]):
             for k0, nk in spans(sizes):
                 if i == 0 or sizes != (CH1 + [CH2])[i - 1]:
@@ -664,18 +713,21 @@ def record(g, core, T, topo, rank):
         ts("CI", "LWi", T.LW[:, 0:640], T.CI[:, :], 0.0, A.add)
         ts("CI", "CI", T.CI[:, :], T.CI[:, :], 4, A.arith_shift_right)
         cp("CI", "TC", T.TC[:, 0:640], T.CI[:, :])
-        ms("TCx", T.TC[:, 640:800], float(EC))
-        ms("LOx", T.LO[:, 640:800], 0.0)
+        fill("TCx", T.TC[:, 640:800], float(EC))
+        fill("LOx", T.LO[:, 640:800], 0.0)
         act("TC", "LWj", T.LW[:, 640:1280], T.TC[:, 0:640], F.Copy, scale=-16.0)
-        tt("LWi LWj", "LO LW", T.LO[:, 0:640], T.LW[:, 0:640], T.LW[:, 640:1280], A.add)
+        for c0 in (0, 320):
+            b = small()
+            mms(b, 320, [("IF", "LWi LW", T.LW[:, c0:c0 + 320]), ("IF", "LWj LW", T.LW[:, 640 + c0:960 + c0])])
+            move(1, "PS%d" % b, "LO%d" % c0, T.LO[:, c0:c0 + 320], PS[b][:, 0:320])
         ts("KI", "KI", T.KI[:, 0:4], T.KI[:, 0:4], 15, A.bitwise_and)
         cp("KI", "PB", T.PB[:, 0:4], T.KI[:, 0:4])
         ts("PB", "PBb", T.PB[:, 4:8], T.PB[:, 0:4], -40.0, A.mult, 1280.0, A.add)
         for u in range(RO):
             act("RQ PBb", "KIU%d" % u, T.KIU[:, 40 * u:40 * u + 40], T.RQ[:, 0:40], F.Identity, scale=-1.0, bias=T.PB[:, 4 + u:5 + u])
         ts("SF", "SFe", T.SF[:, 22:23], P16, 0.0, A.not_equal, ONE, A.mult)
-        ms("FA", T.FA[:, :], 1.0)
-        ms("NG", T.NG[:, :], -1.0)
+        fill("FA", T.FA[:, :], 1.0)
+        fill("NG", T.NG[:, :], -1.0)
         for u in range(RO):
             ts("KP PB", "TRI%d" % u, T.TRI[:, 128 * u:128 * u + 128], T.KP[:, 16 - 3 * u:144 - 3 * u], T.PB[:, u:u + 1], A.is_gt)
         ts("KP", "KP", T.KP[:, :], T.KP[:, :], 0.0, A.not_equal)
@@ -693,10 +745,10 @@ def record(g, core, T, topo, rank):
         iota("DU2", T.DU2[:, :], [[0, 5], [16, 32]], 0)
         act("DU2 SF", "DU2", T.DU2[:, :], T.DU2[:, :], F.Identity, bias=P16)
         act("Z16 SFe", "ONM", T.ONM[:, :], T.Z16[:, 0:512], F.Identity, bias=T.SF[:, 22:23])
-        ms("ONB", T.ONB[:, :], 1.0)
-        ms("FL", T.FL[:, :], 1.0)
-        ms("CAP", T.CAP[:, :], float(K1))
-        ms("QC0", T.QC[:, 15:16], 0.0)
+        fill("ONB", T.ONB[:, :], 1.0)
+        fill("FL", T.FL[:, :], 1.0)
+        fill("CAP", T.CAP[:, :], float(K1))
+        fill("QC0", T.QC[:, 15:16], 0.0)
         scan("FL CAP", "QC", T.QC[:, 16:16 + C], T.FL[:, :], T.CAP[:, :], 0.0, A.add, A.min)
         ts("OO", "TH5", T.TH5[:, 0:8], T.OO[:, 0:8], 0.5, A.add)
         for u in range(1, RO):
@@ -706,7 +758,7 @@ def record(g, core, T, topo, rank):
             act("RQ", "OFFb%d" % u, T.OFF[:, 8 * u + VC:8 * u + 8], T.RQ[:, VC:8], F.Identity, scale=16.0, bias=2.0 * lo + n)
         ts("OO", "DM", T.DM[:, 0:7], T.OO[:, 0:7], 2.0, A.mult, 64.0, A.add)
 
-    def camera_flags(u, scale=1.0):
+    def camera_flags(u):
         st, b = (SC * u) % C, small()
         src = [(T.FL, "FL", 0, "ID", SC), (T.QC, "QC", 16, "NI", SC), (T.QC, "QC QC0", 15, "ID", SC),
                (T.MC, "MC", 0, "BO", st), (T.MC, "MC", 288, "BO", st), (T.M16, "M16", 0, "BO", st), (T.M16, "M16", 288, "BO", st)]
@@ -716,7 +768,8 @@ def record(g, core, T, topo, rank):
             mms(b, C - sh, [(m, key, buf[:, c0 + sh:c0 + C])], False, last and sh == 0)
             if sh:
                 mms(b, sh, [(m, key, buf[:, c0:c0 + sh])], False, last, C - sh)
-        ts("PS%d" % b, "FL", T.FL[:, :], PS[b][:, 0:C], 0.5, A.is_gt, scale, A.mult)
+        either(0, "PS%d" % b, "FL", T.FL[:, :], PS[b][:, 0:C], lambda: s.activation(T.FL[:, :], PS[b][:, 0:C], F.Sign),
+               lambda: v.tensor_scalar(T.FL[:, :], PS[b][:, 0:C], 0.5, None, A.is_gt))
 
     def killed(m, c0, n):
         return [(m, key, buf[:, r + c0:r + c0 + n]) for buf, key, r in ((T.MC, "MC", 288), (T.MC, "MCb", 576), (T.M16, "M16", 288), (T.M16, "M16", 576))]
@@ -728,8 +781,8 @@ def record(g, core, T, topo, rank):
             mms(b, ns, [("IF", "CTL", T.CTL[:, s0:s0 + ns])] + killed("IXN", s0, ns))
             ts("PS%d" % b, keys("XO", 0, ns), T.XO[:, 0:ns], PS[b][:, 0:ns], float(XN), A.min)
         b = small()
-        mms(b, C, killed("IXN", 0, C))
-        tt("PS%d CTL" % b, "CTL", T.CTL[:, 0:C], T.CTL[:, 0:C], PS[b][:, 0:C], A.max)
+        mms(b, C, [("IF", "CTL", T.CTL[:, 0:C])] + killed("IXN", 0, C))
+        move(1, "PS%d" % b, "CTL", T.CTL[:, 0:C], PS[b][:, 0:C])
 
     def camera_list(u):
         st, (s0, ns), (lo, hi, wrap) = SC * u, SURE[u], listed(u)
@@ -767,15 +820,17 @@ def record(g, core, T, topo, rank):
 
     def finals(ch, nk):
         sb = sbuf(ch)
-        return sb + "n " + " ".join("%s%d" % (sb, k) for k in range(7)), T[sb][:, 0:6 * SW + 16 + 16 * nk]
+        return sb + "n " + " ".join("%s%d " % (sb, k) + part(sb, k, 0, 64 if k < 6 else nk) for k in range(7)), T[sb][:, 0:6 * SW + 16 + 16 * nk]
 
     def passes(name, ch, k0, n):
-        key = keys(name, k0, k0 + n)
+        sb, h = sbuf(ch), n // 2 if n >= HALVES else n
         for k in range(8):
-            sb, a, b = sbuf(ch), (k + 5) % 7, (k + 6) % 7
-            d1 = T.CP[:, 0:16 * n] if k == 0 else T[sb][:, a * SW + 15:a * SW + 15 + 16 * n]
-            scan(key + (" CP" if k == 0 else " %s%d" % (sb, a)), "%s%d" % (sb, b), T[sb][:, b * SW + 16:b * SW + 16 + 16 * n],
-                 seg(name, k0, k0 + n), d1, 1024.0, A.min, A.max)
+            a, b = (k + 5) % 7, (k + 6) % 7
+            for i in range(0, n, h):
+                d1 = T.CP[:, 0:16 * h] if k == 0 else T[sb][:, a * SW + 15 + 16 * i:a * SW + 15 + 16 * (i + h)]
+                rd = " CP" if k == 0 else " %s%d " % (sb, a) + part(sb, a, max(i - 1, 0), i + h)
+                scan(keys(name, k0 + i, k0 + i + h) + rd, part(sb, b, i, i + h), T[sb][:, b * SW + 16 + 16 * i:b * SW + 16 + 16 * (i + h)],
+                     seg(name, k0 + i, k0 + i + h), d1, 1024.0, A.min, A.max)
 
     def pucol(k0):
         return k0 // 16 + k0 // 16 % 2
@@ -785,7 +840,7 @@ def record(g, core, T, topo, rank):
         w0, w1 = k0 // 16, k1 // 16
         b, b2, w = small(), small(), w1 - w0
         fold(b, "UH", w0, w1, keys("UH", k0, k1))
-        ts("PS%d" % b, "KB", T.KB[:, 0:w], PS[b][:, 0:w], 0.25, A.mult, 128.25 + 4 * plus, A.add)
+        linear("PS%d" % b, "KB", T.KB[:, 0:w], PS[b][:, 0:w], 0.25, 128.25 + 4 * plus)
         mms(b2, w, [("I16", keys("FN", 16 * (fn + w0), 16 * (fn + w1)), T.FN[:, fn + w0:fn + w1]), ("ISW", "KB", T.KB[:, 0:w])])
         cuts = [w0] + [a // 16 for a, nk in chunks[1:] if a // 16 % 2] + [w1]
         for a, e in zip(cuts[:-1], cuts[1:]):
@@ -795,27 +850,25 @@ def record(g, core, T, topo, rank):
     def median(ch, k0, nk):
         return finals(ch, nk)[0] + " " + keys("PU", k0, k0 + nk), ind(finals(ch, nk)[1], T.PU[:, pucol(k0):pucol(k0) + nk // 16])
 
-    def spread(ch, k0, nk):
-        b = small()
-        mm("PC%d ID" % ch, "PS%d" % b, PS[b][0:nk, 0:128], T.PC[:, k0:k0 + nk], T.ID[:, :])
-        move(1, "PS%d" % b, "PT%d" % ch, T.PT[0:nk, 128 * ch:128 * ch + 128], PS[b][0:nk, 0:128])
-
     def wide(ch, k0, nk, m, src):
         for a in range(k0, k0 + nk, 32):
             e = min(k0 + nk, a + 32)
             b, n = nextbank(), 16 * (e - a)
             mms(b, n, [(m,) + src(a, e)], True, False)
-            mm("PT%d EXP" % ch, "PS%d" % b, PS[b][:, 0:n], T.PT[0:nk, 128 * ch:128 * ch + 128], T.EXP[0:nk, 16 * (a - k0):16 * (e - k0)], False, True)
+            group("PC%d ID" % ch, "PS%d" % b, [(PS[b][:, j:n:16], T.ID[:, :], T.PC[:, a:e], False, j == 15) for j in range(16)])
             yield a, e, b
 
     def near(name, k0, nk):
+        lack = []
         for a in range(k0, k0 + nk, 32):
             e = min(k0 + nk, a + 32)
-            ts(keys(name, a, e), keys(name, a, e), seg(name, a, e), seg(name, a, e), 12.5, A.is_le)
+            if under(keys(name, a, e), keys(name, a, e), seg(name, a, e), seg(name, a, e), 12.5):
+                lack.append((a - k0, e - k0))
+        return lack
 
     def port_places(c0, n, more):
         b = small()
-        act("CTL", "DEAD", T.DEAD[:, 0:n], T.CTL[:, c0:c0 + n], F.Relu, bias=1.0 - XN)
+        relu("CTL", "DEAD", T.DEAD[:, 0:n], T.CTL[:, c0:c0 + n], 1.0 - XN)
         mms(b, n, [("NBG", "DEAD", T.DEAD[:, 0:n]), ("I16", "PTR", T.PTR[:, c0:c0 + n])] + more)
         ts("PS%d SFd" % b, "GU", T.GU[:, 0:n], PS[b][:, 0:n], T.SF[:, 21:22], A.add, 0.0, A.max)
 
@@ -846,6 +899,7 @@ def record(g, core, T, topo, rank):
         both = [(0, ns, lambda buf: buf[:, s0:s0 + ns], ""), (ns, K1, lambda buf: ind(buf[:, :], T.WL[:, 0:(K1 - ns) // 16]), " WL")]
         both = [p for p in both if p[1] > p[0]]
         parts = [(a, min(a + 32, K1)) for a in range(0, K1, 32)]
+        lv, uh1 = [0] * K1, [0] * K2
 
         def obs(a, e):
             return ("O0 O1" if u else "O0", seg("O", a, e, s0)) if e <= ns else (keys("OG", a, e), seg("OG", a, e))
@@ -856,13 +910,13 @@ def record(g, core, T, topo, rank):
                     move(ON["OG"][a // 32], "O0 O1 OU", keys("OG", a, e), seg("OG", a, e), ind(T.O[:, :], T.OU[:, a:e]))
         for a, e, tab, wl in both:
             if wl or u == 0:
-                cp("CTL" + wl, keys("XO", a, e), T.XO[:, a:e], tab(T.CTL))
+                ts("CTL" + wl, keys("XO", a, e), T.XO[:, a:e], tab(T.CTL), float(XN), A.min)
             tt("CTO CTOx DU1" + wl, keys("FO", a, e), T.FO[:, a:e], tab(T.CTO), T.DU1[:, a:e], A.min)
             cp(keys("FO", a, e), keys("FU", a, e), T.FU[:, a:e], T.FO[:, a:e])
             if wl:
                 move(1, "CTL WL", "XF", T.XF[:, a:e], tab(T.CTL))
-            act("XF" if wl else "CTL", keys("LV", a, e), T.LV[:, a:e], T.XF[:, a:e] if wl else tab(T.CTL), F.Sign, scale=-1.0, bias=XN - 0.5)
-        for a, e in parts:
+            lv[a:e] = [under("XF" if wl else "CTL", keys("LV", a, e), T.LV[:, a:e], T.XF[:, a:e] if wl else tab(T.CTL), XN - 0.5)] * (e - a)
+        for a, e in [(a, a + n) for a, n in spans(FCALLS[u])]:
             act(keys("FU", a, e) + " ONA", "WA0 WA8", ind(T.WA[:, 0:12032], T.FU[:, a:e]), T.ONA[:, 0:16 * (e - a)], F.Silu)
         dma("a", "WA0", "M32", T.M32[:, 0:640], T.WA[0:128:16, 0:10240], 320)
         dma("s", "Z32 M32", "WA8", T.WA[8:128:16, 864:864 + MW], T.Z32[:, :], 432)
@@ -882,12 +936,12 @@ def record(g, core, T, topo, rank):
         for grp in groups(ch1, UG1[u]):
             a, e, b = grp[0][0], grp[-1][0] + grp[-1][1], small()
             fold(b, "D", a, e)
-            ts("PS%d" % b, keys("UH", a, e), T.UH[:, a:e], PS[b][:, 0:e - a], 4088.0, A.is_lt, 2.0, A.mult)
-            pick_places(grp, 10 * fn_of(u), 0)
+            uh1[a:e] = [under("PS%d" % b, keys("UH", a, e), T.UH[:, a:e], PS[b][:, 0:e - a], 4088.0)] * (e - a)
+            pick_places(grp, 10 * fn_of(u), uh1[a])
         track_list(u)
         for a in range(0, K2, 32):
             move(ON["PG"][a // 32], "PTR CU", keys("PG", a, a + 32), seg("PG", a, a + 32), ind(T.PTR[:, :], T.CU[:, a:a + 32]))
-        act("LO LOx TL", "MO", T.MO[:, :], ind(T.LO[:, :], T.TL[:, 0:10]), F.Identity, bias=1.0)
+        linear("LO0 LO320 LOx TL", "MO", T.MO[:, :], ind(T.LO[:, :], T.TL[:, 0:10]), 1.0, 1.0)
         logk = "LOGn"
         border = 0 if u and not listed(u)[2] else (ns if u else 0) + 24
 
@@ -900,33 +954,32 @@ def record(g, core, T, topo, rank):
             r, k1 = slice(k0, k0 + nk), k0 + nk
             passes("D", ch, k0, nk)
             move(ON["PC1"], median(ch, k0, nk)[0], "PC%d" % ch, T.PC[:, r], median(ch, k0, nk)[1])
-            spread(ch, k0, nk)
             for a, e, b in wide(ch, k0, nk, "NI", lambda a, e: (keys("D", a, e), seg("D", a, e))):
                 act("PS%d" % b, keys("D", a, e), seg("D", a, e), PS[b][:, 0:16 * (e - a)], F.Abs)
+            clips = {}
             for a, e, b in wide(ch, k0, nk, "ID", obs):
-                if ON["CLIP"][a // 32]:
-                    act("PS%d" % b, keys("OG", a, e), seg("OG", a, e), PS[b][:, 0:16 * (e - a)], F.Relu, scale=-1.0, bias=255.0)
-                else:
-                    ts("PS%d" % b, keys("OG", a, e), seg("OG", a, e), PS[b][:, 0:16 * (e - a)], 255.0, A.min)
-            near("D", k0, nk)
+                clips[a] = upper("PS%d" % b, keys("OG", a, e), seg("OG", a, e), PS[b][:, 0:16 * (e - a)])
+            lack = near("D", k0, nk)
             b, uh = small(), keys("UH", k0, k1)
-            mms(b, nk, [("I50", uh, T.UH[:, r])], True, False)
+            opening(b, nk, [("I50", uh, T.UH[:, r])], lack, "I16")
             fold(b, "D", k0, k1, st=False)
-            ts("PS%d" % b, "FIT%d" % ch, T.FIT[:, r], PS[b][:, 0:nk], 111.5, A.is_gt)
+            fit = under("PS%d" % b, "FIT%d" % ch, T.FIT[:, r], PS[b][:, 0:nk], 123.0 - 50 * uh1[k0], -1.0)
             b, b2 = small(), small()
-            mms(b, nk, [("I50", keys("LV", k0, k1), T.LV[:, r]), ("N50", uh, T.UH[:, r]), ("M1", "FIT%d" % ch, T.FIT[:, r])])
-            ts("PS%d" % b, "NONE%d" % ch, T.NONE[:, r], PS[b][:, 0:nk], 55.5, A.is_lt)
-            mms(b2, nk, [("I50", uh, T.UH[:, r]), ("M2", "FIT%d" % ch, T.FIT[:, r])])
-            ts("PS%d" % b2, keys("DIE", k0, k1), T.DIE[:, r], PS[b2][:, 0:nk], 105.5, A.is_ge, float(XN), A.mult)
+            opening(b, nk, [("I50", keys("LV", k0, k1), T.LV[:, r]), ("N50", uh, T.UH[:, r])], [], "")
+            group("FIT%d BO I50" % ch, "PS%d" % b, [(PS[b][:, 0:nk], mat(m), T.FIT[:, r], False, m == "BO") for m in ("I50", "BO")])
+            none = under("PS%d" % b, "NONE%d" % ch, T.NONE[:, r], PS[b][:, 0:nk], 111.0 - 50 * lv[k0] + 50 * uh1[k0] - 66 * fit)
+            mms(b2, nk, [("I50", uh, T.UH[:, r])], True, False)
+            group("FIT%d BO N50" % ch, "PS%d" % b2, [(PS[b2][:, 0:nk], mat(m), T.FIT[:, r], False, m == "BO") for m in ("N50", "BO")])
+            dies("PS%d" % b2, keys("DIE", k0, k1), T.DIE[:, r], PS[b2][:, 0:nk], 111.0 - 50 * uh1[k0] + 34 * fit)
             for a in range(k0, k1, 32):
                 e = min(k1, a + 32)
-                b, n, clip = nextbank(), 16 * (e - a), ON["CLIP"][a // 32]
-                mms(b, n, [("NI" if clip else "ID", keys("OG", a, e), seg("OG", a, e))], True, False)
+                b, n, clip = nextbank(), 16 * (e - a), clips[a]
+                mms(b, n, [("NI" if clip else "ID", keys("OG", a, e) + " NI ID", seg("OG", a, e))], True, False)
                 group("NONE%d " % ch + " ".join("SEL%d" % j for j in range(16)), "PS%d" % b,
                       [(PS[b][:, j:n:16], T.SEL[:, 128 * j:128 * j + 128], T.NONE[:, a:e], False, j == 15) for j in range(16)])
                 key = "LOG%d_%d" % (u, a)
                 logk += " " + key
-                relu("PS%d" % b, key, T.LOG[:, lb + 16 * a:lb + 16 * e], PS[b][:, 0:n], 255.0 * clip)
+                relu("PS%d" % b, key, T.LOG[:, lb + 16 * a:lb + 16 * e], PS[b][:, 0:n], 255.0 * clip + 512.0 * none)
             if k0 < border <= k1:
                 send_b(k1)
         for a, e, tab, wl in both:
@@ -941,37 +994,37 @@ def record(g, core, T, topo, rank):
         for a in range(0, K2, 32):
             move(ON["BG"][a // 32], wk + " " + keys("IU", a, a + 32), keys("BG", a, a + 32), seg("BG", a, a + 32), ind(win, T.IU[:, a:a + 32]))
         move(1, "TC TCx TL", "CF", T.CF[:, :], ind(T.TC[:, :], T.TL[:, 0:10]))
-        act("CF", "PEN", T.PEN[:, :], T.CF[:, :], F.Relu, bias=-287.0)
+        relu("CF", "PEN", T.PEN[:, :], T.CF[:, :], -287.0)
         move(ON["XOLD"], "X Xb Xd TL", "XOLD", T.XOLD[:, :], ind(T.X[:, 0:800], T.TL[:, 0:10]))
         for grp in groups(ch2, UG2):
             a, e, b = grp[0][0], grp[-1][0] + grp[-1][1], small()
             fold(b, "BG", a, e)
-            act("PS%d" % b, keys("UH", a, e), T.UH[:, a:e], PS[b][:, 0:e - a], F.Sign, scale=-1.0, bias=10000.0)
-            pick_places(grp, 10 * RO, 1)
+            uh1[a:e] = [under("PS%d" % b, keys("UH", a, e), T.UH[:, a:e], PS[b][:, 0:e - a], 10000.0)] * (e - a)
+            pick_places(grp, 10 * RO, uh1[a])
             b = small()
             mms(b, e - a, [("BO", keys("UH", a, e), T.UH[:, a:e])])
-            act("PS%d" % b, keys("NH", a, e), T.NH[:, a:e], PS[b][:, 0:e - a], F.Relu, scale=-1.0, bias=5.0 - 16)
+            below("PS%d" % b, keys("NH", a, e), T.NH[:, a:e], PS[b][:, 0:e - a], 5.0 - 16 * uh1[a])
         for ch, (k0, nk) in enumerate(ch2):
             r, k1 = slice(k0, k0 + nk), k0 + nk
             passes("BG", ch, k0, nk)
             mk, med = median(ch, k0, nk)
             move(ON["PC2"], mk, "PC%d" % ch, T.PC[:, r], med)
             tt(mk + " XOLD", "NE%d" % ch, T.NE[:, r], med, T.XOLD[:, r], A.not_equal)
-            spread(ch, k0, nk)
             for a, e, b in wide(ch, k0, nk, "NI", lambda a, e: (keys("BG", a, e), seg("BG", a, e))):
                 act("PS%d" % b, keys("PG", a, e), seg("PG", a, e), PS[b][:, 0:16 * (e - a)], F.Abs)
             b = small()
             mms(b, nk, [("BO", "NE%d" % ch, T.NE[:, r])])
-            act("PS%d" % b, "SN%d" % ch, T.SN[:, r], PS[b][:, 0:nk], F.Relu, bias=1.0, scale=-1.0)
+            below("PS%d" % b, "SN%d" % ch, T.SN[:, r], PS[b][:, 0:nk], 1.0)
             port = [("IF", "CF", T.CF[:, r]), ("I864", "MO", T.MO[:, r]), ("NBG", "PEN", T.PEN[:, r])]
             b, b2 = small(), small()
             mms(b, nk, port + [("I288", "SN%d" % ch, T.SN[:, r])])
-            act("PS%d" % b, "P1%d" % ch, T.P1[:, r], PS[b][:, 0:nk], F.Identity, bias=288.0)
+            linear("PS%d" % b, "P1%d" % ch, T.P1[:, r], PS[b][:, 0:nk], 1.0, 288.0)
             mms(b2, nk, port + [("NBG", "SN%d" % ch, T.SN[:, r])])
             tt("PS%d DU2" % b2, "P0%d" % ch, T.P0[:, r], PS[b2][:, 0:nk], T.DU2[:, r], A.max)
-            near("PG", k0, nk)
+            lack = near("PG", k0, nk)
             b = small()
-            mms(b, nk, [("I23", keys("UH", k0, k1), T.UH[:, r]), ("I23", "ONB", T.ONB[:, 0:nk]), ("N19", keys("NH", k0, k1), T.NH[:, r])], True, False)
+            opening(b, nk, [("I23", keys("UH", k0, k1), T.UH[:, r]), ("N19", keys("NH", k0, k1), T.NH[:, r])] +
+                    [("I23", "", T.ONB[:, 0:nk])] * uh1[k0], lack, "N18")
             fold(b, "PG", k0, k1, st=False, z=144)
             tt("PS%d P1%d" % (b, ch), "P1%d" % ch, T.P1[:, r], PS[b][:, 0:nk], T.P1[:, r], A.min)
             tt("P0%d P1%d" % (ch, ch), "P1%d" % ch, T.P1[:, r], T.P1[:, r], T.P0[:, r], A.max)
@@ -1011,11 +1064,11 @@ def record(g, core, T, topo, rank):
     port_places(272, 16, killed("NBG", 272, 16))
     ts(wk + " GU", "SG", T.SG[:, 0:256], ind(T.LOG[:, 384:400 + RO * 1792], T.GU[:, 0:16]), 512.0, A.min)
     dma("s", "SG", "", T.yb[:, :], T.SG[:, 0:256], 64)
-    camera_flags(RO, 32.0)
+    camera_flags(RO)
     b, b2 = small(), small()
     mms(b, C, [("IF", "CTL", T.CTL[:, 0:C])] + killed("IXN", 0, C))
     ts("PS%d" % b, "JK0", T.JK[:, :], PS[b][:, 0:C], XN - 0.5, A.is_lt)
-    mms(b2, C, [("BO", "JK0", T.JK[:, :]), ("ID", "FL", T.FL[:, :])])
-    act("PS%d" % b2, "M32", T.M32[:, 0:C], PS[b2][:, 0:C], F.Copy)
+    mms(b2, C, [("BO", "JK0", T.JK[:, :]), ("I32", "FL", T.FL[:, :])])
+    move(1, "PS%d" % b2, "M32", T.M32[:, 0:C], PS[b2][:, 0:C])
     dma("a", "M32", "", T.yc[:, :], T.M32[0:128:16, 0:C], 9)
     emit()

@@ -2,14 +2,16 @@ from concourse.mybir import AluOpType, AxisListType, ActivationFunctionType
 from concourse.bass import DstId, RemoteDMATransfer
 A = AluOpType
 F = ActivationFunctionType
-BF, F32, I32, U16 = "bfloat16", "float32", "int32", "uint16"
+BF, F16, F32, I32, U16 = "bfloat16", "float16", "float32", "int32", "uint16"
 C, NT, K1, K2, RO, SC = 288, 640, 112, 160, 4, 72
 XN = 1184
 EC = 312
-MW = 13824
 SW = 1040
-ONE = 1.278465
 BIG = 16384.0
+ZP, ZZ = 288, 432
+ZE2, ZS2 = 576, 720
+ROUND = 1.5 * 2 ** 23
+PIECES = ((7, 7), (14, 7), (21, 7), (28, 8))
 
 
 def sure_cameras():
@@ -26,60 +28,75 @@ CH1 = [(32, 64, 16), (64, 32, 16), (32, 32, 32, 16), (32, 64, 16)]
 CH2 = (64, 64, 32)
 UG1 = [(1, 3), (1, 3), (1, 4), (1, 3)]
 UG2 = (1, 3)
-IG2 = (1, 2, 3)
-TIMES = (0.0009, 1.56, 3.8, 0.05, 0.00046, 0.2, 1.5, 200.0, 1.9, 2.0)
+IG2 = (1, 3)
+TIMES = (0.0009, 1.56, 3.8, 0.05, 0.00046, 0.27, 1.5, 200.0, 1.9, 2.0)
 T_CYC, T_GATH, T_SCAT, T_FIX, T_PE, T_HOP, T_DMA, T_KB, T_REMOTE, T_FIRST = TIMES
+T_GAP = 0.005
 HALVES = 32
-FCALLS = [(32, 32, 32, 16), (32, 32, 32, 16), (32, 32, 32, 16), (32, 32, 32, 16)]
-MCALLS = (16, 16, 16, 16, 16, 16, 16, 16, 32)
-ON = dict(LW=0, SG=0, PC1=0, PC2=1, XOLD=1, CLIP=(1, 1, 1, 1), LOG=(1, 1, 1, 1), OG=(1, 1, 1, 1), PG=(1, 0, 1, 0, 1), BG=(0, 1, 1, 1, 1))
-MA = 80
+FUSE1 = [(1, 1, 1), (1, 1, 1), (1, 1, 1, 1), (1, 1, 1)]
+FUSE2 = (0, 0, 1)
+TURN1 = [(0, 1, 0), (1, 0, 0), (0, 0, 0, 0), (0, 1, 0)]
+TURN2 = (1, 0, 0)
+VC = (0, 0, 1, 2)
+ROWS = [("aa", "va"), ("aa", "va"), ("aa", "va"), ("vv", "aa")]
+JOINT = (0, 0, 0, 1)
+XA = (32, 64, 32, 32)
+DIFF = (1, 0, 0)
+FIRST = (112, 64, 64, 32)
+SPLIT = 1
+BATCH = 8
+LEVELS = (14, 28, 36, 36)
+ON = dict(LW=1, SG=1, PC1=1, PC2=1, XOLD=1, OG=(1, 1, 1, 1), PG=(1, 1, 1, 1, 1), BG=(1, 1, 1, 1, 1))
 PLAN = {}
 TURNS = 3
-ROUNDS = 10
-STEPS = 500
+ROUNDS = 30
+STEPS = 600
 STRETCH = 100
 PATIENCE = 500
 TABU = 14
 JITTER = 0.1
 SEED = 1
-WORTH = ((0.92, 0.2), (1.3, 0.2))
+WORTH = ((0.92, 0.25), (1.3, 0.3))
 
 
 def spans(sizes):
     return [(sum(sizes[:i]), n) for i, n in enumerate(sizes)]
 
 
-CALLS = [(a, a + n) for a, n in spans(MCALLS)]
-SCALED = dict(I50=50.0, N50=-50.0, IXN=float(XN), I864=864.0, NBG=-BIG, I288=288.0, I23=23.0 * 8192, N19=-524288.0,
-              ISW=float(SW), I16=16.0, NI=-1.0, N18=-262144.0, I32=32.0)
+SCALED = dict(I50=50.0, N50=-50.0, NBG=-BIG, I23=23.0 * 8192, N19=-524288.0, I31=31.0, I1K=1024.0, N62=-62.0, N20K=-20480.0,
+              I16=16.0, NI=-1.0, N18=-262144.0, I32=32.0, I116=1.0 / 16, IW=41.0 / 1024, NW=-41.0 / 1024)
+MIXED = ("IB", "NB", "RIB", "R50", "RN50", "PXN", "PBG", "PBO")
 SB = {
-    "WA": (MW + 864, F32), "WB": (MW + 864, BF), "ONA": (16 * max(max(f) for f in FCALLS), F32), "ONM": (512, F32), "ONB": (512, BF),
+    "ONB": (64, BF), "OA": (48 * 128, BF), "OB": (36 * K2, F16), "OM": (34 * K2, BF), "DF": (72, F32),
+    "OF": (25 * 128, F16),
+    "TG": (2 * K1, F16), "HG": (K1, BF), "HT": (128, BF), "ZT": (6 * K2, F16), "MT": (K2, BF), "JT": (2 * K2, BF),
+    "SM": (272, F32), "SJ": (132, I32), "KJ": (640, I32), "PCT": (256, BF), "REP": (1024, BF), "ST": (432, BF), "LVL": (64, BF), "MK": (16, F32), "PN": (K1, BF), "P0X": (128, BF),
     "O": (4608, BF), "LOG": (400 + RO * 1792, BF), "OG": (1792, BF), "PG": (2560, BF), "FS": (640, BF), "FN": (64, BF),
-    "M32": (864, F32), "M16": (864, BF), "MC": (864, BF), "Z32": (864, F32), "Z16": (864, BF),
+    "MC": (576, BF), "Z16": (288, BF),
     "CTL": (432, F32), "CTO": (432, F32), "OO": (432, F32), "PTR": (432, BF), "PTD": (448, BF),
     "TC": (800, F32), "LO": (800, BF), "LW": (1280, F32), "TID": (640, F32), "DI": (160, F32), "X": (1200, BF),
-    "SEL": (2048, BF), "CP": (1024, BF), "D": (1792, BF), "BG": (2560, BF), "S": (7 * SW, BF), "SS": (7 * SW, BF), "KP": (640, BF), "DG": (160, BF),
+    "JW": (128, BF), "SH": (140, BF), "IX": (128 * len(MIXED), BF),
+    "SEL": (1024, BF), "CP": (512, BF), "D": (1792, BF), "BG": (2560, BF), "S": (7 * SW, BF), "SS": (7 * SW, BF), "KP": (160, BF),
     "ID": (128, BF), "BO": (128, BF), "II": (128 * len(SCALED), BF),
-    "PM": (384, BF), "TRI": (512, BF), "ZE": (288, BF), "RQ": (128, F32), "RG": (128, F32),
+    "PM": (384, BF), "TRI": (512, BF), "ZE": (864, BF), "RQ": (128, F32), "RG": (128, F32),
     "SI": (16, I32), "SF": (32, F32), "D16": (16, F32), "CI": (640, I32),
     "SNX": (384, BF), "SNB": (384, BF), "SG": (384, BF),
-    "DU1": (112, F32), "DU2": (160, F32), "KIU": (160, F32), "OFF": (32, F32), "DM": (16, F32),
+    "KIU": (160, F32), "OFF": (32, F32), "DM": (16, F32),
     "TH5": (16, F32), "PB": (16, F32), "FL": (288, BF), "QC": (304, BF), "NP": (288, BF), "CAP": (288, BF),
-    "JK": (288, BF), "FG": (288, BF), "ACC": (8, F32), "W1": (16, F32), "W2": (16, F32), "W3": (16, F32),
-    "WL": (8, U16), "XO": (112, U16), "OU": (112, U16), "FU": (112, U16), "XF": (112, F32), "FO": (112, F32),
-    "UH": (160, BF), "LV": (112, BF), "FIT": (112, BF), "NONE": (112, BF),
-    "DIE": (112, F32), "KI": (16, I32), "KB": (16, BF), "PU": (16, U16), "PC": (160, BF),
+    "JK": (7 * 288, BF), "LH": (160, F16), "ACC": (8, F32), "W1": (16, F32), "W2": (16, F32), "W3": (16, F32),
+    "WL": (8, U16), "XO": (112, U16), "OU": (112, U16), "XF": (112, F32),
+    "UH": (160, BF), "LV": (112, BF), "FIT": (112, BF), "NONE": (224, BF),
+    "DIE": (112, F32), "KI": (16, I32), "KB": (40, BF), "PU": (16, U16), "PC": (160, BF),
     "DEAD": (32, BF), "GU": (32, U16),
     "FB": (40, BF), "FA": (40, BF), "PP": (40, BF), "NG": (40, BF), "B1": (40, F32), "B2": (40, BF), "BU": (40, U16),
-    "L1": (160, F32), "L2": (160, F32), "TL": (16, U16), "CF": (160, F32), "CU": (160, U16),
-    "IU": (160, U16), "MO": (160, BF), "PEN": (160, BF), "IF": (128, F32), "NH": (160, BF), "XOLD": (160, BF), "NE": (160, BF),
-    "SN": (160, BF), "P0": (160, F32), "P1": (160, F32), "MU": (160, U16), "YT": (40, F32),
+    "TL": (16, U16), "CF": (160, F32), "CU": (160, U16),
+    "IU": (160, U16), "MO": (160, BF), "IF": (128, F32), "NH": (160, BF), "XOLD": (160, BF), "NE": (160, BF),
+    "P0": (160, F32), "YT": (40, F32),
 }
 SCRATCH = {k: ("sbuf", [128, v[0]], v[1]) for k, v in SB.items()}
 for _b in range(8):
     SCRATCH["PS%d" % _b] = ("psum", [128, 512], F32)
-NDMA = 40
+NDMA = 16
 SEMAPHORES = ["cv", "ca", "ct", "cg", "loc0", "loc1"] + ["arr%d" % i for i in range(8)] + ["dm%d" % i for i in range(NDMA)]
 
 
@@ -134,7 +151,7 @@ def waits(kind, q, qd):
     return kind == READS or kind == FOLLOWS and not q == qd == "t" or kind == SHARES and q != qd
 
 
-def plan(nodes, users):
+def plan(nodes, users, init=None):
     n = len(nodes)
     queue, busy, lat = [x[0] for x in nodes], [x[1] for x in nodes], [x[2] for x in nodes]
     comp = [x[5] for x in nodes]
@@ -354,6 +371,12 @@ def plan(nodes, users):
     for i in range(n - 1, -1, -1):
         level[i] = max([lat[i]] + [level[e[0]] + busy[i] + e[1] for e in post[i]])
     start = settle(place(sorted(range(n), key=lambda k: -level[k]), pre, False), pre, post, TURNS)[1]
+    if init:
+        for i in either:
+            if queue[i] != init[1][i]:
+                swap(i)
+        pre, post = links({})
+        start = init[0]
     best = None
     for turn in range(ROUNDS):
         bank, extra = banks(backwards(start, post), links({})[1])
@@ -400,13 +423,13 @@ def record(g, core, T, topo, rank):
         rd, wr = rd.split(), wr.split()
         for k in wr:
             for e in ([writer[k]] if k in writer else []) + readers.get(k, []):
-                deps[e] = max(deps.get(e, AFTER), AFTER if k == "order" else FOLLOWS)
+                deps[e] = max(deps.get(e, AFTER), AFTER if k.startswith("order") else FOLLOWS)
         for k in rd:
             if k.startswith("PS"):
                 deps.update((e, max(deps.get(e, AFTER), SHARES)) for e in readers.get(k, []))
             if k in writer:
                 deps[writer[k]] = READS
-        nodes.append((q, busy, lat, deps, issue, comp, other))
+        nodes.append((q, busy, lat, deps, issue, comp, other, wr[0] if wr else ""))
         for k in rd + wr:
             if k.startswith("PS"):
                 users.setdefault(k, []).append(len(nodes) - 1)
@@ -477,8 +500,21 @@ def record(g, core, T, topo, rank):
         if isinstance(ins[0], tuple):
             return T_FIX + ins[0][1] * T_GATH * T_CYC
         if plain is None:
-            plain = 0.5 if all(SCRATCH[a.name][2] in (BF, U16) for a in [out] + ins) else 1.0
-        return max(64.0, size(out) * plain) * T_CYC
+            plain = 0.5 if all(SCRATCH[a.name][2] in (BF, F16, U16) for a in [out] + ins) else 1.0
+        return max(64.0, size(out) * plain) * T_CYC + T_GAP
+
+    def batch(rd, wr, calls, q="v"):
+        names, step = [], BATCH if q == "v" else BATCH // 2
+        for i in range(0, len(calls), step):
+            def issue(some=calls[i:i + step]):
+                for c in some:
+                    (v.tensor_scalar if q == "v" else s.activation)(*c).then_inc(T.sem[own[q]], 1)
+                total[own[q]] = total.get(own[q], 0) + len(some)
+                return own[q], total[own[q]]
+            dur = sum(cost(c[0], [c[1]], None) if q == "v" else cost(c[0], [c[1]], 1.0) + 0.015 for c in calls[i:i + step])
+            names.append((wr % (i // step)).split()[0])
+            node(q, rd, wr % (i // step), dur, dur, issue, True)
+        return " ".join(names)
 
     def ap(x):
         return x[0] if isinstance(x, tuple) else x
@@ -510,10 +546,10 @@ def record(g, core, T, topo, rank):
     def group(rd, wr, calls):
         def issue():
             for c in calls:
-                t.matmul(*c).then_inc(T.sem.ct, 1)
+                (t.matmul if len(c) == 5 else t.transpose)(*c).then_inc(T.sem.ct, 1)
             total["ct"] = total.get("ct", 0) + len(calls)
             return "ct", total["ct"]
-        dur = sum(max(64, size(c[2])) * T_PE * (4 if SCRATCH[c[2].name][2] == F32 else 1) for c in calls)
+        dur = sum(max(min(64, size(c[1])), size(c[2])) * T_PE * (4 if SCRATCH[c[2].name][2] == F32 else 1) for c in calls)
         node("t", rd, wr, dur, dur, issue, True)
 
     def mm(rd, wr, out, lhsT, rhs, st=True, sp=True):
@@ -526,8 +562,11 @@ def record(g, core, T, topo, rank):
             op("g", "", wr, 0.13 + 2 * size(out) * T_CYC, lambda: g.iota(out, pat, base, ch, allow_small_or_imprecise_dtypes=True))
 
     def either(on_scalar, rd, wr, out, in_, on_a, on_v):
-        q = PLAN["queue"][len(nodes)] if PLAN else "va"[on_scalar]
+        q = PLAN["queue"][len(nodes)] if PLAN else "vaa"[on_scalar]
         da, dv = cost(out, [in_], 1.0) + 0.015, cost(out, [in_], None)
+        if on_scalar == 2:
+            op(q, rd, wr, da, on_a)
+            return 1
         op(q, rd, wr, da if q == "a" else dv, on_a if q == "a" else on_v, ("v", dv) if q == "a" else ("a", da))
         return int(q == "a")
 
@@ -558,23 +597,26 @@ def record(g, core, T, topo, rank):
     PS = []
 
     def small():
-        PS.append(T["PS%d" % (PLAN["bank"]["PS%d" % len(PS)] if PLAN else 0)])
+        PS.append(T["PS%d" % (PLAN["bank"].get("PS%d" % len(PS), 0) if PLAN else 0)])
         return len(PS) - 1
     nextbank = small
 
-    def mat(name):
+    def mat(name, first=0, step=1):
         if name in SCALED:
             i = list(SCALED).index(name)
-            return T.II[:, 128 * i:128 * i + 128]
-        return T[name][:, :]
+            return T.II[:, 128 * i + first:128 * i + 128:step]
+        if name in MIXED:
+            i = MIXED.index(name)
+            return T.IX[:, 128 * i:128 * i + 128]
+        return T[name][:, first:128:step]
 
     def mms(b, n, terms, st=True, sp=True, c0=0):
         for i, (m, rd, x) in enumerate(terms):
             mm(rd + " " + m, "PS%d" % b, PS[b][:, c0:c0 + n], mat(m), x, st and i == 0, sp and i == len(terms) - 1)
 
-    def opening(b, n, terms, lack, m):
-        calls = [(PS[b][:, 0:n], mat(x[0]), x[2], i == 0, False) for i, x in enumerate(terms)]
-        calls += [(PS[b][:, a:e], mat(m), T.ONB[:, a:e], False, False) for a, e in lack]
+    def opening(b, n, terms, lack, m, c0=0):
+        calls = [(PS[b][:, c0:c0 + n], mat(x[0]), x[2], i == 0, False) for i, x in enumerate(terms)]
+        calls += [(PS[b][:, c0 + a:c0 + e], mat(m), T.ONB[:, a:e], False, False) for a, e in lack]
         group(" ".join(x[0] + " " + x[1] for x in terms) + " ONB " + m, "PS%d" % b, calls)
 
     def seg(name, k0, k1, c0=0):
@@ -589,9 +631,9 @@ def record(g, core, T, topo, rank):
     def E(j, z=0):
         return T.ZE[:, z + 15 - j:z + 143 - j]
 
-    def fold(b, name, k0, k1, rd=None, st=True, sp=True, z=0):
-        group((rd or keys(name, k0, k1)) + " ZE ZS", "PS%d" % b,
-              [(PS[b][:, 0:k1 - k0], E(j, z), col(name, j, k0, k1), st and j == 0, sp and j == 15) for j in range(16)])
+    def fold(b, name, k0, k1, rd=None, st=True, sp=True, z=0, c0=0):
+        group((rd or keys(name, k0, k1)) + " ZE ZS ZP ZE2 ZS2", "PS%d" % b,
+              [(PS[b][:, c0:c0 + k1 - k0], E(j, z), col(name, j, k0, k1), st and j == 0, sp and j == 15) for j in range(16)])
 
     def exchange(n, srckey, src, after=""):
         snd, key, loc = (T.SNX, "SNX", "loc0") if n % 2 == 0 else (T.SNB, "SNB", "loc1")
@@ -633,29 +675,29 @@ def record(g, core, T, topo, rank):
     iota("RQ", T.RQ[:, :], [[1, 128]], 0)
     iota("OO", T.OO[:, :], [[16, 432]], 0)
     iota("RG", T.RG[:, :], [[16, 8], [0, 16]], 0)
-    ms("Z32", T.Z32[:, :], 0.0)
-    dma("s", "Z32", "WA0", T.WA[0:128:16, 0:10240], T.Z32[:, 0:640], 320)
+    for c0 in (0, 1024, 4096, 5120):
+        ms("OAz%d" % c0, T.OA[:, c0:c0 + 1024], 0.0)
     for i, m in enumerate((16, 32, 48, 15, 112)):
         ts("SI", "SI%d" % i, T.SI[:, 8 + i:9 + i], T.SI[:, 0:1], m, A.bitwise_and)
-    cp("SI SI0 SI1 SI2 SI3 SI4", "SF", T.SF[:, 0:13], T.SI[:, 0:13])
+    ts("SI", "SI5", T.SI[:, 13:14], T.SI[:, 0:1], 7, A.bitwise_and)
+    ts("SI", "SI6", T.SI[:, 14:15], T.SI[:, 0:1], 3, A.arith_shift_right)
+    ts("SI", "SI7", T.SI[:, 15:16], T.SI[:, 0:1], 31, A.bitwise_and)
+    cp("SI SI0 SI1 SI2 SI3 SI4 SI5 SI6 SI7", "SF", T.SF[:, 0:16], T.SI[:, 0:16])
     PF, P16, GC = T.SF[:, 0:1], T.SF[:, 11:12], T.SF[:, 12:13]
     ts("SF", "SFb", T.SF[:, 16:19], T.SF[:, 8:11], -2.0, A.mult, PF, A.add)
     for d in (1, 2, 3):
         ts("RQ SF SFb", "PM%d" % d, T.PM[:, 128 * (d - 1):128 * d], T.RQ[:, :], -16.0 * d, A.add, T.SF[:, 15 + d:16 + d], A.is_equal)
     exchange(0, "Xb", T.X)
-    ms("ONA", T.ONA[:, :], ONE)
     ts("OO SF", "OO", T.OO[:, :], T.OO[:, :], P16, A.add, 4607.0, A.min)
-    ts("CI", "CTO", T.CTO[:, 0:288], T.CI[:, 0:288], 10240.0, A.is_ge, 20000.0, A.mult)
-    ts("OO", "DU1", T.DU1[:, :], T.OO[:, 0:112], 10240.0, A.add)
-    tt("CTO CI", "CTO", T.CTO[:, 0:288], T.CTO[:, 0:288], T.CI[:, 0:288], A.add)
     ts("CI", "CIb", T.CI[:, 288:576], T.CI[:, 0:288], 4, A.arith_shift_right)
-    ms("CTOx", T.CTO[:, 288:432], 30000.0)
-    ts("CIb", "CTL", T.CTL[:, 0:288], T.CI[:, 288:576], 640.0, A.is_ge, 160.0, A.mult)
+    cp("CIb", "CTO", T.CTO[:, 0:288], T.CI[:, 288:576])
+    ms("CTOx", T.CTO[:, 288:432], 1023.0)
+    ts("CI", "CTL CTLs", T.CTL[:, 0:288], T.CI[:, 0:288], 10240.0, A.is_ge, 160.0, A.mult)
     ms("CTLx", T.CTL[:, 288:432], float(XN))
-    tt("CTL CIb CTLx", "CTL", T.CTL[:, 0:288], T.CTL[:, 0:288], T.CI[:, 288:576], A.add)
+    tt("CTL CIb CTLx", "CTL CTLs", T.CTL[:, 0:288], T.CTL[:, 0:288], T.CI[:, 288:576], A.add)
     ms("Xd", T.X[:, 640:800], 512.0)
     ms("Xn", T.X[:, XN:1200], 512.0)
-    iota("CP", T.CP[:, :], [[0, 64], [1, 16]], 0)
+    iota("CP", T.CP[:, :], [[0, 32], [2048, 16]], 1024 - 15 * 2048)
     dma("s", "", "CI CIb", T.CI[:, :], T.tv[:, :], 320)
     dma("s", "CI", "O1", T.O[:, 1792:4608], T.obs[:, 1792:4608], 704)
 
@@ -666,7 +708,7 @@ def record(g, core, T, topo, rank):
         return " ".join("%s%d_%d" % (sb, k, i) for i in range(a // 8, (e + 7) // 8))
 
     def fill(wr, out, val):
-        either(0, "O0", wr, out, out, lambda: s.activation(out, T.O[:, 0:size(out)], F.Identity, scale=0.0, bias=val), lambda: v.memset(out, val))
+        either(1, "OAz0", wr, out, out, lambda: s.activation(out, T.OA[:, 0:size(out)], F.Identity, bias=val), lambda: v.memset(out, val))
 
     def constants():
         ts("RQ SF", "ID", T.ID[:, :], T.RQ[:, :], PF, A.is_equal)
@@ -674,18 +716,50 @@ def record(g, core, T, topo, rank):
         ms("ZE", T.ZE[:, 0:144], 0.0)
         cp("BO ZE", "ZE", T.ZE[:, 15:143:16], T.BO[:, 0:128:16])
         act("ZE", "ZS", T.ZE[:, 144:288], T.ZE[:, 0:144], F.Copy, scale=-BIG)
+        act("ZE", "ZS2", T.ZE[:, ZS2:ZS2 + 144], T.ZE[:, 0:144], F.Copy, scale=-2 * BIG)
+        act("ZE", "ZE2", T.ZE[:, ZE2:ZE2 + 144], T.ZE[:, 0:144], F.Copy, scale=2.0)
+        ms("DF", T.DF[:, 0:36], 0.0)
+        for x0, n in PIECES:
+            ts("RQ SF", "DF", T.DF[:, x0:x0 + n - 1], T.RQ[:, x0 + 1:x0 + n], PF, A.is_equal, 0.5, A.mult)
+        ts("RQ SF", "DFi", T.DF[:, 36:72], T.RQ[:, 0:36], PF, A.is_equal, 0.5, A.mult)
+        tt("DF DFi", "DF", T.DF[:, 0:36], T.DF[:, 36:72], T.DF[:, 0:36], A.subtract)
+        act("DF", "DF DFi", T.DF[:, 36:72], T.DF[:, 0:36], F.Copy, scale=-1.0)
+        iota("REP", T.REP[:, 512:1024], [[1, 32], [0, 16]], 0)
+        ts("REP SF", "REPa", T.REP[:, 0:512], T.REP[:, 512:1024], T.SF[:, 15:16], A.is_equal)
+        ts("REP REPa SF", "REP", T.REP[:, 512:1024], T.REP[:, 512:1024], T.SF[:, 15:16], A.is_equal, SCALED["IW"], A.mult)
+        ts("SF", "SFp", T.SF[:, 24:25], T.SF[:, 13:14], 16.0, A.mult, T.SF[:, 14:15], A.add)
+        ts("SF", "SFq", T.SF[:, 25:26], T.SF[:, 13:14], 16.0, A.mult)
+        ts("RQ SFp", "PXN", mat("PXN"), T.RQ[:, :], T.SF[:, 24:25], A.is_equal, float(XN), A.mult)
+        act("PXN", "PBG", mat("PBG"), mat("PXN"), F.Copy, scale=-16.0)
+        ts("RG SFq", "PBO", mat("PBO"), T.RG[:, :], T.SF[:, 25:26], A.is_equal)
         for name, x in SCALED.items():
             act("ID", name, mat(name), T.ID[:, :], F.Copy, scale=x)
         act("ID", "IF", T.IF[:, :], T.ID[:, :], F.Copy)
         ts("RQ SF", "D16", T.D16[:, :], T.RQ[:, 0:16], P16, A.is_equal, 512.0, A.mult)
         iota("PTD", T.PTD[:, :], [[1, 448]], 25 - 256)
-        fill("PTR", T.PTR[:, :], 24.0 - 256)
-        iota("PTR", T.PTR[:, 288:312], [[1, 24]], -256)
+        iota("LVL", T.LVL[:, :], [[1, 64]], 0)
+        ts("SF", "MK0", T.MK[:, 0:1], P16, 13.5, A.is_lt)
+        ts("SF", "MK1", T.MK[:, 1:2], P16, 13.5, A.is_lt, 24.0 - 256, A.mult)
+        ts("SF", "MK2", T.MK[:, 2:3], P16, 0.0, A.is_equal, 16.0, A.mult)
+        ts("SF", "MK3", T.MK[:, 3:4], P16, 14.0, A.is_equal)
+        ts("SF", "MK4", T.MK[:, 4:5], P16, 15.0, A.is_equal)
+        ts("MK3 MK4", "MK5", T.MK[:, 5:6], T.MK[:, 3:4], 256.0, A.mult, T.MK[:, 4:5], A.add)
+        ms("MK8", T.MK[:, 8:16], 2.0)
+        ms("Z16", T.Z16[:, :], 0.0)
+        scan("MK8 MK4 Z16", "MK8", T.W3[:, 8:16], T.MK[:, 8:16], T.Z16[:, 0:8], T.MK[:, 4:5], A.mult, A.add)
+        ts("MK8", "MK8", T.MK[:, 8:16], T.W3[:, 8:16], 0.5, A.mult)
+        st = batch("LVL MK3 MK8", "ST%d", [(T.ST[:, r:432:8], T.LVL[:, 0:54], T.MK[:, 3:4], T.MK[:, 8 + r:9 + r], A.mult, A.add) for r in range(8)])
+        ts(st + " MK1", "PTR ST", T.PTR[:, :], T.ST[:, :], T.MK[:, 1:2], A.add)
+        ts("LVL MK0", "LVL", T.LVL[:, 0:24], T.LVL[:, 0:24], -256.0, A.add, T.MK[:, 0:1], A.mult)
+        tt("LVL ST", "PTR", T.PTR[:, 288:312], T.LVL[:, 0:24], T.ST[:, 288:312], A.add)
+        ts("PTD MK0", "PTD", T.PTD[:, :], T.PTD[:, :], T.MK[:, 0:1], A.mult)
+        act("ZE MK2", "ZP", T.ZE[:, ZP:ZP + 144], T.ZE[:, 0:144], F.Copy, scale=T.MK[:, 2:3])
+        act("ZE MK5", "ZZ", T.ZE[:, ZZ:ZZ + 144], T.ZE[:, 0:144], F.Copy, scale=T.MK[:, 5:6])
+        act("BO MK2", "P0X", T.P0X[:, :], T.BO[:, :], F.Copy, scale=T.MK[:, 2:3])
         iota("KI", T.KI[:, 0:4], [[-3, 4]], 48, 1, True)
-        iota("KP", T.KP[:, :], [[0, 40], [1, 16]], 0)
+        iota("KP", T.KP[:, :], [[0, 10], [1, 16]], 0)
         iota("TID", T.TID[:, :], [[1, 40], [40, 16]], 64)
         iota("DI", T.DI[:, :], [[1, 160]], 704)
-        ts("CP", "CP", T.CP[:, :], T.CP[:, :], -14.5, A.add, 2048.0, A.mult)
         for ch in range(2):
             sb, gap = sbuf(ch), SW - 16 - 16 * CH1[0][ch]
             for k in range(7):
@@ -698,7 +772,19 @@ def record(g, core, T, topo, rank):
                     c0 = 10 * fn_of(i) + k0 // 16
                     act("OO", keys("FN", 16 * c0, 16 * c0 + nk), T.FN[:, c0:c0 + nk // 16], T.OO[:, 0:nk // 16], F.Copy)
         ts("SF", "SFd", T.SF[:, 21:22], P16, 4096.0 - 384, A.add)
-        for j in range(16):
+        fill("JW", T.JW[:, :], 0.0)
+        fill("SHz", T.SH[:, 0:12], 0.0)
+        ts("SF", "MK6", T.MK[:, 6:7], P16, 3.5, A.is_lt, float(SW), A.mult)
+        act("ID MK6", "SH", T.SH[:, 12:140], T.ID[:, :], F.Copy, scale=T.MK[:, 6:7])
+        ts("SF", "MK7", T.MK[:, 7:8], P16, 7.5, A.is_lt, 16.0, A.mult)
+        ts("SF MK7", "MK7", T.MK[:, 7:8], T.MK[:, 7:8], -8.0, A.add, PF, A.add)
+        ts("RQ MK7", "R50", mat("R50"), T.RQ[:, :], T.MK[:, 7:8], A.is_equal, 50.0, A.mult)
+        act("R50", "RN50", mat("RN50"), mat("R50"), F.Copy, scale=-1.0)
+        for name, m in (("IB", "I50"), ("NB", "N50"), ("RIB", "R50")):
+            b = small()
+            mms(b, 128, [("ID", "BO", T.BO[:, :]), ("ID", m, mat(m))])
+            move(1, "PS%d" % b, name, mat(name), PS[b][:, 0:128])
+        for j in range(8):
             act("BO D16", "SEL%d" % j, T.SEL[:, 128 * j:128 * j + 128], T.BO[:, :], F.Copy, scale=T.D16[:, j:j + 1])
 
     def fn_of(i):
@@ -707,34 +793,23 @@ def record(g, core, T, topo, rank):
         return i
 
     def constants2():
-        ms("Z16", T.Z16[:, :], 0.0)
-        dma("s", "Z16 TC", "WB", T.WB[0:128:16, 864:864 + MW], T.Z16[:, :], 216)
-        ts("KP SF", "DG", T.DG[:, :], T.KP[:, 0:160], P16, A.is_equal)
-        ts("CI", "LWi", T.LW[:, 0:640], T.CI[:, :], 0.0, A.add)
+        ts("CI", "KJ0_0 KJ1_0", T.KJ[:, :], T.CI[:, :], 15, A.bitwise_and)
         ts("CI", "CI", T.CI[:, :], T.CI[:, :], 4, A.arith_shift_right)
-        cp("CI", "TC", T.TC[:, 0:640], T.CI[:, :])
+        move(1, "CI", "TC", T.TC[:, 0:640], T.CI[:, :])
+        move(1, "KJ0_0 KJ1_0", "LO", T.LO[:, 0:640], T.KJ[:, :])
         fill("TCx", T.TC[:, 640:800], float(EC))
         fill("LOx", T.LO[:, 640:800], 0.0)
-        act("TC", "LWj", T.LW[:, 640:1280], T.TC[:, 0:640], F.Copy, scale=-16.0)
-        for c0 in (0, 320):
-            b = small()
-            mms(b, 320, [("IF", "LWi LW", T.LW[:, c0:c0 + 320]), ("IF", "LWj LW", T.LW[:, 640 + c0:960 + c0])])
-            move(1, "PS%d" % b, "LO%d" % c0, T.LO[:, c0:c0 + 320], PS[b][:, 0:320])
         ts("KI", "KI", T.KI[:, 0:4], T.KI[:, 0:4], 15, A.bitwise_and)
         cp("KI", "PB", T.PB[:, 0:4], T.KI[:, 0:4])
         ts("PB", "PBb", T.PB[:, 4:8], T.PB[:, 0:4], -40.0, A.mult, 1280.0, A.add)
         for u in range(RO):
             act("RQ PBb", "KIU%d" % u, T.KIU[:, 40 * u:40 * u + 40], T.RQ[:, 0:40], F.Identity, scale=-1.0, bias=T.PB[:, 4 + u:5 + u])
-        ts("SF", "SFe", T.SF[:, 22:23], P16, 0.0, A.not_equal, ONE, A.mult)
         fill("FA", T.FA[:, :], 1.0)
         fill("NG", T.NG[:, :], -1.0)
         for u in range(RO):
             ts("KP PB", "TRI%d" % u, T.TRI[:, 128 * u:128 * u + 128], T.KP[:, 16 - 3 * u:144 - 3 * u], T.PB[:, u:u + 1], A.is_gt)
-        ts("KP", "KP", T.KP[:, :], T.KP[:, :], 0.0, A.not_equal)
         for u in range(RO):
             tt("TRI%d BO" % u, "TRI%d" % u, T.TRI[:, 128 * u:128 * u + 128], T.TRI[:, 128 * u:128 * u + 128], T.BO[:, :], A.mult)
-
-    VC = 2
 
     def listed(u):
         s0, ns = SURE[u]
@@ -742,9 +817,6 @@ def record(g, core, T, topo, rank):
         return (0, C, True) if wrap else (SC * u, s0 + K1, False)
 
     def constants3():
-        iota("DU2", T.DU2[:, :], [[0, 5], [16, 32]], 0)
-        act("DU2 SF", "DU2", T.DU2[:, :], T.DU2[:, :], F.Identity, bias=P16)
-        act("Z16 SFe", "ONM", T.ONM[:, :], T.Z16[:, 0:512], F.Identity, bias=T.SF[:, 22:23])
         fill("ONB", T.ONB[:, :], 1.0)
         fill("FL", T.FL[:, :], 1.0)
         fill("CAP", T.CAP[:, :], float(K1))
@@ -754,35 +826,122 @@ def record(g, core, T, topo, rank):
         for u in range(1, RO):
             lo, hi, wrap = listed(u)
             n = hi - lo - SURE[u][1]
-            act("RQ", "OFFa%d" % u, T.OFF[:, 8 * u:8 * u + VC], T.RQ[:, 0:VC], F.Identity, scale=32.0, bias=2.0 * lo)
-            act("RQ", "OFFb%d" % u, T.OFF[:, 8 * u + VC:8 * u + 8], T.RQ[:, VC:8], F.Identity, scale=16.0, bias=2.0 * lo + n)
+            vc = VC[u]
+            if vc:
+                act("RQ", "OFFa%d" % u, T.OFF[:, 8 * u:8 * u + vc], T.RQ[:, 0:vc], F.Identity, scale=32.0, bias=2.0 * lo)
+            act("RQ", "OFFb%d" % u, T.OFF[:, 8 * u + vc:8 * u + 8], T.RQ[:, vc:8], F.Identity, scale=16.0, bias=2.0 * lo + n)
         ts("OO", "DM", T.DM[:, 0:7], T.OO[:, 0:7], 2.0, A.mult, 64.0, A.add)
 
     def camera_flags(u):
         st, b = (SC * u) % C, small()
-        src = [(T.FL, "FL", 0, "ID", SC), (T.QC, "QC", 16, "NI", SC), (T.QC, "QC QC0", 15, "ID", SC),
-               (T.MC, "MC", 0, "BO", st), (T.MC, "MC", 288, "BO", st), (T.M16, "M16", 0, "BO", st), (T.M16, "M16", 288, "BO", st)]
+        n = 8 * LEVELS[u - 1]
+        src = [(T.FL, "FL", 0, "ID", SC, C), (T.QC, "QC", 16, "NI", SC, C), (T.QC, "QC QC0", 15, "ID", SC, C), (T.MC, "MCb", C, "PBO", st, n)]
         mms(b, C, [("ID", "Z16", T.Z16[:, 0:C])], True, False)
-        for i, (buf, key, c0, m, sh) in enumerate(src):
+        for i, (buf, key, c0, m, sh, end) in enumerate(src):
             last = i == len(src) - 1
-            mms(b, C - sh, [(m, key, buf[:, c0 + sh:c0 + C])], False, last and sh == 0)
+            mms(b, end - sh, [(m, key, buf[:, c0 + sh:c0 + end])], False, last and sh == 0)
             if sh:
                 mms(b, sh, [(m, key, buf[:, c0:c0 + sh])], False, last, C - sh)
         either(0, "PS%d" % b, "FL", T.FL[:, :], PS[b][:, 0:C], lambda: s.activation(T.FL[:, :], PS[b][:, 0:C], F.Sign),
                lambda: v.tensor_scalar(T.FL[:, :], PS[b][:, 0:C], 0.5, None, A.is_gt))
 
     def killed(m, c0, n):
-        return [(m, key, buf[:, r + c0:r + c0 + n]) for buf, key, r in ((T.MC, "MC", 288), (T.MC, "MCb", 576), (T.M16, "M16", 288), (T.M16, "M16", 576))]
+        return [(m, "MC", T.MC[:, c0:c0 + n])]
 
     def kills(u):
-        s0, ns = SURE[u]
-        if ns:
-            b = small()
-            mms(b, ns, [("IF", "CTL", T.CTL[:, s0:s0 + ns])] + killed("IXN", s0, ns))
-            ts("PS%d" % b, keys("XO", 0, ns), T.XO[:, 0:ns], PS[b][:, 0:ns], float(XN), A.min)
-        b = small()
-        mms(b, C, [("IF", "CTL", T.CTL[:, 0:C])] + killed("IXN", 0, C))
-        move(1, "PS%d" % b, "CTL", T.CTL[:, 0:C], PS[b][:, 0:C])
+        b, n = small(), 8 * LEVELS[u - 1]
+        mms(b, n, [("IF", "CTL", T.CTL[:, 0:n])] + killed("PXN", 0, n))
+        move(1, "PS%d" % b, "CTL", T.CTL[:, 0:n], PS[b][:, 0:n])
+
+    OBK = " ".join("OB%d" % i for i in range(60))
+
+    def track_flags(u):
+        linear("TG0 TG1", "HG", T.HG[:, :], T.TG[:, 0:K1], 1.0 / 40, 129.0 - 19.5 / 40)
+        linear("TG0 TG1", "TH", T.TG[:, K1:2 * K1], T.TG[:, 0:K1], 0.5, 1023.75)
+        b, b2, b3 = small(), small(), small()
+        mm("HG ID", "PS%d" % b3, PS[b3][0:K1, 0:128], T.HG[:, :], T.ID[:, :])
+        terms = [("I31", T.TG[:, 0:K1]), ("I1K", T.TG[:, K1:2 * K1]), ("N62", T.TG[:, K1:2 * K1]), ("N20K", T.HG[:, :])]
+        group("TG0 TG1 TH HG I31 I1K N62 N20K", "PS%d" % b, [(PS[b][0:K1, 0:128], x, mat(m), m == "I31", m == "N20K") for m, x in terms])
+        move(1, "PS%d" % b3, "HT", T.HT[0:K1, :], PS[b3][0:K1, 0:128])
+        oa = batch("HT", "OA%d orderF", [(T.OA[0:K1, 128 * (16 + a):128 * (17 + a)], T.HT[0:K1, :], 129.0 + a, None, A.is_equal) for a in range(16)])
+        for i in range(5):
+            z = T.OF[0:K1, 128 * (20 + i):128 * (21 + i)]
+            linear("PS%d" % b, "ZF%d" % i, z, PS[b][0:K1, 0:128], 1.0, 1.0 - 962 * 1024 + 20480 * 129 - 4096 * i - 2048)
+            oa += " " + batch("ZF%d" % i, "OF%d_%%d orderF" % i, [(T.OF[0:K1, 128 * (4 * i + k):128 * (4 * i + k + 1)], z, 1024.0 * (k - 2), 1024.0 * (k - 1), A.max, A.min)
+                                                          for k in range(4)])
+        for q in range(4):
+            group(oa + " OAz0 OAz1024 OAz4096 OAz5120", "PS%d" % b2,
+                  [(PS[b2][32 * q:32 * q + 32, 0:20], T.OA[0:K1, 2048 * (1 - c // 16 % 2) + c:2048 * (3 - c // 16 % 2):128], T.OF[0:K1, c:2560:128],
+                    c % 32 == 0, c % 32 == 31) for c in range(32 * q, 32 * q + 32)])
+        linear("PS%d" % b2, "SJf", T.SJ[:, 72:92], PS[b2][:, 0:20], 1.0, 2.0 ** 23)
+        kf = batch("SJf", "KF%d", [(T.SJ[:, 92 + e:132:2], T.SJ[:, 72:92], 31 << 5 * e, None, A.bitwise_and) for e in range(2)])
+        tt(kf + " FA", "FB", T.FB[:, :], T.SJ[:, 92:132], T.FA[:, :], A.is_lt)
+
+    def turned(b, c0, k0, k1, terms, last=None, half=None):
+        calls = []
+        if half == 0 and k0 >= 128:
+            calls.append((PS[b][:, c0:c0 + 32], T.Z16[:, 0:128], T.Z16[:, 0:32], True, False))
+        for q in range(4 if k0 >= 128 else 1):
+            for i, (m, x, a, e) in enumerate(terms if half != 1 else ()):
+                stop = last is None and i == len(terms) - 1
+                if k0 < 128:
+                    calls.append((PS[b][a:e, c0:c0 + 128], x, mat(m), i == 0, stop))
+                else:
+                    calls.append((PS[b][32 * q:32 * q + 32, c0:c0 + 32], x, mat(m, q, 4), i == 0 and half is None, stop))
+            js = range(16) if k0 < 128 else range(q, 16, 4)
+            for j in js if last and half != 0 else ():
+                out = PS[b][k0:k1, c0 + j:c0 + 128:16] if k0 < 128 else PS[b][32 * q:32 * q + 32, c0 + j // 4:c0 + 32:4]
+                calls.append((out, col(last[0], j, k0, k1), T.ZE[:, last[1] + 15:last[1] + 143:16], not terms, j == js[-1] or not terms))
+        return calls
+
+    def camera_rows(u):
+        nb, b, b2 = LEVELS[u], small(), small()
+        for k0, nk in spans((128, 32)):
+            group(keys("PG", k0, k0 + nk) + " ZZ", "PS%d" % b, turned(b, k0 // 128 * 128, k0, k0 + nk, [], ("PG", ZZ)))
+        nv = PIECES[0][0]
+        if nv:
+            linear("PS%d" % b, "ZT0", T.ZT[:, 0:K2], PS[b][:, 0:K2], 1.0, -256.0 * 7)
+            batch("ZT0", "OB%d", [(T.OB[:, K2 * x:K2 * x + K2], T.ZT[:, 0:K2], 256.0 * (x - 7), 256.0 * (x - 6), A.max, A.min) for x in range(nv)])
+        for i, (x0, n) in enumerate(PIECES):
+            if x0 < nb:
+                z = T.ZT[:, K2 * i + K2:K2 * i + 2 * K2]
+                act("PS%d" % b, "ZT%d" % (i + 1), z, PS[b][:, 0:K2], F.Relu, scale=-1.0, bias=256.0 * (x0 + n))
+                batch("ZT%d" % (i + 1), "OB%d%%d" % (i + 1), [(T.OB[:, K2 * x:K2 * x + K2], z, F.Relu, 256.0 * (x0 + n - x), -1.0) for x in range(x0, x0 + n)], "a")
+        group("MO I116", "PS%d" % b2, turned(b2, 0, 0, 128, [("I116", T.MO[:, 0:128], 0, 128)]) + turned(b2, 128, 128, K2, [("I116", T.MO[:, 128:K2], 128, K2)]))
+        move(1, "PS%d" % b2, "MT", T.MT[:, :], PS[b2][:, 0:K2])
+
+    def port_rows(u, i, b, c0, n, bs):
+        nb, j0, key = LEVELS[u], K2 * i + c0, "%d_%d" % (i, c0)
+        tt("PS%d MT" % b, "JT" + key, T.JT[:, j0:j0 + n], PS[b][:, c0:c0 + n], T.MT[:, c0:c0 + n], A.min)
+        q, r0 = ROWS[u][i][c0 // 128], 17 * K2 * i
+        if u == 0 or q != ROWS[u - 1][i][c0 // 128]:
+            fill("OMz" + key, T.OM[:, r0 + 16 * K2 + c0:r0 + 16 * K2 + c0 + n], -1.0 * (q == "a"))
+        made[key] = " OMz%s " % key + batch("JT" + key, "OM" + key + "_%d", [
+            (T.OM[:, r0 + K2 * a + c0:r0 + K2 * a + c0 + n], T.JT[:, j0:j0 + n]) +
+            (((a + 0.5) / 16, 2.0, A.is_gt, A.mult) if q == "v" else (F.Sign, -(a + 0.5) / 16)) for a in range(16)], q)
+        if JOINT[u] and i:
+            return
+        rows, m = made[key] + made["1_%d" % c0] * JOINT[u], 17 + 17 * JOINT[u]
+        for a in range(c0, c0 + n, 32):
+            gs = [(c, c // 16 if c < 128 else (c - 128) // 4) for c in range(a, a + 32)]
+            group(OBK + " Z16" + rows, "PS%d" % bs, [(PS[bs][0:nb, 0:8 * m], T.Z16[:, 0:nb], T.Z16[:, 0:8 * m], True, False)] * (a == 0) +
+                  [(PS[bs][0:nb, x:8 * m:8], T.OB[:, c:K2 * nb:K2], T.OM[:, r0 + c:r0 + m * K2:K2], False, c == K2 - 1) for c, x in gs])
+
+    made = {}
+
+    def marks(u, i, b):
+        if JOINT[u] and i:
+            return
+        nb, b2, kinds = LEVELS[u], small(), (0, 1) if JOINT[u] else (i,)
+        s0, c0, n = 136 * i, C * i, len(kinds)
+        sj, sm, sk = T.SJ[:, 36 * i:36 * i + n * nb], " ".join("SM%d" % x for x in kinds), " ".join("SJ%d" % x for x in kinds)
+        move(1, "PS%d" % b, sm, T.SM[0:nb, s0:s0 + 136 * n], PS[b][0:nb, 0:136 * n])
+        group(sm + " DF", "PS%d" % b2, [(PS[b2][:, nb * k:nb * k + nb], T.SM[0:nb, s0 + 136 * k + 8 * x:s0 + 136 * k + 8 * x + 128], T.DF[0:nb, 36 * x:36 * x + nb], x == 0, x == 1)
+                                        for k in range(n) for x in (0, 1)])
+        linear("PS%d" % b2, sk, sj, PS[b2][:, 0:n * nb], 1.0, 2.0 ** 23)
+        kj = batch(sk, "KJ%d_%%d" % i + " KJ1_0" * JOINT[u], [(T.KJ[:, c0 + r:c0 + 8 * n * nb:8], sj, 1 << r, None, A.bitwise_and) for r in range(8)])
+        for x in kinds:
+            move(0, kj, ("MC", "MCb")[x], T.MC[:, C * x:C * x + 8 * nb], T.KJ[:, C * x:C * x + 8 * nb])
 
     def camera_list(u):
         st, (s0, ns), (lo, hi, wrap) = SC * u, SURE[u], listed(u)
@@ -799,9 +958,9 @@ def record(g, core, T, topo, rank):
         else:
             cp("QC", "NPb", T.NP[:, 0:a], T.QC[:, 16:16 + a])
             ts("QC", "NPc", T.NP[:, a:n], T.QC[:, 16 + a + ns:16 + n + ns], -float(ns), A.add)
-        for m in range(VC, w):
-            act("NP NPb NPc TH5", "ACC%d " % m + keys("PG", 32 * (m - VC), 32 * (m - VC + 1)), T.PG[:, 512 * (m - VC):512 * (m - VC) + n - 16 * m],
-                T.NP[:, 16 * m:n], F.Sign, bias=T.TH5[:, m:m + 1], scale=-1.0, accum_out=T.ACC[:, m:m + 1])
+        vc = VC[u]
+        for m in range(vc, w):
+            act("NP NPb NPc TH5", "ACC%d JK%d" % (m, m), T.JK[:, C * m:C * m + n - 16 * m], T.NP[:, 16 * m:n], F.Sign, bias=T.TH5[:, m:m + 1], scale=-1.0, accum_out=T.ACC[:, m:m + 1])
         off, offk = T.OFF[:, 8 * u:8 * u + w], "OFFa%d OFFb%d" % (u, u)
         if wrap:
             ts("QC OO", "W1", T.W1[:, 0:w], T.OO[:, 0:w], float(ns), A.add, qn, A.is_ge)
@@ -811,12 +970,11 @@ def record(g, core, T, topo, rank):
         if ns:
             ts("NPb OO", "W1b", T.W1[:, 8:8 + w], T.OO[:, 0:w], T.NP[:, a - 1:a], A.is_ge, 2.0 * ns, A.mult)
             tt("W1b " + offk, "W1", T.W1[:, 0:w], T.W1[:, 8:8 + w], off, A.add)
-        for m in range(VC):
-            jk = (T.JK, T.FG)[m % 2]
-            ts("NP NPb NPc TH5", "JK%d" % (m % 2), jk[:, 0:n], T.NP[:, 0:n], T.TH5[:, m:m + 1], A.is_le, 2.0, A.mult)
-            red("JK%d" % (m % 2), "ACC%d" % m, T.ACC[:, m:m + 1], jk[:, 16 * m:n])
+        for m in range(vc):
+            ts("NP NPb NPc TH5", "JK%d" % m, T.JK[:, C * m:C * m + n], T.NP[:, 0:n], T.TH5[:, m:m + 1], A.is_le, 2.0, A.mult)
+            red("JK%d" % m, "ACC%d" % m, T.ACC[:, m:m + 1], T.JK[:, C * m + 16 * m:C * m + n])
         tt("W1 " + " ".join("ACC%d" % m for m in range(w)), "W2", T.W2[:, 0:w], T.W1[:, 0:w], T.ACC[:, 0:w], A.add)
-        ts("W2", "WL", T.WL[:, 0:w], T.W2[:, 0:w], 0.5, A.mult)
+        linear("W2", "WL", T.WL[:, 0:w], T.W2[:, 0:w], 0.5, 0.0)
 
     def finals(ch, nk):
         sb = sbuf(ch)
@@ -839,29 +997,45 @@ def record(g, core, T, topo, rank):
         k0, k1 = chunks[0][0], chunks[-1][0] + chunks[-1][1]
         w0, w1 = k0 // 16, k1 // 16
         b, b2, w = small(), small(), w1 - w0
-        fold(b, "UH", w0, w1, keys("UH", k0, k1))
-        linear("PS%d" % b, "KB", T.KB[:, 0:w], PS[b][:, 0:w], 0.25, 128.25 + 4 * plus)
-        mms(b2, w, [("I16", keys("FN", 16 * (fn + w0), 16 * (fn + w1)), T.FN[:, fn + w0:fn + w1]), ("ISW", "KB", T.KB[:, 0:w])])
+        group(keys("UH", k0, k1) + " ZE", "PS%d" % b, [(PS[b][:, 0:4 * w], E(j), T.UH[:, k0 + j:k1:4], j == 0, j == 3) for j in range(4)])
+        linear("PS%d" % b, "KB", T.KB[:, 0:4 * w], PS[b][:, 0:4 * w], 0.25, 128.25 + 4 * plus)
+        mms(b2, w, [("I16", keys("FN", 16 * (fn + w0), 16 * (fn + w1)), T.FN[:, fn + w0:fn + w1])], True, False)
+        group("KB SH SHz", "PS%d" % b2, [(PS[b2][:, 0:w], T.SH[:, 12 - 4 * i:140 - 4 * i], T.KB[:, i:4 * w:4], False, i == 3) for i in range(4)])
         cuts = [w0] + [a // 16 for a, nk in chunks[1:] if a // 16 % 2] + [w1]
         for a, e in zip(cuts[:-1], cuts[1:]):
-            ts("PS%d" % b2, keys("PU", 16 * a, 16 * e), T.PU[:, pucol(16 * a):pucol(16 * a) + e - a], PS[b2][:, a - w0:e - w0],
-               31.0 - 130 * SW, A.add, 0.0, A.max)
+            relu("PS%d" % b2, keys("PU", 16 * a, 16 * e), T.PU[:, pucol(16 * a):pucol(16 * a) + e - a], PS[b2][:, a - w0:e - w0], 31.0 - 130 * SW)
 
     def median(ch, k0, nk):
         return finals(ch, nk)[0] + " " + keys("PU", k0, k0 + nk), ind(finals(ch, nk)[1], T.PU[:, pucol(k0):pucol(k0) + nk // 16])
 
-    def wide(ch, k0, nk, m, src):
+    def wide(ch, k0, nk, m, src, m2="ID"):
         for a in range(k0, k0 + nk, 32):
             e = min(k0 + nk, a + 32)
             b, n = nextbank(), 16 * (e - a)
             mms(b, n, [(m,) + src(a, e)], True, False)
-            group("PC%d ID" % ch, "PS%d" % b, [(PS[b][:, j:n:16], T.ID[:, :], T.PC[:, a:e], False, j == 15) for j in range(16)])
+            if turn[0]:
+                c0, r0 = 128 * (ch % 2), 512 * (m2 != "ID")
+                mm("PCT%d REP" % (ch % 2), "PS%d" % b, PS[b][:, 0:n], T.PCT[a - k0:e - k0, c0:c0 + 128], T.REP[a - k0:e - k0, r0:r0 + n], False, True)
+            else:
+                group("PC%d %s" % (ch, m2), "PS%d" % b, [(PS[b][:, j:n:16], mat(m2), T.PC[:, a:e], False, j == 15) for j in range(16)])
             yield a, e, b
 
-    def near(name, k0, nk):
+    turn = [0]
+
+    def turn_medians(ch, k0, nk, on):
+        turn[0] = on
+        if on:
+            b = small()
+            mm("PC%d ID" % ch, "PS%d" % b, PS[b][0:nk, 0:128], T.PC[:, k0:k0 + nk], T.ID[:, :])
+            move(1, "PS%d" % b, "PCT%d" % (ch % 2), T.PCT[0:nk, 128 * (ch % 2):128 * (ch % 2) + 128], PS[b][0:nk, 0:128])
+
+    def near(name, src, ch, k0, nk, fused):
         lack = []
-        for a in range(k0, k0 + nk, 32):
-            e = min(k0 + nk, a + 32)
+        for a, e, b in wide(ch, k0, nk, "NW" if fused else "NI", lambda a, e: (keys(src, a, e), seg(src, a, e)), "IW" if fused else "ID"):
+            if fused:
+                ts("PS%d" % b, keys(name, a, e), seg(name, a, e), PS[b][:, 0:16 * (e - a)], ROUND, A.add, ROUND, A.is_equal)
+                continue
+            act("PS%d" % b, keys(name, a, e), seg(name, a, e), PS[b][:, 0:16 * (e - a)], F.Abs)
             if under(keys(name, a, e), keys(name, a, e), seg(name, a, e), seg(name, a, e), 12.5):
                 lack.append((a - k0, e - k0))
         return lack
@@ -869,13 +1043,11 @@ def record(g, core, T, topo, rank):
     def port_places(c0, n, more):
         b = small()
         relu("CTL", "DEAD", T.DEAD[:, 0:n], T.CTL[:, c0:c0 + n], 1.0 - XN)
-        mms(b, n, [("NBG", "DEAD", T.DEAD[:, 0:n]), ("I16", "PTR", T.PTR[:, c0:c0 + n])] + more)
-        ts("PS%d SFd" % b, "GU", T.GU[:, 0:n], PS[b][:, 0:n], T.SF[:, 21:22], A.add, 0.0, A.max)
+        mms(b, n, [("NBG", "DEAD", T.DEAD[:, 0:n]), ("P0X", "PTR", T.PTR[:, c0:c0 + n])] + more)
+        relu("PS%d SFd" % b, "GU", T.GU[:, 0:n], PS[b][:, 0:n], T.SF[:, 21:22])
 
     def track_list(u):
         b = small()
-        scan("M32 KP", "FS", T.FS[:, :], T.KP[:, :], T.M32[:, 0:640], 0.0, A.mult, A.max)
-        tt("FS FA", "FB", T.FB[:, :], T.FA[:, :], T.FS[:, 15:640:16], A.is_gt)
         scan("FB NG", "PP", T.PP[:, :], T.FB[:, :], T.NG[:, :], 0.0, A.add, A.add)
         tt("FB KIU%d" % u, "B1", T.B1[:, :], T.FB[:, :], T.KIU[:, 40 * u:40 * u + 40], A.mult)
         mm("PP TRI%d" % u, "PS%d" % b, PS[b][:, 0:2], T.TRI[:, 128 * u:128 * u + 128], T.PP[:, 38:40])
@@ -884,10 +1056,11 @@ def record(g, core, T, topo, rank):
         ts("PP PS%d" % b, "B2", T.B2[:, :], T.PP[:, :], PS[b][:, 1:2], A.add, -K2 - 0.5, A.is_gt)
         tt("B2 FB", "FA", T.FA[:, :], T.B2[:, :], T.FB[:, :], A.max)
         move(ON["LW"], "BU TID", "LW", ind(T.LW[:, :], T.BU[:, :]), T.TID[:, :], F.Silu)
-        tt("LW DG", "L1", T.L1[:, :], T.LW[:, 0:K2], T.DG[:, :], A.mult)
-        scan("L1 KP", "L2", T.L2[:, :], T.KP[:, 0:K2], T.L1[:, :], 0.0, A.mult, A.add)
-        ts("L2", "TL", T.TL[:, 0:10], T.L2[:, 15:K2:16], -63.75, A.add)
-        cp("TL TC TCx", "CU", T.CU[:, :], ind(T.TC[:, :], T.TL[:, 0:10]))
+        move(1, "LW", "LH", T.LH[:, :], T.LW[:, 0:K2])
+        b = small()
+        fold(b, "LH", 0, 10, "LH", z=ZP)
+        linear("PS%d" % b, "TL", T.TL[:, 0:10], PS[b][:, 0:10], 1.0 / 16, -64.0)
+        move(1, "TL TC TCx", "CU", T.CU[:, :], ind(T.TC[:, :], T.TL[:, 0:10]))
 
     def groups(chunks, ends):
         return [chunks[a:e] for a, e in zip((0,) + tuple(ends[:-1]), ends)]
@@ -904,34 +1077,37 @@ def record(g, core, T, topo, rank):
         def obs(a, e):
             return ("O0 O1" if u else "O0", seg("O", a, e, s0)) if e <= ns else (keys("OG", a, e), seg("OG", a, e))
         if ns < K1:
-            cp("OO WL", "OU", T.OU[:, ns:K1], both[-1][2](T.OO))
+            move(1, "OO WL", "OU", T.OU[:, ns:K1], both[-1][2](T.OO))
             for a, e in parts:
                 if a >= ns:
                     move(ON["OG"][a // 32], "O0 O1 OU", keys("OG", a, e), seg("OG", a, e), ind(T.O[:, :], T.OU[:, a:e]))
         for a, e, tab, wl in both:
-            if wl or u == 0:
-                ts("CTL" + wl, keys("XO", a, e), T.XO[:, a:e], tab(T.CTL), float(XN), A.min)
-            tt("CTO CTOx DU1" + wl, keys("FO", a, e), T.FO[:, a:e], tab(T.CTO), T.DU1[:, a:e], A.min)
-            cp(keys("FO", a, e), keys("FU", a, e), T.FU[:, a:e], T.FO[:, a:e])
+            ts("CTL WL" if wl else "CTLs", keys("XO", a, e), T.XO[:, a:e], tab(T.CTL), float(XN), A.min)
+            move(1, "CTO CTOx" + wl, "TG1" if wl else "TG0", T.TG[:, a:e], tab(T.CTO))
             if wl:
                 move(1, "CTL WL", "XF", T.XF[:, a:e], tab(T.CTL))
-            lv[a:e] = [under("XF" if wl else "CTL", keys("LV", a, e), T.LV[:, a:e], T.XF[:, a:e] if wl else tab(T.CTL), XN - 0.5)] * (e - a)
-        for a, e in [(a, a + n) for a, n in spans(FCALLS[u])]:
-            act(keys("FU", a, e) + " ONA", "WA0 WA8", ind(T.WA[:, 0:12032], T.FU[:, a:e]), T.ONA[:, 0:16 * (e - a)], F.Silu)
-        dma("a", "WA0", "M32", T.M32[:, 0:640], T.WA[0:128:16, 0:10240], 320)
-        dma("s", "Z32 M32", "WA8", T.WA[8:128:16, 864:864 + MW], T.Z32[:, :], 432)
-        if u < RO - 1:
-            dma("s", "Z32", "WA0", T.WA[0:128:16, 0:10240], T.Z32[:, 0:640], 320)
+            lv[a:e] = [under("XF" if wl else "CTLs", keys("LV", a, e), T.LV[:, a:e], T.XF[:, a:e] if wl else tab(T.CTL), XN - 0.5)] * (e - a)
         if u == 0:
             constants()
             constants2()
             constants3()
         move(1, "DI", "LW", T.LW[:, 0:K2], T.DI[:, :])
         for a, e, tab, wl in both:
-            cp("PTD" + wl, "PTR", tab(T.PTR), T.PTD[:, K1 * u + a:K1 * u + e])
+            if wl:
+                tt("PTD ST WL", "PN", T.PN[:, a:e], tab(T.ST), T.PTD[:, K1 * u + a:K1 * u + e], A.add)
+                cp("PN WL", "PTR", tab(T.PTR), T.PN[:, a:e])
+            else:
+                tt("PTD ST", "PTR", tab(T.PTR), tab(T.ST), T.PTD[:, K1 * u + a:K1 * u + e], A.add)
         port_places(0, 24, [])
+        track_flags(u)
         for a, e in parts:
-            tt("X Xb Xd Xn XG " + keys("XO", a, e) + " " + obs(a, e)[0], keys("D", a, e) + " " + keys("XR", a, e), seg("D", a, e),
+            if a >= XA[u]:
+                b, x = small(), seg("BG", a, e)
+                move(2, "X Xb Xd Xn XG " + keys("XO", a, e), keys("BG", a, e) + " " + keys("XR", a, e), x, ind(T.X[:, :], T.XO[:, a:e]))
+                mms(b, 16 * (e - a), [("NI",) + obs(a, e), ("ID", keys("BG", a, e), x)])
+                move(1, "PS%d" % b, keys("D", a, e), seg("D", a, e), PS[b][:, 0:16 * (e - a)])
+                continue
+            tt("X Xb Xd Xn XG " + keys("XO", a, e) + " " + obs(a, e)[0], keys("D", a, e) + " " + keys("XR", a, e) + " orderF" * (a >= FIRST[u]), seg("D", a, e),
                ind(T.X[:, :], T.XO[:, a:e]), obs(a, e)[1], A.subtract)
         for grp in groups(ch1, UG1[u]):
             a, e, b = grp[0][0], grp[-1][0] + grp[-1][1], small()
@@ -941,7 +1117,7 @@ def record(g, core, T, topo, rank):
         track_list(u)
         for a in range(0, K2, 32):
             move(ON["PG"][a // 32], "PTR CU", keys("PG", a, a + 32), seg("PG", a, a + 32), ind(T.PTR[:, :], T.CU[:, a:a + 32]))
-        linear("LO0 LO320 LOx TL", "MO", T.MO[:, :], ind(T.LO[:, :], T.TL[:, 0:10]), 1.0, 1.0)
+        linear("LO LOx TL", "MO", T.MO[:, :], ind(T.LO[:, :], T.TL[:, 0:10]), 1.0, 1.0)
         logk = "LOGn"
         border = 0 if u and not listed(u)[2] else (ns if u else 0) + 24
 
@@ -954,47 +1130,47 @@ def record(g, core, T, topo, rank):
             r, k1 = slice(k0, k0 + nk), k0 + nk
             passes("D", ch, k0, nk)
             move(ON["PC1"], median(ch, k0, nk)[0], "PC%d" % ch, T.PC[:, r], median(ch, k0, nk)[1])
-            for a, e, b in wide(ch, k0, nk, "NI", lambda a, e: (keys("D", a, e), seg("D", a, e))):
-                act("PS%d" % b, keys("D", a, e), seg("D", a, e), PS[b][:, 0:16 * (e - a)], F.Abs)
+            turn_medians(ch, k0, nk, TURN1[u][ch])
+            lack = near("D", "D", ch, k0, nk, FUSE1[u][ch])
             clips = {}
             for a, e, b in wide(ch, k0, nk, "ID", obs):
                 clips[a] = upper("PS%d" % b, keys("OG", a, e), seg("OG", a, e), PS[b][:, 0:16 * (e - a)])
-            lack = near("D", k0, nk)
             b, uh = small(), keys("UH", k0, k1)
             opening(b, nk, [("I50", uh, T.UH[:, r])], lack, "I16")
-            fold(b, "D", k0, k1, st=False)
+            fold(b, "D", k0, k1, st=False, z=ZE2 * FUSE1[u][ch])
             fit = under("PS%d" % b, "FIT%d" % ch, T.FIT[:, r], PS[b][:, 0:nk], 123.0 - 50 * uh1[k0], -1.0)
             b, b2 = small(), small()
-            opening(b, nk, [("I50", keys("LV", k0, k1), T.LV[:, r]), ("N50", uh, T.UH[:, r])], [], "")
-            group("FIT%d BO I50" % ch, "PS%d" % b, [(PS[b][:, 0:nk], mat(m), T.FIT[:, r], False, m == "BO") for m in ("I50", "BO")])
-            none = under("PS%d" % b, "NONE%d" % ch, T.NONE[:, r], PS[b][:, 0:nk], 111.0 - 50 * lv[k0] + 50 * uh1[k0] - 66 * fit)
+            group("Z16 ID I50 N50 R50 RN50 " + keys("LV", k0, k1) + " " + uh, "PS%d" % b, [(PS[b][:, 0:2 * nk], T.ID[:, :], T.Z16[:, 0:2 * nk], True, False)] +
+                  [(PS[b][:, i:2 * nk:2], mat(m), x, False, False) for i, m, x in ((0, "I50", T.LV[:, r]), (0, "N50", T.UH[:, r]), (1, "R50", T.LV[:, r]), (1, "RN50", T.UH[:, r]))])
+            group("FIT%d IB RIB" % ch, "PS%d" % b, [(PS[b][:, i:2 * nk:2], mat(m), T.FIT[:, r], False, i == 1) for i, m in enumerate(("IB", "RIB"))])
+            none = under("PS%d" % b, "NONE%d" % ch, T.NONE[:, 2 * k0:2 * k1], PS[b][:, 0:2 * nk], 111.0 - 50 * lv[k0] + 50 * uh1[k0] - 66 * fit)
             mms(b2, nk, [("I50", uh, T.UH[:, r])], True, False)
-            group("FIT%d BO N50" % ch, "PS%d" % b2, [(PS[b2][:, 0:nk], mat(m), T.FIT[:, r], False, m == "BO") for m in ("N50", "BO")])
+            mms(b2, nk, [("NB", "FIT%d" % ch, T.FIT[:, r])], False, True)
             dies("PS%d" % b2, keys("DIE", k0, k1), T.DIE[:, r], PS[b2][:, 0:nk], 111.0 - 50 * uh1[k0] + 34 * fit)
             for a in range(k0, k1, 32):
                 e = min(k1, a + 32)
-                b, n, clip = nextbank(), 16 * (e - a), clips[a]
+                b, n, clip, key = nextbank(), 16 * (e - a), clips[a], "LOG%d_%d" % (u, a)
                 mms(b, n, [("NI" if clip else "ID", keys("OG", a, e) + " NI ID", seg("OG", a, e))], True, False)
-                group("NONE%d " % ch + " ".join("SEL%d" % j for j in range(16)), "PS%d" % b,
-                      [(PS[b][:, j:n:16], T.SEL[:, 128 * j:128 * j + 128], T.NONE[:, a:e], False, j == 15) for j in range(16)])
-                key = "LOG%d_%d" % (u, a)
+                group("NONE%d " % ch + " ".join("SEL%d" % j for j in range(8)), "PS%d" % b,
+                      [(PS[b][:, j:n:8], T.SEL[:, 128 * j:128 * j + 128], T.NONE[:, 2 * a:2 * e], False, j == 7) for j in range(8)])
                 logk += " " + key
                 relu("PS%d" % b, key, T.LOG[:, lb + 16 * a:lb + 16 * e], PS[b][:, 0:n], 255.0 * clip + 512.0 * none)
             if k0 < border <= k1:
                 send_b(k1)
         for a, e, tab, wl in both:
-            tt(keys("DIE", a, e) + (" XF WL" if wl else " CTL"), "CTL", tab(T.CTL), T.DIE[:, a:e], T.XF[:, a:e] if wl else tab(T.CTL), A.max)
+            tt(keys("DIE", a, e) + (" XF WL" if wl else " CTL"), "CTL CTLs", tab(T.CTL), T.DIE[:, a:e], T.XF[:, a:e] if wl else tab(T.CTL), A.max)
         ch2 = spans(CH2)
         for grp in groups(ch2, IG2):
             a, e, b = grp[0][0], grp[-1][0] + grp[-1][1], small()
             mms(b, e - a, [("ID", "MO", T.MO[:, a:e])], True, False)
-            fold(b, "PG", a, e, st=False)
-            ts("PS%d" % b, keys("IU", a, e), T.IU[:, a:e], PS[b][:, 0:e - a], 4095.0, A.add)
+            fold(b, "PG", a, e, st=False, z=ZP)
+            linear("PS%d" % b, keys("IU", a, e), T.IU[:, a:e], PS[b][:, 0:e - a], 1.0, 4095.0)
+        camera_rows(u)
+        bc, br, bs, bs2, ones = small(), small(), small(), small(), []
         win, wk = T.LOG[:, 0:lb + 1792], logk + " LG"
         for a in range(0, K2, 32):
             move(ON["BG"][a // 32], wk + " " + keys("IU", a, a + 32), keys("BG", a, a + 32), seg("BG", a, a + 32), ind(win, T.IU[:, a:a + 32]))
         move(1, "TC TCx TL", "CF", T.CF[:, :], ind(T.TC[:, :], T.TL[:, 0:10]))
-        relu("CF", "PEN", T.PEN[:, :], T.CF[:, :], -287.0)
         move(ON["XOLD"], "X Xb Xd TL", "XOLD", T.XOLD[:, :], ind(T.X[:, 0:800], T.TL[:, 0:10]))
         for grp in groups(ch2, UG2):
             a, e, b = grp[0][0], grp[-1][0] + grp[-1][1], small()
@@ -1009,44 +1185,48 @@ def record(g, core, T, topo, rank):
             passes("BG", ch, k0, nk)
             mk, med = median(ch, k0, nk)
             move(ON["PC2"], mk, "PC%d" % ch, T.PC[:, r], med)
-            tt(mk + " XOLD", "NE%d" % ch, T.NE[:, r], med, T.XOLD[:, r], A.not_equal)
-            for a, e, b in wide(ch, k0, nk, "NI", lambda a, e: (keys("BG", a, e), seg("BG", a, e))):
-                act("PS%d" % b, keys("PG", a, e), seg("PG", a, e), PS[b][:, 0:16 * (e - a)], F.Abs)
-            b = small()
-            mms(b, nk, [("BO", "NE%d" % ch, T.NE[:, r])])
-            below("PS%d" % b, "SN%d" % ch, T.SN[:, r], PS[b][:, 0:nk], 1.0)
-            port = [("IF", "CF", T.CF[:, r]), ("I864", "MO", T.MO[:, r]), ("NBG", "PEN", T.PEN[:, r])]
-            b, b2 = small(), small()
-            mms(b, nk, port + [("I288", "SN%d" % ch, T.SN[:, r])])
-            linear("PS%d" % b, "P1%d" % ch, T.P1[:, r], PS[b][:, 0:nk], 1.0, 288.0)
-            mms(b2, nk, port + [("NBG", "SN%d" % ch, T.SN[:, r])])
-            tt("PS%d DU2" % b2, "P0%d" % ch, T.P0[:, r], PS[b2][:, 0:nk], T.DU2[:, r], A.max)
-            lack = near("PG", k0, nk)
-            b = small()
-            opening(b, nk, [("I23", keys("UH", k0, k1), T.UH[:, r]), ("N19", keys("NH", k0, k1), T.NH[:, r])] +
-                    [("I23", "", T.ONB[:, 0:nk])] * uh1[k0], lack, "N18")
-            fold(b, "PG", k0, k1, st=False, z=144)
-            tt("PS%d P1%d" % (b, ch), "P1%d" % ch, T.P1[:, r], PS[b][:, 0:nk], T.P1[:, r], A.min)
-            tt("P0%d P1%d" % (ch, ch), "P1%d" % ch, T.P1[:, r], T.P1[:, r], T.P0[:, r], A.max)
-            cp("P1%d" % ch, "MU%d" % ch, T.MU[:, r], T.P1[:, r])
-            ts("PS%d" % b, "P0%d" % ch, T.P0[:, r], PS[b][:, 0:nk], 0.0, A.is_gt, float(EC), A.mult)
-            for a, e in CALLS:
-                if k0 <= a < k1 and e <= MA:
-                    act("MU%d ONM" % ch, "WA0 WA8", ind(T.WA[:, :], T.MU[:, a:e]), T.ONM[:, 0:16 * (e - a)], F.Silu)
-                elif k0 <= a < k1:
-                    cp("MU%d ONB" % ch, "WB", ind(T.WB[:, :], T.MU[:, a:e]), T.ONB[:, 0:16 * (e - a)])
+            if DIFF[ch]:
+                b = small()
+                mms(b, nk, [("NI", "XOLD", T.XOLD[:, r]), ("ID", "PC%d" % ch, T.PC[:, r])])
+                act("PS%d" % b, "NE%d" % ch, T.NE[:, r], PS[b][:, 0:nk], F.Abs)
+            else:
+                tt(mk + " XOLD", "NE%d" % ch, T.NE[:, r], med, T.XOLD[:, r], A.not_equal)
+            c0, zs = k0 // 128 * 128, ZS2 if FUSE2[ch] else 144
+            if k0 == 128:
+                bc = small()
+            if k1 in (128, K2):
+                group(" ".join("NE%d" % i for i in range(ch + 1)) + " BO", "PS%d" % bc, turned(bc, c0, c0, k1, [("BO", T.NE[:, c0:k1], c0, k1)]))
+                port_rows(u, 1, bc, c0, k1 - c0, bs)
+            if k1 == K2:
+                marks(u, 1, bs)
+            turn_medians(ch, k0, nk, TURN2[ch])
+            lack = near("PG", "BG", ch, k0, nk, FUSE2[ch])
+            ones = ones * (k0 != c0) + [("I23", T.ONB[:, 0:nk], k0, k1)] * uh1[k0] + [("N18", T.ONB[:, 0:e - a], k0 + a, k0 + e) for a, e in lack]
+            if k0 == 128 and SPLIT:
+                br = small()
+            if k1 in (128, K2):
+                group(keys("UH", c0, k1) + " " + keys("NH", c0, k1) + " I23 N19 N18 ONB Z16", "PS%d" % br,
+                      turned(br, c0, c0, k1, [("I23", T.UH[:, c0:k1], c0, k1), ("N19", T.NH[:, c0:k1], c0, k1)] + ones, ("PG", zs), 0) )
+                group("ZS ZS2 " + keys("PG", c0, k1), "PS%d" % br, turned(br, c0, c0, k1, [0], ("PG", zs), 1))
+            if k1 == K2 or k1 == 128 and SPLIT:
+                port_rows(u, 0, br, c0 * SPLIT, k1 - c0 * SPLIT, bs2)
+            if k1 == K2:
+                marks(u, 0, bs2)
+                b = small()
+                mm("JT0_0 ID", "PS%d" % b, PS[b][:, 0:128], T.JT[:, 0:128], T.ID[:, :])
+                for q in range(4):
+                    move(1, "JT0_0 JT0_128 JW", "JW%d" % q, T.JW[32 * q:32 * q + 32, q:128:4], T.JT[32 * q:32 * q + 32, 128:K2])
+                mm("JW0 JW1 JW2 JW3 REP", "PS%d" % b, PS[b][:, 128:K2], T.JW[:, :], T.REP[:, 0:512:16])
+                ts("PS%d" % b, "P0", T.P0[:, :], PS[b][:, 0:K2], 0.0, A.is_gt, float(EC), A.mult)
 
         def every(name):
             return " ".join("%s%d" % (name, ch) for ch in range(len(CH2)))
-        dma("a", "WA8", "M32", T.M32[:, :], T.WA[8:128:16, 864:864 + MW], 432)
         cp(every("PC") + " TL", "X Xb Xd", ind(T.X[:, 0:800], T.TL[:, 0:10]), T.PC[:, :])
-        dma("s", "WB", "M16", T.M16[:, :], T.WB[0:128:16, 864:864 + MW], 216)
         if u < RO - 1:
             exchange(2 * u + 2, "X", T.X)
-            dma("s", "Z16", "WB", T.WB[0:128:16, 864:864 + MW], T.Z16[:, :], 216)
         else:
             dma("s", "X", "", T.yx[:, :], T.X[:, 0:640], 160)
-        tt(every("P0") + " CF TL", "TC TCx", ind(T.TC[:, :], T.TL[:, 0:10]), T.P0[:, :], T.CF[:, :], A.max)
+        tt("P0 CF TL", "TC TCx", ind(T.TC[:, :], T.TL[:, 0:10]), T.P0[:, :], T.CF[:, :], A.max)
         if u == RO - 1:
             b = small()
             ts("TC", "FS", T.FS[:, :], T.TC[:, 0:640], EC - 0.5, A.is_lt)
@@ -1055,20 +1235,18 @@ def record(g, core, T, topo, rank):
             mms(b, 40, [("ID", "FB", T.FB[:, :])], False, True)
             cp("PS%d" % b, "YT", T.YT[:, :], PS[b][:, 0:40])
             dma("s", "YT", "", T.yt[:, :], T.YT[:, :], 20)
-        move(1, "M32", "MC", T.MC[:, 0:576], T.M32[:, 0:576])
-        move(1, "M32", "MCb", T.MC[:, 576:864], T.M32[:, 576:864])
         if u < RO - 1:
             kills(u + 1)
             camera_flags(u + 1)
             camera_list(u + 1)
-    port_places(272, 16, killed("NBG", 272, 16))
+    port_places(272, 16, killed("PBG", 272, 16))
     ts(wk + " GU", "SG", T.SG[:, 0:256], ind(T.LOG[:, 384:400 + RO * 1792], T.GU[:, 0:16]), 512.0, A.min)
     dma("s", "SG", "", T.yb[:, :], T.SG[:, 0:256], 64)
     camera_flags(RO)
     b, b2 = small(), small()
-    mms(b, C, [("IF", "CTL", T.CTL[:, 0:C])] + killed("IXN", 0, C))
-    ts("PS%d" % b, "JK0", T.JK[:, :], PS[b][:, 0:C], XN - 0.5, A.is_lt)
-    mms(b2, C, [("BO", "JK0", T.JK[:, :]), ("I32", "FL", T.FL[:, :])])
-    move(1, "PS%d" % b2, "M32", T.M32[:, 0:C], PS[b2][:, 0:C])
-    dma("a", "M32", "", T.yc[:, :], T.M32[0:128:16, 0:C], 9)
+    mms(b, C, [("IF", "CTL", T.CTL[:, 0:C])] + killed("PXN", 0, C))
+    ts("PS%d" % b, "JK0", T.JK[:, 0:C], PS[b][:, 0:C], XN - 0.5, A.is_lt)
+    mms(b2, C, [("BO", "JK0", T.JK[:, 0:C]), ("I32", "FL", T.FL[:, :])])
+    move(1, "PS%d" % b2, "CTO", T.CTO[:, 0:C], PS[b2][:, 0:C])
+    dma("a", "CTO", "", T.yc[:, :], T.CTO[0:128:16, 0:C], 9)
     emit()

@@ -31,6 +31,7 @@ UG2 = (1, 3)
 IG2 = (1, 3)
 TIMES = (0.0009, 1.56, 3.8, 0.05, 0.00046, 0.27, 1.5, 200.0, 1.9, 2.0)
 T_CYC, T_GATH, T_SCAT, T_FIX, T_PE, T_HOP, T_DMA, T_KB, T_REMOTE, T_FIRST = TIMES
+T_ISSUE = 0.06
 T_GAP = 0.005
 HALVES = 32
 FUSE1 = [(1, 1, 1), (1, 1, 1), (1, 1, 1, 1), (1, 1, 1)]
@@ -38,10 +39,10 @@ FUSE2 = (0, 0, 1)
 TURN1 = [(0, 1, 0), (1, 0, 0), (0, 0, 0, 0), (0, 1, 0)]
 TURN2 = (1, 0, 0)
 VC = (0, 0, 1, 2)
-ROWS = [("aa", "va"), ("aa", "va"), ("aa", "va"), ("vv", "aa")]
-JOINT = (0, 0, 0, 1)
-XA = (32, 64, 32, 32)
-DIFF = (1, 0, 0)
+ROWS = ("aa", "aa", "aa", "aa")
+RIGHT = "avvv"
+XA = (32, 32, 32, 32)
+DIFF = (1, 2, 0)
 FIRST = (112, 64, 64, 32)
 SPLIT = 1
 BATCH = 8
@@ -49,7 +50,7 @@ LEVELS = (14, 28, 36, 36)
 ON = dict(LW=1, SG=1, PC1=1, PC2=1, XOLD=1, OG=(1, 1, 1, 1), PG=(1, 1, 1, 1, 1), BG=(1, 1, 1, 1, 1))
 PLAN = {}
 TURNS = 3
-ROUNDS = 30
+ROUNDS = 24
 STEPS = 600
 STRETCH = 100
 PATIENCE = 500
@@ -63,38 +64,45 @@ def spans(sizes):
     return [(sum(sizes[:i]), n) for i, n in enumerate(sizes)]
 
 
+def times(nk):
+    return 4 if nk == 16 else 2
+
+
 SCALED = dict(I50=50.0, N50=-50.0, NBG=-BIG, I23=23.0 * 8192, N19=-524288.0, I31=31.0, I1K=1024.0, N62=-62.0, N20K=-20480.0,
-              I16=16.0, NI=-1.0, N18=-262144.0, I32=32.0, I116=1.0 / 16, IW=41.0 / 1024, NW=-41.0 / 1024)
-MIXED = ("IB", "NB", "RIB", "R50", "RN50", "PXN", "PBG", "PBO")
+              I16=16.0, NI=-1.0, N18=-262144.0, I32=32.0, I512=512.0, I116=1.0 / 16, IW=41.0 / 1024, NW=-41.0 / 1024)
+MIXED = ("IB", "NB", "RIB", "R50", "RN50")
 SB = {
-    "ONB": (64, BF), "OA": (48 * 128, BF), "OB": (36 * K2, F16), "OM": (34 * K2, BF), "DF": (72, F32),
+    "ONB": (64, BF), "OA": (32 * 128, BF), "OB": (36 * K2, F16), "OM": (17 * K2, BF), "DF": (72, F32),
+    "LA": (32 * K2, BF), "RB": (19 * K2, BF), "AB": (320, BF), "SC": (40, F16), "ZK": (40, BF),
     "OF": (25 * 128, F16),
     "TG": (2 * K1, F16), "HG": (K1, BF), "HT": (128, BF), "ZT": (6 * K2, F16), "MT": (K2, BF), "JT": (2 * K2, BF),
-    "SM": (272, F32), "SJ": (132, I32), "KJ": (640, I32), "PCT": (256, BF), "REP": (1024, BF), "ST": (432, BF), "LVL": (64, BF), "MK": (16, F32), "PN": (K1, BF), "P0X": (128, BF),
-    "O": (4608, BF), "LOG": (400 + RO * 1792, BF), "OG": (1792, BF), "PG": (2560, BF), "FS": (640, BF), "FN": (64, BF),
-    "MC": (576, BF), "Z16": (288, BF),
+    "SM": (256, F32), "SJ": (132, I32), "KJ": (640, I32), "DL": (32, F32), "YC": (18, F32), "LF": (C, BF), "JA": (K2, BF), "ST": (432, BF), "LVL": (64, BF), "MK": (16, F32), "PN": (K1, BF), "P0X": (128, BF),
+    "O": (4608, BF), "LOG": (400 + RO * 1792, BF), "OG": (1792, BF), "PG": (2560, BF), "FS": (800, BF), "FN": (100, BF),
+    "Z16": (288, BF),
     "CTL": (432, F32), "CTO": (432, F32), "OO": (432, F32), "PTR": (432, BF), "PTD": (448, BF),
-    "TC": (800, F32), "LO": (800, BF), "LW": (1280, F32), "TID": (640, F32), "DI": (160, F32), "X": (1200, BF),
-    "JW": (128, BF), "SH": (140, BF), "IX": (128 * len(MIXED), BF),
-    "SEL": (1024, BF), "CP": (512, BF), "D": (1792, BF), "BG": (2560, BF), "S": (7 * SW, BF), "SS": (7 * SW, BF), "KP": (160, BF),
+    "TC": (800, F32), "LO": (800, BF), "LW": (1280, F32), "TID": (640, F32), "X": (1200, BF),
+    "JW": (K2, BF), "SH": (264, BF), "IX": (128 * len(MIXED), BF),
+    "SEL": (2048, BF), "CP": (512, BF), "D": (1792, BF), "BG": (2560, BF), "S": (7 * SW, BF), "SS": (7 * SW, BF), "KP": (160, BF),
     "ID": (128, BF), "BO": (128, BF), "II": (128 * len(SCALED), BF),
-    "PM": (384, BF), "TRI": (512, BF), "ZE": (864, BF), "RQ": (128, F32), "RG": (128, F32),
+    "TV": (640, I32), "TRI": (512, BF), "ZE": (864, BF), "RQ": (128, F32), "RG": (128, F32),
     "SI": (16, I32), "SF": (32, F32), "D16": (16, F32), "CI": (640, I32),
-    "SNX": (384, BF), "SNB": (384, BF), "SG": (384, BF),
+    "SG": (384, BF),
     "KIU": (160, F32), "OFF": (32, F32), "DM": (16, F32),
     "TH5": (16, F32), "PB": (16, F32), "FL": (288, BF), "QC": (304, BF), "NP": (288, BF), "CAP": (288, BF),
     "JK": (7 * 288, BF), "LH": (160, F16), "ACC": (8, F32), "W1": (16, F32), "W2": (16, F32), "W3": (16, F32),
     "WL": (8, U16), "XO": (112, U16), "OU": (112, U16), "XF": (112, F32),
     "UH": (160, BF), "LV": (112, BF), "FIT": (112, BF), "NONE": (224, BF),
-    "DIE": (112, F32), "KI": (16, I32), "KB": (40, BF), "PU": (16, U16), "PC": (160, BF),
+    "DIE": (112, F32), "KI": (16, I32), "KB": (40, BF), "PU": (20, U16), "PC": (320, BF),
     "DEAD": (32, BF), "GU": (32, U16),
     "FB": (40, BF), "FA": (40, BF), "PP": (40, BF), "NG": (40, BF), "B1": (40, F32), "B2": (40, BF), "BU": (40, U16),
     "TL": (16, U16), "CF": (160, F32), "CU": (160, U16),
-    "IU": (160, U16), "MO": (160, BF), "IF": (128, F32), "NH": (160, BF), "XOLD": (160, BF), "NE": (160, BF),
+    "IU": (160, U16), "MO": (160, BF), "NH": (160, BF), "XOLD": (224, BF), "NE": (192, BF),
     "P0": (160, F32), "YT": (40, F32),
 }
 SCRATCH = {k: ("sbuf", [128, v[0]], v[1]) for k, v in SB.items()}
-for _b in range(8):
+SCRATCH["PSM"] = ("psum", [128, 8, 17], F32)
+BANKS = 7
+for _b in range(BANKS):
     SCRATCH["PS%d" % _b] = ("psum", [128, 512], F32)
 NDMA = 16
 SEMAPHORES = ["cv", "ca", "ct", "cg", "loc0", "loc1"] + ["arr%d" % i for i in range(8)] + ["dm%d" % i for i in range(NDMA)]
@@ -156,6 +164,7 @@ def plan(nodes, users, init=None):
     queue, busy, lat = [x[0] for x in nodes], [x[1] for x in nodes], [x[2] for x in nodes]
     comp = [x[5] for x in nodes]
     either = [i for i in range(n) if nodes[i][6]]
+    pair = [{x[0]: x[6][0], x[6][0]: x[0]} if x[6] else {x[0]: x[0]} for x in nodes]
 
     def links(extra):
         pre, post = [[] for _ in range(n)], [[] for _ in range(n)]
@@ -210,11 +219,11 @@ def plan(nodes, users, init=None):
         return best
 
     def banks(start, post):
-        bank, extra, last = {}, {}, [(-1e9 - b, None) for b in range(8)]
+        bank, extra, last = {}, {}, [(-1e9 - b, None) for b in range(BANKS)]
         post, start = [[e[0] for e in p] for p in post], list(start)
         for k in sorted(users, key=lambda k: start[users[k][0]]):
             first = users[k][0]
-            for b in sorted(range(8), key=lambda b: last[b][0]):
+            for b in sorted(range(BANKS), key=lambda b: last[b][0]):
                 old = users[last[b][1]] if last[b][1] is not None else []
                 seen, todo = {first}, [first] if last[b][0] > start[first] else []
                 while todo:
@@ -225,7 +234,7 @@ def plan(nodes, users, init=None):
                 if not seen.intersection(old):
                     break
             else:
-                raise ValueError("more than eight products at a time")
+                raise ValueError("more products at a time than banks")
             extra[first] = {i: FOLLOWS for i in old}
             for i in old:
                 post[i].append(first)
@@ -287,7 +296,7 @@ def plan(nodes, users, init=None):
                 dep[i] = x
                 q = queue[i]
                 p = last[q]
-                beside[i] = last["a" if q == "v" else "v"]
+                beside[i] = last[pair[i][q]]
                 before[i], behind[p], last[q] = p, i, i
                 y = head[p] + span[p]
                 head[i] = x if x > y else y
@@ -431,7 +440,7 @@ def record(g, core, T, topo, rank):
                 deps[writer[k]] = READS
         nodes.append((q, busy, lat, deps, issue, comp, other, wr[0] if wr else ""))
         for k in rd + wr:
-            if k.startswith("PS"):
+            if k.startswith("PS") and k != "PSM":
                 users.setdefault(k, []).append(len(nodes) - 1)
         for k in rd:
             readers.setdefault(k, []).append(len(nodes) - 1)
@@ -448,15 +457,47 @@ def record(g, core, T, topo, rank):
 
     ndma = [0]
 
-    def dma(q, rd, wr, out, in_, kb):
+    def dma(qs, rd, wr, pairs, kb, most=8):
         sem = "dm%d" % ndma[0]
         ndma[0] += 1
+        first = len(nodes)
+        for i, q in enumerate(qs):
+            def issue(q=q, some=pairs[i::len(qs)]):
+                total[sem] = 16 * len(pairs)
+                for out, in_ in some:
+                    Q[q].dma_start(out, in_).then_inc(T.sem[sem], 16)
+                return sem, 16 * len(pairs)
+            busy = T_ISSUE * most / len(qs)
+            if i == len(qs) - 1:
+                node(q, rd, wr, busy, busy + T_DMA + kb / T_KB, issue)
+        deps = nodes.pop()
+        for i, q in enumerate(qs[:-1]):
+            def issue(q=q, some=pairs[i::len(qs)]):
+                for out, in_ in some:
+                    Q[q].dma_start(out, in_).then_inc(T.sem[sem], 16)
+                return sem, 16 * len(pairs)
+            nodes.append((q, deps[1], deps[1], dict(deps[3]), issue, False, None, deps[7]))
+            deps[3][len(nodes) - 1] = AFTER
+        nodes.append(deps)
+        for k in rd.split():
+            readers[k] = [len(nodes) - 1 if e == first else e for e in readers[k]]
+        for k in wr.split():
+            writer[k] = len(nodes) - 1
 
-        def issue():
-            total[sem] = 16
-            Q[q].dma_start(out, in_).then_inc(T.sem[sem], 16)
-            return sem, 16
-        node(q, rd, wr, 0.06, T_DMA + kb / T_KB, issue)
+    def runs():
+        out = []
+        for gr in range(8):
+            if out and out[-1][1] + out[-1][2] == 16 * (gr ^ rank):
+                out[-1][2] += 16
+            else:
+                out.append([16 * gr, 16 * (gr ^ rank), 16])
+        return out
+
+    def load(qs, rd, wr, buf, src, c0, c1, kb):
+        dma(qs, rd, wr, [(buf[p:p + n, c0:c1], src[r:r + n, c0:c1]) for r, p, n in runs()], kb)
+
+    def store(qs, rd, dst, buf, c1, kb):
+        dma(qs, rd, "", [(dst[r:r + n, :], buf[p:p + n, 0:c1]) for r, p, n in runs()], kb)
 
     def emit():
         if not PLAN:
@@ -635,11 +676,8 @@ def record(g, core, T, topo, rank):
         group((rd or keys(name, k0, k1)) + " ZE ZS ZP ZE2 ZS2", "PS%d" % b,
               [(PS[b][:, c0:c0 + k1 - k0], E(j, z), col(name, j, k0, k1), st and j == 0, sp and j == 15) for j in range(16)])
 
-    def exchange(n, srckey, src, after=""):
-        snd, key, loc = (T.SNX, "SNX", "loc0") if n % 2 == 0 else (T.SNB, "SNB", "loc1")
-        b = small()
-        group(srckey + " PM1 PM2 PM3", "PS%d" % b, [(PS[b][:, c0:c0 + 128], T.PM[:, c0:c0 + 128], src[:, c0:c0 + 128], True, True) for c0 in (0, 128, 256)])
-        move(1, "PS%d" % b, key, snd[:, :], PS[b][:, 0:384])
+    def exchange(n, key, snd, c0=0, after=""):
+        loc = "loc%d" % (n % 2)
         arr = 0
         for far in (True, False):
             trs, used = [], 0
@@ -650,7 +688,7 @@ def record(g, core, T, topo, rank):
                     used += len(eng)
                     rid, pid = topo.addr(T.cores[rank ^ d] if rl is None else rl, core)
                     trs.append(RemoteDMATransfer(dst_ids=[DstId(rid=rid, pnc=pid)], dma_engine_mask=bits(eng),
-                                                 remote_sem=T.sem["arr%d" % n], src=snd[:, 128 * (d - 1):128 * d],
+                                                 remote_sem=T.sem["arr%d" % n], src=snd[:, c0 + 128 * (d - 1):c0 + 128 * d],
                                                  dst=landing(T, n, d) if rl is None else T.O[:, 128 * n:128 * n + 128]))
                     prl = relay_of(T, topo, rank ^ d, d)
                     arr += len(topo.engines(T.cores[rank ^ d] if prl is None else prl, core))
@@ -667,26 +705,23 @@ def record(g, core, T, topo, rank):
         node("x", "sent%d1" % n, "handed%d" % n, 0.01, T_REMOTE + (T_FIRST if n == 0 else 0.0), arrive)
         node("x", "handed%d sent%d0" % (n, n), "XG" if n % 2 == 0 else "LG", 0.01, 0.01 - T_HOP, arrive)
 
-    dma("s", "", "Xb", T.X[:, 0:384], T.x0[:, 0:384], 96)
-    dma("a", "", "CI CIb", T.CI[:, 0:288], T.ct[:, :], 144)
-    dma("s", "", "X", T.X[:, 384:640], T.x0[:, 384:640], 64)
-    dma("s", "", "O0", T.O[:, 0:1792], T.obs[:, 0:1792], 448)
+    load("as", "", "Xb", T.X, T.x0, 0, 384, 96)
+    load("as", "", "CI CIb", T.CI, T.ct, 0, 288, 144)
+    load("s", "", "X", T.X, T.x0, 384, 640, 64)
+    load("s", "", "O0", T.O, T.obs, 0, 1792, 448)
     iota("SI", T.SI[:, 0:8], [[0, 8]], 0, 1, True)
     iota("RQ", T.RQ[:, :], [[1, 128]], 0)
     iota("OO", T.OO[:, :], [[16, 432]], 0)
     iota("RG", T.RG[:, :], [[16, 8], [0, 16]], 0)
-    for c0 in (0, 1024, 4096, 5120):
+    for c0 in (0, 1024):
         ms("OAz%d" % c0, T.OA[:, c0:c0 + 1024], 0.0)
-    for i, m in enumerate((16, 32, 48, 15, 112)):
+    for i, m in enumerate((14, 12, 0, 15, 112)):
         ts("SI", "SI%d" % i, T.SI[:, 8 + i:9 + i], T.SI[:, 0:1], m, A.bitwise_and)
     ts("SI", "SI5", T.SI[:, 13:14], T.SI[:, 0:1], 7, A.bitwise_and)
     ts("SI", "SI6", T.SI[:, 14:15], T.SI[:, 0:1], 3, A.arith_shift_right)
     ts("SI", "SI7", T.SI[:, 15:16], T.SI[:, 0:1], 31, A.bitwise_and)
     cp("SI SI0 SI1 SI2 SI3 SI4 SI5 SI6 SI7", "SF", T.SF[:, 0:16], T.SI[:, 0:16])
     PF, P16, GC = T.SF[:, 0:1], T.SF[:, 11:12], T.SF[:, 12:13]
-    ts("SF", "SFb", T.SF[:, 16:19], T.SF[:, 8:11], -2.0, A.mult, PF, A.add)
-    for d in (1, 2, 3):
-        ts("RQ SF SFb", "PM%d" % d, T.PM[:, 128 * (d - 1):128 * d], T.RQ[:, :], -16.0 * d, A.add, T.SF[:, 15 + d:16 + d], A.is_equal)
     exchange(0, "Xb", T.X)
     ts("OO SF", "OO", T.OO[:, :], T.OO[:, :], P16, A.add, 4607.0, A.min)
     ts("CI", "CIb", T.CI[:, 288:576], T.CI[:, 0:288], 4, A.arith_shift_right)
@@ -698,8 +733,8 @@ def record(g, core, T, topo, rank):
     ms("Xd", T.X[:, 640:800], 512.0)
     ms("Xn", T.X[:, XN:1200], 512.0)
     iota("CP", T.CP[:, :], [[0, 32], [2048, 16]], 1024 - 15 * 2048)
-    dma("s", "", "CI CIb", T.CI[:, :], T.tv[:, :], 320)
-    dma("s", "CI", "O1", T.O[:, 1792:4608], T.obs[:, 1792:4608], 704)
+    load("s", "", "TV", T.TV, T.tv, 0, 640, 320)
+    load("s", "TV", "O1", T.O, T.obs, 1792, 4608, 704)
 
     def sbuf(ch):
         return "SS" if ch % 2 else "S"
@@ -707,8 +742,11 @@ def record(g, core, T, topo, rank):
     def part(sb, k, a, e):
         return " ".join("%s%d_%d" % (sb, k, i) for i in range(a // 8, (e + 7) // 8))
 
-    def fill(wr, out, val):
-        either(1, "OAz0", wr, out, out, lambda: s.activation(out, T.OA[:, 0:size(out)], F.Identity, bias=val), lambda: v.memset(out, val))
+    def fill(wr, out, val, step=0):
+        q = PLAN["queue"][len(nodes)] if PLAN else "g"
+        dg, dv = 0.13 + 2 * size(out) * T_CYC, cost(out, [out], None)
+        op(q, "", wr, dg if q == "g" else dv, (lambda: g.iota(out, [[step, size(out)]], int(val), 0, allow_small_or_imprecise_dtypes=True)) if q == "g" else
+           (lambda: v.memset(out, val)), None if step else ("v", dv) if q == "g" else ("g", dg))
 
     def constants():
         ts("RQ SF", "ID", T.ID[:, :], T.RQ[:, :], PF, A.is_equal)
@@ -724,22 +762,15 @@ def record(g, core, T, topo, rank):
         ts("RQ SF", "DFi", T.DF[:, 36:72], T.RQ[:, 0:36], PF, A.is_equal, 0.5, A.mult)
         tt("DF DFi", "DF", T.DF[:, 0:36], T.DF[:, 36:72], T.DF[:, 0:36], A.subtract)
         act("DF", "DF DFi", T.DF[:, 36:72], T.DF[:, 0:36], F.Copy, scale=-1.0)
-        iota("REP", T.REP[:, 512:1024], [[1, 32], [0, 16]], 0)
-        ts("REP SF", "REPa", T.REP[:, 0:512], T.REP[:, 512:1024], T.SF[:, 15:16], A.is_equal)
-        ts("REP REPa SF", "REP", T.REP[:, 512:1024], T.REP[:, 512:1024], T.SF[:, 15:16], A.is_equal, SCALED["IW"], A.mult)
-        ts("SF", "SFp", T.SF[:, 24:25], T.SF[:, 13:14], 16.0, A.mult, T.SF[:, 14:15], A.add)
-        ts("SF", "SFq", T.SF[:, 25:26], T.SF[:, 13:14], 16.0, A.mult)
-        ts("RQ SFp", "PXN", mat("PXN"), T.RQ[:, :], T.SF[:, 24:25], A.is_equal, float(XN), A.mult)
-        act("PXN", "PBG", mat("PBG"), mat("PXN"), F.Copy, scale=-16.0)
-        ts("RG SFq", "PBO", mat("PBO"), T.RG[:, :], T.SF[:, 25:26], A.is_equal)
+        for x in (0, 1):
+            ts("RQ SF", "DL%d" % x, T.DL[:, 16 * x:16 * x + 16], T.RQ[:, 0:16], PF, A.is_equal, (x - 0.5) * BIG, A.mult)
         for name, x in SCALED.items():
             act("ID", name, mat(name), T.ID[:, :], F.Copy, scale=x)
-        act("ID", "IF", T.IF[:, :], T.ID[:, :], F.Copy)
         ts("RQ SF", "D16", T.D16[:, :], T.RQ[:, 0:16], P16, A.is_equal, 512.0, A.mult)
         iota("PTD", T.PTD[:, :], [[1, 448]], 25 - 256)
         iota("LVL", T.LVL[:, :], [[1, 64]], 0)
-        ts("SF", "MK0", T.MK[:, 0:1], P16, 13.5, A.is_lt)
-        ts("SF", "MK1", T.MK[:, 1:2], P16, 13.5, A.is_lt, 24.0 - 256, A.mult)
+        ts("SF", "MK0", T.MK[:, 0:1], P16, 11.5, A.is_lt)
+        ts("SF", "MK1", T.MK[:, 1:2], P16, 11.5, A.is_lt, 24.0 - 256, A.mult)
         ts("SF", "MK2", T.MK[:, 2:3], P16, 0.0, A.is_equal, 16.0, A.mult)
         ts("SF", "MK3", T.MK[:, 3:4], P16, 14.0, A.is_equal)
         ts("SF", "MK4", T.MK[:, 4:5], P16, 15.0, A.is_equal)
@@ -749,33 +780,44 @@ def record(g, core, T, topo, rank):
         scan("MK8 MK4 Z16", "MK8", T.W3[:, 8:16], T.MK[:, 8:16], T.Z16[:, 0:8], T.MK[:, 4:5], A.mult, A.add)
         ts("MK8", "MK8", T.MK[:, 8:16], T.W3[:, 8:16], 0.5, A.mult)
         st = batch("LVL MK3 MK8", "ST%d", [(T.ST[:, r:432:8], T.LVL[:, 0:54], T.MK[:, 3:4], T.MK[:, 8 + r:9 + r], A.mult, A.add) for r in range(8)])
-        ts(st + " MK1", "PTR ST", T.PTR[:, :], T.ST[:, :], T.MK[:, 1:2], A.add)
+        iota("JK0 JK1", T.JK[:, 0:432], [[0, 24], [1, 18]], 0)
+        iota("JK1 JK2", T.JK[:, 432:864], [[1, 24], [0, 18]], 1)
+        for i in range(2):
+            act("ID D16", "JK%d" % (3 + i), T.JK[:, 864 + 288 * i:992 + 288 * i], T.ID[:, :], F.Copy, scale=T.D16[:, 12 + i:13 + i])
+        b = small()
+        group(st + " I512 JK0 JK1 JK2 JK3 JK4", "PS%d" % b, [(PS[b][:, 0:432], mat("I512"), T.ST[:, :], True, False), (PS[b][:, 0:432], T.JK[:, 864:992], T.JK[:, 0:432], False, False),
+                                                         (PS[b][:, 0:432], T.JK[:, 1152:1280], T.JK[:, 432:864], False, True)])
+        linear("PS%d" % b, "ST " + st, T.ST[:, :], PS[b][:, 0:432], 1.0 / 512, 0.0)
+        ts("ST MK1", "PTR", T.PTR[:, :], T.ST[:, :], T.MK[:, 1:2], A.add)
         ts("LVL MK0", "LVL", T.LVL[:, 0:24], T.LVL[:, 0:24], -256.0, A.add, T.MK[:, 0:1], A.mult)
         tt("LVL ST", "PTR", T.PTR[:, 288:312], T.LVL[:, 0:24], T.ST[:, 288:312], A.add)
         ts("PTD MK0", "PTD", T.PTD[:, :], T.PTD[:, :], T.MK[:, 0:1], A.mult)
         act("ZE MK2", "ZP", T.ZE[:, ZP:ZP + 144], T.ZE[:, 0:144], F.Copy, scale=T.MK[:, 2:3])
-        act("ZE MK5", "ZZ", T.ZE[:, ZZ:ZZ + 144], T.ZE[:, 0:144], F.Copy, scale=T.MK[:, 5:6])
+        for i, (row, x) in enumerate(((13, 2.0 ** -14), (12, 2.0 ** -9), (None, 1.0), (12, 2.0 ** -9), (13, 2.0 ** -14))):
+            ts("BO D16 MK5", "ZK%d" % i, T.ZK[:, 8 * i:8 * i + 8], T.BO[:, 0:128:16], T.MK[:, 5:6] if row is None else T.D16[:, row:row + 1], A.mult, x, A.mult)
         act("BO MK2", "P0X", T.P0X[:, :], T.BO[:, :], F.Copy, scale=T.MK[:, 2:3])
         iota("KI", T.KI[:, 0:4], [[-3, 4]], 48, 1, True)
         iota("KP", T.KP[:, :], [[0, 10], [1, 16]], 0)
         iota("TID", T.TID[:, :], [[1, 40], [40, 16]], 64)
-        iota("DI", T.DI[:, :], [[1, 160]], 704)
         for ch in range(2):
-            sb, gap = sbuf(ch), SW - 16 - 16 * CH1[0][ch]
+            sb = sbuf(ch)
             for k in range(7):
-                fill("%s%d " % (sb, k) + (part(sb, k - 1, CH1[0][ch], 64) if k else ""), T[sb][:, max(k * SW - gap, 8):k * SW + 16], 1024.0)
+                fill("%s%d " % (sb, k), T[sb][:, max(k * SW, 8):k * SW + 16], 1024.0)
             fill(sb + "n", T[sb][:, 0:8], 512.0)
         fill("LOGn", T.LOG[:, 384:400], 1024.0)
         for i, sizes in enumerate(CH1 + [CH2]):
             for k0, nk in spans(sizes):
-                if i == 0 or sizes != (CH1 + [CH2])[i - 1]:
-                    c0 = 10 * fn_of(i) + k0 // 16
-                    act("OO", keys("FN", 16 * c0, 16 * c0 + nk), T.FN[:, c0:c0 + nk // 16], T.OO[:, 0:nk // 16], F.Copy)
+                if fn_of(i) == i:
+                    c0, w = 20 * i + k0 // 8, times(nk) * nk // 16
+                    iota("FN%d" % (20 * i), T.FN[:, c0:c0 + w], [[256 // times(nk), w]], 0)
         ts("SF", "SFd", T.SF[:, 21:22], P16, 4096.0 - 384, A.add)
-        fill("JW", T.JW[:, :], 0.0)
-        fill("SHz", T.SH[:, 0:12], 0.0)
+        ts("SF", "SFu", T.SF[:, 16:17], T.SF[:, 8:9], 8.0, A.mult, 31.0 - 130 * SW, A.add)
+        ts("SF SFu", "SFu", T.SF[:, 17:18], T.SF[:, 9:10], 4.0, A.mult, 31.0 - 130 * SW, A.add)
+        fill("SHz", T.SH[:, 0:8], 0.0)
         ts("SF", "MK6", T.MK[:, 6:7], P16, 3.5, A.is_lt, float(SW), A.mult)
-        act("ID MK6", "SH", T.SH[:, 12:140], T.ID[:, :], F.Copy, scale=T.MK[:, 6:7])
+        iota("SH", T.SH[:, 8:136], [[16, 8], [1, 8], [0, 2]], 0)
+        iota("SH4", T.SH[:, 136:264], [[16, 8], [1, 4], [0, 4]], 0)
+        ts("SH SH4 SF MK6", "SH SH4", T.SH[:, 8:264], T.SH[:, 8:264], PF, A.is_equal, T.MK[:, 6:7], A.mult)
         ts("SF", "MK7", T.MK[:, 7:8], P16, 7.5, A.is_lt, 16.0, A.mult)
         ts("SF MK7", "MK7", T.MK[:, 7:8], T.MK[:, 7:8], -8.0, A.add, PF, A.add)
         ts("RQ MK7", "R50", mat("R50"), T.RQ[:, :], T.MK[:, 7:8], A.is_equal, 50.0, A.mult)
@@ -784,18 +826,19 @@ def record(g, core, T, topo, rank):
             b = small()
             mms(b, 128, [("ID", "BO", T.BO[:, :]), ("ID", m, mat(m))])
             move(1, "PS%d" % b, name, mat(name), PS[b][:, 0:128])
-        for j in range(8):
-            act("BO D16", "SEL%d" % j, T.SEL[:, 128 * j:128 * j + 128], T.BO[:, :], F.Copy, scale=T.D16[:, j:j + 1])
+        for j in range(16):
+            out = T.SEL[:, 128 * j:128 * j + 128]
+            either(1, "BO D16", "SEL%d" % j, out, T.BO[:, :], lambda out=out, j=j: s.activation(out, T.BO[:, :], F.Copy, scale=T.D16[:, j:j + 1]),
+                   lambda out=out, j=j: v.tensor_scalar(out, T.BO[:, :], T.D16[:, j:j + 1], None, A.mult))
+        fill("LAz", T.LA[:, 0:16 * K2], 0.0)
 
     def fn_of(i):
-        while 0 < i < RO and CH1[i] == CH1[i - 1]:
-            i -= 1
-        return i
+        return CH1.index(CH1[i]) if i < RO else i
 
     def constants2():
-        ts("CI", "KJ0_0 KJ1_0", T.KJ[:, :], T.CI[:, :], 15, A.bitwise_and)
-        ts("CI", "CI", T.CI[:, :], T.CI[:, :], 4, A.arith_shift_right)
-        move(1, "CI", "TC", T.TC[:, 0:640], T.CI[:, :])
+        ts("TV", "KJ0_0 KJ1_0", T.KJ[:, :], T.TV[:, :], 15, A.bitwise_and)
+        ts("TV", "TV", T.TV[:, :], T.TV[:, :], 4, A.arith_shift_right)
+        move(1, "TV", "TC", T.TC[:, 0:640], T.TV[:, :])
         move(1, "KJ0_0 KJ1_0", "LO", T.LO[:, 0:640], T.KJ[:, :])
         fill("TCx", T.TC[:, 640:800], float(EC))
         fill("LOx", T.LO[:, 640:800], 0.0)
@@ -834,26 +877,26 @@ def record(g, core, T, topo, rank):
 
     def camera_flags(u):
         st, b = (SC * u) % C, small()
-        n = 8 * LEVELS[u - 1]
-        src = [(T.FL, "FL", 0, "ID", SC, C), (T.QC, "QC", 16, "NI", SC, C), (T.QC, "QC QC0", 15, "ID", SC, C), (T.MC, "MCb", C, "PBO", st, n)]
+        src = [(T.FL, "FL", 0, "ID"), (T.QC, "QC", 16, "NI"), (T.QC, "QC QC0", 15, "ID")]
         mms(b, C, [("ID", "Z16", T.Z16[:, 0:C])], True, False)
-        for i, (buf, key, c0, m, sh, end) in enumerate(src):
-            last = i == len(src) - 1
-            mms(b, end - sh, [(m, key, buf[:, c0 + sh:c0 + end])], False, last and sh == 0)
-            if sh:
-                mms(b, sh, [(m, key, buf[:, c0:c0 + sh])], False, last, C - sh)
+        for buf, key, c0, m in src:
+            mms(b, C - SC, [(m, key, buf[:, c0 + SC:c0 + C])], False, False)
+            mms(b, SC, [(m, key, buf[:, c0:c0 + SC])], False, False, C - SC)
+        calls = [(PS[b][:, (18 * a - st) % C:(18 * a - st) % C + 18], T.SEL[:, 128 * a:128 * a + 128], T.SC[:, c0:c0 + 18], False, False)
+                 for a in range(eighteens(u - 1)) for c0 in ((0, 21) if RIGHT[u - 1] == "a" else (0,))]
+        group("SC SCn " + " ".join("SEL%d" % j for j in range(16)), "PS%d" % b, calls[:-1] + [calls[-1][:4] + (True,)])
         either(0, "PS%d" % b, "FL", T.FL[:, :], PS[b][:, 0:C], lambda: s.activation(T.FL[:, :], PS[b][:, 0:C], F.Sign),
                lambda: v.tensor_scalar(T.FL[:, :], PS[b][:, 0:C], 0.5, None, A.is_gt))
 
-    def killed(m, c0, n):
-        return [(m, "MC", T.MC[:, c0:c0 + n])]
+    def eighteens(u):
+        return (8 * LEVELS[u] + 17) // 18
 
     def kills(u):
-        b, n = small(), 8 * LEVELS[u - 1]
-        mms(b, n, [("IF", "CTL", T.CTL[:, 0:n])] + killed("PXN", 0, n))
-        move(1, "PS%d" % b, "CTL", T.CTL[:, 0:n], PS[b][:, 0:n])
+        n = 8 * LEVELS[u - 1]
+        tt("KJ0_0 CTL", "CTL", T.CTL[:, 0:n], T.KJ[:, 0:n], T.CTL[:, 0:n], A.max)
 
     OBK = " ".join("OB%d" % i for i in range(60))
+    RBK = " ".join("RB%d" % i for i in range(10))
 
     def track_flags(u):
         linear("TG0 TG1", "HG", T.HG[:, :], T.TG[:, 0:K1], 1.0 / 40, 129.0 - 19.5 / 40)
@@ -870,9 +913,9 @@ def record(g, core, T, topo, rank):
             oa += " " + batch("ZF%d" % i, "OF%d_%%d orderF" % i, [(T.OF[0:K1, 128 * (4 * i + k):128 * (4 * i + k + 1)], z, 1024.0 * (k - 2), 1024.0 * (k - 1), A.max, A.min)
                                                           for k in range(4)])
         for q in range(4):
-            group(oa + " OAz0 OAz1024 OAz4096 OAz5120", "PS%d" % b2,
-                  [(PS[b2][32 * q:32 * q + 32, 0:20], T.OA[0:K1, 2048 * (1 - c // 16 % 2) + c:2048 * (3 - c // 16 % 2):128], T.OF[0:K1, c:2560:128],
-                    c % 32 == 0, c % 32 == 31) for c in range(32 * q, 32 * q + 32)])
+            group(oa + " OAz0 OAz1024", "PS%d" % b2,
+                  [(PS[b2][32 * q:32 * q + 16 + (c & 16), 0:20], T.OA[0:K1, 2048 - 128 * (c & 16) + c:4096:128], T.OF[0:K1, c:2560:128],
+                    c % 32 == 31, c % 32 == 0) for c in range(32 * q + 31, 32 * q - 1, -1)])
         linear("PS%d" % b2, "SJf", T.SJ[:, 72:92], PS[b2][:, 0:20], 1.0, 2.0 ** 23)
         kf = batch("SJf", "KF%d", [(T.SJ[:, 92 + e:132:2], T.SJ[:, 72:92], 31 << 5 * e, None, A.bitwise_and) for e in range(2)])
         tt(kf + " FA", "FB", T.FB[:, :], T.SJ[:, 92:132], T.FA[:, :], A.is_lt)
@@ -896,52 +939,97 @@ def record(g, core, T, topo, rank):
 
     def camera_rows(u):
         nb, b, b2 = LEVELS[u], small(), small()
-        for k0, nk in spans((128, 32)):
-            group(keys("PG", k0, k0 + nk) + " ZZ", "PS%d" % b, turned(b, k0 // 128 * 128, k0, k0 + nk, [], ("PG", ZZ)))
-        nv = PIECES[0][0]
+        zk = " ZK0 ZK1 ZK2 ZK3 ZK4"
+        group(keys("PG", 0, 128) + zk, "PS%d" % b, [(PS[b][:, j:384:16], col("PG", j, 0, 128), T.ZK[:, 0:24], True, True) for j in range(16)])
+        group(keys("PG", 128, K2) + zk, "PS%d" % b, [(PS[b][32 * (j % 4):32 * (j % 4) + 32, 384 + j // 4:480:4], col("PG", j, 128, K2), T.ZK[:, 16:40], True, True)
+                                                     for j in range(16)])
+        move(1, "PS%d" % b, "AB", T.AB[:, 0:256], PS[b][:, 0:256])
+        move(1, "PS%d" % b, "ABb", T.AB[:, 256:320], PS[b][:, 416:480])
+        if RIGHT[u] == "a":
+            if u == 0 or RIGHT[u - 1] != "a":
+                fill("RB8", T.RB[:, 0:K2], 1.0)
+                fill("RB9", T.RB[:, 18 * K2:19 * K2], -1.0)
+            batch("AB ABb", "RB%d", [(T.RB[:, K2 * x:K2 * x + K2], T.AB[:, 128:288], F.Sign, 0.5 - x) for x in range(1, 18)], "a")
+        else:
+            batch("AB ABb", "RB%d RB8", [(T.RB[:, K2 * x:K2 * x + K2], T.AB[:, 128:288], float(x), None, A.is_equal) for x in range(18)])
+        group("MO I116", "PS%d" % b2, turned(b2, 0, 0, 128, [("I116", T.MO[:, 0:128], 0, 128)]) + turned(b2, 128, 128, K2, [("I116", T.MO[:, 128:K2], 128, K2)]))
+        if u == RO - 1:
+            ts("AB", "MT", T.MT[:, 0:128], T.AB[:, 0:128], 0.5, A.is_equal)
+            ts("ABb", "MTb", T.MT[:, 128:K2], T.AB[:, 288:320], 0.5, A.is_equal)
+            tt("PS%d MT MTb" % b2, "MT MTb", T.MT[:, :], PS[b2][:, 0:K2], T.MT[:, :], A.min)
+            fill(OBK, T.OB[:, 0:16 * K2], 0.0)
+            return
+        move(1, "PS%d" % b2, "MT", T.MT[:, :], PS[b2][:, 0:K2])
+        nv, z0 = PIECES[0][0], PS[b][:, 256:416]
         if nv:
-            linear("PS%d" % b, "ZT0", T.ZT[:, 0:K2], PS[b][:, 0:K2], 1.0, -256.0 * 7)
+            linear("PS%d" % b, "ZT0", T.ZT[:, 0:K2], z0, 1.0, -256.0 * 7)
             batch("ZT0", "OB%d", [(T.OB[:, K2 * x:K2 * x + K2], T.ZT[:, 0:K2], 256.0 * (x - 7), 256.0 * (x - 6), A.max, A.min) for x in range(nv)])
         for i, (x0, n) in enumerate(PIECES):
             if x0 < nb:
                 z = T.ZT[:, K2 * i + K2:K2 * i + 2 * K2]
-                act("PS%d" % b, "ZT%d" % (i + 1), z, PS[b][:, 0:K2], F.Relu, scale=-1.0, bias=256.0 * (x0 + n))
+                act("PS%d" % b, "ZT%d" % (i + 1), z, z0, F.Relu, scale=-1.0, bias=256.0 * (x0 + n))
                 batch("ZT%d" % (i + 1), "OB%d%%d" % (i + 1), [(T.OB[:, K2 * x:K2 * x + K2], z, F.Relu, 256.0 * (x0 + n - x), -1.0) for x in range(x0, x0 + n)], "a")
-        group("MO I116", "PS%d" % b2, turned(b2, 0, 0, 128, [("I116", T.MO[:, 0:128], 0, 128)]) + turned(b2, 128, 128, K2, [("I116", T.MO[:, 128:K2], 128, K2)]))
-        move(1, "PS%d" % b2, "MT", T.MT[:, :], PS[b2][:, 0:K2])
 
-    def port_rows(u, i, b, c0, n, bs):
-        nb, j0, key = LEVELS[u], K2 * i + c0, "%d_%d" % (i, c0)
-        tt("PS%d MT" % b, "JT" + key, T.JT[:, j0:j0 + n], PS[b][:, c0:c0 + n], T.MT[:, c0:c0 + n], A.min)
-        q, r0 = ROWS[u][i][c0 // 128], 17 * K2 * i
-        if u == 0 or q != ROWS[u - 1][i][c0 // 128]:
-            fill("OMz" + key, T.OM[:, r0 + 16 * K2 + c0:r0 + 16 * K2 + c0 + n], -1.0 * (q == "a"))
-        made[key] = " OMz%s " % key + batch("JT" + key, "OM" + key + "_%d", [
-            (T.OM[:, r0 + K2 * a + c0:r0 + K2 * a + c0 + n], T.JT[:, j0:j0 + n]) +
+    def columns(a):
+        return [(c, c // 16 if c < 128 else (c - 128) // 4) for c in range(a, a + 32)]
+
+    def port_rows(u, b, c0, n):
+        nb, key, last = LEVELS[u], "0_%d" % c0, u == RO - 1
+        tt("PS%d MT" % b, "JT" + key, T.JT[:, c0:c0 + n], PS[b][:, c0:c0 + n], T.MT[:, c0:c0 + n], A.min)
+        if last:
+            nb, by = 16, living[0]
+            tt("PS%d AB ABb" % b, "JA" + key, T.JA[:, c0:c0 + n], PS[b][:, c0:c0 + n], T.AB[:, 288:320] if c0 else T.AB[:, 0:128], A.min)
+            rows = " " + batch("JA%s OB0" % key, "LB" + key + "_%d", [(T.OB[:, K2 * (16 + a) + c0:K2 * (16 + a) + c0 + n], T.JA[:, c0:c0 + n], (a + 1.0) / 32, -1.0, A.is_equal, A.mult)
+                                                                      for a in range(16)])
+            for a in range(c0, c0 + n, 32):
+                group(RBK + " OB0" + rows, "PS%d" % by, [(PS[by][32 * (x // 2):32 * (x // 2) + 16 * (x % 2) + 16, 0:18], T.OB[:, 16 * K2 * (1 - x % 2) + c:32 * K2:K2],
+                                                          T.RB[:, c:18 * K2:K2], False, False) for c, x in columns(a)])
+        q = ROWS[u][c0 // 128]
+        if u == 0 or q != ROWS[u - 1][c0 // 128]:
+            fill("OMz" + key, T.OM[:, 16 * K2 + c0:16 * K2 + c0 + n], -1.0 * (q == "a"))
+        rows = " OMz%s " % key + batch("JT" + key, "OM" + key + "_%d", [
+            (T.OM[:, K2 * a + c0:K2 * a + c0 + n], T.JT[:, c0:c0 + n]) +
             (((a + 0.5) / 16, 2.0, A.is_gt, A.mult) if q == "v" else (F.Sign, -(a + 0.5) / 16)) for a in range(16)], q)
-        if JOINT[u] and i:
-            return
-        rows, m = made[key] + made["1_%d" % c0] * JOINT[u], 17 + 17 * JOINT[u]
         for a in range(c0, c0 + n, 32):
-            gs = [(c, c // 16 if c < 128 else (c - 128) // 4) for c in range(a, a + 32)]
-            group(OBK + " Z16" + rows, "PS%d" % bs, [(PS[bs][0:nb, 0:8 * m], T.Z16[:, 0:nb], T.Z16[:, 0:8 * m], True, False)] * (a == 0) +
-                  [(PS[bs][0:nb, x:8 * m:8], T.OB[:, c:K2 * nb:K2], T.OM[:, r0 + c:r0 + m * K2:K2], False, c == K2 - 1) for c, x in gs])
+            group((RBK if last else OBK) + " Z16" + rows, "PSM", [(T.PSM[0:nb, :, :], T.Z16[:, 0:nb], T.Z16[:, 0:136], True, False)] * (a == 0) +
+                  [(T.PSM[0:nb, x, :], T.RB[:, 2 * K2 + c:18 * K2:K2] if last else T.OB[:, c:K2 * nb:K2], T.OM[:, c:17 * K2:K2], False, c == K2 - 1)
+                   for c, x in columns(a)])
 
-    made = {}
+    living = []
 
-    def marks(u, i, b):
-        if JOINT[u] and i:
-            return
-        nb, b2, kinds = LEVELS[u], small(), (0, 1) if JOINT[u] else (i,)
-        s0, c0, n = 136 * i, C * i, len(kinds)
-        sj, sm, sk = T.SJ[:, 36 * i:36 * i + n * nb], " ".join("SM%d" % x for x in kinds), " ".join("SJ%d" % x for x in kinds)
-        move(1, "PS%d" % b, sm, T.SM[0:nb, s0:s0 + 136 * n], PS[b][0:nb, 0:136 * n])
-        group(sm + " DF", "PS%d" % b2, [(PS[b2][:, nb * k:nb * k + nb], T.SM[0:nb, s0 + 136 * k + 8 * x:s0 + 136 * k + 8 * x + 128], T.DF[0:nb, 36 * x:36 * x + nb], x == 0, x == 1)
-                                        for k in range(n) for x in (0, 1)])
-        linear("PS%d" % b2, sk, sj, PS[b2][:, 0:n * nb], 1.0, 2.0 ** 23)
-        kj = batch(sk, "KJ%d_%%d" % i + " KJ1_0" * JOINT[u], [(T.KJ[:, c0 + r:c0 + 8 * n * nb:8], sj, 1 << r, None, A.bitwise_and) for r in range(8)])
-        for x in kinds:
-            move(0, kj, ("MC", "MCb")[x], T.MC[:, C * x:C * x + 8 * nb], T.KJ[:, C * x:C * x + 8 * nb])
+    def standing(bs):
+        b, by, st = small(), small(), SC * (RO - 1)
+        living.append(by)
+        ts("CTL", "JK0", T.JK[:, 0:C], T.CTL[:, 0:C], XN - 0.5, A.is_lt)
+        group("JK0 ZE", "PS%d" % by, [(PS[by][:, 0:18], E(a), T.JK[:, 18 * a:18 * a + 18], a == 0, False) for a in range(16)])
+        mms(b, C, [("ID", "FL", T.FL[:, :]), ("ID", "QC QC0", T.QC[:, 15:15 + C])])
+        relu("PS%d" % b, "LF", T.LF[:, :], PS[b][:, 0:C], -float(K1))
+        group("LF ZE", "PS%d" % bs, [(PS[bs][:, 0:18], E(a), T.LF[:, (18 * a - st) % C:(18 * a - st) % C + 18], a == 0, False) for a in range(16)])
+
+    def marks(u):
+        nb, b2 = LEVELS[u], small()
+        for x in (0, 1):
+            move(1, "PSM", "SM%d" % x, T.SM[0:nb, 128 * x:128 * x + 128], T.PSM[0:nb, :, x:x + 16])
+        group("SM0 SM1 DF", "PS%d" % b2, [(PS[b2][:, 0:nb], T.SM[0:nb, 128 * x:128 * x + 128], T.DF[0:nb, 36 * x:36 * x + nb], x == 0, x == 1) for x in (0, 1)])
+        linear("PS%d" % b2, "SJ0", T.SJ[:, 0:nb], PS[b2][:, 0:nb], 2048.0, 0.0)
+        batch("SJ0", "KJ0_%d", [(T.KJ[:, r:8 * nb:8], T.SJ[:, 0:nb], 2048 << r, None, A.bitwise_and) for r in range(8)])
+
+    def change_rows(u, b, c0, n, bs):
+        na, w, j0, key = eighteens(u), 18 + (RIGHT[u] == "a"), K2 + c0, "1_%d" % c0
+        tt("PS%d AB ABb" % b, "JT" + key, T.JT[:, j0:j0 + n], PS[b][:, c0:c0 + n], T.AB[:, 288:320] if c0 else T.AB[:, 0:128], A.min)
+        rows = " LAz " + batch("JT" + key, "LA" + key + "_%d", [(T.LA[:, K2 * (16 + a) + c0:K2 * (16 + a) + c0 + n], T.JT[:, j0:j0 + n], (a + 1.0) / 32, None, A.is_equal)
+                                                               for a in range(na)])
+        for a in range(c0, c0 + n, 32):
+            group(RBK + " Z16" + rows, "PS%d" % bs, [(PS[bs][:, 0:w], T.Z16[:, 0:128], T.Z16[:, 0:w], True, False)] * (a == 0 and u < RO - 1) +
+                  [(PS[bs][32 * (x // 2):32 * (x // 2) + 16 * (x % 2) + na, 0:w], T.LA[:, 16 * K2 * (1 - x % 2) + c:K2 * (16 + na):K2], T.RB[:, c:w * K2:K2],
+                    False, c >= 128 and c % 8 == 7) for c, x in columns(a)])
+        if c0 and u == RO - 1:
+            either(1, "PS%d" % bs, "SC", T.SC[:, 0:w], PS[bs][:, 0:w], lambda: s.activation(T.SC[:, 0:w], PS[bs][:, 0:w], F.Sign),
+                   lambda: v.tensor_scalar(T.SC[:, 0:w], PS[bs][:, 0:w], 0.5, None, A.is_gt))
+        elif c0:
+            move(1, "PS%d" % bs, "SC", T.SC[:, 0:w], PS[bs][:, 0:w])
+            if RIGHT[u] == "a":
+                linear("PS%d" % bs, "SCn", T.SC[:, 20:20 + w], PS[bs][:, 0:w], -1.0, 0.0)
 
     def camera_list(u):
         st, (s0, ns), (lo, hi, wrap) = SC * u, SURE[u], listed(u)
@@ -990,44 +1078,32 @@ def record(g, core, T, topo, rank):
                 scan(keys(name, k0 + i, k0 + i + h) + rd, part(sb, b, i, i + h), T[sb][:, b * SW + 16 + 16 * i:b * SW + 16 + 16 * (i + h)],
                      seg(name, k0 + i, k0 + i + h), d1, 1024.0, A.min, A.max)
 
-    def pucol(k0):
-        return k0 // 16 + k0 // 16 % 2
-
     def pick_places(chunks, fn, plus):
         k0, k1 = chunks[0][0], chunks[-1][0] + chunks[-1][1]
-        w0, w1 = k0 // 16, k1 // 16
-        b, b2, w = small(), small(), w1 - w0
-        group(keys("UH", k0, k1) + " ZE", "PS%d" % b, [(PS[b][:, 0:4 * w], E(j), T.UH[:, k0 + j:k1:4], j == 0, j == 3) for j in range(4)])
-        linear("PS%d" % b, "KB", T.KB[:, 0:4 * w], PS[b][:, 0:4 * w], 0.25, 128.25 + 4 * plus)
-        mms(b2, w, [("I16", keys("FN", 16 * (fn + w0), 16 * (fn + w1)), T.FN[:, fn + w0:fn + w1])], True, False)
-        group("KB SH SHz", "PS%d" % b2, [(PS[b2][:, 0:w], T.SH[:, 12 - 4 * i:140 - 4 * i], T.KB[:, i:4 * w:4], False, i == 3) for i in range(4)])
-        cuts = [w0] + [a // 16 for a, nk in chunks[1:] if a // 16 % 2] + [w1]
-        for a, e in zip(cuts[:-1], cuts[1:]):
-            relu("PS%d" % b2, keys("PU", 16 * a, 16 * e), T.PU[:, pucol(16 * a):pucol(16 * a) + e - a], PS[b2][:, a - w0:e - w0], 31.0 - 130 * SW)
+        k2 = k1 - (16 if times(chunks[-1][1]) == 4 else 0)
+        b, b2, w, w2, w4 = small(), small(), (k1 - k0) // 4, (k2 - k0) // 8, (k1 - k2) // 4
+        group(keys("UH", k0, k1) + " ZE", "PS%d" % b, [(PS[b][:, 0:w], E(j), T.UH[:, k0 + j:k1:4], j == 0, j == 3) for j in range(4)])
+        linear("PS%d" % b, "KB", T.KB[:, 0:w], PS[b][:, 0:w], 0.25, 128.25 + 4 * plus)
+        mms(b2, w2 + w4, [("ID", "FN%d" % fn, T.FN[:, fn + k0 // 8:fn + k0 // 8 + w2 + w4])], True, False)
+        calls = [(PS[b2][:, 0:w2], T.SH[:, 8 - 8 * i:136 - 8 * i], T.KB[:, i:2 * w2:2], False, False) for i in range(2 if w2 else 0)]
+        calls += [(PS[b2][:, w2:w2 + w4], T.SH[:, 136:264], T.KB[:, 2 * w2:w], False, False)] * (w4 > 0)
+        group("KB SH SHz SH4", "PS%d" % b2, calls[:-1] + [calls[-1][:4] + (True,)])
+        if w2:
+            relu("PS%d SFu" % b2, keys("PU", k0, k2), T.PU[:, k0 // 8:k2 // 8], PS[b2][:, 0:w2], T.SF[:, 16:17])
+        if w4:
+            relu("PS%d SFu" % b2, keys("PU", k2, k1), T.PU[:, k2 // 8:k2 // 8 + w4], PS[b2][:, w2:w2 + w4], T.SF[:, 17:18])
 
-    def median(ch, k0, nk):
-        return finals(ch, nk)[0] + " " + keys("PU", k0, k0 + nk), ind(finals(ch, nk)[1], T.PU[:, pucol(k0):pucol(k0) + nk // 16])
+    def median(ch, k0, nk, last=False):
+        rd, win = (part(sbuf(ch), 6, 0, nk), T[sbuf(ch)][:, 6 * SW + 16:6 * SW + 16 + 16 * nk]) if last else finals(ch, nk)
+        return rd + " " + keys("PU", k0, k0 + nk), ind(win, T.PU[:, k0 // 8:k0 // 8 + times(nk) * nk // 16])
 
     def wide(ch, k0, nk, m, src, m2="ID"):
         for a in range(k0, k0 + nk, 32):
             e = min(k0 + nk, a + 32)
-            b, n = nextbank(), 16 * (e - a)
+            b, n, w = nextbank(), 16 * (e - a), 16 // times(nk)
             mms(b, n, [(m,) + src(a, e)], True, False)
-            if turn[0]:
-                c0, r0 = 128 * (ch % 2), 512 * (m2 != "ID")
-                mm("PCT%d REP" % (ch % 2), "PS%d" % b, PS[b][:, 0:n], T.PCT[a - k0:e - k0, c0:c0 + 128], T.REP[a - k0:e - k0, r0:r0 + n], False, True)
-            else:
-                group("PC%d %s" % (ch, m2), "PS%d" % b, [(PS[b][:, j:n:16], mat(m2), T.PC[:, a:e], False, j == 15) for j in range(16)])
+            group("PC%d %s" % (ch, m2), "PS%d" % b, [(PS[b][:, j:n:w], mat(m2), T.PC[:, 2 * a:2 * a + 64], False, j == w - 1) for j in range(w)])
             yield a, e, b
-
-    turn = [0]
-
-    def turn_medians(ch, k0, nk, on):
-        turn[0] = on
-        if on:
-            b = small()
-            mm("PC%d ID" % ch, "PS%d" % b, PS[b][0:nk, 0:128], T.PC[:, k0:k0 + nk], T.ID[:, :])
-            move(1, "PS%d" % b, "PCT%d" % (ch % 2), T.PCT[0:nk, 128 * (ch % 2):128 * (ch % 2) + 128], PS[b][0:nk, 0:128])
 
     def near(name, src, ch, k0, nk, fused):
         lack = []
@@ -1043,7 +1119,9 @@ def record(g, core, T, topo, rank):
     def port_places(c0, n, more):
         b = small()
         relu("CTL", "DEAD", T.DEAD[:, 0:n], T.CTL[:, c0:c0 + n], 1.0 - XN)
-        mms(b, n, [("NBG", "DEAD", T.DEAD[:, 0:n]), ("P0X", "PTR", T.PTR[:, c0:c0 + n])] + more)
+        mms(b, n, [("NBG", "DEAD", T.DEAD[:, 0:n]), ("P0X", "PTR", T.PTR[:, c0:c0 + n])], True, not more)
+        if more:
+            group("SM0 SM1 DL0 DL1", "PS%d" % b, [(PS[b][:, 0:n], T.SM[0:16, 128 * x:128 * x + 128], T.DL[0:16, 16 * x:16 * x + 16], False, x == 1) for x in (0, 1)])
         relu("PS%d SFd" % b, "GU", T.GU[:, 0:n], PS[b][:, 0:n], T.SF[:, 21:22])
 
     def track_list(u):
@@ -1091,14 +1169,19 @@ def record(g, core, T, topo, rank):
             constants()
             constants2()
             constants3()
-        move(1, "DI", "LW", T.LW[:, 0:K2], T.DI[:, :])
+        if u:
+            fill("LW", T.LW[:, 0:K2], 704, 1)
+        else:
+            op("a", "RQ", "LW", 1.45, lambda: s.activation(T.LW[:, 0:128], T.RQ[:, :], F.Silu, bias=704.0))
+            act("RQ", "LW", T.LW[:, 128:K2], T.RQ[:, 0:32], F.Silu, bias=832.0)
         for a, e, tab, wl in both:
             if wl:
                 tt("PTD ST WL", "PN", T.PN[:, a:e], tab(T.ST), T.PTD[:, K1 * u + a:K1 * u + e], A.add)
                 cp("PN WL", "PTR", tab(T.PTR), T.PN[:, a:e])
             else:
                 tt("PTD ST", "PTR", tab(T.PTR), tab(T.ST), T.PTD[:, K1 * u + a:K1 * u + e], A.add)
-        port_places(0, 24, [])
+        if u:
+            port_places(0, 24, False)
         track_flags(u)
         for a, e in parts:
             if a >= XA[u]:
@@ -1110,10 +1193,15 @@ def record(g, core, T, topo, rank):
             tt("X Xb Xd Xn XG " + keys("XO", a, e) + " " + obs(a, e)[0], keys("D", a, e) + " " + keys("XR", a, e) + " orderF" * (a >= FIRST[u]), seg("D", a, e),
                ind(T.X[:, :], T.XO[:, a:e]), obs(a, e)[1], A.subtract)
         for grp in groups(ch1, UG1[u]):
+            if u == 0:
+                fill(keys("UH", 0, K1), T.UH[:, 0:K1], 2.0)
+                ts("FN0 SFu", keys("PU", 0, K1 - 16), T.PU[:, 0:12], T.FN[:, 0:12], T.SF[:, 16:17], A.add, 130.0 * SW - 16, A.add)
+                ts("FN0 SFu", keys("PU", K1 - 16, K1), T.PU[:, 12:16], T.FN[:, 12:16], T.SF[:, 17:18], A.add, 130.0 * SW - 16, A.add)
+                break
             a, e, b = grp[0][0], grp[-1][0] + grp[-1][1], small()
             fold(b, "D", a, e)
             uh1[a:e] = [under("PS%d" % b, keys("UH", a, e), T.UH[:, a:e], PS[b][:, 0:e - a], 4088.0)] * (e - a)
-            pick_places(grp, 10 * fn_of(u), uh1[a])
+            pick_places(grp, 20 * fn_of(u), uh1[a])
         track_list(u)
         for a in range(0, K2, 32):
             move(ON["PG"][a // 32], "PTR CU", keys("PG", a, a + 32), seg("PG", a, a + 32), ind(T.PTR[:, :], T.CU[:, a:a + 32]))
@@ -1122,15 +1210,18 @@ def record(g, core, T, topo, rank):
         border = 0 if u and not listed(u)[2] else (ns if u else 0) + 24
 
         def send_b(end):
+            if u == 0:
+                exchange(1, "LOG0_0", T.LOG, lb, " " + keys("XR", 0, K1))
+                return
             move(ON["SG"], logk + " GU", "SG", T.SG[:, :], ind(T.LOG[:, 384:lb + 16 * end], T.GU[:, 0:24]))
-            exchange(2 * u + 1, "SG", T.SG, " " + keys("XR", 0, K1))
+            exchange(2 * u + 1, "SG", T.SG, 0, " " + keys("XR", 0, K1))
         if not border:
             send_b(0)
         for ch, (k0, nk) in enumerate(ch1):
             r, k1 = slice(k0, k0 + nk), k0 + nk
             passes("D", ch, k0, nk)
-            move(ON["PC1"], median(ch, k0, nk)[0], "PC%d" % ch, T.PC[:, r], median(ch, k0, nk)[1])
-            turn_medians(ch, k0, nk, TURN1[u][ch])
+            mk, med = median(ch, k0, nk, u == 0)
+            move(ON["PC1"], mk, "PC%d" % ch, T.PC[:, 2 * k0:2 * k0 + times(nk) * nk], med)
             lack = near("D", "D", ch, k0, nk, FUSE1[u][ch])
             clips = {}
             for a, e, b in wide(ch, k0, nk, "ID", obs):
@@ -1166,17 +1257,18 @@ def record(g, core, T, topo, rank):
             fold(b, "PG", a, e, st=False, z=ZP)
             linear("PS%d" % b, keys("IU", a, e), T.IU[:, a:e], PS[b][:, 0:e - a], 1.0, 4095.0)
         camera_rows(u)
-        bc, br, bs, bs2, ones = small(), small(), small(), small(), []
+        bc, br, bs, ones = small(), small(), small(), []
+        if u == RO - 1:
+            standing(bs)
         win, wk = T.LOG[:, 0:lb + 1792], logk + " LG"
         for a in range(0, K2, 32):
             move(ON["BG"][a // 32], wk + " " + keys("IU", a, a + 32), keys("BG", a, a + 32), seg("BG", a, a + 32), ind(win, T.IU[:, a:a + 32]))
-        move(1, "TC TCx TL", "CF", T.CF[:, :], ind(T.TC[:, :], T.TL[:, 0:10]))
-        move(ON["XOLD"], "X Xb Xd TL", "XOLD", T.XOLD[:, :], ind(T.X[:, 0:800], T.TL[:, 0:10]))
+        move(ON["XOLD"], "X Xb Xd TL", "XOLD", T.XOLD[:, 0:K2], ind(T.X[:, 0:800], T.TL[:, 0:10]))
         for grp in groups(ch2, UG2):
             a, e, b = grp[0][0], grp[-1][0] + grp[-1][1], small()
             fold(b, "BG", a, e)
             uh1[a:e] = [under("PS%d" % b, keys("UH", a, e), T.UH[:, a:e], PS[b][:, 0:e - a], 10000.0)] * (e - a)
-            pick_places(grp, 10 * RO, uh1[a])
+            pick_places(grp, 20 * RO, uh1[a])
             b = small()
             mms(b, e - a, [("BO", keys("UH", a, e), T.UH[:, a:e])])
             below("PS%d" % b, keys("NH", a, e), T.NH[:, a:e], PS[b][:, 0:e - a], 5.0 - 16 * uh1[a])
@@ -1184,22 +1276,25 @@ def record(g, core, T, topo, rank):
             r, k1 = slice(k0, k0 + nk), k0 + nk
             passes("BG", ch, k0, nk)
             mk, med = median(ch, k0, nk)
-            move(ON["PC2"], mk, "PC%d" % ch, T.PC[:, r], med)
-            if DIFF[ch]:
+            move(ON["PC2"], mk, "PC%d" % ch, T.PC[:, 2 * k0:2 * k1], med)
+            ne = T.NE[:, k0 // 128 * 128:k1]
+            if DIFF[ch] == 1:
                 b = small()
-                mms(b, nk, [("NI", "XOLD", T.XOLD[:, r]), ("ID", "PC%d" % ch, T.PC[:, r])])
+                mms(b, nk, [("NI", "XOLD", T.XOLD[:, r]), ("ID", "PC%d" % ch, T.PC[:, 2 * k0:2 * k1:2])])
                 act("PS%d" % b, "NE%d" % ch, T.NE[:, r], PS[b][:, 0:nk], F.Abs)
+            elif DIFF[ch] == 2:
+                tt("PC%d XOLD" % ch, "NE%d" % ch, T.NE[:, r], T.PC[:, 2 * k0:2 * k1:2], T.XOLD[:, r], A.not_equal)
             else:
-                tt(mk + " XOLD", "NE%d" % ch, T.NE[:, r], med, T.XOLD[:, r], A.not_equal)
+                for i in range(2):
+                    move(1, "XOLD", "XO2_%d" % i, T.XOLD[:, K2 + i:K2 + 2 * nk:2], T.XOLD[:, r])
+                tt(mk + " XO2_0 XO2_1", "NE%d" % ch, T.NE[:, k0:k0 + 2 * nk], med, T.XOLD[:, K2:K2 + 2 * nk], A.not_equal)
+                ne = T.NE[:, k0:k0 + 2 * nk:2]
             c0, zs = k0 // 128 * 128, ZS2 if FUSE2[ch] else 144
             if k0 == 128:
                 bc = small()
             if k1 in (128, K2):
-                group(" ".join("NE%d" % i for i in range(ch + 1)) + " BO", "PS%d" % bc, turned(bc, c0, c0, k1, [("BO", T.NE[:, c0:k1], c0, k1)]))
-                port_rows(u, 1, bc, c0, k1 - c0, bs)
-            if k1 == K2:
-                marks(u, 1, bs)
-            turn_medians(ch, k0, nk, TURN2[ch])
+                group(" ".join("NE%d" % i for i in range(ch + 1)) + " BO", "PS%d" % bc, turned(bc, c0, c0, k1, [("BO", ne, c0, k1)]))
+                change_rows(u, bc, c0, k1 - c0, bs)
             lack = near("PG", "BG", ch, k0, nk, FUSE2[ch])
             ones = ones * (k0 != c0) + [("I23", T.ONB[:, 0:nk], k0, k1)] * uh1[k0] + [("N18", T.ONB[:, 0:e - a], k0 + a, k0 + e) for a, e in lack]
             if k0 == 128 and SPLIT:
@@ -1209,44 +1304,51 @@ def record(g, core, T, topo, rank):
                       turned(br, c0, c0, k1, [("I23", T.UH[:, c0:k1], c0, k1), ("N19", T.NH[:, c0:k1], c0, k1)] + ones, ("PG", zs), 0) )
                 group("ZS ZS2 " + keys("PG", c0, k1), "PS%d" % br, turned(br, c0, c0, k1, [0], ("PG", zs), 1))
             if k1 == K2 or k1 == 128 and SPLIT:
-                port_rows(u, 0, br, c0 * SPLIT, k1 - c0 * SPLIT, bs2)
+                port_rows(u, br, c0 * SPLIT, k1 - c0 * SPLIT)
             if k1 == K2:
-                marks(u, 0, bs2)
+                if u < RO - 1:
+                    marks(u)
                 b = small()
-                mm("JT0_0 ID", "PS%d" % b, PS[b][:, 0:128], T.JT[:, 0:128], T.ID[:, :])
-                for q in range(4):
-                    move(1, "JT0_0 JT0_128 JW", "JW%d" % q, T.JW[32 * q:32 * q + 32, q:128:4], T.JT[32 * q:32 * q + 32, 128:K2])
-                mm("JW0 JW1 JW2 JW3 REP", "PS%d" % b, PS[b][:, 128:K2], T.JW[:, :], T.REP[:, 0:512:16])
-                ts("PS%d" % b, "P0", T.P0[:, :], PS[b][:, 0:K2], 0.0, A.is_gt, float(EC), A.mult)
+                mm("JT0_0 JA0_0 ID", "PS%d" % b, PS[b][:, 0:128], (T.JT if u < RO - 1 else T.JA)[:, 0:128], T.ID[:, :])
+                group(keys("UH", k0, k1) + " " + keys("NH", k0, k1) + " I23 N19 N18 ONB", "PS%d" % b,
+                      [(PS[b][:, a:e], mat(m), x, i == 0, False) for i, (m, x, a, e) in enumerate([("I23", T.UH[:, r], k0, k1), ("N19", T.NH[:, r], k0, k1)] + ones)])
+                fold(b, "PG", k0, k1, st=False, z=zs, c0=k0)
+                if u < RO - 1:
+                    ts("PS%d" % b, "P0", T.P0[:, :], PS[b][:, 0:K2], 0.0, A.is_gt, float(EC), A.mult)
+                else:
+                    ts("PS%d" % b, "MO", T.MO[:, :], PS[b][:, 0:K2], 0.0, A.is_le)
 
         def every(name):
             return " ".join("%s%d" % (name, ch) for ch in range(len(CH2)))
-        cp(every("PC") + " TL", "X Xb Xd", ind(T.X[:, 0:800], T.TL[:, 0:10]), T.PC[:, :])
+        cp(every("PC") + " TL", "X Xb Xd", ind(T.X[:, 0:800], T.TL[:, 0:10]), T.PC[:, 0:2 * K2:2])
         if u < RO - 1:
-            exchange(2 * u + 2, "X", T.X)
+            exchange(2 * u + 2, "Xb", T.X)
         else:
-            dma("s", "X", "", T.yx[:, :], T.X[:, 0:640], 160)
-        tt("P0 CF TL", "TC TCx", ind(T.TC[:, :], T.TL[:, 0:10]), T.P0[:, :], T.CF[:, :], A.max)
-        if u == RO - 1:
+            store("s", "X Xb", T.yx, T.X, 640, 160)
+        if u < RO - 1:
+            linear("CU", "CF", T.CF[:, :], T.CU[:, :], 1.0, 0.0)
+            tt("P0 CF TL", "TC TCx", ind(T.TC[:, :], T.TL[:, 0:10]), T.P0[:, :], T.CF[:, :], A.max)
+        else:
             b = small()
-            ts("TC", "FS", T.FS[:, :], T.TC[:, 0:640], EC - 0.5, A.is_lt)
+            ts("TC TCx", "FS", T.FS[:, :], T.TC[:, :], EC - 0.5, A.is_lt)
+            ts("CU", "JW", T.JW[:, :], T.CU[:, :], EC - 0.5, A.is_lt)
+            tt("MO JW TL", "FS", ind(T.FS[:, :], T.TL[:, 0:10]), T.MO[:, :], T.JW[:, :], A.mult)
             ts("FA", "FB", T.FB[:, :], T.FA[:, :], -32.0, A.mult, 32.0, A.add)
             group("FS ZE", "PS%d" % b, [(PS[b][:, 0:40], E(a), T.FS[:, 40 * a:40 * a + 40], a == 0, False) for a in range(16)])
             mms(b, 40, [("ID", "FB", T.FB[:, :])], False, True)
             cp("PS%d" % b, "YT", T.YT[:, :], PS[b][:, 0:40])
-            dma("s", "YT", "", T.yt[:, :], T.YT[:, :], 20)
+            dma("s", "YT", "", [(T.yt[r // 16:(r + n) // 16, :], T.YT[p:p + n, :]) for r, p, n in runs()], 20)
         if u < RO - 1:
             kills(u + 1)
             camera_flags(u + 1)
             camera_list(u + 1)
-    port_places(272, 16, killed("PBG", 272, 16))
+    for x in (0, 1):
+        move(1, "PSM", "SM%d" % x, T.SM[0:16, 128 * x:128 * x + 128], T.PSM[0:16, :, x:x + 16])
+    port_places(272, 16, True)
     ts(wk + " GU", "SG", T.SG[:, 0:256], ind(T.LOG[:, 384:400 + RO * 1792], T.GU[:, 0:16]), 512.0, A.min)
-    dma("s", "SG", "", T.yb[:, :], T.SG[:, 0:256], 64)
-    camera_flags(RO)
-    b, b2 = small(), small()
-    mms(b, C, [("IF", "CTL", T.CTL[:, 0:C])] + killed("PXN", 0, C))
-    ts("PS%d" % b, "JK0", T.JK[:, 0:C], PS[b][:, 0:C], XN - 0.5, A.is_lt)
-    mms(b2, C, [("BO", "JK0", T.JK[:, 0:C]), ("I32", "FL", T.FL[:, :])])
-    move(1, "PS%d" % b2, "CTO", T.CTO[:, 0:C], PS[b2][:, 0:C])
-    dma("a", "CTO", "", T.yc[:, :], T.CTO[0:128:16, 0:C], 9)
+    store("as", "SG", T.yb, T.SG, 256, 64)
+    b = living[0]
+    mms(b, 18, [("I32", "SC", T.SC[:, 0:18])], False, True)
+    move(1, "PS%d" % b, "YC", T.YC[:, :], PS[b][:, 0:18])
+    dma("as", "YC", "", [(T.yc[r // 16:(r + n) // 16, :], T.YC[p:p + n, :]) for r, p, n in runs()], 9)
     emit()

from concourse.mybir import AluOpType, AxisListType, ActivationFunctionType
from concourse.bass import DstId, RemoteDMATransfer
A = AluOpType
F = ActivationFunctionType
BF, F16, F32, I32, U16 = "bfloat16", "float16", "float32", "int32", "uint16"
C, NT, K1, K2, RO, SC = 288, 640, 112, 160, 4, 72
XN = 1184
EC = 312
SW = 1040
BIG = 16384.0
ZP, ZZ = 288, 432
ZE2, ZS2 = 576, 720
ROUND = 1.5 * 2 ** 23
PIECES = ((7, 7), (14, 7), (21, 7), (28, 8))


def sure_cameras():
    out, reach = [], 0
    for u in range(RO):
        n = max(min(K1 - (reach - SC * u), C - reach), 0)
        out.append((reach, n if u == 0 else n // 32 * 32))
        reach = min(reach + K1, C)
    return out


SURE = sure_cameras()
CH1 = [(32, 64, 16), (64, 32, 16), (32, 32, 32, 16), (32, 64, 16)]
CH2 = (64, 64, 32)
UG1 = [(1, 3), (1, 3), (1, 4), (1, 3)]
UG2 = (1, 3)
IG2 = (1, 3)
TIMES = (0.0009, 1.56, 3.8, 0.05, 0.00046, 0.27, 1.5, 200.0, 1.9, 2.0)
T_CYC, T_GATH, T_SCAT, T_FIX, T_PE, T_HOP, T_DMA, T_KB, T_REMOTE, T_FIRST = TIMES
T_ISSUE = 0.06
T_GAP = 0.005
HALVES = 32
FUSE1 = [(1, 1, 1), (1, 1, 1), (1, 1, 1, 1), (1, 1, 1)]
FUSE2 = (0, 0, 1)
TURN1 = [(0, 1, 0), (1, 0, 0), (0, 0, 0, 0), (0, 1, 0)]
TURN2 = (1, 0, 0)
VC = (0, 0, 1, 2)
ROWS = ("aa", "aa", "aa", "aa")
RIGHT = "avvv"
XA = (32, 32, 32, 32)
DIFF = (1, 2, 0)
FIRST = (112, 64, 64, 32)
SPLIT = 1
BATCH = 8
LEVELS = (14, 28, 36, 36)
ON = dict(LW=1, SG=1, PC1=1, PC2=1, XOLD=1, OG=(1, 1, 1, 1), PG=(1, 1, 1, 1, 1), BG=(1, 1, 1, 1, 1))
PLAN = {}
TURNS = 3
ROUNDS = 24
STEPS = 600
STRETCH = 100
PATIENCE = 500
TABU = 14
JITTER = 0.1
SEED = 1
WORTH = ((0.92, 0.25), (1.3, 0.3))


def spans(sizes):
    return [(sum(sizes[:i]), n) for i, n in enumerate(sizes)]


def times(nk):
    return 4 if nk == 16 else 2


SCALED = dict(I50=50.0, N50=-50.0, NBG=-BIG, I23=23.0 * 8192, N19=-524288.0, I31=31.0, I1K=1024.0, N62=-62.0, N20K=-20480.0,
              I16=16.0, NI=-1.0, N18=-262144.0, I32=32.0, I512=512.0, I116=1.0 / 16, IW=41.0 / 1024, NW=-41.0 / 1024)
MIXED = ("IB", "NB", "RIB", "R50", "RN50")
SB = {
    "ONB": (64, BF), "OA": (32 * 128, BF), "OB": (36 * K2, F16), "OM": (17 * K2, BF), "DF": (72, F32),
    "LA": (32 * K2, BF), "RB": (19 * K2, BF), "AB": (320, BF), "SC": (40, F16), "ZK": (40, BF),
    "OF": (25 * 128, F16),
    "TG": (2 * K1, F16), "HG": (K1, BF), "HT": (128, BF), "ZT": (6 * K2, F16), "MT": (K2, BF), "JT": (2 * K2, BF),
    "SM": (256, F32), "SJ": (132, I32), "KJ": (640, I32), "DL": (32, F32), "YC": (18, F32), "LF": (C, BF), "JA": (K2, BF), "ST": (432, BF), "LVL": (64, BF), "MK": (16, F32), "PN": (K1, BF), "P0X": (128, BF),
    "O": (4608, BF), "LOG": (400 + RO * 1792, BF), "OG": (1792, BF), "PG": (2560, BF), "FS": (800, BF), "FN": (100, BF),
    "Z16": (288, BF),
    "CTL": (432, F32), "CTO": (432, F32), "OO": (432, F32), "PTR": (432, BF), "PTD": (448, BF),
    "TC": (800, F32), "LO": (800, BF), "LW": (1280, F32), "TID": (640, F32), "X": (1200, BF),
    "JW": (K2, BF), "SH": (264, BF), "IX": (128 * len(MIXED), BF),
    "SEL": (2048, BF), "CP": (512, BF), "D": (1792, BF), "BG": (2560, BF), "S": (7 * SW, BF), "SS": (7 * SW, BF), "KP": (160, BF),
    "ID": (128, BF), "BO": (128, BF), "II": (128 * len(SCALED), BF),
    "TV": (640, I32), "TRI": (512, BF), "ZE": (864, BF), "RQ": (128, F32), "RG": (128, F32),
    "SI": (16, I32), "SF": (32, F32), "D16": (16, F32), "CI": (640, I32),
    "SG": (384, BF),
    "KIU": (160, F32), "OFF": (32, F32), "DM": (16, F32),
    "TH5": (16, F32), "PB": (16, F32), "FL": (288, BF), "QC": (304, BF), "NP": (288, BF), "CAP": (288, BF),
    "JK": (7 * 288, BF), "LH": (160, F16), "ACC": (8, F32), "W1": (16, F32), "W2": (16, F32), "W3": (16, F32),
    "WL": (8, U16), "XO": (112, U16), "OU": (112, U16), "XF": (112, F32),
    "UH": (160, BF), "LV": (112, BF), "FIT": (112, BF), "NONE": (224, BF),
    "DIE": (112, F32), "KI": (16, I32), "KB": (40, BF), "PU": (20, U16), "PC": (320, BF),
    "DEAD": (32, BF), "GU": (32, U16),
    "FB": (40, BF), "FA": (40, BF), "PP": (40, BF), "NG": (40, BF), "B1": (40, F32), "B2": (40, BF), "BU": (40, U16),
    "TL": (16, U16), "CF": (160, F32), "CU": (160, U16),
    "IU": (160, U16), "MO": (160, BF), "NH": (160, BF), "XOLD": (224, BF), "NE": (192, BF),
    "P0": (160, F32), "YT": (40, F32),
}
SCRATCH = {k: ("sbuf", [128, v[0]], v[1]) for k, v in SB.items()}
SCRATCH["PSM"] = ("psum", [128, 8, 17], F32)
BANKS = 7
for _b in range(BANKS):
    SCRATCH["PS%d" % _b] = ("psum", [128, 512], F32)
NDMA = 16
SEMAPHORES = ["cv", "ca", "ct", "cg", "loc0", "loc1"] + ["arr%d" % i for i in range(8)] + ["dm%d" % i for i in range(NDMA)]


def relay_of(T, topo, r, d):
    src = T.cores[r]
    far = [e for e in (1, 2, 3) if not topo.may_write(src, T.cores[r ^ e])]
    if d not in far:
        return None
    can = [c for c in topo.cores_of(src) if T.rank_of(c) is None and topo.may_write(c, T.cores[r ^ d])]
    can.sort(key=lambda c: (topo.die(c) != topo.die(src), c))
    return can[far.index(d) % len(can)]


def share(T, topo, r, d):
    rl = relay_of(T, topo, r, d)
    if rl is None:
        return topo.engines(T.cores[r], T.cores[r ^ d])
    far = [e for e in (1, 2, 3) if relay_of(T, topo, r, e) is not None]
    eng = topo.engines(T.cores[r], rl)
    n = 1
    while 2 * n * len(far) <= len(eng):
        n *= 2
    return eng[n * far.index(d):n * far.index(d) + n]


def bits(engines):
    return sum(1 << e for e in engines)


def landing(T, n, d):
    return T.X[:, 800 + 128 * (d - 1):800 + 128 * d] if n % 2 == 0 else T.LOG[:, 128 * (d - 1):128 * d]


def relay_program(g, core, T, topo):
    for r in range(len(T.cores)):
        for d in (1, 2, 3):
            if relay_of(T, topo, r, d) == core:
                dst = T.cores[r ^ d]
                rid, pid = topo.addr(dst, core)
                eng = topo.engines(core, dst)
                for n in range(2 * RO):
                    g.wait_ge(T.sem["arr%d" % n], len(share(T, topo, r, d)))
                    g.remote_dma(landing(T, n, d), T.O[:, 128 * n:128 * n + 128], T.sem["arr%d" % n], T.sem.loc0,
                                 pid, rid, bits(eng))
                g.wait_ge(T.sem.loc0, 2 * RO * len(eng))


READS, FOLLOWS, SHARES, AFTER = 3, 2, 1, 0


def waits(kind, q, qd):
    return kind == READS or kind == FOLLOWS and not q == qd == "t" or kind == SHARES and q != qd


def plan(nodes, users, init=None):
    n = len(nodes)
    queue, busy, lat = [x[0] for x in nodes], [x[1] for x in nodes], [x[2] for x in nodes]
    comp = [x[5] for x in nodes]
    either = [i for i in range(n) if nodes[i][6]]
    pair = [{x[0]: x[6][0], x[6][0]: x[0]} if x[6] else {x[0]: x[0]} for x in nodes]

    def links(extra):
        pre, post = [[] for _ in range(n)], [[] for _ in range(n)]
        for i in range(n):
            for d, kind in list(nodes[i][3].items()) + list(extra.get(i, {}).items()):
                w = waits(kind, queue[i] if comp[i] else None, queue[d] if comp[d] else None)
                pre[i].append((d, lat[d] + T_HOP if w else busy[d], w))
                post[d].append((i, lat[d] - busy[d] + T_HOP if w else 0.0))
        return pre, post

    def place(seq, edges, back):
        at0, slots = [0.0] * n, {q: [] for q in "vatgsx"}
        for i in seq:
            b = busy[i]
            if back:
                at = max([lat[i] - b] + [at0[e[0]] + busy[e[0]] + e[1] for e in edges[i]])
            else:
                at = max([0.0] + [at0[e[0]] + e[1] for e in edges[i]])
            row = slots[queue[i]]
            lo = len(row)
            while lo and row[lo - 1][1] > at:
                lo -= 1
            while lo < len(row) and at + b > row[lo][0] + 1e-9:
                at = max(at, row[lo][1])
                lo += 1
            row.insert(lo, (at, at + b))
            at0[i] = at
        return at0

    def worth(start, pre):
        seq, out = sorted(range(n), key=lambda k: start[k]), 0.0
        for speed, hop in WORTH:
            free, at = {q: 0.0 for q in "vatgsx"}, [0.0] * n
            for i in seq:
                x = max([free[queue[i]]] + [at[d] + hop for d, gap, w in pre[i] if w])
                f = speed if comp[i] else 1.0
                free[queue[i]] = x + busy[i] * f
                at[i] = x + lat[i] * f
            out += max(at)
        return out

    def backwards(start, post):
        late = place(sorted(range(n), key=lambda k: -start[k] - busy[k]), post, True)
        return [-late[k] - busy[k] for k in range(n)]

    def settle(start, pre, post, turns):
        best = (worth(start, pre), start)
        for _ in range(turns):
            late = backwards(start, post)
            start = place(sorted(range(n), key=lambda k: late[k]), pre, False)
            best = min(best, (worth(start, pre), start))
        return best

    def banks(start, post):
        bank, extra, last = {}, {}, [(-1e9 - b, None) for b in range(BANKS)]
        post, start = [[e[0] for e in p] for p in post], list(start)
        for k in sorted(users, key=lambda k: start[users[k][0]]):
            first = users[k][0]
            for b in sorted(range(BANKS), key=lambda b: last[b][0]):
                old = users[last[b][1]] if last[b][1] is not None else []
                seen, todo = {first}, [first] if last[b][0] > start[first] else []
                while todo:
                    for e in post[todo.pop()]:
                        if e not in seen and start[e] <= last[b][0]:
                            seen.add(e)
                            todo.append(e)
                if not seen.intersection(old):
                    break
            else:
                raise ValueError("more products at a time than banks")
            extra[first] = {i: FOLLOWS for i in old}
            for i in old:
                post[i].append(first)
            todo = [i for i in old if start[i] >= start[first]]
            while todo:
                d = todo.pop()
                for e in post[d]:
                    if start[e] <= start[d]:
                        start[e] = start[d] + 1e-3
                        todo.append(e)
            bank[k], last[b] = b, (0.0, k)
            last = [(max(start[i] + lat[i] for i in users[x[1]]), x[1]) if x[1] is not None else x for x in last]
        return bank, extra

    def swap(i):
        other = nodes[i][6] if queue[i] == nodes[i][0] else nodes[i][:2]
        queue[i], busy[i], lat[i] = other[0], other[1], other[1]

    seed = [SEED]

    def draw():
        seed[0] = (seed[0] * 1103515245 + 12345) % 2147483648
        return seed[0] / 2147483648

    def improve(start, extra, turns):
        seq = sorted(range(n), key=lambda k: start[k])
        full, anc = [dict(nodes[i][3]) for i in range(n)], [0] * n
        for i, more in extra.items():
            for d, kind in more.items():
                full[i][d] = max(kind, full[i].get(d, AFTER))
        for i in seq:
            deep = 0
            for d in full[i]:
                deep |= anc[d]
            for d in full[i]:
                anc[i] |= 1 << d
            anc[i] |= deep
            full[i] = {d: kind for d, kind in full[i].items() if not (deep >> d & 1 and comp[d])}
        needing = [[] for _ in range(n)]
        for i in range(n):
            for d in full[i]:
                needing[d].append(i)

        def gap(d, i):
            return lat[d] + T_HOP if waits(full[i][d], queue[i] if comp[i] else None, queue[d] if comp[d] else None) else busy[d]
        pre = [[(d, gap(d, i)) for d in full[i]] for i in range(n)]
        post = [[(i, gap(d, i)) for i in needing[d]] for d in range(n)]
        head, tail, dep, need = [0.0] * (n + 1), [0.0] * (n + 1), [0.0] * n, [0.0] * n
        before, behind, beside = [n] * (n + 1), [n] * (n + 1), [n] * n
        span = busy + [0.0]

        def ways(part, last, following):
            last = dict(last)
            for i in part:
                x = 0.0
                for d, w in pre[i]:
                    if head[d] + w > x:
                        x = head[d] + w
                dep[i] = x
                q = queue[i]
                p = last[q]
                beside[i] = last[pair[i][q]]
                before[i], behind[p], last[q] = p, i, i
                y = head[p] + span[p]
                head[i] = x if x > y else y
            for q, p in last.items():
                behind[p] = following[q]
            length = 0.0
            for i in reversed(part):
                x = lat[i]
                for e, w in post[i]:
                    if tail[e] + w > x:
                        x = tail[e] + w
                need[i] = x
                y = span[i] + tail[behind[i]]
                tail[i] = x = x if x > y else y
                if head[i] + x > length:
                    length = head[i] + x
            return length

        def turn_over(i):
            swap(i)
            span[i] = busy[i]
            for x in [i] + needing[i]:
                pre[x] = [(d, gap(d, x)) for d in full[x]]
            for x in [i] + list(full[i]):
                post[x] = [(e, gap(x, e)) for e in needing[x]]
        none = {q: n for q in "vatgsx"}
        for lo in range(-int(STRETCH * draw() / 2), n, STRETCH // 2):
            ways(seq, none, none)
            seq.sort(key=lambda k: head[k])
            lo, hi = max(lo, 0), min(lo + STRETCH, n)
            part, last, following = seq[lo:hi], dict(none), dict(none)
            last.update((queue[k], k) for k in seq[:lo])
            following.update((queue[k], k) for k in reversed(seq[hi:]))
            inside, best, tabu = set(part), None, {}
            for turn in range(turns + 1):
                length = ways(part, last, following)
                if best is None or length < best[0] - 1e-9:
                    best = (length, list(part), list(queue), turn)
                if turn > best[3] + PATIENCE:
                    break
                pick = None
                for i in [k for k in part if head[k] + tail[k] > length - 1e-6]:
                    j = behind[i]
                    if j in inside and head[j] < head[i] + span[i] + 1e-6 and head[j] + tail[j] > length - 1e-6 and not anc[j] >> i & 1:
                        p = before[i]
                        hj = max(dep[j], head[p] + span[p])
                        ti = max(need[i], span[i] + tail[behind[j]])
                        x = max(hj + max(need[j], span[j] + ti), max(dep[i], hj + span[j]) + ti) + JITTER * draw()
                        if (tabu.get((j, i), -1) < turn or x < best[0]) and (pick is None or x < pick[0]):
                            pick = (x, i, j)
                    if nodes[i][6] and tabu.get(i, -1) < turn:
                        b, p = (nodes[i][6] if queue[i] == nodes[i][0] else nodes[i])[1], beside[i]
                        x = max(dep[i], head[p] + span[p]) + max(need[i] + b - span[i], b + tail[behind[p]]) + JITTER * draw()
                        if p < n and (pick is None or x < pick[0]):
                            pick = (x, i, None)
                if pick is None:
                    break
                x, i, j = pick
                if j is None:
                    turn_over(i)
                    tabu[i] = turn + TABU * 4
                else:
                    a, e = part.index(i), part.index(j)
                    late, early = {i}, []
                    for k in part[a + 1:e]:
                        if before[k] in late or any(d in late for d in full[k]):
                            late.add(k)
                        else:
                            early.append(k)
                    part[a:e + 1] = early + [j] + [k for k in part[a:e] if k in late]
                    tabu[(i, j)] = turn + TABU + int(TABU * draw())
            seq[lo:hi] = best[1]
            for i in either:
                if queue[i] != best[2][i]:
                    turn_over(i)
        ways(seq, none, none)
        return head[:n]

    pre, post = links({})
    level = [0.0] * n
    for i in range(n - 1, -1, -1):
        level[i] = max([lat[i]] + [level[e[0]] + busy[i] + e[1] for e in post[i]])
    start = settle(place(sorted(range(n), key=lambda k: -level[k]), pre, False), pre, post, TURNS)[1]
    if init:
        for i in either:
            if queue[i] != init[1][i]:
                swap(i)
        pre, post = links({})
        start = init[0]
    best = None
    for turn in range(ROUNDS):
        bank, extra = banks(backwards(start, post), links({})[1])
        pre, post = links(extra)
        key, left = list(start), [len(p) for p in pre]
        todo = [i for i in range(n) if not left[i]]
        while todo:
            d = todo.pop()
            for e in post[d]:
                key[e[0]] = max(key[e[0]], key[d] + 1e-6)
                left[e[0]] -= 1
                if not left[e[0]]:
                    todo.append(e[0])
        start = settle(place(sorted(range(n), key=lambda k: key[k]), pre, False), pre, post, TURNS)[1]
        start = improve(start, extra, STEPS)
        pre, post = links(extra)
        got = settle(start, pre, post, TURNS)
        start = got[1]
        if best is None or got[0] < best[0]:
            best = got + (bank, extra, list(queue))
    PLAN.update(worth=best[0], start=best[1], bank=best[2], extra=best[3], queue=best[4])


def rank_program(g, core, T, topo):
    rank = T.rank_of(core)
    if rank is None:
        relay_program(g, core, T, topo)
        return
    if not PLAN:
        record(g, core, T, topo, rank)
    record(g, core, T, topo, rank)


def record(g, core, T, topo, rank):
    Q = {"v": g.vector, "a": g.scalar, "t": g.tensor, "g": g, "s": g.sync}
    own = {"v": "cv", "a": "ca", "t": "ct", "g": "cg"}
    total = {}
    known = {q: {} for q in Q}
    writer, readers, users = {}, {}, {}
    nodes = []

    def node(q, rd, wr, busy, lat, issue, comp=False, other=None):
        deps = {}
        rd, wr = rd.split(), wr.split()
        for k in wr:
            for e in ([writer[k]] if k in writer else []) + readers.get(k, []):
                deps[e] = max(deps.get(e, AFTER), AFTER if k.startswith("order") else FOLLOWS)
        for k in rd:
            if k.startswith("PS"):
                deps.update((e, max(deps.get(e, AFTER), SHARES)) for e in readers.get(k, []))
            if k in writer:
                deps[writer[k]] = READS
        nodes.append((q, busy, lat, deps, issue, comp, other, wr[0] if wr else ""))
        for k in rd + wr:
            if k.startswith("PS") and k != "PSM":
                users.setdefault(k, []).append(len(nodes) - 1)
        for k in rd:
            readers.setdefault(k, []).append(len(nodes) - 1)
        for k in wr:
            writer[k] = len(nodes) - 1
            readers[k] = []

    def op(q, rd, wr, dur, call, other=None):
        def issue():
            total[own[q]] = total.get(own[q], 0) + 1
            call().then_inc(T.sem[own[q]], 1)
            return own[q], total[own[q]]
        node(q, rd, wr, dur, dur, issue, True, other)

    ndma = [0]

    def dma(qs, rd, wr, pairs, kb, most=8):
        sem = "dm%d" % ndma[0]
        ndma[0] += 1
        first = len(nodes)
        for i, q in enumerate(qs):
            def issue(q=q, some=pairs[i::len(qs)]):
                total[sem] = 16 * len(pairs)
                for out, in_ in some:
                    Q[q].dma_start(out, in_).then_inc(T.sem[sem], 16)
                return sem, 16 * len(pairs)
            busy = T_ISSUE * most / len(qs)
            if i == len(qs) - 1:
                node(q, rd, wr, busy, busy + T_DMA + kb / T_KB, issue)
        deps = nodes.pop()
        for i, q in enumerate(qs[:-1]):
            def issue(q=q, some=pairs[i::len(qs)]):
                for out, in_ in some:
                    Q[q].dma_start(out, in_).then_inc(T.sem[sem], 16)
                return sem, 16 * len(pairs)
            nodes.append((q, deps[1], deps[1], dict(deps[3]), issue, False, None, deps[7]))
            deps[3][len(nodes) - 1] = AFTER
        nodes.append(deps)
        for k in rd.split():
            readers[k] = [len(nodes) - 1 if e == first else e for e in readers[k]]
        for k in wr.split():
            writer[k] = len(nodes) - 1

    def runs():
        out = []
        for gr in range(8):
            if out and out[-1][1] + out[-1][2] == 16 * (gr ^ rank):
                out[-1][2] += 16
            else:
                out.append([16 * gr, 16 * (gr ^ rank), 16])
        return out

    def load(qs, rd, wr, buf, src, c0, c1, kb):
        dma(qs, rd, wr, [(buf[p:p + n, c0:c1], src[r:r + n, c0:c1]) for r, p, n in runs()], kb)

    def store(qs, rd, dst, buf, c1, kb):
        dma(qs, rd, "", [(dst[r:r + n, :], buf[p:p + n, 0:c1]) for r, p, n in runs()], kb)

    def emit():
        if not PLAN:
            plan(nodes, users)
            return
        n, start = len(nodes), PLAN["start"]
        event = [None] * n
        for i in sorted(range(n), key=lambda k: start[k]):
            q, deps = nodes[i][0], dict(PLAN["extra"].get(i, {}))
            for d, kind in nodes[i][3].items():
                deps[d] = max(kind, deps.get(d, AFTER))
            if q != "x":
                for d in sorted(deps, key=lambda k: (-event[k][1], k)):
                    sem, cnt, clock = event[d]
                    if waits(deps[d], q if nodes[i][5] else None, nodes[d][0] if nodes[d][5] else None):
                        if known[q].get(sem, 0) < cnt:
                            Q[q].wait_ge(T.sem[sem], cnt)
                            known[q][sem] = cnt
                        for k, c in clock.items():
                            known[q][k] = max(known[q].get(k, 0), c)
            sem, cnt = nodes[i][4]()
            event[i] = (sem, cnt, dict(known[q]) if q != "x" else {})
        for sem, cnt in total.items():
            if known["g"].get(sem, 0) < cnt:
                g.wait_ge(T.sem[sem], cnt)

    v, s, t = g.vector, g.scalar, g.tensor

    def size(ap):
        n = 1
        for e in list(ap.shape)[1:]:
            n *= int(e)
        return n

    def ind(win, off):
        return (win.indirect(off), 16 * size(off))

    def cost(out, ins, plain):
        if isinstance(out, tuple):
            return T_FIX + out[1] * T_SCAT * T_CYC
        if isinstance(ins[0], tuple):
            return T_FIX + ins[0][1] * T_GATH * T_CYC
        if plain is None:
            plain = 0.5 if all(SCRATCH[a.name][2] in (BF, F16, U16) for a in [out] + ins) else 1.0
        return max(64.0, size(out) * plain) * T_CYC + T_GAP

    def batch(rd, wr, calls, q="v"):
        names, step = [], BATCH if q == "v" else BATCH // 2
        for i in range(0, len(calls), step):
            def issue(some=calls[i:i + step]):
                for c in some:
                    (v.tensor_scalar if q == "v" else s.activation)(*c).then_inc(T.sem[own[q]], 1)
                total[own[q]] = total.get(own[q], 0) + len(some)
                return own[q], total[own[q]]
            dur = sum(cost(c[0], [c[1]], None) if q == "v" else cost(c[0], [c[1]], 1.0) + 0.015 for c in calls[i:i + step])
            names.append((wr % (i // step)).split()[0])
            node(q, rd, wr % (i // step), dur, dur, issue, True)
        return " ".join(names)

    def ap(x):
        return x[0] if isinstance(x, tuple) else x

    def ts(rd, wr, out, in0, s1, o1, s2=None, o2=None):
        if o2 is None:
            op("v", rd, wr, cost(out, [in0], None), lambda: v.tensor_scalar(ap(out), ap(in0), s1, None, o1))
        else:
            op("v", rd, wr, cost(out, [in0], None), lambda: v.tensor_scalar(ap(out), ap(in0), s1, s2, o1, o2))

    def tt(rd, wr, out, a, b, o):
        op("v", rd, wr, cost(out, [a], 1.0 if "PS" in rd else 2.0), lambda: v.tensor_tensor(ap(out), ap(a), b, o))

    def cp(rd, wr, out, in_):
        op("v", rd, wr, cost(out, [in_], None), lambda: v.tensor_copy(ap(out), ap(in_)))

    def ms(wr, out, val):
        op("v", "", wr, cost(out, [out], None), lambda: v.memset(out, val))

    def scan(rd, wr, out, d0, d1, ini, o0, o1):
        op("v", rd, wr, cost(out, [d0, d1], None), lambda: v.tensor_tensor_scan(out, d0, d1, ini, o0, o1))

    def red(rd, wr, out, in_):
        op("v", rd, wr, cost(in_, [in_], 1.0), lambda: v.tensor_reduce(out, in_, AxisListType.X, A.add))

    def act(rd, wr, out, in_, f, **kw):
        op("a", rd, wr, cost(out, [in_], 1.0) + 0.015, lambda: s.activation(ap(out), ap(in_), f, **kw))

    def group(rd, wr, calls):
        def issue():
            for c in calls:
                (t.matmul if len(c) == 5 else t.transpose)(*c).then_inc(T.sem.ct, 1)
            total["ct"] = total.get("ct", 0) + len(calls)
            return "ct", total["ct"]
        dur = sum(max(min(64, size(c[1])), size(c[2])) * T_PE * (4 if SCRATCH[c[2].name][2] == F32 else 1) for c in calls)
        node("t", rd, wr, dur, dur, issue, True)

    def mm(rd, wr, out, lhsT, rhs, st=True, sp=True):
        group(rd, wr, [(out, lhsT, rhs, st, sp)])

    def iota(wr, out, pat, base, ch=0, exact=False):
        if exact:
            op("g", "", wr, 0.13 + 2 * size(out) * T_CYC, lambda: g.iota(out, pat, base, ch))
        else:
            op("g", "", wr, 0.13 + 2 * size(out) * T_CYC, lambda: g.iota(out, pat, base, ch, allow_small_or_imprecise_dtypes=True))

    def either(on_scalar, rd, wr, out, in_, on_a, on_v):
        q = PLAN["queue"][len(nodes)] if PLAN else "vaa"[on_scalar]
        da, dv = cost(out, [in_], 1.0) + 0.015, cost(out, [in_], None)
        if on_scalar == 2:
            op(q, rd, wr, da, on_a)
            return 1
        op(q, rd, wr, da if q == "a" else dv, on_a if q == "a" else on_v, ("v", dv) if q == "a" else ("a", da))
        return int(q == "a")

    def under(rd, wr, out, in_, x, sign=1.0):
        return either(1, rd, wr, out, in_, lambda: s.activation(out, in_, F.Sign, scale=-sign, bias=sign * x),
                      lambda: v.tensor_scalar(out, in_, x, 2.0, A.is_lt if sign > 0 else A.is_gt, A.mult))

    def linear(rd, wr, out, in_, scale, plus):
        either(1, rd, wr, out, in_, lambda: s.activation(ap(out), ap(in_), F.Identity, scale=scale, bias=plus),
               lambda: v.tensor_scalar(ap(out), ap(in_), scale, plus, A.mult, A.add))

    def move(on_scalar, rd, wr, out, in_, f=F.Copy):
        either(on_scalar, rd, wr, out, in_, lambda: s.activation(ap(out), ap(in_), f), lambda: v.tensor_copy(ap(out), ap(in_)))

    def relu(rd, wr, out, in_, plus):
        either(1, rd, wr, out, in_, lambda: s.activation(out, in_, F.Relu, bias=plus), lambda: v.tensor_scalar(out, in_, plus, 0.0, A.add, A.max))

    def below(rd, wr, out, in_, x):
        either(1, rd, wr, out, in_, lambda: s.activation(out, in_, F.Relu, scale=-1.0, bias=x), lambda: v.tensor_scalar(out, in_, x, None, A.is_lt))

    def upper(rd, wr, out, in_):
        return either(1, rd, wr, out, in_, lambda: s.activation(out, in_, F.Relu, scale=-1.0, bias=255.0), lambda: v.tensor_scalar(out, in_, 255.0, None, A.min))

    def dies(rd, wr, out, in_, x):
        either(1, rd, wr, out, in_, lambda: s.activation(out, in_, F.Relu, scale=float(XN), bias=-x * XN),
               lambda: v.tensor_scalar(out, in_, x, float(XN), A.is_gt, A.mult))

    PS = []

    def small():
        PS.append(T["PS%d" % (PLAN["bank"].get("PS%d" % len(PS), 0) if PLAN else 0)])
        return len(PS) - 1
    nextbank = small

    def mat(name, first=0, step=1):
        if name in SCALED:
            i = list(SCALED).index(name)
            return T.II[:, 128 * i + first:128 * i + 128:step]
        if name in MIXED:
            i = MIXED.index(name)
            return T.IX[:, 128 * i:128 * i + 128]
        return T[name][:, first:128:step]

    def mms(b, n, terms, st=True, sp=True, c0=0):
        for i, (m, rd, x) in enumerate(terms):
            mm(rd + " " + m, "PS%d" % b, PS[b][:, c0:c0 + n], mat(m), x, st and i == 0, sp and i == len(terms) - 1)

    def opening(b, n, terms, lack, m, c0=0):
        calls = [(PS[b][:, c0:c0 + n], mat(x[0]), x[2], i == 0, False) for i, x in enumerate(terms)]
        calls += [(PS[b][:, c0 + a:c0 + e], mat(m), T.ONB[:, a:e], False, False) for a, e in lack]
        group(" ".join(x[0] + " " + x[1] for x in terms) + " ONB " + m, "PS%d" % b, calls)

    def seg(name, k0, k1, c0=0):
        return T[name][:, 16 * (c0 + k0):16 * (c0 + k1)]

    def col(name, j, k0, k1):
        return T[name][:, 16 * k0 + j:16 * k1:16]

    def keys(name, k0, k1):
        return " ".join("%s_%d" % (name, b) for b in range(k0 // 16, (k1 + 15) // 16))

    def E(j, z=0):
        return T.ZE[:, z + 15 - j:z + 143 - j]

    def fold(b, name, k0, k1, rd=None, st=True, sp=True, z=0, c0=0):
        group((rd or keys(name, k0, k1)) + " ZE ZS ZP ZE2 ZS2", "PS%d" % b,
              [(PS[b][:, c0:c0 + k1 - k0], E(j, z), col(name, j, k0, k1), st and j == 0, sp and j == 15) for j in range(16)])

    def exchange(n, key, snd, c0=0, after=""):
        loc = "loc%d" % (n % 2)
        arr = 0
        for far in (True, False):
            trs, used = [], 0
            for d in (1, 2, 3):
                rl = relay_of(T, topo, rank, d)
                if (rl is not None) == far:
                    eng = share(T, topo, rank, d)
                    used += len(eng)
                    rid, pid = topo.addr(T.cores[rank ^ d] if rl is None else rl, core)
                    trs.append(RemoteDMATransfer(dst_ids=[DstId(rid=rid, pnc=pid)], dma_engine_mask=bits(eng),
                                                 remote_sem=T.sem["arr%d" % n], src=snd[:, c0 + 128 * (d - 1):c0 + 128 * d],
                                                 dst=landing(T, n, d) if rl is None else T.O[:, 128 * n:128 * n + 128]))
                    prl = relay_of(T, topo, rank ^ d, d)
                    arr += len(topo.engines(T.cores[rank ^ d] if prl is None else prl, core))

            def send(trs=trs, used=used):
                g.remote_dma_fused(trs, local_sem=T.sem[loc])
                total[loc] = total.get(loc, 0) + used
                return loc, total[loc]
            node("g", key + after, "order sent%d%d" % (n, far), 0.3 + (T_FIRST if n == 0 and far else 0.0), T_REMOTE + (T_FIRST if n == 0 and far else 0.0), send)

        def arrive():
            total["arr%d" % n] = arr
            return "arr%d" % n, arr
        node("x", "sent%d1" % n, "handed%d" % n, 0.01, T_REMOTE + (T_FIRST if n == 0 else 0.0), arrive)
        node("x", "handed%d sent%d0" % (n, n), "XG" if n % 2 == 0 else "LG", 0.01, 0.01 - T_HOP, arrive)

    load("as", "", "Xb", T.X, T.x0, 0, 384, 96)
    load("as", "", "CI CIb", T.CI, T.ct, 0, 288, 144)
    load("s", "", "X", T.X, T.x0, 384, 640, 64)
    load("s", "", "O0", T.O, T.obs, 0, 1792, 448)
    iota("SI", T.SI[:, 0:8], [[0, 8]], 0, 1, True)
    iota("RQ", T.RQ[:, :], [[1, 128]], 0)
    iota("OO", T.OO[:, :], [[16, 432]], 0)
    iota("RG", T.RG[:, :], [[16, 8], [0, 16]], 0)
    for c0 in (0, 1024):
        ms("OAz%d" % c0, T.OA[:, c0:c0 + 1024], 0.0)
    for i, m in enumerate((14, 12, 0, 15, 112)):
        ts("SI", "SI%d" % i, T.SI[:, 8 + i:9 + i], T.SI[:, 0:1], m, A.bitwise_and)
    ts("SI", "SI5", T.SI[:, 13:14], T.SI[:, 0:1], 7, A.bitwise_and)
    ts("SI", "SI6", T.SI[:, 14:15], T.SI[:, 0:1], 3, A.arith_shift_right)
    ts("SI", "SI7", T.SI[:, 15:16], T.SI[:, 0:1], 31, A.bitwise_and)
    cp("SI SI0 SI1 SI2 SI3 SI4 SI5 SI6 SI7", "SF", T.SF[:, 0:16], T.SI[:, 0:16])
    PF, P16, GC = T.SF[:, 0:1], T.SF[:, 11:12], T.SF[:, 12:13]
    exchange(0, "Xb", T.X)
    ts("OO SF", "OO", T.OO[:, :], T.OO[:, :], P16, A.add, 4607.0, A.min)
    ts("CI", "CIb", T.CI[:, 288:576], T.CI[:, 0:288], 4, A.arith_shift_right)
    cp("CIb", "CTO", T.CTO[:, 0:288], T.CI[:, 288:576])
    ms("CTOx", T.CTO[:, 288:432], 1023.0)
    ts("CI", "CTL CTLs", T.CTL[:, 0:288], T.CI[:, 0:288], 10240.0, A.is_ge, 160.0, A.mult)
    ms("CTLx", T.CTL[:, 288:432], float(XN))
    tt("CTL CIb CTLx", "CTL CTLs", T.CTL[:, 0:288], T.CTL[:, 0:288], T.CI[:, 288:576], A.add)
    ms("Xd", T.X[:, 640:800], 512.0)
    ms("Xn", T.X[:, XN:1200], 512.0)
    iota("CP", T.CP[:, :], [[0, 32], [2048, 16]], 1024 - 15 * 2048)
    load("s", "", "TV", T.TV, T.tv, 0, 640, 320)
    load("s", "TV", "O1", T.O, T.obs, 1792, 4608, 704)

    def sbuf(ch):
        return "SS" if ch % 2 else "S"

    def part(sb, k, a, e):
        return " ".join("%s%d_%d" % (sb, k, i) for i in range(a // 8, (e + 7) // 8))

    def fill(wr, out, val, step=0):
        q = PLAN["queue"][len(nodes)] if PLAN else "g"
        dg, dv = 0.13 + 2 * size(out) * T_CYC, cost(out, [out], None)
        op(q, "", wr, dg if q == "g" else dv, (lambda: g.iota(out, [[step, size(out)]], int(val), 0, allow_small_or_imprecise_dtypes=True)) if q == "g" else
           (lambda: v.memset(out, val)), None if step else ("v", dv) if q == "g" else ("g", dg))

    def constants():
        ts("RQ SF", "ID", T.ID[:, :], T.RQ[:, :], PF, A.is_equal)
        ts("RG SF", "BO", T.BO[:, :], T.RG[:, :], GC, A.is_equal)
        ms("ZE", T.ZE[:, 0:144], 0.0)
        cp("BO ZE", "ZE", T.ZE[:, 15:143:16], T.BO[:, 0:128:16])
        act("ZE", "ZS", T.ZE[:, 144:288], T.ZE[:, 0:144], F.Copy, scale=-BIG)
        act("ZE", "ZS2", T.ZE[:, ZS2:ZS2 + 144], T.ZE[:, 0:144], F.Copy, scale=-2 * BIG)
        act("ZE", "ZE2", T.ZE[:, ZE2:ZE2 + 144], T.ZE[:, 0:144], F.Copy, scale=2.0)
        ms("DF", T.DF[:, 0:36], 0.0)
        for x0, n in PIECES:
            ts("RQ SF", "DF", T.DF[:, x0:x0 + n - 1], T.RQ[:, x0 + 1:x0 + n], PF, A.is_equal, 0.5, A.mult)
        ts("RQ SF", "DFi", T.DF[:, 36:72], T.RQ[:, 0:36], PF, A.is_equal, 0.5, A.mult)
        tt("DF DFi", "DF", T.DF[:, 0:36], T.DF[:, 36:72], T.DF[:, 0:36], A.subtract)
        act("DF", "DF DFi", T.DF[:, 36:72], T.DF[:, 0:36], F.Copy, scale=-1.0)
        for x in (0, 1):
            ts("RQ SF", "DL%d" % x, T.DL[:, 16 * x:16 * x + 16], T.RQ[:, 0:16], PF, A.is_equal, (x - 0.5) * BIG, A.mult)
        for name, x in SCALED.items():
            act("ID", name, mat(name), T.ID[:, :], F.Copy, scale=x)
        ts("RQ SF", "D16", T.D16[:, :], T.RQ[:, 0:16], P16, A.is_equal, 512.0, A.mult)
        iota("PTD", T.PTD[:, :], [[1, 448]], 25 - 256)
        iota("LVL", T.LVL[:, :], [[1, 64]], 0)
        ts("SF", "MK0", T.MK[:, 0:1], P16, 11.5, A.is_lt)
        ts("SF", "MK1", T.MK[:, 1:2], P16, 11.5, A.is_lt, 24.0 - 256, A.mult)
        ts("SF", "MK2", T.MK[:, 2:3], P16, 0.0, A.is_equal, 16.0, A.mult)
        ts("SF", "MK3", T.MK[:, 3:4], P16, 14.0, A.is_equal)
        ts("SF", "MK4", T.MK[:, 4:5], P16, 15.0, A.is_equal)
        ts("MK3 MK4", "MK5", T.MK[:, 5:6], T.MK[:, 3:4], 256.0, A.mult, T.MK[:, 4:5], A.add)
        ms("MK8", T.MK[:, 8:16], 2.0)
        ms("Z16", T.Z16[:, :], 0.0)
        scan("MK8 MK4 Z16", "MK8", T.W3[:, 8:16], T.MK[:, 8:16], T.Z16[:, 0:8], T.MK[:, 4:5], A.mult, A.add)
        ts("MK8", "MK8", T.MK[:, 8:16], T.W3[:, 8:16], 0.5, A.mult)
        st = batch("LVL MK3 MK8", "ST%d", [(T.ST[:, r:432:8], T.LVL[:, 0:54], T.MK[:, 3:4], T.MK[:, 8 + r:9 + r], A.mult, A.add) for r in range(8)])
        iota("JK0 JK1", T.JK[:, 0:432], [[0, 24], [1, 18]], 0)
        iota("JK1 JK2", T.JK[:, 432:864], [[1, 24], [0, 18]], 1)
        for i in range(2):
            act("ID D16", "JK%d" % (3 + i), T.JK[:, 864 + 288 * i:992 + 288 * i], T.ID[:, :], F.Copy, scale=T.D16[:, 12 + i:13 + i])
        b = small()
        group(st + " I512 JK0 JK1 JK2 JK3 JK4", "PS%d" % b, [(PS[b][:, 0:432], mat("I512"), T.ST[:, :], True, False), (PS[b][:, 0:432], T.JK[:, 864:992], T.JK[:, 0:432], False, False),
                                                         (PS[b][:, 0:432], T.JK[:, 1152:1280], T.JK[:, 432:864], False, True)])
        linear("PS%d" % b, "ST " + st, T.ST[:, :], PS[b][:, 0:432], 1.0 / 512, 0.0)
        ts("ST MK1", "PTR", T.PTR[:, :], T.ST[:, :], T.MK[:, 1:2], A.add)
        ts("LVL MK0", "LVL", T.LVL[:, 0:24], T.LVL[:, 0:24], -256.0, A.add, T.MK[:, 0:1], A.mult)
        tt("LVL ST", "PTR", T.PTR[:, 288:312], T.LVL[:, 0:24], T.ST[:, 288:312], A.add)
        ts("PTD MK0", "PTD", T.PTD[:, :], T.PTD[:, :], T.MK[:, 0:1], A.mult)
        act("ZE MK2", "ZP", T.ZE[:, ZP:ZP + 144], T.ZE[:, 0:144], F.Copy, scale=T.MK[:, 2:3])
        for i, (row, x) in enumerate(((13, 2.0 ** -14), (12, 2.0 ** -9), (None, 1.0), (12, 2.0 ** -9), (13, 2.0 ** -14))):
            ts("BO D16 MK5", "ZK%d" % i, T.ZK[:, 8 * i:8 * i + 8], T.BO[:, 0:128:16], T.MK[:, 5:6] if row is None else T.D16[:, row:row + 1], A.mult, x, A.mult)
        act("BO MK2", "P0X", T.P0X[:, :], T.BO[:, :], F.Copy, scale=T.MK[:, 2:3])
        iota("KI", T.KI[:, 0:4], [[-3, 4]], 48, 1, True)
        iota("KP", T.KP[:, :], [[0, 10], [1, 16]], 0)
        iota("TID", T.TID[:, :], [[1, 40], [40, 16]], 64)
        for ch in range(2):
            sb = sbuf(ch)
            for k in range(7):
                fill("%s%d " % (sb, k), T[sb][:, max(k * SW, 8):k * SW + 16], 1024.0)
            fill(sb + "n", T[sb][:, 0:8], 512.0)
        fill("LOGn", T.LOG[:, 384:400], 1024.0)
        for i, sizes in enumerate(CH1 + [CH2]):
            for k0, nk in spans(sizes):
                if fn_of(i) == i:
                    c0, w = 20 * i + k0 // 8, times(nk) * nk // 16
                    iota("FN%d" % (20 * i), T.FN[:, c0:c0 + w], [[256 // times(nk), w]], 0)
        ts("SF", "SFd", T.SF[:, 21:22], P16, 4096.0 - 384, A.add)
        ts("SF", "SFu", T.SF[:, 16:17], T.SF[:, 8:9], 8.0, A.mult, 31.0 - 130 * SW, A.add)
        ts("SF SFu", "SFu", T.SF[:, 17:18], T.SF[:, 9:10], 4.0, A.mult, 31.0 - 130 * SW, A.add)
        fill("SHz", T.SH[:, 0:8], 0.0)
        ts("SF", "MK6", T.MK[:, 6:7], P16, 3.5, A.is_lt, float(SW), A.mult)
        iota("SH", T.SH[:, 8:136], [[16, 8], [1, 8], [0, 2]], 0)
        iota("SH4", T.SH[:, 136:264], [[16, 8], [1, 4], [0, 4]], 0)
        ts("SH SH4 SF MK6", "SH SH4", T.SH[:, 8:264], T.SH[:, 8:264], PF, A.is_equal, T.MK[:, 6:7], A.mult)
        ts("SF", "MK7", T.MK[:, 7:8], P16, 7.5, A.is_lt, 16.0, A.mult)
        ts("SF MK7", "MK7", T.MK[:, 7:8], T.MK[:, 7:8], -8.0, A.add, PF, A.add)
        ts("RQ MK7", "R50", mat("R50"), T.RQ[:, :], T.MK[:, 7:8], A.is_equal, 50.0, A.mult)
        act("R50", "RN50", mat("RN50"), mat("R50"), F.Copy, scale=-1.0)
        for name, m in (("IB", "I50"), ("NB", "N50"), ("RIB", "R50")):
            b = small()
            mms(b, 128, [("ID", "BO", T.BO[:, :]), ("ID", m, mat(m))])
            move(1, "PS%d" % b, name, mat(name), PS[b][:, 0:128])
        for j in range(16):
            out = T.SEL[:, 128 * j:128 * j + 128]
            either(1, "BO D16", "SEL%d" % j, out, T.BO[:, :], lambda out=out, j=j: s.activation(out, T.BO[:, :], F.Copy, scale=T.D16[:, j:j + 1]),
                   lambda out=out, j=j: v.tensor_scalar(out, T.BO[:, :], T.D16[:, j:j + 1], None, A.mult))
        fill("LAz", T.LA[:, 0:16 * K2], 0.0)

    def fn_of(i):
        return CH1.index(CH1[i]) if i < RO else i

    def constants2():
        ts("TV", "KJ0_0 KJ1_0", T.KJ[:, :], T.TV[:, :], 15, A.bitwise_and)
        ts("TV", "TV", T.TV[:, :], T.TV[:, :], 4, A.arith_shift_right)
        move(1, "TV", "TC", T.TC[:, 0:640], T.TV[:, :])
        move(1, "KJ0_0 KJ1_0", "LO", T.LO[:, 0:640], T.KJ[:, :])
        fill("TCx", T.TC[:, 640:800], float(EC))
        fill("LOx", T.LO[:, 640:800], 0.0)
        ts("KI", "KI", T.KI[:, 0:4], T.KI[:, 0:4], 15, A.bitwise_and)
        cp("KI", "PB", T.PB[:, 0:4], T.KI[:, 0:4])
        ts("PB", "PBb", T.PB[:, 4:8], T.PB[:, 0:4], -40.0, A.mult, 1280.0, A.add)
        for u in range(RO):
            act("RQ PBb", "KIU%d" % u, T.KIU[:, 40 * u:40 * u + 40], T.RQ[:, 0:40], F.Identity, scale=-1.0, bias=T.PB[:, 4 + u:5 + u])
        fill("FA", T.FA[:, :], 1.0)
        fill("NG", T.NG[:, :], -1.0)
        for u in range(RO):
            ts("KP PB", "TRI%d" % u, T.TRI[:, 128 * u:128 * u + 128], T.KP[:, 16 - 3 * u:144 - 3 * u], T.PB[:, u:u + 1], A.is_gt)
        for u in range(RO):
            tt("TRI%d BO" % u, "TRI%d" % u, T.TRI[:, 128 * u:128 * u + 128], T.TRI[:, 128 * u:128 * u + 128], T.BO[:, :], A.mult)

    def listed(u):
        s0, ns = SURE[u]
        wrap = s0 + K1 > C
        return (0, C, True) if wrap else (SC * u, s0 + K1, False)

    def constants3():
        fill("ONB", T.ONB[:, :], 1.0)
        fill("FL", T.FL[:, :], 1.0)
        fill("CAP", T.CAP[:, :], float(K1))
        fill("QC0", T.QC[:, 15:16], 0.0)
        scan("FL CAP", "QC", T.QC[:, 16:16 + C], T.FL[:, :], T.CAP[:, :], 0.0, A.add, A.min)
        ts("OO", "TH5", T.TH5[:, 0:8], T.OO[:, 0:8], 0.5, A.add)
        for u in range(1, RO):
            lo, hi, wrap = listed(u)
            n = hi - lo - SURE[u][1]
            vc = VC[u]
            if vc:
                act("RQ", "OFFa%d" % u, T.OFF[:, 8 * u:8 * u + vc], T.RQ[:, 0:vc], F.Identity, scale=32.0, bias=2.0 * lo)
            act("RQ", "OFFb%d" % u, T.OFF[:, 8 * u + vc:8 * u + 8], T.RQ[:, vc:8], F.Identity, scale=16.0, bias=2.0 * lo + n)
        ts("OO", "DM", T.DM[:, 0:7], T.OO[:, 0:7], 2.0, A.mult, 64.0, A.add)

    def camera_flags(u):
        st, b = (SC * u) % C, small()
        src = [(T.FL, "FL", 0, "ID"), (T.QC, "QC", 16, "NI"), (T.QC, "QC QC0", 15, "ID")]
        mms(b, C, [("ID", "Z16", T.Z16[:, 0:C])], True, False)
        for buf, key, c0, m in src:
            mms(b, C - SC, [(m, key, buf[:, c0 + SC:c0 + C])], False, False)
            mms(b, SC, [(m, key, buf[:, c0:c0 + SC])], False, False, C - SC)
        calls = [(PS[b][:, (18 * a - st) % C:(18 * a - st) % C + 18], T.SEL[:, 128 * a:128 * a + 128], T.SC[:, c0:c0 + 18], False, False)
                 for a in range(eighteens(u - 1)) for c0 in ((0, 21) if RIGHT[u - 1] == "a" else (0,))]
        group("SC SCn " + " ".join("SEL%d" % j for j in range(16)), "PS%d" % b, calls[:-1] + [calls[-1][:4] + (True,)])
        either(0, "PS%d" % b, "FL", T.FL[:, :], PS[b][:, 0:C], lambda: s.activation(T.FL[:, :], PS[b][:, 0:C], F.Sign),
               lambda: v.tensor_scalar(T.FL[:, :], PS[b][:, 0:C], 0.5, None, A.is_gt))

    def eighteens(u):
        return (8 * LEVELS[u] + 17) // 18

    def kills(u):
        n = 8 * LEVELS[u - 1]
        tt("KJ0_0 CTL", "CTL", T.CTL[:, 0:n], T.KJ[:, 0:n], T.CTL[:, 0:n], A.max)

    OBK = " ".join("OB%d" % i for i in range(60))
    RBK = " ".join("RB%d" % i for i in range(10))

    def track_flags(u):
        linear("TG0 TG1", "HG", T.HG[:, :], T.TG[:, 0:K1], 1.0 / 40, 129.0 - 19.5 / 40)
        linear("TG0 TG1", "TH", T.TG[:, K1:2 * K1], T.TG[:, 0:K1], 0.5, 1023.75)
        b, b2, b3 = small(), small(), small()
        mm("HG ID", "PS%d" % b3, PS[b3][0:K1, 0:128], T.HG[:, :], T.ID[:, :])
        terms = [("I31", T.TG[:, 0:K1]), ("I1K", T.TG[:, K1:2 * K1]), ("N62", T.TG[:, K1:2 * K1]), ("N20K", T.HG[:, :])]
        group("TG0 TG1 TH HG I31 I1K N62 N20K", "PS%d" % b, [(PS[b][0:K1, 0:128], x, mat(m), m == "I31", m == "N20K") for m, x in terms])
        move(1, "PS%d" % b3, "HT", T.HT[0:K1, :], PS[b3][0:K1, 0:128])
        oa = batch("HT", "OA%d orderF", [(T.OA[0:K1, 128 * (16 + a):128 * (17 + a)], T.HT[0:K1, :], 129.0 + a, None, A.is_equal) for a in range(16)])
        for i in range(5):
            z = T.OF[0:K1, 128 * (20 + i):128 * (21 + i)]
            linear("PS%d" % b, "ZF%d" % i, z, PS[b][0:K1, 0:128], 1.0, 1.0 - 962 * 1024 + 20480 * 129 - 4096 * i - 2048)
            oa += " " + batch("ZF%d" % i, "OF%d_%%d orderF" % i, [(T.OF[0:K1, 128 * (4 * i + k):128 * (4 * i + k + 1)], z, 1024.0 * (k - 2), 1024.0 * (k - 1), A.max, A.min)
                                                          for k in range(4)])
        for q in range(4):
            group(oa + " OAz0 OAz1024", "PS%d" % b2,
                  [(PS[b2][32 * q:32 * q + 16 + (c & 16), 0:20], T.OA[0:K1, 2048 - 128 * (c & 16) + c:4096:128], T.OF[0:K1, c:2560:128],
                    c % 32 == 31, c % 32 == 0) for c in range(32 * q + 31, 32 * q - 1, -1)])
        linear("PS%d" % b2, "SJf", T.SJ[:, 72:92], PS[b2][:, 0:20], 1.0, 2.0 ** 23)
        kf = batch("SJf", "KF%d", [(T.SJ[:, 92 + e:132:2], T.SJ[:, 72:92], 31 << 5 * e, None, A.bitwise_and) for e in range(2)])
        tt(kf + " FA", "FB", T.FB[:, :], T.SJ[:, 92:132], T.FA[:, :], A.is_lt)

    def turned(b, c0, k0, k1, terms, last=None, half=None):
        calls = []
        if half == 0 and k0 >= 128:
            calls.append((PS[b][:, c0:c0 + 32], T.Z16[:, 0:128], T.Z16[:, 0:32], True, False))
        for q in range(4 if k0 >= 128 else 1):
            for i, (m, x, a, e) in enumerate(terms if half != 1 else ()):
                stop = last is None and i == len(terms) - 1
                if k0 < 128:
                    calls.append((PS[b][a:e, c0:c0 + 128], x, mat(m), i == 0, stop))
                else:
                    calls.append((PS[b][32 * q:32 * q + 32, c0:c0 + 32], x, mat(m, q, 4), i == 0 and half is None, stop))
            js = range(16) if k0 < 128 else range(q, 16, 4)
            for j in js if last and half != 0 else ():
                out = PS[b][k0:k1, c0 + j:c0 + 128:16] if k0 < 128 else PS[b][32 * q:32 * q + 32, c0 + j // 4:c0 + 32:4]
                calls.append((out, col(last[0], j, k0, k1), T.ZE[:, last[1] + 15:last[1] + 143:16], not terms, j == js[-1] or not terms))
        return calls

    def camera_rows(u):
        nb, b, b2 = LEVELS[u], small(), small()
        zk = " ZK0 ZK1 ZK2 ZK3 ZK4"
        group(keys("PG", 0, 128) + zk, "PS%d" % b, [(PS[b][:, j:384:16], col("PG", j, 0, 128), T.ZK[:, 0:24], True, True) for j in range(16)])
        group(keys("PG", 128, K2) + zk, "PS%d" % b, [(PS[b][32 * (j % 4):32 * (j % 4) + 32, 384 + j // 4:480:4], col("PG", j, 128, K2), T.ZK[:, 16:40], True, True)
                                                     for j in range(16)])
        move(1, "PS%d" % b, "AB", T.AB[:, 0:256], PS[b][:, 0:256])
        move(1, "PS%d" % b, "ABb", T.AB[:, 256:320], PS[b][:, 416:480])
        if RIGHT[u] == "a":
            if u == 0 or RIGHT[u - 1] != "a":
                fill("RB8", T.RB[:, 0:K2], 1.0)
                fill("RB9", T.RB[:, 18 * K2:19 * K2], -1.0)
            batch("AB ABb", "RB%d", [(T.RB[:, K2 * x:K2 * x + K2], T.AB[:, 128:288], F.Sign, 0.5 - x) for x in range(1, 18)], "a")
        else:
            batch("AB ABb", "RB%d RB8", [(T.RB[:, K2 * x:K2 * x + K2], T.AB[:, 128:288], float(x), None, A.is_equal) for x in range(18)])
        group("MO I116", "PS%d" % b2, turned(b2, 0, 0, 128, [("I116", T.MO[:, 0:128], 0, 128)]) + turned(b2, 128, 128, K2, [("I116", T.MO[:, 128:K2], 128, K2)]))
        if u == RO - 1:
            ts("AB", "MT", T.MT[:, 0:128], T.AB[:, 0:128], 0.5, A.is_equal)
            ts("ABb", "MTb", T.MT[:, 128:K2], T.AB[:, 288:320], 0.5, A.is_equal)
            tt("PS%d MT MTb" % b2, "MT MTb", T.MT[:, :], PS[b2][:, 0:K2], T.MT[:, :], A.min)
            fill(OBK, T.OB[:, 0:16 * K2], 0.0)
            return
        move(1, "PS%d" % b2, "MT", T.MT[:, :], PS[b2][:, 0:K2])
        nv, z0 = PIECES[0][0], PS[b][:, 256:416]
        if nv:
            linear("PS%d" % b, "ZT0", T.ZT[:, 0:K2], z0, 1.0, -256.0 * 7)
            batch("ZT0", "OB%d", [(T.OB[:, K2 * x:K2 * x + K2], T.ZT[:, 0:K2], 256.0 * (x - 7), 256.0 * (x - 6), A.max, A.min) for x in range(nv)])
        for i, (x0, n) in enumerate(PIECES):
            if x0 < nb:
                z = T.ZT[:, K2 * i + K2:K2 * i + 2 * K2]
                act("PS%d" % b, "ZT%d" % (i + 1), z, z0, F.Relu, scale=-1.0, bias=256.0 * (x0 + n))
                batch("ZT%d" % (i + 1), "OB%d%%d" % (i + 1), [(T.OB[:, K2 * x:K2 * x + K2], z, F.Relu, 256.0 * (x0 + n - x), -1.0) for x in range(x0, x0 + n)], "a")

    def columns(a):
        return [(c, c // 16 if c < 128 else (c - 128) // 4) for c in range(a, a + 32)]

    def port_rows(u, b, c0, n):
        nb, key, last = LEVELS[u], "0_%d" % c0, u == RO - 1
        tt("PS%d MT" % b, "JT" + key, T.JT[:, c0:c0 + n], PS[b][:, c0:c0 + n], T.MT[:, c0:c0 + n], A.min)
        if last:
            nb, by = 16, living[0]
            tt("PS%d AB ABb" % b, "JA" + key, T.JA[:, c0:c0 + n], PS[b][:, c0:c0 + n], T.AB[:, 288:320] if c0 else T.AB[:, 0:128], A.min)
            rows = " " + batch("JA%s OB0" % key, "LB" + key + "_%d", [(T.OB[:, K2 * (16 + a) + c0:K2 * (16 + a) + c0 + n], T.JA[:, c0:c0 + n], (a + 1.0) / 32, -1.0, A.is_equal, A.mult)
                                                                      for a in range(16)])
            for a in range(c0, c0 + n, 32):
                group(RBK + " OB0" + rows, "PS%d" % by, [(PS[by][32 * (x // 2):32 * (x // 2) + 16 * (x % 2) + 16, 0:18], T.OB[:, 16 * K2 * (1 - x % 2) + c:32 * K2:K2],
                                                          T.RB[:, c:18 * K2:K2], False, False) for c, x in columns(a)])
        q = ROWS[u][c0 // 128]
        if u == 0 or q != ROWS[u - 1][c0 // 128]:
            fill("OMz" + key, T.OM[:, 16 * K2 + c0:16 * K2 + c0 + n], -1.0 * (q == "a"))
        rows = " OMz%s " % key + batch("JT" + key, "OM" + key + "_%d", [
            (T.OM[:, K2 * a + c0:K2 * a + c0 + n], T.JT[:, c0:c0 + n]) +
            (((a + 0.5) / 16, 2.0, A.is_gt, A.mult) if q == "v" else (F.Sign, -(a + 0.5) / 16)) for a in range(16)], q)
        for a in range(c0, c0 + n, 32):
            group((RBK if last else OBK) + " Z16" + rows, "PSM", [(T.PSM[0:nb, :, :], T.Z16[:, 0:nb], T.Z16[:, 0:136], True, False)] * (a == 0) +
                  [(T.PSM[0:nb, x, :], T.RB[:, 2 * K2 + c:18 * K2:K2] if last else T.OB[:, c:K2 * nb:K2], T.OM[:, c:17 * K2:K2], False, c == K2 - 1)
                   for c, x in columns(a)])

    living = []

    def standing(bs):
        b, by, st = small(), small(), SC * (RO - 1)
        living.append(by)
        ts("CTL", "JK0", T.JK[:, 0:C], T.CTL[:, 0:C], XN - 0.5, A.is_lt)
        group("JK0 ZE", "PS%d" % by, [(PS[by][:, 0:18], E(a), T.JK[:, 18 * a:18 * a + 18], a == 0, False) for a in range(16)])
        mms(b, C, [("ID", "FL", T.FL[:, :]), ("ID", "QC QC0", T.QC[:, 15:15 + C])])
        relu("PS%d" % b, "LF", T.LF[:, :], PS[b][:, 0:C], -float(K1))
        group("LF ZE", "PS%d" % bs, [(PS[bs][:, 0:18], E(a), T.LF[:, (18 * a - st) % C:(18 * a - st) % C + 18], a == 0, False) for a in range(16)])

    def marks(u):
        nb, b2 = LEVELS[u], small()
        for x in (0, 1):
            move(1, "PSM", "SM%d" % x, T.SM[0:nb, 128 * x:128 * x + 128], T.PSM[0:nb, :, x:x + 16])
        group("SM0 SM1 DF", "PS%d" % b2, [(PS[b2][:, 0:nb], T.SM[0:nb, 128 * x:128 * x + 128], T.DF[0:nb, 36 * x:36 * x + nb], x == 0, x == 1) for x in (0, 1)])
        linear("PS%d" % b2, "SJ0", T.SJ[:, 0:nb], PS[b2][:, 0:nb], 2048.0, 0.0)
        batch("SJ0", "KJ0_%d", [(T.KJ[:, r:8 * nb:8], T.SJ[:, 0:nb], 2048 << r, None, A.bitwise_and) for r in range(8)])

    def change_rows(u, b, c0, n, bs):
        na, w, j0, key = eighteens(u), 18 + (RIGHT[u] == "a"), K2 + c0, "1_%d" % c0
        tt("PS%d AB ABb" % b, "JT" + key, T.JT[:, j0:j0 + n], PS[b][:, c0:c0 + n], T.AB[:, 288:320] if c0 else T.AB[:, 0:128], A.min)
        rows = " LAz " + batch("JT" + key, "LA" + key + "_%d", [(T.LA[:, K2 * (16 + a) + c0:K2 * (16 + a) + c0 + n], T.JT[:, j0:j0 + n], (a + 1.0) / 32, None, A.is_equal)
                                                               for a in range(na)])
        for a in range(c0, c0 + n, 32):
            group(RBK + " Z16" + rows, "PS%d" % bs, [(PS[bs][:, 0:w], T.Z16[:, 0:128], T.Z16[:, 0:w], True, False)] * (a == 0 and u < RO - 1) +
                  [(PS[bs][32 * (x // 2):32 * (x // 2) + 16 * (x % 2) + na, 0:w], T.LA[:, 16 * K2 * (1 - x % 2) + c:K2 * (16 + na):K2], T.RB[:, c:w * K2:K2],
                    False, c >= 128 and c % 8 == 7) for c, x in columns(a)])
        if c0 and u == RO - 1:
            either(1, "PS%d" % bs, "SC", T.SC[:, 0:w], PS[bs][:, 0:w], lambda: s.activation(T.SC[:, 0:w], PS[bs][:, 0:w], F.Sign),
                   lambda: v.tensor_scalar(T.SC[:, 0:w], PS[bs][:, 0:w], 0.5, None, A.is_gt))
        elif c0:
            move(1, "PS%d" % bs, "SC", T.SC[:, 0:w], PS[bs][:, 0:w])
            if RIGHT[u] == "a":
                linear("PS%d" % bs, "SCn", T.SC[:, 20:20 + w], PS[bs][:, 0:w], -1.0, 0.0)

    def camera_list(u):
        st, (s0, ns), (lo, hi, wrap) = SC * u, SURE[u], listed(u)
        w, n = (K1 - ns) // 16, hi - lo - ns
        scan("FL CAP", "QC", T.QC[:, 16:16 + C], T.FL[:, :], T.CAP[:, :], 0.0, A.add, A.min)
        qa, qn = T.QC[:, 15 + C - st:16 + C - st], T.QC[:, 15 + C:16 + C]
        a = s0 - lo
        if wrap:
            ts("QC", "NP", T.NP[:, 0:st], T.QC[:, 16 + C - st:16 + C], qa, A.subtract)
            ts("QC", "NPb", T.NP[:, st:a], T.QC[:, 16:16 + a - st], qn, A.add, qa, A.subtract)
            if ns:
                ts("QC", "W3", T.W3[:, 0:1], qn, qa, A.subtract, -float(ns), A.add)
                ts("QC W3", "NPc", T.NP[:, a:n], T.QC[:, 16 + s0 + ns - st:16 + C - st], T.W3[:, 0:1], A.add)
        else:
            cp("QC", "NPb", T.NP[:, 0:a], T.QC[:, 16:16 + a])
            ts("QC", "NPc", T.NP[:, a:n], T.QC[:, 16 + a + ns:16 + n + ns], -float(ns), A.add)
        vc = VC[u]
        for m in range(vc, w):
            act("NP NPb NPc TH5", "ACC%d JK%d" % (m, m), T.JK[:, C * m:C * m + n - 16 * m], T.NP[:, 16 * m:n], F.Sign, bias=T.TH5[:, m:m + 1], scale=-1.0, accum_out=T.ACC[:, m:m + 1])
        off, offk = T.OFF[:, 8 * u:8 * u + w], "OFFa%d OFFb%d" % (u, u)
        if wrap:
            ts("QC OO", "W1", T.W1[:, 0:w], T.OO[:, 0:w], float(ns), A.add, qn, A.is_ge)
            tt("W1 DM", "W1", T.W1[:, 0:w], T.W1[:, 0:w], T.DM[:, 0:w], A.mult)
            tt("W1 " + offk, "W1", T.W1[:, 0:w], T.W1[:, 0:w], off, A.add)
            off, offk = T.W1[:, 0:w], "W1"
        if ns:
            ts("NPb OO", "W1b", T.W1[:, 8:8 + w], T.OO[:, 0:w], T.NP[:, a - 1:a], A.is_ge, 2.0 * ns, A.mult)
            tt("W1b " + offk, "W1", T.W1[:, 0:w], T.W1[:, 8:8 + w], off, A.add)
        for m in range(vc):
            ts("NP NPb NPc TH5", "JK%d" % m, T.JK[:, C * m:C * m + n], T.NP[:, 0:n], T.TH5[:, m:m + 1], A.is_le, 2.0, A.mult)
            red("JK%d" % m, "ACC%d" % m, T.ACC[:, m:m + 1], T.JK[:, C * m + 16 * m:C * m + n])
        tt("W1 " + " ".join("ACC%d" % m for m in range(w)), "W2", T.W2[:, 0:w], T.W1[:, 0:w], T.ACC[:, 0:w], A.add)
        linear("W2", "WL", T.WL[:, 0:w], T.W2[:, 0:w], 0.5, 0.0)

    def finals(ch, nk):
        sb = sbuf(ch)
        return sb + "n " + " ".join("%s%d " % (sb, k) + part(sb, k, 0, 64 if k < 6 else nk) for k in range(7)), T[sb][:, 0:6 * SW + 16 + 16 * nk]

    def passes(name, ch, k0, n):
        sb, h = sbuf(ch), n // 2 if n >= HALVES else n
        for k in range(8):
            a, b = (k + 5) % 7, (k + 6) % 7
            for i in range(0, n, h):
                d1 = T.CP[:, 0:16 * h] if k == 0 else T[sb][:, a * SW + 15 + 16 * i:a * SW + 15 + 16 * (i + h)]
                rd = " CP" if k == 0 else " %s%d " % (sb, a) + part(sb, a, max(i - 1, 0), i + h)
                scan(keys(name, k0 + i, k0 + i + h) + rd, part(sb, b, i, i + h), T[sb][:, b * SW + 16 + 16 * i:b * SW + 16 + 16 * (i + h)],
                     seg(name, k0 + i, k0 + i + h), d1, 1024.0, A.min, A.max)

    def pick_places(chunks, fn, plus):
        k0, k1 = chunks[0][0], chunks[-1][0] + chunks[-1][1]
        k2 = k1 - (16 if times(chunks[-1][1]) == 4 else 0)
        b, b2, w, w2, w4 = small(), small(), (k1 - k0) // 4, (k2 - k0) // 8, (k1 - k2) // 4
        group(keys("UH", k0, k1) + " ZE", "PS%d" % b, [(PS[b][:, 0:w], E(j), T.UH[:, k0 + j:k1:4], j == 0, j == 3) for j in range(4)])
        linear("PS%d" % b, "KB", T.KB[:, 0:w], PS[b][:, 0:w], 0.25, 128.25 + 4 * plus)
        mms(b2, w2 + w4, [("ID", "FN%d" % fn, T.FN[:, fn + k0 // 8:fn + k0 // 8 + w2 + w4])], True, False)
        calls = [(PS[b2][:, 0:w2], T.SH[:, 8 - 8 * i:136 - 8 * i], T.KB[:, i:2 * w2:2], False, False) for i in range(2 if w2 else 0)]
        calls += [(PS[b2][:, w2:w2 + w4], T.SH[:, 136:264], T.KB[:, 2 * w2:w], False, False)] * (w4 > 0)
        group("KB SH SHz SH4", "PS%d" % b2, calls[:-1] + [calls[-1][:4] + (True,)])
        if w2:
            relu("PS%d SFu" % b2, keys("PU", k0, k2), T.PU[:, k0 // 8:k2 // 8], PS[b2][:, 0:w2], T.SF[:, 16:17])
        if w4:
            relu("PS%d SFu" % b2, keys("PU", k2, k1), T.PU[:, k2 // 8:k2 // 8 + w4], PS[b2][:, w2:w2 + w4], T.SF[:, 17:18])

    def median(ch, k0, nk, last=False):
        rd, win = (part(sbuf(ch), 6, 0, nk), T[sbuf(ch)][:, 6 * SW + 16:6 * SW + 16 + 16 * nk]) if last else finals(ch, nk)
        return rd + " " + keys("PU", k0, k0 + nk), ind(win, T.PU[:, k0 // 8:k0 // 8 + times(nk) * nk // 16])

    def wide(ch, k0, nk, m, src, m2="ID"):
        for a in range(k0, k0 + nk, 32):
            e = min(k0 + nk, a + 32)
            b, n, w = nextbank(), 16 * (e - a), 16 // times(nk)
            mms(b, n, [(m,) + src(a, e)], True, False)
            group("PC%d %s" % (ch, m2), "PS%d" % b, [(PS[b][:, j:n:w], mat(m2), T.PC[:, 2 * a:2 * a + 64], False, j == w - 1) for j in range(w)])
            yield a, e, b

    def near(name, src, ch, k0, nk, fused):
        lack = []
        for a, e, b in wide(ch, k0, nk, "NW" if fused else "NI", lambda a, e: (keys(src, a, e), seg(src, a, e)), "IW" if fused else "ID"):
            if fused:
                ts("PS%d" % b, keys(name, a, e), seg(name, a, e), PS[b][:, 0:16 * (e - a)], ROUND, A.add, ROUND, A.is_equal)
                continue
            act("PS%d" % b, keys(name, a, e), seg(name, a, e), PS[b][:, 0:16 * (e - a)], F.Abs)
            if under(keys(name, a, e), keys(name, a, e), seg(name, a, e), seg(name, a, e), 12.5):
                lack.append((a - k0, e - k0))
        return lack

    def port_places(c0, n, more):
        b = small()
        relu("CTL", "DEAD", T.DEAD[:, 0:n], T.CTL[:, c0:c0 + n], 1.0 - XN)
        mms(b, n, [("NBG", "DEAD", T.DEAD[:, 0:n]), ("P0X", "PTR", T.PTR[:, c0:c0 + n])], True, not more)
        if more:
            group("SM0 SM1 DL0 DL1", "PS%d" % b, [(PS[b][:, 0:n], T.SM[0:16, 128 * x:128 * x + 128], T.DL[0:16, 16 * x:16 * x + 16], False, x == 1) for x in (0, 1)])
        relu("PS%d SFd" % b, "GU", T.GU[:, 0:n], PS[b][:, 0:n], T.SF[:, 21:22])

    def track_list(u):
        b = small()
        scan("FB NG", "PP", T.PP[:, :], T.FB[:, :], T.NG[:, :], 0.0, A.add, A.add)
        tt("FB KIU%d" % u, "B1", T.B1[:, :], T.FB[:, :], T.KIU[:, 40 * u:40 * u + 40], A.mult)
        mm("PP TRI%d" % u, "PS%d" % b, PS[b][:, 0:2], T.TRI[:, 128 * u:128 * u + 128], T.PP[:, 38:40])
        tt("PP B1", "B1", T.B1[:, :], T.B1[:, :], T.PP[:, :], A.subtract)
        ts("B1 PS%d" % b, "BU", T.BU[:, :], T.B1[:, :], PS[b][:, 1:2], A.subtract, -1.0, A.add)
        ts("PP PS%d" % b, "B2", T.B2[:, :], T.PP[:, :], PS[b][:, 1:2], A.add, -K2 - 0.5, A.is_gt)
        tt("B2 FB", "FA", T.FA[:, :], T.B2[:, :], T.FB[:, :], A.max)
        move(ON["LW"], "BU TID", "LW", ind(T.LW[:, :], T.BU[:, :]), T.TID[:, :], F.Silu)
        move(1, "LW", "LH", T.LH[:, :], T.LW[:, 0:K2])
        b = small()
        fold(b, "LH", 0, 10, "LH", z=ZP)
        linear("PS%d" % b, "TL", T.TL[:, 0:10], PS[b][:, 0:10], 1.0 / 16, -64.0)
        move(1, "TL TC TCx", "CU", T.CU[:, :], ind(T.TC[:, :], T.TL[:, 0:10]))

    def groups(chunks, ends):
        return [chunks[a:e] for a, e in zip((0,) + tuple(ends[:-1]), ends)]

    for u in range(RO):
        lb = 400 + 1792 * u
        s0, ns = SURE[u]
        ch1 = spans(CH1[u])
        both = [(0, ns, lambda buf: buf[:, s0:s0 + ns], ""), (ns, K1, lambda buf: ind(buf[:, :], T.WL[:, 0:(K1 - ns) // 16]), " WL")]
        both = [p for p in both if p[1] > p[0]]
        parts = [(a, min(a + 32, K1)) for a in range(0, K1, 32)]
        lv, uh1 = [0] * K1, [0] * K2

        def obs(a, e):
            return ("O0 O1" if u else "O0", seg("O", a, e, s0)) if e <= ns else (keys("OG", a, e), seg("OG", a, e))
        if ns < K1:
            move(1, "OO WL", "OU", T.OU[:, ns:K1], both[-1][2](T.OO))
            for a, e in parts:
                if a >= ns:
                    move(ON["OG"][a // 32], "O0 O1 OU", keys("OG", a, e), seg("OG", a, e), ind(T.O[:, :], T.OU[:, a:e]))
        for a, e, tab, wl in both:
            ts("CTL WL" if wl else "CTLs", keys("XO", a, e), T.XO[:, a:e], tab(T.CTL), float(XN), A.min)
            move(1, "CTO CTOx" + wl, "TG1" if wl else "TG0", T.TG[:, a:e], tab(T.CTO))
            if wl:
                move(1, "CTL WL", "XF", T.XF[:, a:e], tab(T.CTL))
            lv[a:e] = [under("XF" if wl else "CTLs", keys("LV", a, e), T.LV[:, a:e], T.XF[:, a:e] if wl else tab(T.CTL), XN - 0.5)] * (e - a)
        if u == 0:
            constants()
            constants2()
            constants3()
        if u:
            fill("LW", T.LW[:, 0:K2], 704, 1)
        else:
            op("a", "RQ", "LW", 1.45, lambda: s.activation(T.LW[:, 0:128], T.RQ[:, :], F.Silu, bias=704.0))
            act("RQ", "LW", T.LW[:, 128:K2], T.RQ[:, 0:32], F.Silu, bias=832.0)
        for a, e, tab, wl in both:
            if wl:
                tt("PTD ST WL", "PN", T.PN[:, a:e], tab(T.ST), T.PTD[:, K1 * u + a:K1 * u + e], A.add)
                cp("PN WL", "PTR", tab(T.PTR), T.PN[:, a:e])
            else:
                tt("PTD ST", "PTR", tab(T.PTR), tab(T.ST), T.PTD[:, K1 * u + a:K1 * u + e], A.add)
        if u:
            port_places(0, 24, False)
        track_flags(u)
        for a, e in parts:
            if a >= XA[u]:
                b, x = small(), seg("BG", a, e)
                move(2, "X Xb Xd Xn XG " + keys("XO", a, e), keys("BG", a, e) + " " + keys("XR", a, e), x, ind(T.X[:, :], T.XO[:, a:e]))
                mms(b, 16 * (e - a), [("NI",) + obs(a, e), ("ID", keys("BG", a, e), x)])
                move(1, "PS%d" % b, keys("D", a, e), seg("D", a, e), PS[b][:, 0:16 * (e - a)])
                continue
            tt("X Xb Xd Xn XG " + keys("XO", a, e) + " " + obs(a, e)[0], keys("D", a, e) + " " + keys("XR", a, e) + " orderF" * (a >= FIRST[u]), seg("D", a, e),
               ind(T.X[:, :], T.XO[:, a:e]), obs(a, e)[1], A.subtract)
        for grp in groups(ch1, UG1[u]):
            if u == 0:
                fill(keys("UH", 0, K1), T.UH[:, 0:K1], 2.0)
                ts("FN0 SFu", keys("PU", 0, K1 - 16), T.PU[:, 0:12], T.FN[:, 0:12], T.SF[:, 16:17], A.add, 130.0 * SW - 16, A.add)
                ts("FN0 SFu", keys("PU", K1 - 16, K1), T.PU[:, 12:16], T.FN[:, 12:16], T.SF[:, 17:18], A.add, 130.0 * SW - 16, A.add)
                break
            a, e, b = grp[0][0], grp[-1][0] + grp[-1][1], small()
            fold(b, "D", a, e)
            uh1[a:e] = [under("PS%d" % b, keys("UH", a, e), T.UH[:, a:e], PS[b][:, 0:e - a], 4088.0)] * (e - a)
            pick_places(grp, 20 * fn_of(u), uh1[a])
        track_list(u)
        for a in range(0, K2, 32):
            move(ON["PG"][a // 32], "PTR CU", keys("PG", a, a + 32), seg("PG", a, a + 32), ind(T.PTR[:, :], T.CU[:, a:a + 32]))
        linear("LO LOx TL", "MO", T.MO[:, :], ind(T.LO[:, :], T.TL[:, 0:10]), 1.0, 1.0)
        logk = "LOGn"
        border = 0 if u and not listed(u)[2] else (ns if u else 0) + 24

        def send_b(end):
            if u == 0:
                exchange(1, "LOG0_0", T.LOG, lb, " " + keys("XR", 0, K1))
                return
            move(ON["SG"], logk + " GU", "SG", T.SG[:, :], ind(T.LOG[:, 384:lb + 16 * end], T.GU[:, 0:24]))
            exchange(2 * u + 1, "SG", T.SG, 0, " " + keys("XR", 0, K1))
        if not border:
            send_b(0)
        for ch, (k0, nk) in enumerate(ch1):
            r, k1 = slice(k0, k0 + nk), k0 + nk
            passes("D", ch, k0, nk)
            mk, med = median(ch, k0, nk, u == 0)
            move(ON["PC1"], mk, "PC%d" % ch, T.PC[:, 2 * k0:2 * k0 + times(nk) * nk], med)
            lack = near("D", "D", ch, k0, nk, FUSE1[u][ch])
            clips = {}
            for a, e, b in wide(ch, k0, nk, "ID", obs):
                clips[a] = upper("PS%d" % b, keys("OG", a, e), seg("OG", a, e), PS[b][:, 0:16 * (e - a)])
            b, uh = small(), keys("UH", k0, k1)
            opening(b, nk, [("I50", uh, T.UH[:, r])], lack, "I16")
            fold(b, "D", k0, k1, st=False, z=ZE2 * FUSE1[u][ch])
            fit = under("PS%d" % b, "FIT%d" % ch, T.FIT[:, r], PS[b][:, 0:nk], 123.0 - 50 * uh1[k0], -1.0)
            b, b2 = small(), small()
            group("Z16 ID I50 N50 R50 RN50 " + keys("LV", k0, k1) + " " + uh, "PS%d" % b, [(PS[b][:, 0:2 * nk], T.ID[:, :], T.Z16[:, 0:2 * nk], True, False)] +
                  [(PS[b][:, i:2 * nk:2], mat(m), x, False, False) for i, m, x in ((0, "I50", T.LV[:, r]), (0, "N50", T.UH[:, r]), (1, "R50", T.LV[:, r]), (1, "RN50", T.UH[:, r]))])
            group("FIT%d IB RIB" % ch, "PS%d" % b, [(PS[b][:, i:2 * nk:2], mat(m), T.FIT[:, r], False, i == 1) for i, m in enumerate(("IB", "RIB"))])
            none = under("PS%d" % b, "NONE%d" % ch, T.NONE[:, 2 * k0:2 * k1], PS[b][:, 0:2 * nk], 111.0 - 50 * lv[k0] + 50 * uh1[k0] - 66 * fit)
            mms(b2, nk, [("I50", uh, T.UH[:, r])], True, False)
            mms(b2, nk, [("NB", "FIT%d" % ch, T.FIT[:, r])], False, True)
            dies("PS%d" % b2, keys("DIE", k0, k1), T.DIE[:, r], PS[b2][:, 0:nk], 111.0 - 50 * uh1[k0] + 34 * fit)
            for a in range(k0, k1, 32):
                e = min(k1, a + 32)
                b, n, clip, key = nextbank(), 16 * (e - a), clips[a], "LOG%d_%d" % (u, a)
                mms(b, n, [("NI" if clip else "ID", keys("OG", a, e) + " NI ID", seg("OG", a, e))], True, False)
                group("NONE%d " % ch + " ".join("SEL%d" % j for j in range(8)), "PS%d" % b,
                      [(PS[b][:, j:n:8], T.SEL[:, 128 * j:128 * j + 128], T.NONE[:, 2 * a:2 * e], False, j == 7) for j in range(8)])
                logk += " " + key
                relu("PS%d" % b, key, T.LOG[:, lb + 16 * a:lb + 16 * e], PS[b][:, 0:n], 255.0 * clip + 512.0 * none)
            if k0 < border <= k1:
                send_b(k1)
        for a, e, tab, wl in both:
            tt(keys("DIE", a, e) + (" XF WL" if wl else " CTL"), "CTL CTLs", tab(T.CTL), T.DIE[:, a:e], T.XF[:, a:e] if wl else tab(T.CTL), A.max)
        ch2 = spans(CH2)
        for grp in groups(ch2, IG2):
            a, e, b = grp[0][0], grp[-1][0] + grp[-1][1], small()
            mms(b, e - a, [("ID", "MO", T.MO[:, a:e])], True, False)
            fold(b, "PG", a, e, st=False, z=ZP)
            linear("PS%d" % b, keys("IU", a, e), T.IU[:, a:e], PS[b][:, 0:e - a], 1.0, 4095.0)
        camera_rows(u)
        bc, br, bs, ones = small(), small(), small(), []
        if u == RO - 1:
            standing(bs)
        win, wk = T.LOG[:, 0:lb + 1792], logk + " LG"
        for a in range(0, K2, 32):
            move(ON["BG"][a // 32], wk + " " + keys("IU", a, a + 32), keys("BG", a, a + 32), seg("BG", a, a + 32), ind(win, T.IU[:, a:a + 32]))
        move(ON["XOLD"], "X Xb Xd TL", "XOLD", T.XOLD[:, 0:K2], ind(T.X[:, 0:800], T.TL[:, 0:10]))
        for grp in groups(ch2, UG2):
            a, e, b = grp[0][0], grp[-1][0] + grp[-1][1], small()
            fold(b, "BG", a, e)
            uh1[a:e] = [under("PS%d" % b, keys("UH", a, e), T.UH[:, a:e], PS[b][:, 0:e - a], 10000.0)] * (e - a)
            pick_places(grp, 20 * RO, uh1[a])
            b = small()
            mms(b, e - a, [("BO", keys("UH", a, e), T.UH[:, a:e])])
            below("PS%d" % b, keys("NH", a, e), T.NH[:, a:e], PS[b][:, 0:e - a], 5.0 - 16 * uh1[a])
        for ch, (k0, nk) in enumerate(ch2):
            r, k1 = slice(k0, k0 + nk), k0 + nk
            passes("BG", ch, k0, nk)
            mk, med = median(ch, k0, nk)
            move(ON["PC2"], mk, "PC%d" % ch, T.PC[:, 2 * k0:2 * k1], med)
            ne = T.NE[:, k0 // 128 * 128:k1]
            if DIFF[ch] == 1:
                b = small()
                mms(b, nk, [("NI", "XOLD", T.XOLD[:, r]), ("ID", "PC%d" % ch, T.PC[:, 2 * k0:2 * k1:2])])
                act("PS%d" % b, "NE%d" % ch, T.NE[:, r], PS[b][:, 0:nk], F.Abs)
            elif DIFF[ch] == 2:
                tt("PC%d XOLD" % ch, "NE%d" % ch, T.NE[:, r], T.PC[:, 2 * k0:2 * k1:2], T.XOLD[:, r], A.not_equal)
            else:
                for i in range(2):
                    move(1, "XOLD", "XO2_%d" % i, T.XOLD[:, K2 + i:K2 + 2 * nk:2], T.XOLD[:, r])
                tt(mk + " XO2_0 XO2_1", "NE%d" % ch, T.NE[:, k0:k0 + 2 * nk], med, T.XOLD[:, K2:K2 + 2 * nk], A.not_equal)
                ne = T.NE[:, k0:k0 + 2 * nk:2]
            c0, zs = k0 // 128 * 128, ZS2 if FUSE2[ch] else 144
            if k0 == 128:
                bc = small()
            if k1 in (128, K2):
                group(" ".join("NE%d" % i for i in range(ch + 1)) + " BO", "PS%d" % bc, turned(bc, c0, c0, k1, [("BO", ne, c0, k1)]))
                change_rows(u, bc, c0, k1 - c0, bs)
            lack = near("PG", "BG", ch, k0, nk, FUSE2[ch])
            ones = ones * (k0 != c0) + [("I23", T.ONB[:, 0:nk], k0, k1)] * uh1[k0] + [("N18", T.ONB[:, 0:e - a], k0 + a, k0 + e) for a, e in lack]
            if k0 == 128 and SPLIT:
                br = small()
            if k1 in (128, K2):
                group(keys("UH", c0, k1) + " " + keys("NH", c0, k1) + " I23 N19 N18 ONB Z16", "PS%d" % br,
                      turned(br, c0, c0, k1, [("I23", T.UH[:, c0:k1], c0, k1), ("N19", T.NH[:, c0:k1], c0, k1)] + ones, ("PG", zs), 0) )
                group("ZS ZS2 " + keys("PG", c0, k1), "PS%d" % br, turned(br, c0, c0, k1, [0], ("PG", zs), 1))
            if k1 == K2 or k1 == 128 and SPLIT:
                port_rows(u, br, c0 * SPLIT, k1 - c0 * SPLIT)
            if k1 == K2:
                if u < RO - 1:
                    marks(u)
                b = small()
                mm("JT0_0 JA0_0 ID", "PS%d" % b, PS[b][:, 0:128], (T.JT if u < RO - 1 else T.JA)[:, 0:128], T.ID[:, :])
                group(keys("UH", k0, k1) + " " + keys("NH", k0, k1) + " I23 N19 N18 ONB", "PS%d" % b,
                      [(PS[b][:, a:e], mat(m), x, i == 0, False) for i, (m, x, a, e) in enumerate([("I23", T.UH[:, r], k0, k1), ("N19", T.NH[:, r], k0, k1)] + ones)])
                fold(b, "PG", k0, k1, st=False, z=zs, c0=k0)
                if u < RO - 1:
                    ts("PS%d" % b, "P0", T.P0[:, :], PS[b][:, 0:K2], 0.0, A.is_gt, float(EC), A.mult)
                else:
                    ts("PS%d" % b, "MO", T.MO[:, :], PS[b][:, 0:K2], 0.0, A.is_le)

        def every(name):
            return " ".join("%s%d" % (name, ch) for ch in range(len(CH2)))
        cp(every("PC") + " TL", "X Xb Xd", ind(T.X[:, 0:800], T.TL[:, 0:10]), T.PC[:, 0:2 * K2:2])
        if u < RO - 1:
            exchange(2 * u + 2, "Xb", T.X)
        else:
            store("s", "X Xb", T.yx, T.X, 640, 160)
        if u < RO - 1:
            linear("CU", "CF", T.CF[:, :], T.CU[:, :], 1.0, 0.0)
            tt("P0 CF TL", "TC TCx", ind(T.TC[:, :], T.TL[:, 0:10]), T.P0[:, :], T.CF[:, :], A.max)
        else:
            b = small()
            ts("TC TCx", "FS", T.FS[:, :], T.TC[:, :], EC - 0.5, A.is_lt)
            ts("CU", "JW", T.JW[:, :], T.CU[:, :], EC - 0.5, A.is_lt)
            tt("MO JW TL", "FS", ind(T.FS[:, :], T.TL[:, 0:10]), T.MO[:, :], T.JW[:, :], A.mult)
            ts("FA", "FB", T.FB[:, :], T.FA[:, :], -32.0, A.mult, 32.0, A.add)
            group("FS ZE", "PS%d" % b, [(PS[b][:, 0:40], E(a), T.FS[:, 40 * a:40 * a + 40], a == 0, False) for a in range(16)])
            mms(b, 40, [("ID", "FB", T.FB[:, :])], False, True)
            cp("PS%d" % b, "YT", T.YT[:, :], PS[b][:, 0:40])
            dma("s", "YT", "", [(T.yt[r // 16:(r + n) // 16, :], T.YT[p:p + n, :]) for r, p, n in runs()], 20)
        if u < RO - 1:
            kills(u + 1)
            camera_flags(u + 1)
            camera_list(u + 1)
    for x in (0, 1):
        move(1, "PSM", "SM%d" % x, T.SM[0:16, 128 * x:128 * x + 128], T.PSM[0:16, :, x:x + 16])
    port_places(272, 16, True)
    ts(wk + " GU", "SG", T.SG[:, 0:256], ind(T.LOG[:, 384:400 + RO * 1792], T.GU[:, 0:16]), 512.0, A.min)
    store("as", "SG", T.yb, T.SG, 256, 64)
    b = living[0]
    mms(b, 18, [("I32", "SC", T.SC[:, 0:18])], False, True)
    move(1, "PS%d" % b, "YC", T.YC[:, :], PS[b][:, 0:18])
    dma("as", "YC", "", [(T.yc[r // 16:(r + n) // 16, :], T.YC[p:p + n, :]) for r, p, n in runs()], 9)
    emit()
